import numpy as np, ml_dtypes
CORES = [25,29,65,69,153,157,193,197]
N = 8
BF = ml_dtypes.bfloat16
def gentries(a):
    return np.ascontiguousarray(a.reshape(8, 16, -1).transpose(0, 2, 1)).reshape(8, -1)
def gtable(e):
    e = np.asarray(e); return np.ascontiguousarray(e.reshape(8, -1, 16).transpose(0, 2, 1)).reshape(128, -1).astype(np.int32)
W, L, K, CAP, NEED, RO = 2048, 128, 4, 48, 10, 4
def take(a, i):
    return np.take_along_axis(a, i.reshape(N, 8, -1), 2).reshape(i.shape)
def shade(rng, h):
    return np.clip(h[:, :, None, :] + rng.integers(-40, 41, (N, 8, 16, h.shape[2])), 0, 255)
def parts(rng):
    h = rng.integers(0, 256, (N, 8, W)); X = shade(rng, h); A = shade(rng, rng.integers(0, 256, (N, 8, L)))
    F = W // 32; pc = np.argsort(rng.random((N, 8, W)), axis=-1); fam = np.argsort(pc, axis=-1) // 32
    first = take(rng.integers(0, W, (N, 8, F)), fam)[:, :, None, :]; size = take(rng.choice(np.array([6, 12, 24, 96]), (N, 8, F)), fam)[:, :, None, :]
    I = take(np.argsort(h, axis=-1), (first + (rng.random((N, 8, 16, W)) * size).astype(np.int64)) % W)
    I = np.where(rng.random((N, 8, 16, W)) < 0.25, rng.integers(0, W, (N, 8, 16, W)), I)
    O = take(pc, 32 * rng.integers(0, F, (N, 8, 1, W)) + rng.integers(0, 32, (N, 8, K, W)))
    mixed = (rng.random((N, 8, 1, W)) < 0.4) | (rng.random((N, 8, K, W)) < 0.1)
    O = np.where(mixed, rng.integers(0, W, (N, 8, K, W)), O)
    return I, X, O, rng.integers(0, W, (N, 8, L)), A, rng.integers(600, 2000, (N, 8, RO))
def pack(I, X, O, g, A, T):
    return {"icol": np.ascontiguousarray(I.reshape(N, 128, W)).astype(np.int32), "pat": np.ascontiguousarray(X.reshape(N, 128, W)).astype(np.float32).astype(BF),
            "alt": np.ascontiguousarray(O.reshape(N, 8 * K, W)).astype(np.int32), "gate": np.stack([gtable(a) for a in g]),
            "acc0": np.ascontiguousarray(A.reshape(N, 128, L)).astype(np.float32).astype(BF), "th": np.ascontiguousarray(T).astype(np.int32)}
def setup_inputs(rng):
    return pack(*parts(rng))
def setup_inputs_spread(rng):
    I, X, O, g, A, T = parts(rng)
    X = np.minimum((np.exp2(8 * rng.random((N, 8, 1, W))) * rng.random((N, 8, 16, W))).astype(np.int64), 255)
    A = np.minimum((np.exp2(8 * rng.random((N, 8, 1, L))) * rng.random((N, 8, 16, L))).astype(np.int64), 255)
    I = np.minimum((W * rng.random((N, 8, 16, W)) ** rng.choice(np.array([1.0, 2.0, 4.0]), (N, 8, 1, W))).astype(np.int64), W - 1)
    O = np.minimum((W * rng.random((N, 8, K, W)) ** rng.choice(np.array([1.0, 2.0, 4.0]), (N, 8, 1, W))).astype(np.int64), W - 1)
    I[:, 1::2] = W - 1 - I[:, 1::2]; O[:, 2::4] = W - 1 - O[:, 2::4]
    T = np.minimum(np.exp2(5 + 7 * rng.random((N, 8, RO))).astype(np.int64), 4080)
    return pack(I, X, O, g, A, T)
def setup_inputs_ends(rng):
    e = np.array([0, W - 1])
    I = np.where(rng.random((N, 8, 1, W)) < 0.25, rng.integers(0, W, (N, 8, 16, W)), e[rng.integers(0, 2, (N, 8, 16, W))])
    O = np.where(rng.random((N, 8, K, W)) < 0.3, rng.integers(0, W, (N, 8, K, W)), e[rng.integers(0, 2, (N, 8, K, W))])
    g = np.where(rng.random((N, 8, L)) < 0.3, rng.integers(0, W, (N, 8, L)), e[rng.integers(0, 2, (N, 8, L))])
    X = 255 * np.where(rng.random((N, 8, 1, W)) < 0.5, rng.integers(0, 2, (N, 8, 1, W)), rng.integers(0, 2, (N, 8, 16, W)))
    A = 255 * np.where(rng.random((N, 8, 1, L)) < 0.5, rng.integers(0, 2, (N, 8, 1, L)), rng.integers(0, 2, (N, 8, 16, L)))
    T = 4080 * ((np.arange(N)[:, None, None] + np.arange(8)[:, None] + np.arange(RO)) % 2)
    T[:, 2, 1:] = 2040; T[:, 5, 1:] = 1785; T[1:N - 1, 6, 0] = 4079
    T[0, :, 0] = 0; T[N - 1, :, 0] = 4080
    X[..., 0] = 0; X[..., W - 1] = 255; A[..., 0] = 0; A[..., L - 1] = 255; g[..., 0] = 0; g[..., L - 1] = W - 1
    X[0, :, 1, :] = X[0, :, 0, :]; A[0, :, 0, :] = 0; A[0, :, 1, :] = 255
    I[N - 1, :, 15, :] = W - 1
    I[N - 1, :, :15, 0] = 0; I[N - 1, 1::2, 3, 0] = W - 1; I[N - 1, :, 0, W - 1] = W - 1; O[N - 1, :, 0, W - 1] = W - 1
    I[1, :, :, 2] = W - 1
    g[N - 1, :, 1] = 1; O[N - 1, :, :, 1] = 1; I[N - 1, :, 0, 1] = 1
    g[N - 1, :, 2] = W - 2; O[N - 1, :, :, W - 2] = W - 2; I[N - 1, :, 0, W - 2] = W - 2
    return pack(I, X, O, g, A, T)
def setup_inputs_corners(rng):
    I, X, O, g, A, T = parts(rng); h = W // 2; want = (0, 1, CAP - 1, CAP, CAP + 1, L, CAP, 2); c = np.arange(W)
    E = np.zeros((N, W), np.int64); warm = np.zeros((N, 40), np.int64); late = np.full(N, -1)
    for r in range(N):
        for u in range(8):
            n = want[(u + r + 5) % 8]; t0 = (0, 1, 7, 254, 255)[(u + 3 * r) % 5]
            q = rng.permutation(W); hot = q[:40].reshape(2, 20); cold = (q[40:h], q[h:])
            x = rng.integers(100, 256, (16, W)); i = rng.integers(0, 16, W)
            near = np.nonzero(rng.random(W) < 0.5)[0]; x[:, near] = 0; x[i[near], near] = t0; x[(i[near] + 1) % 16, near] = 1
            hs = q[:40]; x[:, hs] = 0; x[i[hs], hs] = t0 * rng.integers(0, 2, 40)
            flip = u % 2 == 1
            X[r, u] = 255 - x if flip else x; A[r, u] = 255 if flip else 0
            e = rng.permutation(W); sa = e[:W // 4]; sb = e[W // 4:h]; dd = e[h:]; sv = np.zeros(W, bool); sv[e[:h]] = True
            cl = rng.integers(0, 2, W); cl[sa] = 0; cl[sb] = 1
            nh = np.where(sv, rng.choice(np.array([NEED, NEED + 1, 16]), W), rng.choice(np.array([0, NEED - 2, NEED - 1]), W))
            rk = (np.arange(16)[:, None] * (2 * rng.integers(0, 8, W) + 1) + rng.integers(0, 16, W)) & 15
            hn = np.where(rk == 0, hot[cl, 0], hot[cl, rng.integers(0, 20, (16, W))])
            cn = np.where(cl == 0, cold[0][rng.integers(0, len(cold[0]), (16, W))], cold[1][rng.integers(0, len(cold[1]), (16, W))])
            I[r, u] = np.where(rk < nh, hn, cn)
            f = np.concatenate([np.array([W - 1, 0]), 1 + rng.permutation(W - 2)]); learn = np.zeros(W, bool); learn[f[:h]] = True
            p1 = rng.integers(0, K, W); p2 = (p1 + 1 + rng.integers(0, K - 1, W)) % K; way = rng.random(W)
            o = dd[rng.integers(0, h, (K, W))]
            one = learn & (way < 0.5); o[p1[one], c[one]] = e[rng.integers(0, h, W)][one]
            own = one & sv & (rng.random(W) < 0.3); o[p1[own], c[own]] = c[own]
            two = learn & (way >= 0.5); o[p1[two], c[two]] = sa[rng.integers(0, W // 4, W)][two]; o[p2[two], c[two]] = sa[rng.integers(0, W // 4, W)][two]
            full = learn & (way >= 0.75); o[:, full] = sb[rng.integers(0, W // 4, (K, W))][:, full]
            apart = ~learn & (way < 0.4); o[p1[apart], c[apart]] = sa[rng.integers(0, W // 4, W)][apart]; o[p2[apart], c[apart]] = sb[rng.integers(0, W // 4, W)][apart]
            O[r, u] = o
            lane = rng.permutation(L); g[r, u, lane[:n]] = f[:n]; g[r, u, lane[n:]] = f[h:h + L - n]
            if u == 7:
                E[r] = e; warm[r] = hs
                if n >= CAP: late[r] = np.sort(lane[:n])[CAP - 1]
            T[r, u, 0] = t0
            if (u + r) % 3 < 2: T[r, u, 1] = 4080 * ((u + r) % 3)
    for r in range(N):
        if late[r] < 0: continue
        z = (r + 1) % N; c0 = int(g[r, 7, late[r]]); s = E[r, :h]; b = s ^ 1
        far = np.max(np.add.reduce(np.abs(X[z, 7][:, I[z, 7][:, b]] - X[z, 7][:, b][:, None, :]), axis=0), axis=0)
        s = s[(far >= 2048) & ~np.isin(s, O[r, 7][:, g[r, 7]]) & ~np.isin(s, warm[r]) & ~np.isin(b, g[z, 7])]
        O[r, 7, :, c0] = E[r, h:][rng.integers(0, h, K)]; O[r, 7, int(rng.integers(0, K)), c0] = rng.choice(s)
    return pack(I, X, O, g, A, T)
def setup_inputs_ties(rng):
    I, X, O, g, A, T = parts(rng); B = 8; c = np.arange(W)
    base = rng.integers(0, 256, (N, 8, 16, B)); sort = np.argsort(rng.random((N, 8, W)), axis=-1) % B; lit = np.argsort(sort, axis=-1, kind="stable")
    rk = (np.arange(16)[:, None] * (2 * rng.integers(0, 8, (N, 8, 1, W)) + 1) + rng.integers(0, 16, (N, 8, 1, W))) & 15
    ty = np.where(rk < rng.integers(NEED - 1, NEED + 1, (N, 8, 1, W)), c % B, (c // B) % B)
    I = take(lit, ty * (W // B) + rng.integers(0, 6, (N, 8, 16, W)))
    X = np.take_along_axis(base, sort[:, :, None, :], 3)
    A = np.take_along_axis(base, rng.integers(0, B, (N, 8, 1, L)), 3); A[..., :16] = base[..., :1]
    O = np.where(rng.random((N, 8, 1, W)) < 0.6, O[:, :, :1] % 64 + 64 * rng.integers(0, W // 64, (N, 8, K, W)), O)
    T[:, :, 0] = np.clip(np.add.reduce(np.abs(base[..., 0] - base[..., 1]), axis=2) + (np.arange(N)[:, None] + np.arange(8)) % 3 - 1, 0, 4080)
    return pack(I, X, O, g, A, T)
def setup_inputs_clash(rng):
    I, X, O, g, A, T = parts(rng)
    q = np.argsort(rng.random((8, W // 2)), axis=-1)[:, :16]; s = np.ascontiguousarray(np.broadcast_to(np.concatenate([2 * q, 2 * q + 1], axis=1), (N, 8, 32)))
    I = np.where(rng.random((N, 8, 16, W)) < 0.8, take(s, rng.integers(0, 32, (N, 8, 16, W))), I)
    O = np.where(rng.random((N, 8, K, W)) < 0.7, take(s, rng.integers(0, 32, (N, 8, K, W))), O)
    g = take(s, rng.integers(0, 32, (N, 8, L))); T = rng.integers(1000, 2600, (N, 8, RO))
    v = rng.integers(0, 21, (N, 3, 16, W)); X[:, 1::3] = np.where(rng.random((N, 3, 1, W)) < 0.5, v, 255 - v)
    v = rng.integers(0, 21, (N, 3, 16, L)); A[:, 1::3] = np.where(rng.random((N, 3, 1, L)) < 0.5, v, 255 - v)
    T[:, 1::3] = rng.integers(3072, 3840, (N, 3, RO))
    return pack(I, X, O, g, A, T)
def check_inputs(d):
    bad = []
    for k, lo, hi in (("icol", 0, W - 1), ("pat", 0, 255), ("alt", 0, W - 1), ("gate", 0, W - 1), ("acc0", 0, 255), ("th", 0, 4080)):
        v = np.asarray(d[k]).astype(np.float64)
        if not (np.min(v) >= lo and np.max(v) <= hi): bad.append("range of " + k)
        elif np.any(v != np.floor(v)): bad.append("whole numbers in " + k)
    return bad
def pick(Xr, n):
    return Xr[np.arange(8).reshape((8,) + (1,) * (n.ndim - 1)), n]
def rewrite(Ir, Xr, c, v, use):
    n = np.take_along_axis(Ir, c[:, None, :], 2)
    far = np.add.reduce(np.abs(pick(Xr, n) - pick(Xr, c)[:, None]), axis=-1); p = np.argmax(far, axis=1)
    for g in range(8):
        j = np.nonzero(use[g])[0]; j = j[np.unique(c[g, j], return_index=True)[1]]
        Ir[g, p[g, j], c[g, j]] = v[g, j]
def reference(icol, pat, alt, gate, acc0, th):
    I = icol.astype(np.int32).reshape(N, 8, 16, W); O = alt.astype(np.int64).reshape(N, 8, K, W); T = th.astype(np.int64)
    X = np.ascontiguousarray(pat.astype(np.float32).astype(np.int32).reshape(N, 8, 16, W).transpose(0, 1, 3, 2))
    A = np.ascontiguousarray(acc0.astype(np.float32).astype(np.int32).reshape(N, 8, 16, L).transpose(0, 1, 3, 2))
    G = np.stack([gentries(a) for a in gate]).astype(np.int64)
    for t in range(RO):
        sent = []
        for r in range(N):
            g = G[r]; o = np.take_along_axis(O[r], g[:, None, :], 2)
            col = np.take_along_axis(I[r], o.reshape(8, 1, K * L), 2).reshape(8, 16, K, L)
            dist = np.add.reduce(np.abs(pick(X[r], col) - A[r][:, None, None, :, :]), axis=-1)
            sv = np.add.reduce((dist <= T[r, :, t].reshape(8, 1, 1, 1)).astype(np.int32), axis=1) >= NEED
            ns = np.add.reduce(sv.astype(np.int32), axis=1); first = np.argmax(sv, axis=1)
            fc = np.take_along_axis(col, first[:, None, None, :], 2)[:, :, 0, :]
            ok = np.ones((8, 16, L), bool)
            for k in range(K):
                ok &= np.any(fc[:, :, None, :] == col[:, None, :, k, :], axis=2) | ~sv[:, None, k, :]
            com = np.take_along_axis(fc, np.argmax(ok, axis=1)[:, None, :], 1)[:, 0].astype(np.int64)
            sole = np.take_along_axis(o, first[:, None, :], 1)[:, 0]
            lrn = (ns == 1) | ((ns >= 2) & np.any(ok, axis=1))
            m = np.where(ns == 1, sole, np.where(lrn, com, o[:, K - 1]))
            rewrite(I[r], X[r], g, m, lrn)
            a = np.zeros((8, CAP), np.int64); b = np.zeros((8, CAP), np.int64); use = np.zeros((8, CAP), bool)
            for u in range(8):
                j = np.nonzero(lrn[u])[0][:CAP]
                a[u, :len(j)] = m[u, j] ^ 1; b[u, :len(j)] = g[u, j] ^ 1; use[u, :len(j)] = True
            sent.append((a, b, use))
            A[r] = np.where(lrn[:, :, None], (A[r] + pick(X[r], m)) >> 1, np.abs(A[r] - pick(X[r], o[:, 0])))
            G[r] = ((m * g >> 4) + 37 * g + int(np.count_nonzero(lrn))) & (W - 1)
        for r in range(N):
            q = (r + 1 + t % (N - 1)) % N; a, b, use = sent[r]
            rewrite(I[q], X[q], a, b, use)
    yc = np.add.reduce(I * np.arange(1, 17, dtype=np.int32).reshape(1, 1, 16, 1), axis=2)
    return {"yc": yc.astype(np.float32), "ya": np.ascontiguousarray(A.transpose(0, 1, 3, 2)).reshape(N, 128, L).astype(np.float32), "yg": G.astype(np.float32)}

@@ -1,0 +1,783 @@
+import numpy as np
+from concourse.mybir import AluOpType as ALU, AxisListType as AX, ActivationFunctionType as AF
+
+W, L, RO = 2048, 128, 4
+DUM = 128
+BIG = 2097152.0
+H16 = "float16"
+NQ = 8
+NA = 16 - NQ
+QD, QA = (NQ + 3) // 4, NQ // 4
+GA = 48
+
+
+def _pack(items):
+    at, n = {}, 0
+    for name, w in items:
+        at[name] = (n, w)
+        n += (w + 15) // 16 * 16
+    return at, n
+
+
+CB, NCB = _pack([("ONES", 128), ("IDN", 128), ("NID", 128), ("MK", 512), ("BO", 8), ("NBO", 8), ("KBO", 8), ("CM", 8), ("BIGSEL", 128), ("WM", 16),
+                 ("VALK", 160), ("VALC", 40), ("X3", 40), ("RANK", 128), ("TRIP", 128), ("TRI2", 128), ("TRI3", 384), ("S48", 48),
+                 ("THA", 32 * NQ), ("THB", 32 * NA), ("NTH", 1024), ("ZR", 128), ("P4096", 16), ("J", 128), ("NM16", 128), ("M3", 384), ("BLK5", 40),
+                 ("F16", 128), ("JG", 128), ("F5", 40), ("JA", 8 * NQ), ("JB", 8 * NA), ("F3", 128), ("F8", 128), ("FP", 128), ("BLKB", 128),
+                 ("KID", 128), ("HID", 128), ("NE3", 768)])
+CH, NCH = _pack([("SELO", 512), ("SIG", 128), ("DEL", 128), ("FSEL", 1024), ("PERM", 128), ("XSEL", 40), ("IDH", 128), ("BOH", 8), ("BLKH", 128),
+                 ("SELG", 1024), ("ONESH", 128), ("NBLK3", 384)])
+CF, NCF = _pack([("P", 8), ("PD", 32), ("FO", 128), ("GO", 4), ("FC", 8), ("FW", 16), ("FX", 40), ("XCONST", 40), ("UB", 8), ("FR", 128),
+                 ("P16", 3), ("IDF", 128), ("NIDF", 128), ("BASEF", 32), ("DUML", 8), ("WT", 128), ("THF", 8), ("BOF", 8), ("LC2F", 32), ("LC16F", 24)])
+LU, NLU = _pack([("LR8", 8), ("LSV", 32), ("LC2", 2 * NQ), ("LAR", 8 * NQ), ("LC16", 24)])
+S, F, B, I32, U = "sbuf", "float32", "bfloat16", "int32", "uint16"
+SCRATCH = {
+    "CB": (S, [128, NCB], B), "CH": (S, [128, NCH], H16), "CF": (S, [128, NCF], F), "LU": (S, [128, NLU], U), "LI": (S, [128, NLU], I32),
+    "PI": (S, [128, 32], I32), "TH": (S, [8, 12], I32), "GI": (S, [128, 8], I32), "GF": (S, [128, 8], F),
+    "IT": (S, [128, W], I32), "IC": (S, [128, W + DUM], F), "AW": (S, [128, W], I32), "X": (S, [128, W + 16], B), "YC": (S, [128, W + DUM], F),
+    "A": (S, [128, L], B), "AR": (S, [128, 128 * NQ], B), "GL": (S, [128, 8], U), "OL": (S, [128, 32], U), "R": (S, [128, L], H16),
+    "cT0": (S, [128, 8], F), "cT1": (S, [128, 8], F), "CMG": (S, [128, L], H16), "CMT": (S, [128, L], H16),
+    "COA": (S, [128, 512 - 128 * QA], U), "COLF": (S, [128, 512], F), "C2": (S, [128, 32 * NQ], U), "C16": (S, [128, 384], H16),
+    "H": (S, [128, 512 * NA], B), "D": (S, [128, 512 * NQ], B), "R2": (S, [128, 512 * NQ], B), "LED": (S, [128, 32, 16], B), "LEA": (S, [128, 32, 16], B),
+    "FI": (S, [128, 32], F), "FL": (S, [128, 8], U), "FC": (S, [128, L], H16), "SV": (S, [128, 32], F), "SVM": (S, [128, 512], B),
+    "AB": (S, [128, 3, 384], F), "EE": (S, [128, 8, 384], B), "XB": (S, [128, 40], F), "XC": (S, [128, 40], F),
+    "S1": (S, [128, 384], F), "S2": (S, [128, L], F), "KC": (S, [128, 16], I32), "KI": (S, [128, 64], I32), "TF": (S, [128, 128], F), "LB": (S, [128, 8], B),
+    "PA": (S, [128, 3, 8, 16], H16), "PB": (S, [128, 3, 8, 16], H16), "EQ3": (S, [128, 384], B), "EQ2": (S, [128, 8, 8, 16], B),
+    "AL": (S, [128, 8], F), "AMG": (S, [128, 64], H16),
+    "ZT": (S, [128, 16], F), "SL2": (S, [128, 8], U), "NM": (S, [128, L], H16), "NL": (S, [128, 8], U), "LR": (S, [128, L], B),
+    "XN": (S, [128, L], B), "AA": (S, [128, L], B), "AH": (S, [128, L], I32),
+    "AO": (S, [128, L], F), "VM": (S, [128, L], H16), "MR": (S, [128, L], F),
+    "CO2": (S, [128, L], U), "CF2": (S, [128, L], F), "XC2": (S, [128, L], B), "G2": (S, [128, 2048], B), "H2": (S, [128, 2048], B),
+    "PM2": (S, [128, L], F), "GE2": (S, [128, 144], B), "DV2": (S, [128, L], F), "WV2": (S, [128, L], F), "NC2": (S, [128, L], F), "YP2": (S, [128, L], F),
+    "CO3": (S, [128, 48], U), "CF3": (S, [128, 48], F), "XC3": (S, [128, 48], B), "G3": (S, [128, 768], B), "H3": (S, [128, 768], B),
+    "PM3": (S, [128, L], F), "GE3": (S, [128, 144], B), "DV3": (S, [128, 48], F), "WV3": (S, [128, 48], F), "NC3": (S, [128, 48], F), "YP3": (S, [128, 48], F),
+    "BF": (S, [128, 8], F), "PX": (S, [128, 8], F), "XT3": (S, [128, L], B), "BM": (S, [128, 48], H16), "G16": (S, [128, 8], H16), "YG": (S, [8, L], F),
+}
+for _t in range(RO):
+    for _n, _w in (("MA", 4), ("MB", 6), ("LA", 4), ("LB", 6)):
+        SCRATCH["%s%d" % (_n, _t)] = (S, [128, _w], U)
+for _n in ("DA", "DB", "PS", "L0", "L1", "DL", "PW", "PQ"):
+    SCRATCH[_n] = ("psum", [128, 512], F)
+SEMAPHORES = ["cv", "ca", "cp", "cg", "snt"] + ["d%d" % k for k in range(16)] + ["%s%d" % (n, t) for n in ("ra", "rb") for t in range(RO)]
+
+
+def route(src, dst, cores, topo):
+    if topo.may_write(src, dst):
+        return [src, dst]
+    near = [c for c in topo.cores_of(src) if c not in cores and topo.may_write(c, dst)]
+    near.sort(key=lambda c: topo.die(c) != topo.die(src))
+    return [src, near[0], dst]
+
+
+def width(src, dst, topo):
+    return len(topo.engines(src, dst))
+
+
+def hand(g, T, topo, src, dst, out, in_, sem):
+    rid, pid = topo.addr(dst, src)
+    g.remote_dma(T[out][:], T[in_][:], T.sem[sem], T.sem["snt"], pid, rid, topo.mask(src, dst))
+    return width(src, dst, topo)
+
+
+def relay_program(g, core, T, topo):
+    cores, n, sent = list(T.cores), len(T.cores), 0
+    for t in range(RO):
+        for r in range(n):
+            way = route(cores[r], cores[(r + 1 + t % (n - 1)) % n], cores, topo)
+            if len(way) == 3 and way[1] == core:
+                for buf, sem in (("LA", "ra"), ("LB", "rb")):
+                    g.wait_ge(T.sem["%s%d" % (sem, t)], width(way[0], core, topo))
+                    sent += hand(g, T, topo, core, way[2], "%s%d" % (buf, t), "%s%d" % (buf, t), "%s%d" % (sem, t))
+    if sent:
+        g.wait_ge(T.sem["snt"], sent)
+
+
+def V(name, *idx):
+    return ("ap", name, idx)
+
+
+def IND(win, off):
+    return ("ind", win, off)
+
+
+def sl(a=None, b=None, s=None):
+    return slice(a, b, s)
+
+
+ALL = sl()
+
+
+def _c(buf, tab):
+    def f(name, a=0, b=None, s=None, rows=ALL):
+        o, w = tab[name]
+        return V(buf, rows, sl(o + a, o + (w if b is None else b), s))
+    return f
+
+
+cb, ch, cf, lu, li = _c("CB", CB), _c("CH", CH), _c("CF", CF), _c("LU", LU), _c("LI", LU)
+
+
+def col(name, a, b=None, s=None, rows=ALL):
+    return V(name, rows, sl(a, a + 1 if b is None else b, s))
+
+
+def span(ap):
+    name, idx = ap[1], ap[2]
+    if name not in SCRATCH:
+        return None
+    sh = SCRATCH[name][1][1:]
+    e = np.arange(int(np.prod(sh))).reshape(sh)[tuple(idx[1:])].reshape(-1)
+    m = np.zeros(int(np.prod(sh)) + 8, np.uint8)
+    m[e] = 1
+    return name, int.from_bytes(np.packbits(m).tobytes(), "big"), int(e.min()), int(e.max())
+
+
+def emit(g, T, ops):
+    queue = {"v": g.vector, "a": g.scalar, "p": g.tensor, "g": g, "s": g.sync}
+    hist, known, count, need = {}, {q: {} for q in queue}, {}, set()
+    for n, o in enumerate(ops):
+        e = o["e"]
+        count[e] = count.get(e, 0) + 1
+        o["pos"] = count[e]
+        deps = set()
+        acc = [(span(a), False) for a in o["r"]] + [(span(a), True) for a in o["w"]]
+        acc = [(s, w) for s, w in acc if s is not None]
+        for (name, m, lo, hi), w in acc:
+            psum = SCRATCH[name][0] == "psum"
+            for (j, m2, lo2, hi2, w2) in hist.get(name, []):
+                same = ops[j]["e"] == e
+                if same and e == "p":
+                    continue
+                if (psum and not same) or ((w or w2) and ((m & m2) if same else (lo <= hi2 and lo2 <= hi))):
+                    deps.add(j)
+        for (name, m, lo, hi), w in acc:
+            h = hist.get(name, [])
+            if w and o["full"]:
+                h = [x for x in h if x[1] & ~m]
+            hist[name] = h + [(n, m, lo, hi, w)]
+        o["waits"] = []
+        if o["q"] is None:
+            o["clock"] = {e: 1}
+            continue
+        k = known[o["q"]]
+        for j in sorted(deps, reverse=True):
+            d = ops[j]
+            if k.get(d["e"], 0) < d["pos"]:
+                o["waits"].append(j)
+                need.add(j)
+                for x, y in d["clock"].items():
+                    k[x] = max(k.get(x, 0), y)
+        o["clock"] = dict(k)
+        o["clock"][e] = o["pos"]
+    raised = {}
+
+    def real(a):
+        if isinstance(a, tuple) and a[0] == "ap":
+            return T[a[1]][a[2]]
+        if isinstance(a, tuple) and a[0] == "ind":
+            return real(a[1]).indirect(real(a[2]))
+        return a
+    for n, o in enumerate(ops):
+        if o["q"] is None:
+            continue
+        q = queue[o["q"]]
+        for j in o["waits"]:
+            q.wait_ge(T.sem[ops[j]["sem"]], ops[j]["val"])
+        ins = o["f"](q, *[real(a) for a in o["a"]])
+        if o["e"] in queue:
+            if n in need:
+                raised[o["e"]] = raised.get(o["e"], 0) + 1
+                o["sem"], o["val"] = "c" + o["e"], raised[o["e"]]
+                ins.then_inc(T.sem[o["sem"]], 1)
+        elif o["dma"]:
+            ins.then_inc(T.sem[o["sem"]], 16)
+    for n, o in enumerate(ops):
+        if o["dma"] and n not in need:
+            queue[o["q"]].wait_ge(T.sem[o["sem"]], 16)
+
+
+def rank_program(g, core, T, topo):
+    rank = T.rank_of(core)
+    if rank is None:
+        relay_program(g, core, T, topo)
+        return
+    cores, N = list(T.cores), len(T.cores)
+    ops, ndma, sent = [], [0], [0]
+
+    def rec(q, f, out, *args, e=None, dma=False, sem=None, val=None):
+        r, w = [], []
+        for a in args:
+            if isinstance(a, tuple):
+                r += [a] if a[0] == "ap" else [a[1], a[2]]
+        full = False
+        if out is not None:
+            if out[0] == "ap":
+                w.append(out)
+                full = out[2][0] == ALL
+            else:
+                w.append(out[1])
+                r.append(out[2])
+        ops.append({"q": q, "e": e or q, "f": f, "a": ([] if out is None else [out]) + list(args), "r": r, "w": w, "full": full,
+                    "dma": dma, "sem": sem, "val": val})
+
+    def dma(q, out, in_):
+        rec(q, lambda x, o, i: x.dma_start(o, i), out, in_, e="d%d" % ndma[0], dma=True, sem="d%d" % ndma[0], val=16)
+        ndma[0] += 1
+
+    def cp(out, in_):
+        rec("v", lambda x, o, i: x.tensor_copy(o, i), out, in_)
+
+    def ms(out, c):
+        rec("v", lambda x, o: x.memset(o, c), out)
+
+    def tt(out, a, b, op):
+        rec("v", lambda x, o, i, j: x.tensor_tensor(o, i, j, op), out, a, b)
+
+    def ts(out, a, s1, op0, s2=None, op1=None):
+        if op1 is None:
+            rec("v", lambda x, o, i, s: x.tensor_scalar(o, i, s, None, op0), out, a, s1)
+        else:
+            rec("v", lambda x, o, i, s, u: x.tensor_scalar(o, i, s, u, op0, op1), out, a, s1, s2)
+
+    def scan(out, d0, d1, init, op0, op1):
+        rec("v", lambda x, o, i, j: x.tensor_tensor_scan(o, i, j, init, op0, op1), out, d0, d1)
+
+    def act(out, in_, func, bias=0.0, scale=1.0):
+        rec("a", lambda x, o, i, b, s: x.activation(o, i, func, bias=b, scale=s), out, in_, bias, scale)
+
+    def mm(out, l, r, start=True, stop=True):
+        rec("p", lambda x, o, i, j: x.matmul(o, i, j, start, stop), out, l, r)
+
+    def iota(out, pat, base=0, cm=0):
+        if SCRATCH[out[1]][2] == I32:
+            rec("g", lambda x, o: x.iota(o, pat, base, cm), out)
+        else:
+            rec("g", lambda x, o: x.iota(o, pat, base, cm, allow_small_or_imprecise_dtypes=True), out)
+
+    def send(t, src, land, sem):
+        way = route(core, cores[(rank + 1 + t % (N - 1)) % N], cores, topo)
+        rec("g", lambda x, i: hand(g, T, topo, core, way[1], land, src, sem), None, V(src, ALL), e="x" + src)
+        sent[0] += width(core, way[1], topo)
+
+    def arrive(t, land, sem):
+        way = route(cores[(rank - 1 - t % (N - 1)) % N], core, cores, topo)
+        rec(None, None, V(land, ALL), e=sem, sem=sem, val=width(way[-2], core, topo))
+
+    EQ, MUL, ADD, SUB, MAX, MIN = ALU.is_equal, ALU.mult, ALU.add, ALU.subtract, ALU.max, ALU.min
+    SHR, AND = ALU.arith_shift_right, ALU.bitwise_and
+    whole = lambda n: V(n, ALL)
+    IW, IS, XW, XS = col("IC", 0, W), col("IC", 0, W + DUM), col("X", 0, W), col("X", 0, W + 16)
+    R1, R8, R48, R49 = sl(0, 1), sl(0, 8), sl(0, 48), sl(0, 49)
+    pd_ = lambda k: cf("PD", k, k + 1)
+    gcol, rcol = pd_(0), pd_(1)
+    Pc = cf("P", 0, 1)
+    ki = lambda k, n=1: col("KI", 8 * k, 8 * (k + n))
+    tf = lambda k, n=1: col("TF", 8 * k, 8 * (k + n))
+
+    def zero(out):
+        n = len(range(*out[2][1].indices(512)))
+        mm(out, cb("ZR", rows=R1), cb("MK", 0, n, rows=R1), True, False)
+
+    ms(cb("ONES"), 1.0)
+    ms(whole("AW"), 0)
+    dma("s", whole("GI"), V("gate", ALL))
+    dma("a", XW, V("pat", ALL))
+    dma("a", whole("A"), V("acc0", ALL))
+    dma("a", col("TH", 0, 4), V("th", ALL))
+    for k in range(2):
+        dma("s", col("IT", 512 * k, 512 * k + 512), col("icol", 512 * k, 512 * k + 512))
+    dma("s", V("AW", sl(0, 128, 4)), V("alt", ALL))
+    for k in range(2, 4):
+        dma("s", col("IT", 512 * k, 512 * k + 512), col("icol", 512 * k, 512 * k + 512))
+
+    iota(col("PI", 0), [[0, 1]], 0, 1)
+    iota(cf("P"), [[-1, 8]], 0, 1)
+    iota(cf("FO"), [[16, 8], [1000, 4], [4, 4]])
+    iota(cf("GO"), [[1000, 4]], 0, 1)
+    iota(li("LAR"), [[1, NQ], [16, 8]])
+    iota(cf("LC2F"), [[1, 4], [128, 4], [8, 2]])
+    iota(cf("LC16F"), [[1, 3], [16, 8]], 1)
+    iota(cb("J"), [[1, 128]])
+    iota(cb("F16"), [[0, 8], [1, 16]])
+    iota(cb("JG"), [[1, 8], [0, 16]])
+    iota(cb("F5"), [[1, 8], [0, 5]])
+    iota(cb("JA"), [[1, 8], [0, NQ]])
+    iota(cb("JB"), [[1, 8], [0, NA]])
+    iota(cb("F3"), [[8, 8], [0, 2], [1, 8]])
+    iota(li("LR8"), [[1, 8]])
+    iota(li("LSV"), [[1, 4], [4, 8]])
+    iota(cf("FC"), [[4, 2], [-1, 4]], 3)
+    iota(cf("BASEF"), [[16, 8], [-1, 4]], 3)
+    iota(cb("F8"), [[8, 16], [0, 8]])
+    iota(cb("FP"), [[16, 8], [-1, 16]], 15)
+    iota(cf("FW"), [[2, 8], [-1, 2]], 1)
+    iota(cf("FX"), [[16, 8], [4, 5]], -4)
+    iota(cf("P16"), [[-16, 3]], 0, 1)
+    iota(cf("DUML"), [[16, 8]])
+    iota(cf("XCONST"), [[0, 8], [-4096, 5]], 16384)
+    iota(cf("UB"), [[-17, 8]], 139)
+    iota(cf("FR"), [[-17, 8], [-1, 16]], 138)
+    iota(cb("S48"), [[1, 48]], -256)
+    iota(cb("NE3"), [[1, 48], [0, 16]])
+
+    def fill(out, n, c):
+        act(out, cb("ONES", 0, n), AF.Identity, scale=float(c))
+
+    def times(out, in_, c):
+        act(out, in_, AF.Identity, scale=c)
+    fill(cb("ZR"), 128, 0)
+    fill(col("IC", W, W + DUM), DUM, 0)
+    fill(col("X", W, W + 16), 16, 0)
+    for k in range(4):
+        fill(V("LED", ALL, sl(8 * k, 8 * k + 8), ALL), 128, 0)
+        fill(V("LEA", ALL, sl(8 * k, 8 * k + 8), ALL), 128, 0)
+    for k in range(3):
+        fill(cb("M3", k, 384, 3), 128, min(k, 1))
+    fill(cb("NM16"), 128, 1)
+    fill(cb("VALC"), 40, BIG)
+    fill(cb("X3"), 40, 0)
+    fill(cb("P4096"), 16, 4096)
+    fill(whole("PM3"), 128, 0)
+    fill(col("GE2", 0, 16), 16, 1)
+    fill(col("GE3", 0, 16), 16, 1)
+    fill(col("YC", W, W + DUM), DUM, 0)
+    fill(cb("NM16", 0, 128, 16), 8, 0)
+    fill(cb("VALC", 0, 40, 5), 8, 0)
+    fill(cb("VALC", 4, 40, 5), 8, 0)
+    for k, (s1, s2) in enumerate([(4, 7), (0, 15), (1, 63), (3, 15), (0, 1), (2, 3), (0, 3), (3, 1), (0, 7)]):
+        ts(col("PI", 8 + k), col("PI", 0), s1, SHR, s2, AND)
+    cp(cf("PD", 0, 9), col("PI", 8, 17))
+    for q in range(4):
+        ts(ch("SELO", 128 * q, 128 * q + 128), cf("FO"), cf("GO", q, q + 1), EQ)
+    cp(lu("LAR"), li("LAR"))
+    cp(whole("GL"), whole("GI"))
+    ts(pd_(10), pd_(7), 4.0, MUL)
+    ts(pd_(11), pd_(6), 4.0, MUL)
+    ts(pd_(12), pd_(8), 16.0, MUL, pd_(10), ADD)
+    ts(pd_(13), pd_(5), 128.0, MUL, pd_(11), ADD)
+    for k in range(4):
+        ts(lu("LC2", NQ // 2 * k, NQ // 2 * (k + 1)), cf("LC2F", 8 * k, 8 * k + NQ // 2), pd_(12), ADD)
+    ts(lu("LC16"), cf("LC16F"), pd_(13), ADD)
+    act(whole("AR"), IND(col("A", 0, L), lu("LAR")), AF.Copy)
+    ts(col("TH", 4, 8), col("TH", 0, 4), 4, SHR)
+    ts(col("TH", 8, 12), col("TH", 0, 4), 15, AND)
+    ts(cf("THF", 0, 4, rows=R8), col("TH", 4, 8), -16.0, MUL)
+    ts(cf("THF", 4, 8, rows=R8), col("TH", 8, 12), -1.0, MUL, -0.5, ADD)
+    for k in range(8):
+        act(cb("NTH", 128 * k, 128 * k + 128, rows=R8), cb("ONES", rows=R8), AF.Identity, scale=cf("THF", k, k + 1, rows=R8))
+    ts(pd_(14), pd_(4), -2.0, MUL, 1.0, ADD)
+    ts(pd_(15), rcol, 1.0, ADD)
+    ts(cb("BO"), cb("J", 0, 8), gcol, EQ)
+    ts(cb("IDN"), cb("J"), Pc, EQ)
+    ts(cb("MK", 0, 128), cb("F16"), rcol, EQ)
+    ts(cb("BLKB"), cb("JG"), gcol, EQ)
+    ts(cb("BLK5"), cb("F5"), gcol, EQ)
+    ts(cb("THA", 0, 8 * NQ), cb("JA"), Pc, EQ)
+    ts(cb("THB", 0, 8 * NA), cb("JB"), Pc, EQ)
+    times(cb("NBO"), cb("BO"), -1.0)
+    times(cb("KBO"), cb("BO"), 1024.0)
+    times(cf("BOF"), cb("BO"), 1.0)
+    for k in range(1, 4):
+        times(cb("THA", 8 * NQ * k, 8 * NQ * (k + 1)), cb("THA", 0, 8 * NQ), 1.0)
+        times(cb("THB", 8 * NA * k, 8 * NA * (k + 1)), cb("THB", 0, 8 * NA), 1.0)
+        times(cb("MK", 128 * k, 128 * k + 128), cb("MK", 0, 128), 1.0)
+    times(cb("BIGSEL"), cb("BLKB"), BIG)
+    for k in range(4):
+        times(cb("VALK", 40 * k, 40 * k + 40), cb("BLK5"), BIG)
+    times(cb("X3", 4, 40, 5), cb("BO"), -2048.0)
+    fill(cb("VALK", 0, 160, 5), 32, 0)
+    for k in range(4):
+        times(cb("VALK", 40 * k + k + 1, 40 * k + 40, 5), cb("BO"), -BIG if k < 3 else 0.0)
+    times(cb("NID"), cb("IDN"), -1.0)
+    times(cb("KID"), cb("IDN"), 1024.0)
+    times(cb("HID"), cb("IDN"), -512.0)
+    times(cf("IDF"), cb("IDN"), 1.0)
+    times(cf("NIDF"), cb("IDN"), -1.0)
+    times(cf("WT"), cb("BLKB"), pd_(15))
+    times(cb("RANK"), cf("FR"), 4096.0)
+    fill(cf("XCONST", 4, 40, 5), 8, 2048)
+    ts(ch("SIG"), cb("F3"), pd_(2), EQ, -1.0, MUL)
+    ts(ch("DEL"), cb("F3"), pd_(2), EQ, pd_(14), MUL)
+    for n in ("LR8", "LSV"):
+        cp(lu(n), li(n))
+    ts(cb("CM"), cf("FC"), gcol, EQ, 1024.0, MUL)
+    ts(cf("BASEF"), cf("BASEF"), pd_(13), ADD)
+    cp(whole("GF"), whole("GI"))
+    ms(cb("CM", 0, 8, 4), 0.0)
+    ts(ch("BOH"), cb("J", 0, 8), gcol, EQ)
+    ts(ch("IDH"), cb("J"), Pc, EQ)
+    ts(cb("TRI2"), cb("J"), Pc, ALU.is_gt)
+    ts(cb("TRIP"), cb("J"), Pc, EQ, -256.0, MUL)
+    ts(ch("BLKH"), cb("JG"), gcol, EQ)
+    tt(cb("TRIP"), cb("TRIP"), cb("TRI2"), ADD)
+    tt(whole("CMG"), IND(col("GF", 0, 8), lu("LR8")), cb("MK", 0, L), MUL)
+    ts(cb("TRI2"), cb("J"), Pc, ALU.is_le, 4096.0, MUL)
+    for pp in range(8):
+        ts(ch("FSEL", 128 * pp, 128 * pp + 128), cb("F8"), cf("P", pp, pp + 1), EQ, 2.0, MUL)
+    mm(col("PS", 128, 136), whole("CMG"), ch("BOH"))
+
+    def options_a():
+        cp(whole("R"), IND(col("AW", 0, W), col("GL", 0, 8)))
+
+    def options_b():
+        for Q in range(4):
+            for q in range(4):
+                mm(col("PS", 96 + 8 * Q, 104 + 8 * Q), ch("SELO", 128 * q, 128 * q + 128), col("R", 4 * Q + q, L, 16), q == 0, q == 3)
+
+    def options_c():
+        cp(whole("OL"), col("PS", 96, 128))
+
+    def columns(k):
+        cp(col("IC", 512 * k, 512 * k + 512), col("IT", 512 * k, 512 * k + 512))
+
+    def consts_b():
+        ts(cf("FX", 0, 40, 5), cf("FX", 0, 40, 5), 16.0, ADD)
+        ts(ch("PERM"), cb("FP"), Pc, EQ)
+        ts(cb("WM"), cf("FW"), pd_(3), EQ, -BIG, MUL)
+        ts(ch("XSEL"), cf("FX"), Pc, EQ)
+        ts(cf("XCONST", 0, 40, 5), cf("UB"), 4096.0, MUL, 2048.0, ADD)
+        cp(whole("cT0"), col("PS", 128, 136))
+        cp(col("KC", 8, 16), col("PS", 128, 136))
+        for k in range(8):
+            ts(ch("SELG", 128 * k, 128 * k + 128), cb("ONES"), cf("BOF", k, k + 1), MUL)
+
+    def consts_c():
+        for k in range(3):
+            ts(ch("NBLK3", 128 * k, 128 * k + 128), cb("JG"), gcol, EQ, -1.0, MUL)
+            ts(cb("TRI3", 128 * k, 128 * k + 128), cb("F16"), cf("P16", k, k + 1), ALU.is_le, 4096.0, MUL)
+        ms(ch("ONESH"), 1.0)
+        ts(cf("DUML"), cf("DUML"), rcol, ADD)
+        ms(whole("AMG"), 0.0)
+        ts(cb("NE3"), cb("NE3"), Pc, EQ, -1.0, MUL)
+
+    columns(0)
+    columns(1)
+    options_a()
+    options_b()
+    consts_b()
+    columns(2)
+    options_c()
+    columns(3)
+
+    def to_list(z, n, out, zt):
+        tt(col("ZT", zt, zt + n), z, cf("DUML", 0, n), MIN)
+        ts(out, col("ZT", zt, zt + n), float(W), ADD)
+
+    def far_mask_a(n, PM, GE):
+        rows = sl(0, n)
+        scan(V(PM, rows, ALL), cb("NM16", rows=rows), V("PQ", rows, sl(0, 128)), 0.0, MUL, MAX)
+        cp(whole("PX"), col(PM, 15, L, 16))
+        tt(col(GE, 16, 144), IND(col("PX", 0, 8), lu("LR8")), whole(PM), EQ)
+
+    def far_mask_b(n, GE):
+        rows = sl(0, n)
+        mm(col("DA", 0, n), cb("MK", 0, L, rows=R1), cb("ONES", 0, n, rows=R1), True, False)
+        mm(col("DA", 0, n), col(GE, 16, 144, rows=rows), cb("IDN", 0, n, rows=rows), False, False)
+        mm(col("DA", 0, n), col(GE, 15, 143, rows=rows), cb("NID", 0, n, rows=rows), False, True)
+
+    def write(n, s, lst, t):
+        tt(whole("WV" + s), col("DA", 0, n), whole("DV" + s), MUL)
+        if t < RO - 1:
+            tt(IND(IS, lst), whole("WV" + s), whole("CF" + s), ADD)
+            return
+        tt(whole("NC" + s), whole("WV" + s), whole("CF" + s), ADD)
+        mm(col("DB", 0, n), cf("WT"), whole("NC" + s))
+        if s == "2":
+            cp(IND(IS, lst), whole("NC" + s))
+        act(whole("YP" + s), col("DB", 0, n), AF.Copy)
+
+    def patch(s, lst):
+        cp(IND(col("YC", 0, W + DUM), lst), whole("YP" + s))
+
+    def ysum(k, bank):
+        mm(whole(bank), cf("WT"), col("IC", 512 * k, 512 * k + 512))
+
+    for t in range(RO):
+        last = t == RO - 1
+        cT, cN = "cT%d" % (t % 2), "cT%d" % (1 - t % 2)
+        cp(whole("COA"), IND(IW, col("OL", 8 * QA, 32)))
+        for q in range(NQ, 16):
+            for u in range(8):
+                o = 4 * (((q // 4 - QA) * 8 + u) * 4 + q % 4)
+                s = 64 * (8 * (q - NQ) + u)
+                act(col("H", s, s + 64), IND(XW, col("COA", o, o + 4)), AF.Abs, bias=col("A", 16 * u + q), scale=-1.0)
+        cp(col("COLF", 0, 128 * QD), IND(IW, col("OL", 0, 8 * QD)))
+        cp(whole("C2"), IND(col("COLF", 0, 128 * QD), lu("LC2")))
+        cp(whole("CO2"), IND(IW, col("GL", 0, 8)))
+        n = 128 * NQ
+        for k in range(4):
+            tt(col("D", n * k, n * k + n), IND(XW, col("C2", 8 * NQ * k, 8 * NQ * (k + 1))), whole("AR"), SUB)
+            if k == 2:
+                cp(col("COLF", 128 * QD, 512), IND(IW, col("OL", 8 * QD, 32)))
+            ts(col("R2", n * k, n * k + n), col("D", n * k, n * k + n), 0.0, MAX, 2.0, MUL)
+        cp(whole("C16"), IND(col("COLF", 0, 512), lu("LC16")))
+        if last:
+            ysum(0, "PW")
+            ysum(1, "PQ")
+            for k in range(2):
+                ysum(2 + k, "L%d" % k)
+                cp(col("YC", 512 * (2 + k), 512 * (3 + k)), whole("L%d" % k))
+        for bank, sel, n in (("DB", "THB", NA), ("DA", "THA", NQ)):
+            mm(col(bank, 0, 32 * n), cb("NTH", 128 * t, 128 * t + 128, rows=R8), cb(sel, rows=R8), True, False)
+            mm(col(bank, 0, 32 * n), cb("NTH", 128 * (4 + t), 128 * (5 + t), rows=R8), cb(sel, rows=R8), False, False)
+
+        def pa(q):
+            for u in range(4):
+                s = 128 * (4 * q + u)
+                mm(col("DB", 8 * NA * u + q, 8 * NA * (u + 1), NA), col("H", s, s + 128), cb("BO"), False, u == 3 and q == NA - 1)
+
+        def pd(k):
+            for q in range(NQ):
+                o, s = col("DA", 8 * NQ * k + q, 8 * NQ * (k + 1), NQ), 128 * (NQ * k + q)
+                mm(o, col("D", s, s + 128), cb("NBO"), False, False)
+                mm(o, col("R2", s, s + 128), cb("BO"), False, k == 3 and q == NQ - 1)
+        done = 0
+        for k in range(4):
+            upto = (NA * (k + 1)) // 4 - 1
+            for q in range(done, upto):
+                pa(q)
+            done = upto
+            pd(k)
+        if t == 0:
+            consts_c()
+        ts(V("LED", ALL, ALL, sl(0, NQ)), col("DA", 0, 32 * NQ), 0.0, ALU.is_gt, 0.40625, SUB)
+        for q in range(done, NA):
+            pa(q)
+        mm(col("DL", 0, 384), ch("DEL"), whole("C16"))
+        if last:
+            act(col("YC", 512, 1024), whole("PQ"), AF.Copy)
+            act(col("YC", 0, 512), whole("PW"), AF.Copy)
+        else:
+            act(whole("CF2"), IND(IW, col("GL", 0, 8)), AF.Copy)
+        act(col("DL", 0, 384), col("DL", 0, 384), AF.Abs)
+        ga = GA // 2 if last else GA
+        act(col("G2", 0, 16 * ga), IND(XW, col("CO2", 0, ga)), AF.Copy)
+        act(whole("XC2"), IND(XW, col("GL", 0, 8)), AF.Copy)
+        led = lambda k: V("LED", ALL, sl(8 * k, 8 * k + 8), ALL)
+        lea = lambda k: V("LEA", ALL, sl(8 * k, 8 * k + 8), ALL)
+        zero(col("PS", 0, 32))
+        for k in range(3):
+            mm(col("PS", 3 - k, 32, 4), led(k), cb("KBO"), False, False)
+        ts(V("LEA", ALL, ALL, sl(NQ, 16)), col("DB", 0, 32 * NA), 0.0, ALU.is_gt, 0.40625, SUB)
+        ts(tf(9), whole(cT), 2176.0, SUB)
+        for u in range(4):
+            mm(col("PS", 8 * u, 8 * u + 8), lea(u), cb("CM"), False, u == 3)
+        zero(col("PQ", 128, 160))
+        for k in range(4):
+            mm(col("PQ", 128 + k, 160, 4), led(k), cb("KBO"), False, False)
+        for u in range(4):
+            mm(col("PQ", 128 + 8 * u, 136 + 8 * u), lea(u), cb("KBO"), False, u == 3)
+        for bank in ("L0", "L1"):
+            mm(col(bank, 0, 384), ch("SIG"), whole("C16"), True, False)
+        scan(whole("FI"), col("PS", 0, 32), cf("BASEF"), 0.0, MIN, MAX)
+        cp(whole("FL"), col("FI", 3, 32, 4))
+        cp(whole("FC"), IND(col("COLF", 0, 512), col("FL", 0, 8)))
+        ts(whole("SV"), col("PQ", 128, 160), 0.0, ALU.is_lt)
+        tt(whole("SVM"), IND(col("SV", 0, 32), lu("LSV")), cb("MK"), MUL)
+        svm = lambda k: col("SVM", 128 * k, 128 * k + 128)
+        banks = ("L0", "L1", "DB")
+
+        def lin(pp):
+            bank = banks[pp % 3]
+            if pp >= 2:
+                mm(col(bank, 0, 384), ch("SIG"), whole("C16"), True, False)
+            for k in range(3):
+                mm(col(bank, 128 * k, 128 * k + 128), ch("FSEL", 128 * pp, 128 * pp + 128), whole("FC"), False, k == 2)
+            act(V("AB", ALL, pp % 3, ALL), col(bank, 0, 384), AF.Abs)
+
+        def member(pp):
+            tt(V("EE", ALL, pp, ALL), V("AB", ALL, pp % 3, ALL), col("DL", 0, 384), EQ)
+
+        def tally(pp):
+            for k in range(3):
+                mm(col("PW", 3 * (7 - pp) + k, 384, 24), V("EE", ALL, pp, sl(128 * k, 128 * k + 128)), cb("WM"), False, pp == 7 and k == 2)
+
+        def same_gate(k):
+            o = col(("DB", "DL")[k // 4], 128 * (k % 4), 128 * (k % 4) + 128)
+            mm(o, ch("SELG", 128 * k, 128 * k + 128), whole("CMG"), True, False)
+            mm(o, cb("IDN"), cb("TRI2"), False, True)
+        for pp in range(3):
+            lin(pp)
+        member(0)
+        zero(col("PW", 0, 384))
+        mm(col("PQ", 0, 128), whole("FC"), ch("PERM"), True, False)
+        mm(col("PQ", 0, 128), cb("ONES", rows=R1), cb("RANK", rows=R1), False, True)
+        for pp in range(3, 8):
+            lin(pp)
+            member(pp - 2)
+            tally(pp - 3)
+            if pp == 3:
+                mm(col("DA", 64, 104), whole("R"), ch("XSEL"), True, False)
+                mm(col("DA", 64, 104), svm(3), cb("X3"), False, True)
+                mm(col("DA", 0, 40), cb("ONES", rows=R1), cb("VALC", rows=R1), True, False)
+                for k in range(4):
+                    mm(col("DA", 0, 40), svm(k), cb("VALK", 40 * k, 40 * k + 40), False, k == 3)
+            if pp == 4:
+                for k in range(3):
+                    mm(col("PW", k, 384, 3), svm(k + 1), cb("BIGSEL"), False, False)
+            if pp == 5:
+                tt(whole("XB"), col("DA", 64, 104), cf("XCONST"), ADD)
+                scan(whole("XC"), col("DA", 0, 40), whole("XB"), 0.0, MIN, MAX)
+        member(6)
+        tally(5)
+        member(7)
+        tally(6)
+        for k in range(4):
+            same_gate(k)
+        tally(7)
+        for k in range(4, 8):
+            same_gate(k)
+        act(col("G2", 16 * ga, 2048), IND(XW, col("CO2", ga, L)), AF.Copy)
+
+        def lin2(b):
+            bank = "L%d" % (b % 2)
+            for j in range(4):
+                mm(col(bank, L * j, L * j + L), cb("IDN"), col("G2", 4 * b + j, 2048, 16), True, False)
+                mm(col(bank, L * j, L * j + L), cb("NID"), whole("XC2"), False, True)
+            act(col("H2", 512 * b, 512 * b + 512), whole(bank), AF.Abs)
+
+        def red2(b):
+            for p in range(4 * b, 4 * b + 4):
+                mm(col("PQ", p, 128, 16), col("H2", L * p, L * p + L), cb("BO"))
+        far2 = [lambda: lin2(0), lambda: lin2(1), lambda: (red2(0), lin2(2)), lambda: (red2(1), lin2(3)), lambda: red2(2), lambda: red2(3)]
+        if last:
+            act(whole("CF2"), IND(IW, col("GL", 0, 8)), AF.Copy)
+            far2 = [lambda: None] + far2
+
+        def far2_next():
+            far2.pop(0)()
+        ts(tf(5), col("XB", 1, 40, 5), 12288.0, SUB)
+        scan(whole("S1"), cb("M3"), col("PW", 0, 384), 0.0, MUL, MAX)
+        scan(whole("S2"), col("S1", 2, 384, 3), col("PQ", 0, 128), BIG, MIN, MAX)
+        far2_next()
+        tt(col("KC", 0, 8), col("S2", 15, 128, 16), col("XC", 4, 40, 5), MIN)
+        ts(ki(0), col("KC", 0, 8), 4095, AND)
+        ts(ki(1, 2), whole("KC"), 1, AND)
+        ts(whole("LB"), ki(0), 2048.0, ALU.is_lt)
+        mm(col("DA", 0, 8), cb("TRIP"), whole("LB"))
+        mm(col("DA", 8, 16), cb("ONES"), whole("LB"))
+        far2_next()
+        ts(ki(3, 2), whole("KC"), W - 1, AND)
+        ts(tf(2, 2), ki(1, 2), -2.0, MUL, -2047.0, ADD)
+        ts(tf(11), ki(0), 2048.0, ALU.is_lt)
+        tt(tf(0, 2), tf(2, 2), ki(3, 2), ADD)
+        far2_next()
+        for k in range(8):
+            ts(V("PA", ALL, ALL, k, ALL), cb("S48"), col("DA", k), EQ, col("TF", k), MUL)
+        for u in range(3):
+            mm(col("PS", 136 + u, 137 + u + u // 2), V("PA", ALL, u, ALL, ALL), ch("ONESH", 0, 1 + u // 2))
+        mm(V("PW", R49, sl(0, 384)), ch("ONESH", 0, 49), whole("PA"), True, False)
+        mm(V("PW", R49, sl(0, 384)), cb("IDN", 0, 49, rows=R48), cb("TRI3", rows=R48), False, False)
+        tt(tf(7), ki(3), tf(5), SUB)
+        tt(tf(10), tf(9), tf(11), MUL)
+        ts(whole("MA%d" % t), col("PS", 136, 140), float(W), ADD)
+        send(t, "MA%d" % t, "LA%d" % t, "ra%d" % t)
+        cp(col("AL", 0, 4), col("PS", 136, 140))
+        tt(tf(8), tf(7), tf(11), MUL)
+        tt(col("AMG", 0, 48), IND(col("AL", 0, 4), lu("LR8", 0, 3)), cb("MK", 0, 48), MUL)
+        tt(tf(12), tf(8), tf(5), ADD)
+        mm(V("PW", R49, sl(0, 384)), col("AMG", 0, 49), ch("NBLK3"), False, True)
+        far2_next()
+        tt(whole("NM"), IND(tf(12), lu("LR8")), cb("MK", 0, L), MUL)
+        mm(col("PS", 176, 184), whole("NM"), ch("BOH"))
+        far2_next()
+        act(whole("LR"), IND(tf(11), lu("LR8")), AF.Copy)
+        ts(V("EQ3", R49, ALL), V("PW", R49, sl(0, 384)), 0.0, EQ)
+        cp(whole("NL"), col("PS", 176, 184))
+        act(whole("XN"), IND(XW, col("NL", 0, 8)), AF.Copy)
+        act(whole("MR"), IND(tf(12), lu("LR8")), AF.Copy)
+        far2_next()
+        for k in range(8):
+            ts(V("PB", ALL, ALL, k, ALL), cb("S48"), col("DA", k), EQ, col("TF", 8 + k), MUL)
+        while far2:
+            far2_next()
+        mm(col("L1", 0, L), cb("IDN"), whole("XN"), True, False)
+        mm(col("L1", 0, L), cb("NID"), whole("A"), False, True)
+        act(whole("AA"), col("L1", 0, L), AF.Abs)
+        for u in range(3):
+            mm(col("PS", 160 + u), V("PA", ALL, u, ALL, ALL), ch("ONESH", 0, 1), True, False)
+            mm(col("PS", 160 + u), V("EQ3", R49, sl(128 * u, 128 * u + 128)), cb("P4096", 0, 1, rows=R49), False, True)
+        for u in range(3):
+            mm(col("PS", 164 + u), V("PB", ALL, u, ALL, ALL), ch("ONESH", 0, 1))
+        mm(col("L0", 0, L), cb("IDN"), whole("XN"), True, False)
+        mm(col("L0", 0, L), cb("IDN"), whole("A"), False, False)
+        mm(col("L0", 0, L), whole("LR"), cb("KID"), False, True)
+        mm(col("L0", L, 2 * L), cb("IDN"), whole("AA"), True, False)
+        mm(col("L0", L, 2 * L), whole("LR"), cb("HID"), False, True)
+        mm(col("L1", 0, L), whole("MR"), cf("IDF"), True, False)
+        mm(col("L1", 0, L), cf("NIDF"), whole("CF2"), False, True)
+        act(whole("DV2"), col("L1", 0, L), AF.Copy)
+        ts(tf(13), tf(10), 128.0, ADD)
+        rec("v", lambda x, o, i: x.tensor_reduce(o, i, AX.X, ADD), col("TF", 120), col("DA", 8, 16))
+        ts(col("MB%d" % t, 3, 6), col("PS", 164, 167), float(W), ADD)
+        to_list(col("PS", 160, 163), 3, col("MB%d" % t, 0, 3), 0)
+        send(t, "MB%d" % t, "LB%d" % t, "rb%d" % t)
+        ts(whole("AH"), col("L0", 0, L), 0.5, MUL, 512.25, SUB)
+        tt(whole("VM"), IND(tf(13), lu("LR8")), cb("MK", 0, L), MUL)
+        tt(whole("AO" if last else "A"), whole("AH"), col("L0", L, 2 * L), MAX)
+        if not last:
+            act(whole("AR"), IND(col("A", 0, L), lu("LAR")), AF.Copy)
+        else:
+            dma("s", V("ya", ALL), whole("AO"))
+        far_mask_a(L, "PM2", "GE2")
+        far_mask_b(L, "GE2")
+        for k in range(8):
+            ts(V("EQ2", ALL, ALL, k, ALL), col(("DB", "DL")[k // 4], 128 * (k % 4), 128 * (k % 4) + 128), col(cT, k), EQ, col("TF", 88 + k), MUL)
+        mm(col("PS", 192, 200), whole("VM"), ch("BOH"), True, False)
+        for u in range(8):
+            mm(col("PS", 192 + u), V("EQ2", ALL, u, ALL, ALL), cb("P4096", 0, 1), False, u == 7)
+        tt(ki(5), ki(3), ki(4), MUL)
+        ts(tf(6), whole(cT), 37.0, MUL, col("TF", 120), ADD)
+        ts(ki(6), ki(5), 4, SHR)
+        to_list(col("PS", 192, 200), 8, whole("SL2"), 8)
+        tt(ki(7), ki(6), tf(6), ADD)
+        write(L, "2", col("SL2", 0, 8), t)
+        ts(col("KC", 8, 16), ki(7), W - 1, AND)
+        arrive(t, "LA%d" % t, "ra%d" % t)
+        la = col("LA%d" % t, 0, 3)
+        cp(whole("CO3"), IND(IS, la))
+        cp(whole("XC3"), IND(XS, la))
+        act(col("G3", 0, 384), IND(XS, col("CO3", 0, 24)), AF.Copy)
+        mm(V("PW", R48, sl(0, L)), whole("XC3"), cb("IDN"))
+        if not last:
+            tt(whole("CMT"), IND(col("KC", 8, 16), lu("LR8")), cb("MK", 0, L), MUL)
+        cp(V("XT3", R48, ALL), V("PW", R48, sl(0, L)))
+        if not last:
+            mm(col("PS", 144, 152), whole("CMT"), ch("BOH"))
+        cp(col("G3", 384, 768), IND(XS, col("CO3", 24, 48)))
+        for b in range(2):
+            mm(col("L%d" % b, 0, 384), V("XT3", R48, ALL), cb("NE3", 384 * b, 384 * b + 384, rows=R48), True, False)
+            mm(col("L%d" % b, 0, 384), cb("IDN"), col("G3", 384 * b, 384 * b + 384), False, True)
+            act(col("H3", 384 * b, 384 * b + 384), col("L%d" % b, 0, 384), AF.Abs)
+        if not last:
+            cp(whole("GL"), col("PS", 144, 152))
+            mm(col("DL", 2 * L, 3 * L), whole("CMT"), ch("IDH"))
+            cp(whole("CF3"), IND(IS, la))
+            options_a()
+            options_b()
+            cp(whole(cN), col("KC", 8, 16))
+        else:
+            cp(whole("CF3"), IND(IS, la))
+            patch("2", col("SL2", 0, 8))
+            cp(whole("G16"), col("KC", 8, 16))
+            mm(V("PS", R8, sl(256, 384)), whole("G16"), ch("IDH"))
+        arrive(t, "LB%d" % t, "rb%d" % t)
+        cp(col("BF", 0, 3), col("LB%d" % t, 3, 6))
+        tt(whole("BM"), IND(col("BF", 0, 3), lu("LR8", 0, 3)), cb("MK", 0, 48), MUL)
+        if not last:
+            cp(whole("CMG"), col("DL", 2 * L, 3 * L))
+            options_c()
+        else:
+            cp(whole("YG"), V("PS", R8, sl(256, 384)))
+            dma("s", V("yg", ALL), whole("YG"))
+        for p in range(16):
+            mm(V("PQ", R48, sl(p, 128, 16)), col("H3", p, 768, 16), cb("BO"))
+        mm(col("PW", 0, 48), ch("BLKH"), whole("BM"), True, False)
+        mm(col("PW", 0, 48), cf("NIDF"), whole("CF3"), False, True)
+        act(whole("DV3"), col("PW", 0, 48), AF.Copy)
+        far_mask_a(48, "PM3", "GE3")
+        far_mask_b(48, "GE3")
+        write(48, "3", col("LB%d" % t, 0, 3), t)
+    patch("3", col("LB%d" % (RO - 1), 0, 3))
+    dma("s", V("yc", ALL), V("YC", sl(0, 128, 16), sl(0, W)))
+    emit(g, T, ops)
+    g.wait_ge(T.sem["snt"], sent[0])

@@ -8,7 +8,7 @@ H16 = "float16"
 NQ = 8
 NA = 16 - NQ
 QD, QA = (NQ + 3) // 4, NQ // 4
-GA = 48
+GA = 32
 
 
 def _pack(items):
@@ -31,7 +31,7 @@ CF, NCF = _pack([("P", 8), ("PD", 32), ("FO", 128), ("GO", 4), ("FC", 8), ("FW",
 LU, NLU = _pack([("LR8", 8), ("LSV", 32), ("LC2", 2 * NQ), ("LAR", 8 * NQ), ("LC16", 24)])
 S, F, B, I32, U = "sbuf", "float32", "bfloat16", "int32", "uint16"
 SCRATCH = {
-    "CB": (S, [128, NCB], B), "CH": (S, [128, NCH], H16), "CF": (S, [128, NCF], F), "LU": (S, [128, NLU], U), "LI": (S, [128, NLU], I32),
+    "CB": (S, [128, NCB], B), "CH": (S, [128, NCH], B), "CF": (S, [128, NCF], F), "LU": (S, [128, NLU], U), "LI": (S, [128, NLU], I32),
     "PI": (S, [128, 32], I32), "TH": (S, [8, 12], I32), "GI": (S, [128, 8], I32), "GF": (S, [128, 8], F),
     "IT": (S, [128, W], I32), "IC": (S, [128, W + DUM], F), "AW": (S, [128, W], I32), "X": (S, [128, W + 16], B), "YC": (S, [128, W + DUM], F),
     "A": (S, [128, L], B), "AR": (S, [128, 128 * NQ], B), "GL": (S, [128, 8], U), "OL": (S, [128, 32], U), "R": (S, [128, L], H16),
@@ -114,6 +114,12 @@ def _c(buf, tab):
 
 
 cb, ch, cf, lu, li = _c("CB", CB), _c("CH", CH), _c("CF", CF), _c("LU", LU), _c("LI", LU)
+_own = ch
+
+
+def ch(name, *a, **k):
+    alias = {"IDH": "IDN", "BOH": "BO", "BLKH": "BLKB", "ONESH": "ONES"}
+    return cb(alias[name], *a, **k) if name in alias else _own(name, *a, **k)
 
 
 def col(name, a, b=None, s=None, rows=ALL):
@@ -339,7 +345,6 @@ def rank_program(g, core, T, topo):
     fill(whole("PM3"), 128, 0)
     fill(col("GE2", 0, 16), 16, 1)
     fill(col("GE3", 0, 16), 16, 1)
-    fill(col("YC", W, W + DUM), DUM, 0)
     fill(cb("NM16", 0, 128, 16), 8, 0)
     fill(cb("VALC", 0, 40, 5), 8, 0)
     fill(cb("VALC", 4, 40, 5), 8, 0)
@@ -349,7 +354,6 @@ def rank_program(g, core, T, topo):
     for q in range(4):
         ts(ch("SELO", 128 * q, 128 * q + 128), cf("FO"), cf("GO", q, q + 1), EQ)
     cp(lu("LAR"), li("LAR"))
-    cp(whole("GL"), whole("GI"))
     ts(pd_(10), pd_(7), 4.0, MUL)
     ts(pd_(11), pd_(6), 4.0, MUL)
     ts(pd_(12), pd_(8), 16.0, MUL, pd_(10), ADD)
@@ -362,8 +366,11 @@ def rank_program(g, core, T, topo):
     ts(col("TH", 8, 12), col("TH", 0, 4), 15, AND)
     ts(cf("THF", 0, 4, rows=R8), col("TH", 4, 8), -16.0, MUL)
     ts(cf("THF", 4, 8, rows=R8), col("TH", 8, 12), -1.0, MUL, -0.5, ADD)
-    for k in range(8):
+
+    def threshold(k):
         act(cb("NTH", 128 * k, 128 * k + 128, rows=R8), cb("ONES", rows=R8), AF.Identity, scale=cf("THF", k, k + 1, rows=R8))
+    threshold(0)
+    threshold(4)
     ts(pd_(14), pd_(4), -2.0, MUL, 1.0, ADD)
     ts(pd_(15), rcol, 1.0, ADD)
     ts(cb("BO"), cb("J", 0, 8), gcol, EQ)
@@ -388,28 +395,24 @@ def rank_program(g, core, T, topo):
     for k in range(4):
         times(cb("VALK", 40 * k + k + 1, 40 * k + 40, 5), cb("BO"), -BIG if k < 3 else 0.0)
     times(cb("NID"), cb("IDN"), -1.0)
-    times(cb("KID"), cb("IDN"), 1024.0)
-    times(cb("HID"), cb("IDN"), -512.0)
-    times(cf("IDF"), cb("IDN"), 1.0)
-    times(cf("NIDF"), cb("IDN"), -1.0)
-    times(cf("WT"), cb("BLKB"), pd_(15))
     times(cb("RANK"), cf("FR"), 4096.0)
     fill(cf("XCONST", 4, 40, 5), 8, 2048)
+    act(cf("XCONST", 0, 40, 5), cf("UB"), AF.Identity, bias=2048.0, scale=4096.0)
+    act(cf("FX", 0, 40, 5), cf("FX", 0, 40, 5), AF.Identity, bias=16.0)
+    act(cf("BASEF"), cf("BASEF"), AF.Identity, bias=pd_(13))
+    act(cf("DUML"), cf("DUML"), AF.Identity, bias=rcol)
+    for k in range(8):
+        times(ch("SELG", 128 * k, 128 * k + 128), cb("ONES"), cf("BOF", k, k + 1))
     ts(ch("SIG"), cb("F3"), pd_(2), EQ, -1.0, MUL)
     ts(ch("DEL"), cb("F3"), pd_(2), EQ, pd_(14), MUL)
     for n in ("LR8", "LSV"):
         cp(lu(n), li(n))
     ts(cb("CM"), cf("FC"), gcol, EQ, 1024.0, MUL)
-    ts(cf("BASEF"), cf("BASEF"), pd_(13), ADD)
-    cp(whole("GF"), whole("GI"))
-    ms(cb("CM", 0, 8, 4), 0.0)
-    ts(ch("BOH"), cb("J", 0, 8), gcol, EQ)
-    ts(ch("IDH"), cb("J"), Pc, EQ)
     ts(cb("TRI2"), cb("J"), Pc, ALU.is_gt)
     ts(cb("TRIP"), cb("J"), Pc, EQ, -256.0, MUL)
-    ts(ch("BLKH"), cb("JG"), gcol, EQ)
+    ms(cb("CM", 0, 8, 4), 0.0)
+    tt(whole("CMG"), IND(col("GI", 0, 8), lu("LR8")), cb("MK", 0, L), MUL)
     tt(cb("TRIP"), cb("TRIP"), cb("TRI2"), ADD)
-    tt(whole("CMG"), IND(col("GF", 0, 8), lu("LR8")), cb("MK", 0, L), MUL)
     ts(cb("TRI2"), cb("J"), Pc, ALU.is_le, 4096.0, MUL)
     for pp in range(8):
         ts(ch("FSEL", 128 * pp, 128 * pp + 128), cb("F8"), cf("P", pp, pp + 1), EQ, 2.0, MUL)
@@ -430,29 +433,38 @@ def rank_program(g, core, T, topo):
         cp(col("IC", 512 * k, 512 * k + 512), col("IT", 512 * k, 512 * k + 512))
 
     def consts_b():
-        ts(cf("FX", 0, 40, 5), cf("FX", 0, 40, 5), 16.0, ADD)
         ts(ch("PERM"), cb("FP"), Pc, EQ)
         ts(cb("WM"), cf("FW"), pd_(3), EQ, -BIG, MUL)
-        ts(ch("XSEL"), cf("FX"), Pc, EQ)
-        ts(cf("XCONST", 0, 40, 5), cf("UB"), 4096.0, MUL, 2048.0, ADD)
         cp(whole("cT0"), col("PS", 128, 136))
         cp(col("KC", 8, 16), col("PS", 128, 136))
-        for k in range(8):
-            ts(ch("SELG", 128 * k, 128 * k + 128), cb("ONES"), cf("BOF", k, k + 1), MUL)
 
     def consts_c():
+        ts(ch("XSEL"), cf("FX"), Pc, EQ)
         for k in range(3):
-            ts(ch("NBLK3", 128 * k, 128 * k + 128), cb("JG"), gcol, EQ, -1.0, MUL)
-            ts(cb("TRI3", 128 * k, 128 * k + 128), cb("F16"), cf("P16", k, k + 1), ALU.is_le, 4096.0, MUL)
-        ms(ch("ONESH"), 1.0)
-        ts(cf("DUML"), cf("DUML"), rcol, ADD)
-        ms(whole("AMG"), 0.0)
-        ts(cb("NE3"), cb("NE3"), Pc, EQ, -1.0, MUL)
+            times(ch("NBLK3", 128 * k, 128 * k + 128), cb("BLKB"), -1.0)
+        times(cb("KID"), cb("IDN"), 1024.0)
+        times(cb("HID"), cb("IDN"), -512.0)
+        times(cf("IDF"), cb("IDN"), 1.0)
+        times(cf("NIDF"), cb("IDN"), -1.0)
+        fill(tf(15), 8, 128)
 
+    def consts_d():
+        for k in range(3):
+            ts(cb("TRI3", 128 * k, 128 * k + 128), cb("F16"), cf("P16", k, k + 1), ALU.is_le, 4096.0, MUL)
+        ms(whole("AMG"), 0.0)
+
+    def consts_e():
+        for k in range(8):
+            if k % 4:
+                threshold(k)
+        times(cf("WT"), cb("BLKB"), pd_(15))
+        fill(col("YC", W, W + DUM), DUM, 0)
+
+    cp(whole("GL"), whole("GI"))
     columns(0)
-    columns(1)
     options_a()
     options_b()
+    columns(1)
     consts_b()
     columns(2)
     options_c()
@@ -475,15 +487,17 @@ def rank_program(g, core, T, topo):
         mm(col("DA", 0, n), col(GE, 15, 143, rows=rows), cb("NID", 0, n, rows=rows), False, True)
 
     def write(n, s, lst, t):
-        tt(whole("WV" + s), col("DA", 0, n), whole("DV" + s), MUL)
-        if t < RO - 1:
+        if s == "3":
+            if t == RO - 1:
+                mm(col("DB", 0, n), cf("WT"), whole("CF3"), True, False)
+            tt(whole("WV3"), col("DA", 0, n), whole("DV3"), MUL)
+        if t < RO - 1 or s == "2":
             tt(IND(IS, lst), whole("WV" + s), whole("CF" + s), ADD)
-            return
-        tt(whole("NC" + s), whole("WV" + s), whole("CF" + s), ADD)
-        mm(col("DB", 0, n), cf("WT"), whole("NC" + s))
-        if s == "2":
-            cp(IND(IS, lst), whole("NC" + s))
-        act(whole("YP" + s), col("DB", 0, n), AF.Copy)
+        if t == RO - 1:
+            if s == "2":
+                mm(col("DB", 0, n), cf("WT"), whole("CF2"), True, False)
+            mm(col("DB", 0, n), cf("WT"), whole("WV" + s), False, True)
+            act(whole("YP" + s), col("DB", 0, n), AF.Copy)
 
     def patch(s, lst):
         cp(IND(col("YC", 0, W + DUM), lst), whole("YP" + s))
@@ -495,20 +509,23 @@ def rank_program(g, core, T, topo):
         last = t == RO - 1
         cT, cN = "cT%d" % (t % 2), "cT%d" % (1 - t % 2)
         cp(whole("COA"), IND(IW, col("OL", 8 * QA, 32)))
+        act(col("COLF", 0, 128 * QD), IND(IW, col("OL", 0, 8 * QD)), AF.Copy)
         for q in range(NQ, 16):
             for u in range(8):
                 o = 4 * (((q // 4 - QA) * 8 + u) * 4 + q % 4)
                 s = 64 * (8 * (q - NQ) + u)
                 act(col("H", s, s + 64), IND(XW, col("COA", o, o + 4)), AF.Abs, bias=col("A", 16 * u + q), scale=-1.0)
-        cp(col("COLF", 0, 128 * QD), IND(IW, col("OL", 0, 8 * QD)))
         cp(whole("C2"), IND(col("COLF", 0, 128 * QD), lu("LC2")))
         cp(whole("CO2"), IND(IW, col("GL", 0, 8)))
         n = 128 * NQ
-        for k in range(4):
-            tt(col("D", n * k, n * k + n), IND(XW, col("C2", 8 * NQ * k, 8 * NQ * (k + 1))), whole("AR"), SUB)
-            if k == 2:
+        for what, k in ("d0", "d1", "r0", "d2", "r1", "c0", "r2", "d3", "r3"):
+            k = int(k)
+            if what == "d":
+                tt(col("D", n * k, n * k + n), IND(XW, col("C2", 8 * NQ * k, 8 * NQ * (k + 1))), whole("AR"), SUB)
+            elif what == "r":
+                ts(col("R2", n * k, n * k + n), col("D", n * k, n * k + n), 0.0, MAX, 2.0, MUL)
+            else:
                 cp(col("COLF", 128 * QD, 512), IND(IW, col("OL", 8 * QD, 32)))
-            ts(col("R2", n * k, n * k + n), col("D", n * k, n * k + n), 0.0, MAX, 2.0, MUL)
         cp(whole("C16"), IND(col("COLF", 0, 512), lu("LC16")))
         if last:
             ysum(0, "PW")
@@ -530,9 +547,11 @@ def rank_program(g, core, T, topo):
                 o, s = col("DA", 8 * NQ * k + q, 8 * NQ * (k + 1), NQ), 128 * (NQ * k + q)
                 mm(o, col("D", s, s + 128), cb("NBO"), False, False)
                 mm(o, col("R2", s, s + 128), cb("BO"), False, k == 3 and q == NQ - 1)
+        if not last:
+            zero(col("PW", 0, 384))
         done = 0
         for k in range(4):
-            upto = (NA * (k + 1)) // 4 - 1
+            upto = (3, 5, 6, 7)[k] * NA // 8
             for q in range(done, upto):
                 pa(q)
             done = upto
@@ -548,17 +567,17 @@ def rank_program(g, core, T, topo):
             act(col("YC", 0, 512), whole("PW"), AF.Copy)
         else:
             act(whole("CF2"), IND(IW, col("GL", 0, 8)), AF.Copy)
-        act(col("DL", 0, 384), col("DL", 0, 384), AF.Abs)
-        ga = GA // 2 if last else GA
-        act(col("G2", 0, 16 * ga), IND(XW, col("CO2", 0, ga)), AF.Copy)
         act(whole("XC2"), IND(XW, col("GL", 0, 8)), AF.Copy)
+        act(tf(9), whole(cT), AF.Identity, bias=-2176.0)
+        act(col("DL", 0, 384), col("DL", 0, 384), AF.Abs)
+        ga = GA // 2 if last or t == 0 else GA
+        act(col("G2", 0, 16 * ga), IND(XW, col("CO2", 0, ga)), AF.Copy)
         led = lambda k: V("LED", ALL, sl(8 * k, 8 * k + 8), ALL)
         lea = lambda k: V("LEA", ALL, sl(8 * k, 8 * k + 8), ALL)
         zero(col("PS", 0, 32))
         for k in range(3):
             mm(col("PS", 3 - k, 32, 4), led(k), cb("KBO"), False, False)
         ts(V("LEA", ALL, ALL, sl(NQ, 16)), col("DB", 0, 32 * NA), 0.0, ALU.is_gt, 0.40625, SUB)
-        ts(tf(9), whole(cT), 2176.0, SUB)
         for u in range(4):
             mm(col("PS", 8 * u, 8 * u + 8), lea(u), cb("CM"), False, u == 3)
         zero(col("PQ", 128, 160))
@@ -598,7 +617,8 @@ def rank_program(g, core, T, topo):
         for pp in range(3):
             lin(pp)
         member(0)
-        zero(col("PW", 0, 384))
+        if last:
+            zero(col("PW", 0, 384))
         mm(col("PQ", 0, 128), whole("FC"), ch("PERM"), True, False)
         mm(col("PQ", 0, 128), cb("ONES", rows=R1), cb("RANK", rows=R1), False, True)
         for pp in range(3, 8):
@@ -614,17 +634,16 @@ def rank_program(g, core, T, topo):
             if pp == 4:
                 for k in range(3):
                     mm(col("PW", k, 384, 3), svm(k + 1), cb("BIGSEL"), False, False)
-            if pp == 5:
-                tt(whole("XB"), col("DA", 64, 104), cf("XCONST"), ADD)
-                scan(whole("XC"), col("DA", 0, 40), whole("XB"), 0.0, MIN, MAX)
         member(6)
         tally(5)
         member(7)
+        tt(whole("XB"), col("DA", 64, 104), cf("XCONST"), ADD)
+        same_gate(0)
+        same_gate(1)
         tally(6)
-        for k in range(4):
-            same_gate(k)
+        same_gate(2)
         tally(7)
-        for k in range(4, 8):
+        for k in range(3, 8):
             same_gate(k)
         act(col("G2", 16 * ga, 2048), IND(XW, col("CO2", ga, L)), AF.Copy)
 
@@ -645,10 +664,12 @@ def rank_program(g, core, T, topo):
 
         def far2_next():
             far2.pop(0)()
-        ts(tf(5), col("XB", 1, 40, 5), 12288.0, SUB)
+        act(tf(14), col("XB", 1, 40, 5), AF.Identity, bias=-12288.0)
+        if t == 0:
+            consts_d()
         scan(whole("S1"), cb("M3"), col("PW", 0, 384), 0.0, MUL, MAX)
+        scan(whole("XC"), col("DA", 0, 40), whole("XB"), 0.0, MIN, MAX)
         scan(whole("S2"), col("S1", 2, 384, 3), col("PQ", 0, 128), BIG, MIN, MAX)
-        far2_next()
         tt(col("KC", 0, 8), col("S2", 15, 128, 16), col("XC", 4, 40, 5), MIN)
         ts(ki(0), col("KC", 0, 8), 4095, AND)
         ts(ki(1, 2), whole("KC"), 1, AND)
@@ -656,48 +677,52 @@ def rank_program(g, core, T, topo):
         mm(col("DA", 0, 8), cb("TRIP"), whole("LB"))
         mm(col("DA", 8, 16), cb("ONES"), whole("LB"))
         far2_next()
+        far2_next()
         ts(ki(3, 2), whole("KC"), W - 1, AND)
         ts(tf(2, 2), ki(1, 2), -2.0, MUL, -2047.0, ADD)
-        ts(tf(11), ki(0), 2048.0, ALU.is_lt)
+        tt(tf(11), tf(9), whole("LB"), MUL)
         tt(tf(0, 2), tf(2, 2), ki(3, 2), ADD)
-        far2_next()
         for k in range(8):
             ts(V("PA", ALL, ALL, k, ALL), cb("S48"), col("DA", k), EQ, col("TF", k), MUL)
         for u in range(3):
             mm(col("PS", 136 + u, 137 + u + u // 2), V("PA", ALL, u, ALL, ALL), ch("ONESH", 0, 1 + u // 2))
         mm(V("PW", R49, sl(0, 384)), ch("ONESH", 0, 49), whole("PA"), True, False)
         mm(V("PW", R49, sl(0, 384)), cb("IDN", 0, 49, rows=R48), cb("TRI3", rows=R48), False, False)
-        tt(tf(7), ki(3), tf(5), SUB)
-        tt(tf(10), tf(9), tf(11), MUL)
+        far2_next()
+        tt(tf(7), ki(3), tf(14), SUB)
         ts(whole("MA%d" % t), col("PS", 136, 140), float(W), ADD)
         send(t, "MA%d" % t, "LA%d" % t, "ra%d" % t)
         cp(col("AL", 0, 4), col("PS", 136, 140))
-        tt(tf(8), tf(7), tf(11), MUL)
+        tt(tf(10), tf(7), whole("LB"), MUL)
         tt(col("AMG", 0, 48), IND(col("AL", 0, 4), lu("LR8", 0, 3)), cb("MK", 0, 48), MUL)
-        tt(tf(12), tf(8), tf(5), ADD)
+        tt(tf(12, 2), tf(10, 2), tf(14, 2), ADD)
         mm(V("PW", R49, sl(0, 384)), col("AMG", 0, 49), ch("NBLK3"), False, True)
-        far2_next()
-        tt(whole("NM"), IND(tf(12), lu("LR8")), cb("MK", 0, L), MUL)
-        mm(col("PS", 176, 184), whole("NM"), ch("BOH"))
-        far2_next()
-        act(whole("LR"), IND(tf(11), lu("LR8")), AF.Copy)
-        ts(V("EQ3", R49, ALL), V("PW", R49, sl(0, 384)), 0.0, EQ)
-        cp(whole("NL"), col("PS", 176, 184))
-        act(whole("XN"), IND(XW, col("NL", 0, 8)), AF.Copy)
-        act(whole("MR"), IND(tf(12), lu("LR8")), AF.Copy)
         far2_next()
         for k in range(8):
             ts(V("PB", ALL, ALL, k, ALL), cb("S48"), col("DA", k), EQ, col("TF", 8 + k), MUL)
-        while far2:
-            far2_next()
-        mm(col("L1", 0, L), cb("IDN"), whole("XN"), True, False)
-        mm(col("L1", 0, L), cb("NID"), whole("A"), False, True)
-        act(whole("AA"), col("L1", 0, L), AF.Abs)
+            if k == 7:
+                ts(V("EQ3", R49, ALL), V("PW", R49, sl(0, 384)), 0.0, EQ)
         for u in range(3):
             mm(col("PS", 160 + u), V("PA", ALL, u, ALL, ALL), ch("ONESH", 0, 1), True, False)
             mm(col("PS", 160 + u), V("EQ3", R49, sl(128 * u, 128 * u + 128)), cb("P4096", 0, 1, rows=R49), False, True)
         for u in range(3):
             mm(col("PS", 164 + u), V("PB", ALL, u, ALL, ALL), ch("ONESH", 0, 1))
+        far2_next()
+        act(tf(8), whole("LB"), AF.Copy)
+        act(whole("LR"), IND(col("LB", 0, 8), lu("LR8")), AF.Copy)
+        act(whole("MR"), IND(tf(12), lu("LR8")), AF.Copy)
+        tt(whole("NM"), IND(tf(12), lu("LR8")), cb("MK", 0, L), MUL)
+        mm(col("PW", 400, 408), whole("NM"), ch("BOH"))
+        to_list(col("PS", 160, 163), 3, col("MB%d" % t, 0, 3), 0)
+        ts(col("MB%d" % t, 3, 6), col("PS", 164, 167), float(W), ADD)
+        send(t, "MB%d" % t, "LB%d" % t, "rb%d" % t)
+        cp(whole("NL"), col("PW", 400, 408))
+        act(whole("XN"), IND(XW, col("NL", 0, 8)), AF.Copy)
+        while far2:
+            far2_next()
+        mm(col("L1", 0, L), cb("IDN"), whole("XN"), True, False)
+        mm(col("L1", 0, L), cb("NID"), whole("A"), False, True)
+        act(whole("AA"), col("L1", 0, L), AF.Abs)
         mm(col("L0", 0, L), cb("IDN"), whole("XN"), True, False)
         mm(col("L0", 0, L), cb("IDN"), whole("A"), False, False)
         mm(col("L0", 0, L), whole("LR"), cb("KID"), False, True)
@@ -706,76 +731,86 @@ def rank_program(g, core, T, topo):
         mm(col("L1", 0, L), whole("MR"), cf("IDF"), True, False)
         mm(col("L1", 0, L), cf("NIDF"), whole("CF2"), False, True)
         act(whole("DV2"), col("L1", 0, L), AF.Copy)
-        ts(tf(13), tf(10), 128.0, ADD)
-        rec("v", lambda x, o, i: x.tensor_reduce(o, i, AX.X, ADD), col("TF", 120), col("DA", 8, 16))
-        ts(col("MB%d" % t, 3, 6), col("PS", 164, 167), float(W), ADD)
-        to_list(col("PS", 160, 163), 3, col("MB%d" % t, 0, 3), 0)
-        send(t, "MB%d" % t, "LB%d" % t, "rb%d" % t)
-        ts(whole("AH"), col("L0", 0, L), 0.5, MUL, 512.25, SUB)
+        rec("v", lambda x, o, i: x.tensor_reduce(o, i, AX.X, ADD), col("TF", 32), col("DA", 8, 16))
+        act(tf(6), whole(cT), AF.Identity, bias=col("TF", 32), scale=37.0)
         tt(whole("VM"), IND(tf(13), lu("LR8")), cb("MK", 0, L), MUL)
+        tt(ki(5), ki(3), ki(4), MUL)
+
+        def first_of_gate(k):
+            ts(V("EQ2", ALL, ALL, k, ALL), col(("DB", "DL")[k // 4], 128 * (k % 4), 128 * (k % 4) + 128), col(cT, k), EQ, col("TF", 64 + k), MUL)
+        first_of_gate(0)
+        scan(whole("PM2"), cb("NM16"), col("PQ", 0, 128), 0.0, MUL, MAX)
+        first_of_gate(1)
+        cp(whole("PX"), col("PM2", 15, L, 16))
+        first_of_gate(2)
+        tt(col("GE2", 16, 144), IND(col("PX", 0, 8), lu("LR8")), whole("PM2"), EQ)
+        far_mask_b(L, "GE2")
+        first_of_gate(3)
+        first_of_gate(4)
+        ts(whole("AH"), col("L0", 0, L), 0.5, MUL, 512.25, SUB)
+        first_of_gate(5)
         tt(whole("AO" if last else "A"), whole("AH"), col("L0", L, 2 * L), MAX)
         if not last:
             act(whole("AR"), IND(col("A", 0, L), lu("LAR")), AF.Copy)
         else:
             dma("s", V("ya", ALL), whole("AO"))
-        far_mask_a(L, "PM2", "GE2")
-        far_mask_b(L, "GE2")
-        for k in range(8):
-            ts(V("EQ2", ALL, ALL, k, ALL), col(("DB", "DL")[k // 4], 128 * (k % 4), 128 * (k % 4) + 128), col(cT, k), EQ, col("TF", 88 + k), MUL)
+        if t == 0:
+            consts_e()
+            ts(cb("NE3"), cb("NE3"), Pc, EQ, -1.0, MUL)
+        for k in range(6, 8):
+            first_of_gate(k)
         mm(col("PS", 192, 200), whole("VM"), ch("BOH"), True, False)
         for u in range(8):
             mm(col("PS", 192 + u), V("EQ2", ALL, u, ALL, ALL), cb("P4096", 0, 1), False, u == 7)
-        tt(ki(5), ki(3), ki(4), MUL)
-        ts(tf(6), whole(cT), 37.0, MUL, col("TF", 120), ADD)
         ts(ki(6), ki(5), 4, SHR)
-        to_list(col("PS", 192, 200), 8, whole("SL2"), 8)
+        tt(whole("WV2"), col("DA", 0, L), whole("DV2"), MUL)
         tt(ki(7), ki(6), tf(6), ADD)
+        to_list(col("PS", 192, 200), 8, whole("SL2"), 8)
         write(L, "2", col("SL2", 0, 8), t)
-        ts(col("KC", 8, 16), ki(7), W - 1, AND)
         arrive(t, "LA%d" % t, "ra%d" % t)
         la = col("LA%d" % t, 0, 3)
         cp(whole("CO3"), IND(IS, la))
         cp(whole("XC3"), IND(XS, la))
         act(col("G3", 0, 384), IND(XS, col("CO3", 0, 24)), AF.Copy)
         mm(V("PW", R48, sl(0, L)), whole("XC3"), cb("IDN"))
+        ts(col("KC", 8, 16), ki(7), W - 1, AND)
+        cp(V("XT3", R48, ALL), V("PW", R48, sl(0, L)))
+        act(whole("CF3"), IND(IS, la), AF.Copy)
+        cp(col("G3", 384, 768), IND(XS, col("CO3", 24, 48)))
         if not last:
             tt(whole("CMT"), IND(col("KC", 8, 16), lu("LR8")), cb("MK", 0, L), MUL)
-        cp(V("XT3", R48, ALL), V("PW", R48, sl(0, L)))
-        if not last:
-            mm(col("PS", 144, 152), whole("CMT"), ch("BOH"))
-        cp(col("G3", 384, 768), IND(XS, col("CO3", 24, 48)))
         for b in range(2):
             mm(col("L%d" % b, 0, 384), V("XT3", R48, ALL), cb("NE3", 384 * b, 384 * b + 384, rows=R48), True, False)
             mm(col("L%d" % b, 0, 384), cb("IDN"), col("G3", 384 * b, 384 * b + 384), False, True)
             act(col("H3", 384 * b, 384 * b + 384), col("L%d" % b, 0, 384), AF.Abs)
         if not last:
-            cp(whole("GL"), col("PS", 144, 152))
+            mm(col("PS", 144, 152), whole("CMT"), ch("BOH"))
             mm(col("DL", 2 * L, 3 * L), whole("CMT"), ch("IDH"))
-            cp(whole("CF3"), IND(IS, la))
-            options_a()
-            options_b()
             cp(whole(cN), col("KC", 8, 16))
+            cp(whole("GL"), col("PS", 144, 152))
+            cp(whole("CMG"), col("DL", 2 * L, 3 * L))
+            options_a()
         else:
-            cp(whole("CF3"), IND(IS, la))
             patch("2", col("SL2", 0, 8))
             cp(whole("G16"), col("KC", 8, 16))
             mm(V("PS", R8, sl(256, 384)), whole("G16"), ch("IDH"))
+        if last:
+            cp(whole("YG"), V("PS", R8, sl(256, 384)))
+            dma("s", V("yg", ALL), whole("YG"))
         arrive(t, "LB%d" % t, "rb%d" % t)
         cp(col("BF", 0, 3), col("LB%d" % t, 3, 6))
         tt(whole("BM"), IND(col("BF", 0, 3), lu("LR8", 0, 3)), cb("MK", 0, 48), MUL)
-        if not last:
-            cp(whole("CMG"), col("DL", 2 * L, 3 * L))
-            options_c()
-        else:
-            cp(whole("YG"), V("PS", R8, sl(256, 384)))
-            dma("s", V("yg", ALL), whole("YG"))
         for p in range(16):
             mm(V("PQ", R48, sl(p, 128, 16)), col("H3", p, 768, 16), cb("BO"))
         mm(col("PW", 0, 48), ch("BLKH"), whole("BM"), True, False)
         mm(col("PW", 0, 48), cf("NIDF"), whole("CF3"), False, True)
         act(whole("DV3"), col("PW", 0, 48), AF.Copy)
+        if not last:
+            options_b()
         far_mask_a(48, "PM3", "GE3")
         far_mask_b(48, "GE3")
+        if not last:
+            options_c()
         write(48, "3", col("LB%d" % t, 0, 3), t)
     patch("3", col("LB%d" % (RO - 1), 0, 3))
     dma("s", V("yc", ALL), V("YC", sl(0, 128, 16), sl(0, W)))

@@ -1,14 +1,17 @@
+import math
 import numpy as np
 from concourse.mybir import AluOpType as ALU, AxisListType as AX, ActivationFunctionType as AF
 
 W, L, RO = 2048, 128, 4
 DUM = 128
 BIG = 2097152.0
+CNT = 65536.0
 H16 = "float16"
-NQ = 8
-NA = 16 - NQ
-QD, QA = (NQ + 3) // 4, NQ // 4
-GA = 32
+NV = 64
+ENG = 8
+FILES = ("H", "D")
+CYCLE, TENSOR, GATHER, SCATTER, WAKE, HOP = 0.00083, 0.00042, 1.56, 3.8, 0.19, 2.3
+PASSES, SHAKE = 30, 0.4
 
 
 def _pack(items):
@@ -19,74 +22,84 @@ def _pack(items):
     return at, n
 
 
-CB, NCB = _pack([("ONES", 128), ("IDN", 128), ("NID", 128), ("MK", 512), ("BO", 8), ("NBO", 8), ("KBO", 8), ("CM", 8), ("BIGSEL", 128), ("WM", 16),
-                 ("VALK", 160), ("VALC", 40), ("X3", 40), ("RANK", 128), ("TRIP", 128), ("TRI2", 128), ("TRI3", 384), ("S48", 48),
-                 ("THA", 32 * NQ), ("THB", 32 * NA), ("NTH", 1024), ("ZR", 128), ("P4096", 16), ("J", 128), ("NM16", 128), ("M3", 384), ("BLK5", 40),
-                 ("F16", 128), ("JG", 128), ("F5", 40), ("JA", 8 * NQ), ("JB", 8 * NA), ("F3", 128), ("F8", 128), ("FP", 128), ("BLKB", 128),
-                 ("KID", 128), ("HID", 128), ("NE3", 768)])
-CH, NCH = _pack([("SELO", 512), ("SIG", 128), ("DEL", 128), ("FSEL", 1024), ("PERM", 128), ("XSEL", 40), ("IDH", 128), ("BOH", 8), ("BLKH", 128),
-                 ("SELG", 1024), ("ONESH", 128), ("NBLK3", 384)])
-CF, NCF = _pack([("P", 8), ("PD", 32), ("FO", 128), ("GO", 4), ("FC", 8), ("FW", 16), ("FX", 40), ("XCONST", 40), ("UB", 8), ("FR", 128),
-                 ("P16", 3), ("IDF", 128), ("NIDF", 128), ("BASEF", 32), ("DUML", 8), ("WT", 128), ("THF", 8), ("BOF", 8), ("LC2F", 32), ("LC16F", 24)])
-LU, NLU = _pack([("LR8", 8), ("LSV", 32), ("LC2", 2 * NQ), ("LAR", 8 * NQ), ("LC16", 24)])
+CB, NCB = _pack([("ONES", 128), ("IDN", 128), ("NID", 128), ("MK", 128), ("BO", 224), ("NBO", 8), ("K2", 40), ("CW", 40), ("TWO", 128),
+                 ("WIDE", 144), ("W0", 144), ("KID", 128), ("THS", 256), ("NTH", 512), ("FG", 384), ("NM16", 256), ("GW", 384), ("G1W", 8), ("WM", 16), ("RANK", 128),
+                 ("TRIP", 128), ("TRI2", 128), ("TRI3", 384), ("S48", 48), ("P4096", 16), ("J", 128), ("M3", 384), ("F16", 128), ("JG", 128),
+                 ("F3", 128), ("F8", 128), ("FP", 128), ("BLKB", 128), ("K4", 128), ("O16", 128), ("C1024", 128),
+                 ("SELO", 512), ("SIG", 128), ("DEL", 128), ("FSEL", 1024), ("PERM", 128), ("XSEL", 48), ("SELG", 1024), ("NBLK3", 384)])
+CF, NCF = _pack([("P", 8), ("PD", 32), ("FO", 128), ("GO", 4), ("FW", 16), ("FX", 48), ("FK", 40), ("FV", 144), ("XCONST", 48), ("UB", 8), ("FR", 128),
+                 ("P16", 3), ("DUML", 8), ("WT", 128), ("SEL8", 128), ("THF", 4), ("THC", 4), ("THP", 12), ("BOF", 8), ("J32", 128), ("E16", 1)])
 S, F, B, I32, U = "sbuf", "float32", "bfloat16", "int32", "uint16"
 SCRATCH = {
-    "CB": (S, [128, NCB], B), "CH": (S, [128, NCH], B), "CF": (S, [128, NCF], F), "LU": (S, [128, NLU], U), "LI": (S, [128, NLU], I32),
-    "PI": (S, [128, 32], I32), "TH": (S, [8, 12], I32), "GI": (S, [128, 8], I32), "GF": (S, [128, 8], F),
+    "CB": (S, [128, NCB], B), "CF": (S, [128, NCF], F), "LR8": (S, [128, 8], U), "LI": (S, [128, 8], I32),
+    "PI": (S, [128, 32], I32), "TH": (S, [16, 12], I32), "GI": (S, [128, 8], I32),
     "IT": (S, [128, W], I32), "IC": (S, [128, W + DUM], F), "AW": (S, [128, W], I32), "X": (S, [128, W + 16], B), "YC": (S, [128, W + DUM], F),
-    "A": (S, [128, L], B), "AR": (S, [128, 128 * NQ], B), "GL": (S, [128, 8], U), "OL": (S, [128, 32], U), "R": (S, [128, L], H16),
-    "cT0": (S, [128, 8], F), "cT1": (S, [128, 8], F), "CMG": (S, [128, L], H16), "CMT": (S, [128, L], H16),
-    "COA": (S, [128, 512 - 128 * QA], U), "COLF": (S, [128, 512], F), "C2": (S, [128, 32 * NQ], U), "C16": (S, [128, 384], H16),
-    "H": (S, [128, 512 * NA], B), "D": (S, [128, 512 * NQ], B), "R2": (S, [128, 512 * NQ], B), "LED": (S, [128, 32, 16], B), "LEA": (S, [128, 32, 16], B),
-    "FI": (S, [128, 32], F), "FL": (S, [128, 8], U), "FC": (S, [128, L], H16), "SV": (S, [128, 32], F), "SVM": (S, [128, 512], B),
-    "AB": (S, [128, 3, 384], F), "EE": (S, [128, 8, 384], B), "XB": (S, [128, 40], F), "XC": (S, [128, 40], F),
-    "S1": (S, [128, 384], F), "S2": (S, [128, L], F), "KC": (S, [128, 16], I32), "KI": (S, [128, 64], I32), "TF": (S, [128, 128], F), "LB": (S, [128, 8], B),
-    "PA": (S, [128, 3, 8, 16], H16), "PB": (S, [128, 3, 8, 16], H16), "EQ3": (S, [128, 384], B), "EQ2": (S, [128, 8, 8, 16], B),
-    "AL": (S, [128, 8], F), "AMG": (S, [128, 64], H16),
-    "ZT": (S, [128, 16], F), "SL2": (S, [128, 8], U), "NM": (S, [128, L], H16), "NL": (S, [128, 8], U), "LR": (S, [128, L], B),
-    "XN": (S, [128, L], B), "AA": (S, [128, L], B), "AH": (S, [128, L], I32),
-    "AO": (S, [128, L], F), "VM": (S, [128, L], H16), "MR": (S, [128, L], F),
-    "CO2": (S, [128, L], U), "CF2": (S, [128, L], F), "XC2": (S, [128, L], B), "G2": (S, [128, 2048], B), "H2": (S, [128, 2048], B),
-    "PM2": (S, [128, L], F), "GE2": (S, [128, 144], B), "DV2": (S, [128, L], F), "WV2": (S, [128, L], F), "NC2": (S, [128, L], F), "YP2": (S, [128, L], F),
+    "NUM": (S, [128, W + 16], F),
+    "A": (S, [128, L], B), "A4": (S, [128, 512], B), "GL": (S, [128, 8], U), "OL": (S, [128, 32], U), "R": (S, [128, L], H16),
+    "cT": (S, [128, 8], F), "C5": (S, [128, 8], F), "CMG": (S, [128, L], H16), "CMT": (S, [128, L], H16),
+    "COA": (S, [128, 512], U), "C16": (S, [128, 512], H16),
+    "H": (S, [128, 4096], B), "D": (S, [128, 4096], B), "R2": (S, [128, 4096], B), "AR": (S, [128, 1024], B), "C2": (S, [128, 256], U),
+    "LE": (S, [128, 512], B), "LE2": (S, [128, L], B), "SC": (S, [128, 512], B),
+    "PG": (S, [128, 512], H16), "PL": (S, [128, 32], U), "DP": (S, [128, 512], B), "RP": (S, [128, 512], B),
+    "XB": (S, [128, 48], F), "KEY": (S, [128, 40], I32), "KA": (S, [128, 8], I32), "KM": (S, [128, L], H16), "FL": (S, [128, 8], U), "FC": (S, [128, L], H16),
+    "SVG": (S, [128, L], B), "XC": (S, [128, 16], F), "AB": (S, [128, 384], F), "EE": (S, [128, 8, 384], B),
+    "S1": (S, [128, 384], F), "S2": (S, [128, L], F), "KC": (S, [128, 16], I32), "KI": (S, [128, 64], I32), "TF": (S, [128, 32], F), "LB": (S, [128, 8], B),
+    "PA": (S, [128, 3, 8, 16], H16), "PB": (S, [128, 3, 8, 16], H16), "EQ3": (S, [128, 384], B), "EQ2": (S, [128, 1024], B),
+    "AL": (S, [128, 8], F), "AMG": (S, [128, 64], H16), "ZT": (S, [128, 8], F), "ZZ": (S, [128, 8], F), "ZM": (S, [128, L], F), "SL2": (S, [128, 8], U),
+    "NM": (S, [128, L], H16), "NL": (S, [128, 8], U), "X0": (S, [128, L], B), "OL0": (S, [128, 8], U), "AA": (S, [128, L], B),
+    "XN": (S, [128, L], B), "AH": (S, [128, L], I32), "AO": (S, [128, L], F),
+    "CO2": (S, [128, L], U), "CF2": (S, [128, L], F), "XC2": (S, [128, L], B),
+    "G2": (S, [128, 2048], B), "H2": (S, [128, 2048], B),
+    "PM2": (S, [128, L], F), "GE2": (S, [128, 144], B), "DV2": (S, [128, L], F), "WV2": (S, [128, L], F), "YP2": (S, [128, L], F),
     "CO3": (S, [128, 48], U), "CF3": (S, [128, 48], F), "XC3": (S, [128, 48], B), "G3": (S, [128, 768], B), "H3": (S, [128, 768], B),
-    "PM3": (S, [128, L], F), "GE3": (S, [128, 144], B), "DV3": (S, [128, 48], F), "WV3": (S, [128, 48], F), "NC3": (S, [128, 48], F), "YP3": (S, [128, 48], F),
-    "BF": (S, [128, 8], F), "PX": (S, [128, 8], F), "XT3": (S, [128, L], B), "BM": (S, [128, 48], H16), "G16": (S, [128, 8], H16), "YG": (S, [8, L], F),
+    "PM3": (S, [128, L], F), "GE3": (S, [128, 144], B), "DV3": (S, [128, 48], F), "WV3": (S, [128, 48], F), "YP3": (S, [128, 48], F),
+    "BG": (S, [128, 48], F), "OH": (S, [128, 48], F), "PX": (S, [128, 8], F), "G16": (S, [128, 8], H16), "YG": (S, [8, L], F),
 }
 for _t in range(RO):
-    for _n, _w in (("MA", 4), ("MB", 6), ("LA", 4), ("LB", 6)):
+    for _n, _w in (("MA", 4), ("MB", 8), ("LA", 4), ("LB", 8)):
         SCRATCH["%s%d" % (_n, _t)] = (S, [128, _w], U)
-for _n in ("DA", "DB", "PS", "L0", "L1", "DL", "PW", "PQ"):
+for _t in range(RO - 1):
+    SCRATCH["PT%d" % _t] = (S, [128, W + DUM], F)
+for _n in ("BV", "BS", "PS", "L0", "L1", "DL", "PW", "PQ"):
     SCRATCH[_n] = ("psum", [128, 512], F)
-SEMAPHORES = ["cv", "ca", "cp", "cg", "snt"] + ["d%d" % k for k in range(16)] + ["%s%d" % (n, t) for n in ("ra", "rb") for t in range(RO)]
+SEMAPHORES = ["cv", "ca", "cp", "cg", "snt"] + ["d%d" % k for k in range(16)] + ["s%s%d" % (n, t) for n in ("LA", "LB", "MA", "MB") for t in range(RO)]
 
 
-def route(src, dst, cores, topo):
+def target(r, t, cores):
+    return cores[(r + 1 + t % (len(cores) - 1)) % len(cores)]
+
+
+def relay(src, cores, topo):
+    own = [r for r, c in enumerate(cores) if c in topo.cores_of(src)]
+    r, t = [(r, t) for t in range(RO) for r in own if not topo.may_write(cores[r], target(r, t, cores))][0]
+    near = [c for c in topo.cores_of(src) if c not in cores and topo.may_write(c, target(r, t, cores))]
+    near.sort(key=lambda c: topo.die(c) != topo.die(cores[r]))
+    return near[0]
+
+
+def first_hop(r, t, cores, topo):
+    src, dst = cores[r], target(r, t, cores)
     if topo.may_write(src, dst):
-        return [src, dst]
-    near = [c for c in topo.cores_of(src) if c not in cores and topo.may_write(c, dst)]
-    near.sort(key=lambda c: topo.die(c) != topo.die(src))
-    return [src, near[0], dst]
+        return dst, "L"
+    return relay(src, cores, topo), "LM"[[c for c in cores if c in topo.cores_of(src)].index(src)]
 
 
-def width(src, dst, topo):
-    return len(topo.engines(src, dst))
-
-
-def hand(g, T, topo, src, dst, out, in_, sem):
+def hand(g, T, topo, src, dst, out, in_):
     rid, pid = topo.addr(dst, src)
-    g.remote_dma(T[out][:], T[in_][:], T.sem[sem], T.sem["snt"], pid, rid, topo.mask(src, dst))
-    return width(src, dst, topo)
+    g.remote_dma(T[out][:], T[in_][:], T.sem["s" + out], T.sem["snt"], pid, rid, sum(1 << e for e in topo.engines(src, dst)[:ENG]))
 
 
 def relay_program(g, core, T, topo):
-    cores, n, sent = list(T.cores), len(T.cores), 0
+    cores, sent = list(T.cores), 0
     for t in range(RO):
-        for r in range(n):
-            way = route(cores[r], cores[(r + 1 + t % (n - 1)) % n], cores, topo)
-            if len(way) == 3 and way[1] == core:
-                for buf, sem in (("LA", "ra"), ("LB", "rb")):
-                    g.wait_ge(T.sem["%s%d" % (sem, t)], width(way[0], core, topo))
-                    sent += hand(g, T, topo, core, way[2], "%s%d" % (buf, t), "%s%d" % (buf, t), "%s%d" % (sem, t))
+        for part in "AB":
+            for r in range(len(cores)):
+                hop, letter = first_hop(r, t, cores, topo)
+                if hop == core:
+                    buf = "%s%s%d" % (letter, part, t)
+                    g.wait_ge(T.sem["s" + buf], ENG)
+                    hand(g, T, topo, core, target(r, t, cores), "L%s%d" % (part, t), buf)
+                    sent += ENG
     if sent:
         g.wait_ge(T.sem["snt"], sent)
 
@@ -113,53 +126,144 @@ def _c(buf, tab):
     return f
 
 
-cb, ch, cf, lu, li = _c("CB", CB), _c("CH", CH), _c("CF", CF), _c("LU", LU), _c("LI", LU)
-_own = ch
-
-
-def ch(name, *a, **k):
-    alias = {"IDH": "IDN", "BOH": "BO", "BLKH": "BLKB", "ONESH": "ONES"}
-    return cb(alias[name], *a, **k) if name in alias else _own(name, *a, **k)
+cb, cf = _c("CB", CB), _c("CF", CF)
 
 
 def col(name, a, b=None, s=None, rows=ALL):
     return V(name, rows, sl(a, a + 1 if b is None else b, s))
 
 
+SPANS, ORDERS = {}, {}
+
+
 def span(ap):
     name, idx = ap[1], ap[2]
     if name not in SCRATCH:
         return None
-    sh = SCRATCH[name][1][1:]
-    e = np.arange(int(np.prod(sh))).reshape(sh)[tuple(idx[1:])].reshape(-1)
-    m = np.zeros(int(np.prod(sh)) + 8, np.uint8)
-    m[e] = 1
-    return name, int.from_bytes(np.packbits(m).tobytes(), "big"), int(e.min()), int(e.max())
+    key = (name, repr(idx[1:]))
+    if key not in SPANS:
+        sh = SCRATCH[name][1][1:]
+        e = np.arange(int(np.prod(sh))).reshape(sh)[tuple(idx[1:])].reshape(-1)
+        m = np.zeros(int(np.prod(sh)) + 8, np.uint8)
+        m[e] = 1
+        SPANS[key] = name, int.from_bytes(np.packbits(m).tobytes(), "big"), int(e.min()), int(e.max()), len(e)
+    return SPANS[key]
 
 
-def emit(g, T, ops):
-    queue = {"v": g.vector, "a": g.scalar, "p": g.tensor, "g": g, "s": g.sync}
-    hist, known, count, need = {}, {q: {} for q in queue}, {}, set()
+def needs(ops, banks):
+    hist, tail, out = {}, {}, []
     for n, o in enumerate(ops):
-        e = o["e"]
-        count[e] = count.get(e, 0) + 1
-        o["pos"] = count[e]
-        deps = set()
-        acc = [(span(a), False) for a in o["r"]] + [(span(a), True) for a in o["w"]]
-        acc = [(s, w) for s, w in acc if s is not None]
-        for (name, m, lo, hi), w in acc:
+        e, deps = o["e"], set()
+        for (name, m, lo, hi, _), w in o["acc"]:
             psum = SCRATCH[name][0] == "psum"
-            for (j, m2, lo2, hi2, w2) in hist.get(name, []):
+            for (j, m2, lo2, hi2, w2) in hist.get((name, True), []) + (hist.get((name, False), []) if w or psum else []):
                 same = ops[j]["e"] == e
                 if same and e == "p":
                     continue
                 if (psum and not same) or ((w or w2) and ((m & m2) if same else (lo <= hi2 and lo2 <= hi))):
                     deps.add(j)
-        for (name, m, lo, hi), w in acc:
-            h = hist.get(name, [])
-            if w and o["full"]:
-                h = [x for x in h if x[1] & ~m]
-            hist[name] = h + [(n, m, lo, hi, w)]
+            if banks and psum and e == "p":
+                start, stop = o["group"]
+                group = tail.get(name, [])
+                deps.update(group if start or stop else group[:1])
+                tail[name] = [n] if start or stop else group + [n]
+        for (name, m, lo, hi, _), w in o["acc"]:
+            if w and o["full"] and (e != "p" or o["group"][0]):
+                for kind in (True, False):
+                    hist[name, kind] = [x for x in hist.get((name, kind), []) if x[1] & ~m]
+            hist.setdefault((name, w), []).append((n, m, lo, hi, w))
+        out.append(deps)
+    return out
+
+
+def cost(o):
+    kind, a = o["kind"], [x for x in o["a"] if isinstance(x, tuple)]
+    size = lambda x: span(x)[4]
+    if kind in ("dma", "send", "arrive"):
+        return {"dma": 0.06, "send": 0.6, "arrive": 0.0}[kind]
+    ind = [x for x in a if x[0] == "ind"]
+    if ind:
+        return (0.05 if o["q"] == "v" else 0.065) + 16 * size(ind[0][2]) * CYCLE * (SCATTER if ind[0] is a[0] else GATHER)
+    n, wide = size(a[0]), [SCRATCH[x[1]][2] in (F, I32) for x in a if size(x) > 1 or x is a[0]]
+    if kind == "mm":
+        return max(min(64, size(a[1])), n) * TENSOR * (4 if wide[1] else 1)
+    if kind == "iota":
+        return 0.13 + 2 * n * CYCLE
+    if kind == "tt":
+        n *= 1 if "psum" in (SCRATCH[a[1][1]][0], SCRATCH[a[2][1]][0]) else 2
+    elif kind != "act" and not any(wide):
+        n /= 2
+    return max(64, n) * CYCLE
+
+
+def arrange(ops):
+    like = tuple(o["lag"] for o in ops)
+    if like in ORDERS:
+        return [ops[n] for n in ORDERS[like]]
+    deps, N = needs(ops, True), len(ops)
+    last, free_ = {}, set()
+    for n, o in enumerate(ops):
+        file = o["q"] if o["kind"] in ("dma", "send") else o["a"][0][1] if o["a"][0][1] in FILES else None
+        if file in last and last[file] not in deps[n]:
+            deps[n].add(last[file])
+            free_.add((last[file], n))
+        if file:
+            last[file] = n
+        if o["kind"] == "arrive":
+            deps[n].add([j for j in range(n) if ops[j]["e"] == o["after"]][0])
+    hold = [cost(o) for o in ops]
+    lag = [o["lag"] for o in ops]
+    gap = lambda j, n: 0.0 if (j, n) in free_ or ops[j]["kind"] == ops[n]["kind"] == "mm" else lag[j] + WAKE
+    users = [[] for _ in ops]
+    for n in range(N):
+        for j in deps[n]:
+            users[j].append(n)
+    way, alike = [0.0] * N, {}
+    for n in reversed(range(N)):
+        key = (ops[n]["q"], ops[n]["a"][0][1])
+        way[n] = hold[n] + max([gap(n, u) + way[u] for u in users[n]] + [lag[n]] + [way[u] for u in alike.get(key, ()) if u - n < 5])
+        alike[key] = (n,)
+
+    def lay(before, after, wait, rank_, ready):
+        left, free, end, pool, order = [len(d) for d in before], {}, [0.0] * N, {}, []
+        for n in range(N):
+            if not left[n]:
+                pool.setdefault(str(ops[n]["q"]), []).append(n)
+        while len(order) < N:
+            t, q = min((max(free.get(q, 0.0), min(ready[n] for n in c)), q) for q, c in pool.items() if c)
+            n = max((n for n in pool[q] if ready[n] <= t), key=lambda n: (rank_[n], -n))
+            soon = [u for u in pool[q] if t < ready[u] < t + hold[n] and rank_[u] > rank_[n]]
+            if soon:
+                u = max(soon, key=lambda u: rank_[u] - ready[u])
+                if max(rank_[u], hold[u] + rank_[n]) + 2 * (ready[u] - t) < max(rank_[n], hold[n] + rank_[u]):
+                    n, t = u, ready[u]
+            pool[q].remove(n)
+            free[q] = end[n] = t + hold[n]
+            order.append(n)
+            for u in after[n]:
+                ready[u] = max(ready[u], end[n] + wait(n, u))
+                left[u] -= 1
+                if not left[u]:
+                    pool.setdefault(str(ops[u]["q"]), []).append(u)
+        return max(e + x for e, x in zip(end, lag)), order, end
+    best = None
+    for k in range(PASSES):
+        laid = lay(deps, users, gap, way, [0.0] * N)
+        best = min(best or laid, laid)
+        shake = {}
+        ends = [e + shake.setdefault((o["q"], o["a"][0][1]), SHAKE * math.sin(n * 12.9898 + k * 78.233 + n * k)) for n, (e, o) in enumerate(zip(best[2], ops))]
+        way = lay(users, deps, lambda n, j: gap(j, n), ends, list(lag))[2]
+    ORDERS[like] = best[1]
+    return [ops[n] for n in best[1]]
+
+
+def emit(g, T, ops):
+    queue = {"v": g.vector, "a": g.scalar, "p": g.tensor, "g": g, "s": g.sync}
+    known, count, need = {q: {} for q in queue}, {}, set()
+    for o, deps in zip(ops, needs(ops, False)):
+        e = o["e"]
+        count[e] = count.get(e, 0) + 1
+        o["pos"] = count[e]
         o["waits"] = []
         if o["q"] is None:
             o["clock"] = {e: 1}
@@ -206,10 +310,10 @@ def rank_program(g, core, T, topo):
     if rank is None:
         relay_program(g, core, T, topo)
         return
-    cores, N = list(T.cores), len(T.cores)
-    ops, ndma, sent = [], [0], [0]
+    cores = list(T.cores)
+    ops, ndma, sent, loaded = [], [0], [0], [0]
 
-    def rec(q, f, out, *args, e=None, dma=False, sem=None, val=None):
+    def rec(kind, q, f, out, *args, e=None, sem=None, val=None, lag=0.0, after=None, group=None):
         r, w = [], []
         for a in args:
             if isinstance(a, tuple):
@@ -222,597 +326,472 @@ def rank_program(g, core, T, topo):
             else:
                 w.append(out[1])
                 r.append(out[2])
-        ops.append({"q": q, "e": e or q, "f": f, "a": ([] if out is None else [out]) + list(args), "r": r, "w": w, "full": full,
-                    "dma": dma, "sem": sem, "val": val})
+        acc = [(span(a), False) for a in r] + [(span(a), True) for a in w]
+        ops.append({"kind": kind, "q": q, "e": e or q, "f": f, "a": ([] if out is None else [out]) + list(args), "full": full, "group": group,
+                    "acc": [x for x in acc if x[0] is not None], "dma": kind == "dma", "sem": sem, "val": val, "lag": lag, "after": after})
 
-    def dma(q, out, in_):
-        rec(q, lambda x, o, i: x.dma_start(o, i), out, in_, e="d%d" % ndma[0], dma=True, sem="d%d" % ndma[0], val=16)
+    def dma(q, out, in_, kb):
+        loaded[0] += kb
+        rec("dma", q, lambda x, o, i: x.dma_start(o, i), out, in_, e="d%d" % ndma[0], sem="d%d" % ndma[0], val=16, lag=2.0 + loaded[0] / 280)
         ndma[0] += 1
 
     def cp(out, in_):
-        rec("v", lambda x, o, i: x.tensor_copy(o, i), out, in_)
+        rec("cp", "v", lambda x, o, i: x.tensor_copy(o, i), out, in_)
 
     def ms(out, c):
-        rec("v", lambda x, o: x.memset(o, c), out)
+        rec("ms", "v", lambda x, o: x.memset(o, c), out)
 
     def tt(out, a, b, op):
-        rec("v", lambda x, o, i, j: x.tensor_tensor(o, i, j, op), out, a, b)
+        rec("tt", "v", lambda x, o, i, j: x.tensor_tensor(o, i, j, op), out, a, b)
 
     def ts(out, a, s1, op0, s2=None, op1=None):
         if op1 is None:
-            rec("v", lambda x, o, i, s: x.tensor_scalar(o, i, s, None, op0), out, a, s1)
+            rec("ts", "v", lambda x, o, i, s: x.tensor_scalar(o, i, s, None, op0), out, a, s1)
         else:
-            rec("v", lambda x, o, i, s, u: x.tensor_scalar(o, i, s, u, op0, op1), out, a, s1, s2)
+            rec("ts", "v", lambda x, o, i, s, u: x.tensor_scalar(o, i, s, u, op0, op1), out, a, s1, s2)
 
     def scan(out, d0, d1, init, op0, op1):
-        rec("v", lambda x, o, i, j: x.tensor_tensor_scan(o, i, j, init, op0, op1), out, d0, d1)
+        rec("scan", "v", lambda x, o, i, j: x.tensor_tensor_scan(o, i, j, init, op0, op1), out, d0, d1)
 
     def act(out, in_, func, bias=0.0, scale=1.0):
-        rec("a", lambda x, o, i, b, s: x.activation(o, i, func, bias=b, scale=s), out, in_, bias, scale)
+        rec("act", "a", lambda x, o, i, b, s: x.activation(o, i, func, bias=b, scale=s), out, in_, bias, scale)
 
     def mm(out, l, r, start=True, stop=True):
-        rec("p", lambda x, o, i, j: x.matmul(o, i, j, start, stop), out, l, r)
+        rec("mm", "p", lambda x, o, i, j: x.matmul(o, i, j, start, stop), out, l, r, group=(start, stop))
 
     def iota(out, pat, base=0, cm=0):
         if SCRATCH[out[1]][2] == I32:
-            rec("g", lambda x, o: x.iota(o, pat, base, cm), out)
+            rec("iota", "g", lambda x, o: x.iota(o, pat, base, cm), out)
         else:
-            rec("g", lambda x, o: x.iota(o, pat, base, cm, allow_small_or_imprecise_dtypes=True), out)
+            rec("iota", "g", lambda x, o: x.iota(o, pat, base, cm, allow_small_or_imprecise_dtypes=True), out)
 
-    def send(t, src, land, sem):
-        way = route(core, cores[(rank + 1 + t % (N - 1)) % N], cores, topo)
-        rec("g", lambda x, i: hand(g, T, topo, core, way[1], land, src, sem), None, V(src, ALL), e="x" + src)
-        sent[0] += width(core, way[1], topo)
+    def send(t, part):
+        hop, letter = first_hop(rank, t, cores, topo)
+        src = "M%s%d" % (part, t)
+        rec("send", "g", lambda x, i: hand(g, T, topo, core, hop, letter + src[1:], src), None, V(src, ALL), e="x" + src)
+        sent[0] += ENG
 
-    def arrive(t, land, sem):
-        way = route(cores[(rank - 1 - t % (N - 1)) % N], core, cores, topo)
-        rec(None, None, V(land, ALL), e=sem, sem=sem, val=width(way[-2], core, topo))
+    def arrive(t, part):
+        src = [r for r in range(len(cores)) if target(r, t, cores) == core][0]
+        hops = 1 if first_hop(src, t, cores, topo)[0] == core else 2
+        land = "L%s%d" % (part, t)
+        rec("arrive", None, None, V(land, ALL), e="s" + land, sem="s" + land, val=ENG, after="xM" + land[1:], lag=hops * (HOP if t else HOP + 1.5))
 
-    EQ, MUL, ADD, SUB, MAX, MIN = ALU.is_equal, ALU.mult, ALU.add, ALU.subtract, ALU.max, ALU.min
+    EQ, MUL, ADD, SUB, MAX, MIN, GT = ALU.is_equal, ALU.mult, ALU.add, ALU.subtract, ALU.max, ALU.min, ALU.is_gt
     SHR, AND = ALU.arith_shift_right, ALU.bitwise_and
     whole = lambda n: V(n, ALL)
-    IW, IS, XW, XS = col("IC", 0, W), col("IC", 0, W + DUM), col("X", 0, W), col("X", 0, W + 16)
-    R1, R8, R48, R49 = sl(0, 1), sl(0, 8), sl(0, 48), sl(0, 49)
-    pd_ = lambda k: cf("PD", k, k + 1)
+    IW, IS, XW, XS, NUM = col("IC", 0, W), col("IC", 0, W + DUM), col("X", 0, W), col("X", 0, W + 16), col("NUM", 0, W + 16)
+    R1, R8, R16, R48, R49 = sl(0, 1), sl(0, 8), sl(0, 16), sl(0, 48), sl(0, 49)
+    pd_ = lambda k, rows=ALL: cf("PD", k, k + 1, rows=rows)
     gcol, rcol = pd_(0), pd_(1)
-    Pc = cf("P", 0, 1)
+    Pc, BO, GL, OL, LR8 = cf("P", 0, 1), cb("BO", 96, 104), col("GL", 0, 8), col("OL", 0, 32), col("LR8", 0, 8)
     ki = lambda k, n=1: col("KI", 8 * k, 8 * (k + n))
     tf = lambda k, n=1: col("TF", 8 * k, 8 * (k + n))
+    part = lambda name, k, n=L: col(name, n * k, n * k + n)
 
-    def zero(out):
-        n = len(range(*out[2][1].indices(512)))
-        mm(out, cb("ZR", rows=R1), cb("MK", 0, n, rows=R1), True, False)
+    def spread(out, src):
+        tt(whole(out), IND(src, LR8), cb("MK"), MUL)
 
     ms(cb("ONES"), 1.0)
     ms(whole("AW"), 0)
-    dma("s", whole("GI"), V("gate", ALL))
-    dma("a", XW, V("pat", ALL))
-    dma("a", whole("A"), V("acc0", ALL))
-    dma("a", col("TH", 0, 4), V("th", ALL))
+    dma("s", whole("GI"), V("gate", ALL), 4)
+    dma("a", whole("A"), V("acc0", ALL), 32)
+    for k in range(4):
+        dma("sa"[k % 2], part("IT", k, 512), part("icol", k, 512), 256)
+    dma("s", V("AW", sl(0, 128, 4)), V("alt", ALL), 256)
+    dma("s", XW, V("pat", ALL), 512)
+    loaded[0] = 0
     for k in range(2):
-        dma("s", col("IT", 512 * k, 512 * k + 512), col("icol", 512 * k, 512 * k + 512))
-    dma("s", V("AW", sl(0, 128, 4)), V("alt", ALL))
-    for k in range(2, 4):
-        dma("s", col("IT", 512 * k, 512 * k + 512), col("icol", 512 * k, 512 * k + 512))
+        dma("a", col("TH", 0, 4, rows=sl(8 * k, 8 * k + 8)), V("th", ALL), 0)
 
     iota(col("PI", 0), [[0, 1]], 0, 1)
     iota(cf("P"), [[-1, 8]], 0, 1)
-    iota(cf("FO"), [[16, 8], [1000, 4], [4, 4]])
-    iota(cf("GO"), [[1000, 4]], 0, 1)
-    iota(li("LAR"), [[1, NQ], [16, 8]])
-    iota(cf("LC2F"), [[1, 4], [128, 4], [8, 2]])
-    iota(cf("LC16F"), [[1, 3], [16, 8]], 1)
     iota(cb("J"), [[1, 128]])
     iota(cb("F16"), [[0, 8], [1, 16]])
     iota(cb("JG"), [[1, 8], [0, 16]])
-    iota(cb("F5"), [[1, 8], [0, 5]])
-    iota(cb("JA"), [[1, 8], [0, NQ]])
-    iota(cb("JB"), [[1, 8], [0, NA]])
+    iota(whole("LI"), [[1, 8]])
+    iota(cf("FO"), [[16, 8], [1000, 4], [4, 4]])
+    iota(cf("GO"), [[1000, 4]], 0, 1)
+    iota(cf("FV"), [[1, 144]], -15)
+    iota(cf("FX", 0, 40), [[16, 8], [-4, 5]], 16)
+    iota(cf("FX", 40, 48), [[16, 8]], 12)
+    iota(cf("FK"), [[1, 8], [-32, 5]], 128)
+    iota(cf("J32"), [[0, 4], [1, 32]])
+    iota(cb("FG"), [[1, 8], [0, 16], [32, 3]], 32)
+    iota(cf("XCONST", 0, 40), [[0, 8], [-4096, 5]], 20480)
+    iota(cf("UB"), [[-17, 8]], 141)
     iota(cb("F3"), [[8, 8], [0, 2], [1, 8]])
-    iota(li("LR8"), [[1, 8]])
-    iota(li("LSV"), [[1, 4], [4, 8]])
-    iota(cf("FC"), [[4, 2], [-1, 4]], 3)
-    iota(cf("BASEF"), [[16, 8], [-1, 4]], 3)
     iota(cb("F8"), [[8, 16], [0, 8]])
     iota(cb("FP"), [[16, 8], [-1, 16]], 15)
     iota(cf("FW"), [[2, 8], [-1, 2]], 1)
-    iota(cf("FX"), [[16, 8], [4, 5]], -4)
+    iota(cf("FR"), [[-17, 8], [-1, 16]], 140)
     iota(cf("P16"), [[-16, 3]], 0, 1)
     iota(cf("DUML"), [[16, 8]])
-    iota(cf("XCONST"), [[0, 8], [-4096, 5]], 16384)
-    iota(cf("UB"), [[-17, 8]], 139)
-    iota(cf("FR"), [[-17, 8], [-1, 16]], 138)
     iota(cb("S48"), [[1, 48]], -256)
-    iota(cb("NE3"), [[1, 48], [0, 16]])
+    iota(NUM, [[1, W + 16]])
+    for t in range(RO - 1):
+        iota(whole("PT%d" % t), [[0, W + DUM]])
 
     def fill(out, n, c):
         act(out, cb("ONES", 0, n), AF.Identity, scale=float(c))
 
     def times(out, in_, c):
         act(out, in_, AF.Identity, scale=c)
-    fill(cb("ZR"), 128, 0)
     fill(col("IC", W, W + DUM), DUM, 0)
-    fill(col("X", W, W + 16), 16, 0)
-    for k in range(4):
-        fill(V("LED", ALL, sl(8 * k, 8 * k + 8), ALL), 128, 0)
-        fill(V("LEA", ALL, sl(8 * k, 8 * k + 8), ALL), 128, 0)
+    fill(col("YC", W, W + DUM), DUM, 0)
+    fill(col("X", W, W + 16), 16, -1024)
     for k in range(3):
         fill(cb("M3", k, 384, 3), 128, min(k, 1))
-    fill(cb("NM16"), 128, 1)
-    fill(cb("VALC"), 40, BIG)
-    fill(cb("X3"), 40, 0)
-    fill(cb("P4096"), 16, 4096)
+    for k in range(2):
+        fill(cb("NM16", L * k, L * k + L), 128, 1)
+    fill(cb("CW"), 40, CNT)
+    fill(cb("CW", 0, 40, 5), 8, 0)
+    fill(cb("NM16", 0, 256, 16), 16, 0)
+    for name, n, c in (("P4096", 16, 4096), ("O16", L, 16), ("C1024", L, -1024), ("TWO", L, 2)):
+        fill(cb(name), n, c)
+    fill(cb("BO", 0, 96), 96, 0)
+    fill(cb("BO", 104, 224), 120, 0)
     fill(whole("PM3"), 128, 0)
     fill(col("GE2", 0, 16), 16, 1)
     fill(col("GE3", 0, 16), 16, 1)
-    fill(cb("NM16", 0, 128, 16), 8, 0)
-    fill(cb("VALC", 0, 40, 5), 8, 0)
-    fill(cb("VALC", 4, 40, 5), 8, 0)
-    for k, (s1, s2) in enumerate([(4, 7), (0, 15), (1, 63), (3, 15), (0, 1), (2, 3), (0, 3), (3, 1), (0, 7)]):
+    for k, (s1, s2) in enumerate([(4, 7), (0, 15), (1, 63), (3, 15), (0, 1), (0, 112), (0, 7), (0, 31), (3, 1)]):
         ts(col("PI", 8 + k), col("PI", 0), s1, SHR, s2, AND)
     cp(cf("PD", 0, 9), col("PI", 8, 17))
-    for q in range(4):
-        ts(ch("SELO", 128 * q, 128 * q + 128), cf("FO"), cf("GO", q, q + 1), EQ)
-    cp(lu("LAR"), li("LAR"))
-    ts(pd_(10), pd_(7), 4.0, MUL)
-    ts(pd_(11), pd_(6), 4.0, MUL)
-    ts(pd_(12), pd_(8), 16.0, MUL, pd_(10), ADD)
-    ts(pd_(13), pd_(5), 128.0, MUL, pd_(11), ADD)
-    for k in range(4):
-        ts(lu("LC2", NQ // 2 * k, NQ // 2 * (k + 1)), cf("LC2F", 8 * k, 8 * k + NQ // 2), pd_(12), ADD)
-    ts(lu("LC16"), cf("LC16F"), pd_(13), ADD)
-    act(whole("AR"), IND(col("A", 0, L), lu("LAR")), AF.Copy)
-    ts(col("TH", 4, 8), col("TH", 0, 4), 4, SHR)
-    ts(col("TH", 8, 12), col("TH", 0, 4), 15, AND)
-    ts(cf("THF", 0, 4, rows=R8), col("TH", 4, 8), -16.0, MUL)
-    ts(cf("THF", 4, 8, rows=R8), col("TH", 8, 12), -1.0, MUL, -0.5, ADD)
-
-    def threshold(k):
-        act(cb("NTH", 128 * k, 128 * k + 128, rows=R8), cb("ONES", rows=R8), AF.Identity, scale=cf("THF", k, k + 1, rows=R8))
-    threshold(0)
-    threshold(4)
+    cp(LR8, whole("LI"))
+    ts(BO, cb("J", 0, 8), gcol, EQ)
+    ts(cb("IDN"), cb("J"), Pc, EQ)
+    ts(cb("MK"), cb("F16"), rcol, EQ)
+    ts(cb("BLKB"), cb("JG"), gcol, EQ)
+    ts(cf("SEL8"), cf("J32"), Pc, EQ)
+    for a in range(4):
+        ts(cb("SELO", L * a, L * a + L), cf("FO"), cf("GO", a, a + 1), EQ)
+    ts(cb("WIDE"), cf("FV"), pd_(5), EQ)
+    ts(pd_(18), rcol, 0.0, EQ)
+    times(cb("W0"), cb("WIDE"), pd_(18))
     ts(pd_(14), pd_(4), -2.0, MUL, 1.0, ADD)
     ts(pd_(15), rcol, 1.0, ADD)
-    ts(cb("BO"), cb("J", 0, 8), gcol, EQ)
-    ts(cb("IDN"), cb("J"), Pc, EQ)
-    ts(cb("MK", 0, 128), cb("F16"), rcol, EQ)
-    ts(cb("BLKB"), cb("JG"), gcol, EQ)
-    ts(cb("BLK5"), cb("F5"), gcol, EQ)
-    ts(cb("THA", 0, 8 * NQ), cb("JA"), Pc, EQ)
-    ts(cb("THB", 0, 8 * NA), cb("JB"), Pc, EQ)
-    times(cb("NBO"), cb("BO"), -1.0)
-    times(cb("KBO"), cb("BO"), 1024.0)
-    times(cf("BOF"), cb("BO"), 1.0)
-    for k in range(1, 4):
-        times(cb("THA", 8 * NQ * k, 8 * NQ * (k + 1)), cb("THA", 0, 8 * NQ), 1.0)
-        times(cb("THB", 8 * NA * k, 8 * NA * (k + 1)), cb("THB", 0, 8 * NA), 1.0)
-        times(cb("MK", 128 * k, 128 * k + 128), cb("MK", 0, 128), 1.0)
-    times(cb("BIGSEL"), cb("BLKB"), BIG)
-    for k in range(4):
-        times(cb("VALK", 40 * k, 40 * k + 40), cb("BLK5"), BIG)
-    times(cb("X3", 4, 40, 5), cb("BO"), -2048.0)
-    fill(cb("VALK", 0, 160, 5), 32, 0)
-    for k in range(4):
-        times(cb("VALK", 40 * k + k + 1, 40 * k + 40, 5), cb("BO"), -BIG if k < 3 else 0.0)
-    times(cb("NID"), cb("IDN"), -1.0)
-    times(cb("RANK"), cf("FR"), 4096.0)
-    fill(cf("XCONST", 4, 40, 5), 8, 2048)
-    act(cf("XCONST", 0, 40, 5), cf("UB"), AF.Identity, bias=2048.0, scale=4096.0)
-    act(cf("FX", 0, 40, 5), cf("FX", 0, 40, 5), AF.Identity, bias=16.0)
-    act(cf("BASEF"), cf("BASEF"), AF.Identity, bias=pd_(13))
+    ts(pd_(16), Pc, 8.0, EQ, BIG / 2, MUL)
+    ts(pd_(17), Pc, 8.0, EQ, BIG, MUL)
+    ts(pd_(19), pd_(8), 16.0, MUL, -16.0, ADD)
+    ts(pd_(20), pd_(8), -1.0, MUL)
+    ts(cb("GW"), cb("FG"), Pc, EQ, -BIG / 2, MUL)
+    ts(cb("G1W"), cb("J", 0, 8), pd_(7), EQ, -BIG, MUL)
+    ts(cb("XSEL"), cf("FX"), Pc, EQ)
+    ts(cb("K2"), cf("FK"), Pc, EQ, CNT, MUL)
+    act(cb("GW"), cb("GW"), AF.Identity, bias=pd_(16))
+    act(cb("G1W"), cb("G1W"), AF.Identity, bias=pd_(17))
+    for k in range(2):
+        ts(cb("THS", L * k, L * k + L), cb("JG"), pd_(6), EQ)
+    for out, src, c in ((cb("NBO"), BO, -1.0), (cf("BOF"), BO, 1.0), (cb("KID"), cb("IDN"), CNT), (cb("NID"), cb("IDN"), -1.0), (cb("K4"), cb("IDN"), -4096.0),
+                        (cb("RANK"), cf("FR"), 4096.0), (cf("WT"), cb("BLKB"), pd_(15))):
+        times(out, src, c)
+    for k in range(3):
+        times(cb("NBLK3", L * k, L * k + L), cb("BLKB"), -1.0)
+        ts(cb("TRI3", L * k, L * k + L), cb("F16"), cf("P16", k, k + 1), ALU.is_le, 4096.0, MUL)
+    act(cf("XCONST", 0, 40, 5), cf("XCONST", 0, 40, 5), AF.Identity, bias=2048.0)
+    act(cf("XCONST", 40, 48), cf("UB"), AF.Identity, bias=2048.0, scale=4096.0)
     act(cf("DUML"), cf("DUML"), AF.Identity, bias=rcol)
     for k in range(8):
-        times(ch("SELG", 128 * k, 128 * k + 128), cb("ONES"), cf("BOF", k, k + 1))
-    ts(ch("SIG"), cb("F3"), pd_(2), EQ, -1.0, MUL)
-    ts(ch("DEL"), cb("F3"), pd_(2), EQ, pd_(14), MUL)
-    for n in ("LR8", "LSV"):
-        cp(lu(n), li(n))
-    ts(cb("CM"), cf("FC"), gcol, EQ, 1024.0, MUL)
-    ts(cb("TRI2"), cb("J"), Pc, ALU.is_gt)
+        times(cb("SELG", L * k, L * k + L), cb("ONES"), cf("BOF", k, k + 1))
+        ts(cb("FSEL", L * k, L * k + L), cb("F8"), cf("P", k, k + 1), EQ, 2.0, MUL)
+    cp(cb("XSEL", 0, 40, 5), cb("XSEL", 40, 48))
+    ts(cb("SIG"), cb("F3"), pd_(2), EQ, -1.0, MUL)
+    ts(cb("DEL"), cb("F3"), pd_(2), EQ)
+    times(cb("DEL"), cb("DEL"), pd_(14))
+    ts(cb("TRI2"), cb("J"), Pc, GT)
     ts(cb("TRIP"), cb("J"), Pc, EQ, -256.0, MUL)
-    ms(cb("CM", 0, 8, 4), 0.0)
-    tt(whole("CMG"), IND(col("GI", 0, 8), lu("LR8")), cb("MK", 0, L), MUL)
     tt(cb("TRIP"), cb("TRIP"), cb("TRI2"), ADD)
     ts(cb("TRI2"), cb("J"), Pc, ALU.is_le, 4096.0, MUL)
-    for pp in range(8):
-        ts(ch("FSEL", 128 * pp, 128 * pp + 128), cb("F8"), cf("P", pp, pp + 1), EQ, 2.0, MUL)
-    mm(col("PS", 128, 136), whole("CMG"), ch("BOH"))
+    ts(cb("PERM"), cb("FP"), Pc, EQ)
+    ts(cb("WM"), cf("FW"), pd_(3), EQ, -BIG, MUL)
+    ms(whole("AMG"), 0.0)
+    cp(cf("THF", rows=R8), col("TH", 0, 4, rows=R8))
+    mm(col("PQ", 0, 4), cf("SEL8", rows=R8), cf("THF", rows=R8))
+    act(cf("THC"), col("PQ", 0, 4), AF.Copy)
+    ts(col("TH", 4, 8), col("TH", 0, 4), 4, SHR)
+    ts(col("TH", 8, 12), col("TH", 0, 4), 15, AND)
+    ts(cf("THP", 0, 4, rows=R16), col("TH", 4, 8), pd_(19, R16), MUL)
+    ts(cf("THP", 4, 8, rows=R16), col("TH", 8, 12), 0.5, ADD, pd_(20, R16), MUL)
+    tt(cf("THP", 8, 12, rows=R16), cf("THP", 0, 4, rows=R16), cf("THP", 4, 8, rows=R16), ADD)
+    for t in range(RO):
+        times(cb("NTH", L * t, L * t + L, rows=R16), cb("ONES", rows=R16), cf("THP", 8 + t, 9 + t, rows=R16))
 
-    def options_a():
-        cp(whole("R"), IND(col("AW", 0, W), col("GL", 0, 8)))
+    def widen():
+        for j in range(4):
+            cp(col("A4", j, 512, 4), whole("A"))
+        for j in range(4):
+            cp(col("AR", j, 1024, 4), col("A4", 0, 256))
 
-    def options_b():
-        for Q in range(4):
-            for q in range(4):
-                mm(col("PS", 96 + 8 * Q, 104 + 8 * Q), ch("SELO", 128 * q, 128 * q + 128), col("R", 4 * Q + q, L, 16), q == 0, q == 3)
+    def gather(out, in_, on_vector):
+        if on_vector:
+            cp(out, in_)
+        else:
+            act(out, in_, AF.Copy)
 
-    def options_c():
-        cp(whole("OL"), col("PS", 96, 128))
+    def options():
+        cp(whole("R"), IND(col("AW", 0, W), GL))
+        for a in range(4):
+            mm(col("PW", 256, 288), cb("SELO", L * a, L * a + L), col("R", a, L, 4), a == 0, a == 3)
+        cp(OL, col("PW", 256, 288))
 
-    def columns(k):
-        cp(col("IC", 512 * k, 512 * k + 512), col("IT", 512 * k, 512 * k + 512))
+    def farthest(n, s):
+        rows, GE, o = sl(0, n), "GE" + s, col("PQ", L, L + n)
+        scan(V("PM" + s, rows, ALL), cb("NM16", 0, L, rows=rows), V("PQ", rows, sl(0, L)), 0.0, MUL, MAX)
+        cp(whole("PX"), col("PM" + s, 15, L, 16))
+        tt(col(GE, 16, 144), IND(col("PX", 0, 8), LR8), whole("PM" + s), EQ)
+        mm(o, cb("MK", rows=R1), cb("ONES", 0, n, rows=R1), True, False)
+        mm(o, col(GE, 16, 144, rows=rows), cb("IDN", 0, n, rows=rows), False, False)
+        mm(o, col(GE, 15, 143, rows=rows), cb("NID", 0, n, rows=rows), False, True)
 
-    def consts_b():
-        ts(ch("PERM"), cb("FP"), Pc, EQ)
-        ts(cb("WM"), cf("FW"), pd_(3), EQ, -BIG, MUL)
-        cp(whole("cT0"), col("PS", 128, 136))
-        cp(col("KC", 8, 16), col("PS", 128, 136))
-
-    def consts_c():
-        ts(ch("XSEL"), cf("FX"), Pc, EQ)
-        for k in range(3):
-            times(ch("NBLK3", 128 * k, 128 * k + 128), cb("BLKB"), -1.0)
-        times(cb("KID"), cb("IDN"), 1024.0)
-        times(cb("HID"), cb("IDN"), -512.0)
-        times(cf("IDF"), cb("IDN"), 1.0)
-        times(cf("NIDF"), cb("IDN"), -1.0)
-        fill(tf(15), 8, 128)
-
-    def consts_d():
-        for k in range(3):
-            ts(cb("TRI3", 128 * k, 128 * k + 128), cb("F16"), cf("P16", k, k + 1), ALU.is_le, 4096.0, MUL)
-        ms(whole("AMG"), 0.0)
-
-    def consts_e():
-        for k in range(8):
-            if k % 4:
-                threshold(k)
-        times(cf("WT"), cb("BLKB"), pd_(15))
-        fill(col("YC", W, W + DUM), DUM, 0)
-
-    cp(whole("GL"), whole("GI"))
-    columns(0)
-    options_a()
-    options_b()
-    columns(1)
-    consts_b()
-    columns(2)
-    options_c()
-    columns(3)
-
-    def to_list(z, n, out, zt):
-        tt(col("ZT", zt, zt + n), z, cf("DUML", 0, n), MIN)
-        ts(out, col("ZT", zt, zt + n), float(W), ADD)
-
-    def far_mask_a(n, PM, GE):
-        rows = sl(0, n)
-        scan(V(PM, rows, ALL), cb("NM16", rows=rows), V("PQ", rows, sl(0, 128)), 0.0, MUL, MAX)
-        cp(whole("PX"), col(PM, 15, L, 16))
-        tt(col(GE, 16, 144), IND(col("PX", 0, 8), lu("LR8")), whole(PM), EQ)
-
-    def far_mask_b(n, GE):
-        rows = sl(0, n)
-        mm(col("DA", 0, n), cb("MK", 0, L, rows=R1), cb("ONES", 0, n, rows=R1), True, False)
-        mm(col("DA", 0, n), col(GE, 16, 144, rows=rows), cb("IDN", 0, n, rows=rows), False, False)
-        mm(col("DA", 0, n), col(GE, 15, 143, rows=rows), cb("NID", 0, n, rows=rows), False, True)
-
-    def write(n, s, lst, t):
-        if s == "3":
-            if t == RO - 1:
-                mm(col("DB", 0, n), cf("WT"), whole("CF3"), True, False)
-            tt(whole("WV3"), col("DA", 0, n), whole("DV3"), MUL)
-        if t < RO - 1 or s == "2":
-            tt(IND(IS, lst), whole("WV" + s), whole("CF" + s), ADD)
-        if t == RO - 1:
-            if s == "2":
-                mm(col("DB", 0, n), cf("WT"), whole("CF2"), True, False)
-            mm(col("DB", 0, n), cf("WT"), whole("WV" + s), False, True)
-            act(whole("YP" + s), col("DB", 0, n), AF.Copy)
-
-    def patch(s, lst):
+    def patch(n, s, bank, lst):
+        mm(col(bank, 0, n), cf("WT"), whole("CF" + s), True, False)
+        mm(col(bank, 0, n), cf("WT"), whole("WV" + s), False, True)
+        act(whole("YP" + s), col(bank, 0, n), AF.Copy)
         cp(IND(col("YC", 0, W + DUM), lst), whole("YP" + s))
 
-    def ysum(k, bank):
-        mm(whole(bank), cf("WT"), col("IC", 512 * k, 512 * k + 512))
+    def abroad(t):
+        more = t < RO - 1
+        la, ld, lb = col("LA%d" % t, 0, 3), col("LB%d" % t, 0, 3), col("LB%d" % t, 4, 7)
+        place = lambda p: part("L%d" % (p // 8), p % 8, 48)
+        arrive(t, "A")
+        cp(whole("CO3"), IND(IS, la))
+        act(whole("XC3"), IND(XS, la), AF.Copy)
+        for p in range(16):
+            mm(place(p), cb("NID"), whole("XC3"), p % 8 == 0, False)
+        if more:
+            act(whole("G3"), IND(XS, whole("CO3")), AF.Copy)
+        else:
+            act(col("G3", 0, 384), IND(XS, col("CO3", 0, 24)), AF.Copy)
+            cp(col("G3", 384, 768), IND(XS, col("CO3", 24, 48)))
+        for p in range(16):
+            mm(place(p), cb("IDN"), col("G3", p, 768, 16), False, p % 8 == 7)
+        for b in range(2):
+            act(part("H3", b, 384), col("L%d" % b, 0, 384), AF.Abs)
+            for p in range(8 * b, 8 * b + 8):
+                mm(V("PQ", R48, sl(p, L, 16)), part("H3", p, 48), BO)
+        act(whole("CF3"), IND(IS, la), AF.Copy)
+        arrive(t, "B")
+        tt(whole("DV3"), IND(NUM, lb), whole("CF3"), SUB)
+        farthest(48, "3")
+        if more:
+            act(whole("BG"), IND(NUM, lb), AF.Identity, bias=-2048.0)
+            act(whole("OH"), col("PQ", L, L + 48), AF.Copy)
+        tt(whole("WV3"), col("PQ", L, L + 48), whole("DV3"), MUL)
+        if more:
+            tt(IND(col("PT%d" % t, 0, W + DUM), ld), whole("OH"), whole("BG"), MUL)
+            cp(whole("PG"), IND(col("PT%d" % t, 0, W), OL))
+            tt(IND(IS, ld), whole("WV3"), whole("CF3"), ADD)
+        if t >= RO - 2:
+            patch(48, "3", "PS", ld)
+
+    widen()
+    cp(GL, whole("GI"))
+    spread("CMG", col("GI", 0, 8))
+    mm(col("PS", 0, 8), whole("CMG"), BO)
+    cp(whole("cT"), col("PS", 0, 8))
+    cp(col("KC", 8, 16), col("PS", 0, 8))
+    for k in range(4):
+        cp(part("IC", k, 512), part("IT", k, 512))
+    options()
 
     for t in range(RO):
-        last = t == RO - 1
-        cT, cN = "cT%d" % (t % 2), "cT%d" % (1 - t % 2)
-        cp(whole("COA"), IND(IW, col("OL", 8 * QA, 32)))
-        act(col("COLF", 0, 128 * QD), IND(IW, col("OL", 0, 8 * QD)), AF.Copy)
-        for q in range(NQ, 16):
-            for u in range(8):
-                o = 4 * (((q // 4 - QA) * 8 + u) * 4 + q % 4)
-                s = 64 * (8 * (q - NQ) + u)
-                act(col("H", s, s + 64), IND(XW, col("COA", o, o + 4)), AF.Abs, bias=col("A", 16 * u + q), scale=-1.0)
-        cp(whole("C2"), IND(col("COLF", 0, 128 * QD), lu("LC2")))
-        cp(whole("CO2"), IND(IW, col("GL", 0, 8)))
-        n = 128 * NQ
-        for what, k in ("d0", "d1", "r0", "d2", "r1", "c0", "r2", "d3", "r3"):
-            k = int(k)
-            if what == "d":
-                tt(col("D", n * k, n * k + n), IND(XW, col("C2", 8 * NQ * k, 8 * NQ * (k + 1))), whole("AR"), SUB)
-            elif what == "r":
-                ts(col("R2", n * k, n * k + n), col("D", n * k, n * k + n), 0.0, MAX, 2.0, MUL)
-            else:
-                cp(col("COLF", 128 * QD, 512), IND(IW, col("OL", 8 * QD, 32)))
-        cp(whole("C16"), IND(col("COLF", 0, 512), lu("LC16")))
-        if last:
-            ysum(0, "PW")
-            ysum(1, "PQ")
-            for k in range(2):
-                ysum(2 + k, "L%d" % k)
-                cp(col("YC", 512 * (2 + k), 512 * (3 + k)), whole("L%d" % k))
-        for bank, sel, n in (("DB", "THB", NA), ("DA", "THA", NQ)):
-            mm(col(bank, 0, 32 * n), cb("NTH", 128 * t, 128 * t + 128, rows=R8), cb(sel, rows=R8), True, False)
-            mm(col(bank, 0, 32 * n), cb("NTH", 128 * (4 + t), 128 * (5 + t), rows=R8), cb(sel, rows=R8), False, False)
-
-        def pa(q):
-            for u in range(4):
-                s = 128 * (4 * q + u)
-                mm(col("DB", 8 * NA * u + q, 8 * NA * (u + 1), NA), col("H", s, s + 128), cb("BO"), False, u == 3 and q == NA - 1)
-
-        def pd(k):
-            for q in range(NQ):
-                o, s = col("DA", 8 * NQ * k + q, 8 * NQ * (k + 1), NQ), 128 * (NQ * k + q)
-                mm(o, col("D", s, s + 128), cb("NBO"), False, False)
-                mm(o, col("R2", s, s + 128), cb("BO"), False, k == 3 and q == NQ - 1)
-        if not last:
-            zero(col("PW", 0, 384))
-        done = 0
+        last, late = t == RO - 1, t > 0
+        for h in (1, 0):
+            cp(part("COA", h, 256), IND(IW, part("OL", h, 16)))
         for k in range(4):
-            upto = (3, 5, 6, 7)[k] * NA // 8
-            for q in range(done, upto):
-                pa(q)
-            done = upto
-            pd(k)
-        if t == 0:
-            consts_c()
-        ts(V("LED", ALL, ALL, sl(0, NQ)), col("DA", 0, 32 * NQ), 0.0, ALU.is_gt, 0.40625, SUB)
-        for q in range(done, NA):
-            pa(q)
-        mm(col("DL", 0, 384), ch("DEL"), whole("C16"))
-        if last:
-            act(col("YC", 512, 1024), whole("PQ"), AF.Copy)
-            act(col("YC", 0, 512), whole("PW"), AF.Copy)
-        else:
-            act(whole("CF2"), IND(IW, col("GL", 0, 8)), AF.Copy)
-        act(whole("XC2"), IND(XW, col("GL", 0, 8)), AF.Copy)
-        act(tf(9), whole(cT), AF.Identity, bias=-2176.0)
-        act(col("DL", 0, 384), col("DL", 0, 384), AF.Abs)
-        ga = GA // 2 if last or t == 0 else GA
-        act(col("G2", 0, 16 * ga), IND(XW, col("CO2", 0, ga)), AF.Copy)
-        led = lambda k: V("LED", ALL, sl(8 * k, 8 * k + 8), ALL)
-        lea = lambda k: V("LEA", ALL, sl(8 * k, 8 * k + 8), ALL)
-        zero(col("PS", 0, 32))
-        for k in range(3):
-            mm(col("PS", 3 - k, 32, 4), led(k), cb("KBO"), False, False)
-        ts(V("LEA", ALL, ALL, sl(NQ, 16)), col("DB", 0, 32 * NA), 0.0, ALU.is_gt, 0.40625, SUB)
-        for u in range(4):
-            mm(col("PS", 8 * u, 8 * u + 8), lea(u), cb("CM"), False, u == 3)
-        zero(col("PQ", 128, 160))
-        for k in range(4):
-            mm(col("PQ", 128 + k, 160, 4), led(k), cb("KBO"), False, False)
-        for u in range(4):
-            mm(col("PQ", 128 + 8 * u, 136 + 8 * u), lea(u), cb("KBO"), False, u == 3)
-        for bank in ("L0", "L1"):
-            mm(col(bank, 0, 384), ch("SIG"), whole("C16"), True, False)
-        scan(whole("FI"), col("PS", 0, 32), cf("BASEF"), 0.0, MIN, MAX)
-        cp(whole("FL"), col("FI", 3, 32, 4))
-        cp(whole("FC"), IND(col("COLF", 0, 512), col("FL", 0, 8)))
-        ts(whole("SV"), col("PQ", 128, 160), 0.0, ALU.is_lt)
-        tt(whole("SVM"), IND(col("SV", 0, 32), lu("LSV")), cb("MK"), MUL)
-        svm = lambda k: col("SVM", 128 * k, 128 * k + 128)
-        banks = ("L0", "L1", "DB")
-
-        def lin(pp):
-            bank = banks[pp % 3]
-            if pp >= 2:
-                mm(col(bank, 0, 384), ch("SIG"), whole("C16"), True, False)
-            for k in range(3):
-                mm(col(bank, 128 * k, 128 * k + 128), ch("FSEL", 128 * pp, 128 * pp + 128), whole("FC"), False, k == 2)
-            act(V("AB", ALL, pp % 3, ALL), col(bank, 0, 384), AF.Abs)
-
-        def member(pp):
-            tt(V("EE", ALL, pp, ALL), V("AB", ALL, pp % 3, ALL), col("DL", 0, 384), EQ)
-
-        def tally(pp):
-            for k in range(3):
-                mm(col("PW", 3 * (7 - pp) + k, 384, 24), V("EE", ALL, pp, sl(128 * k, 128 * k + 128)), cb("WM"), False, pp == 7 and k == 2)
-
-        def same_gate(k):
-            o = col(("DB", "DL")[k // 4], 128 * (k % 4), 128 * (k % 4) + 128)
-            mm(o, ch("SELG", 128 * k, 128 * k + 128), whole("CMG"), True, False)
+            cp(part("C2", k, NV), col("COA", k, 256, 4))
+        mm(col("DL", 256, 304), whole("R"), cb("XSEL"))
+        tt(whole("XB"), col("DL", 256, 304), cf("XCONST"), ADD)
+        for k in range(8):
+            o = part(("PQ", "DL")[k // 4], k % 4)
+            mm(o, cb("SELG", L * k, L * k + L), whole("CMG"), True, False)
             mm(o, cb("IDN"), cb("TRI2"), False, True)
-        for pp in range(3):
-            lin(pp)
-        member(0)
+        for k in range(8):
+            ts(part("EQ2", k), part(("PQ", "DL")[k // 4], k % 4), col("cT", k), EQ, 4096.0, MUL)
+        act(whole("XC2"), IND(XW, GL), AF.Copy)
         if last:
-            zero(col("PW", 0, 384))
-        mm(col("PQ", 0, 128), whole("FC"), ch("PERM"), True, False)
-        mm(col("PQ", 0, 128), cb("ONES", rows=R1), cb("RANK", rows=R1), False, True)
-        for pp in range(3, 8):
-            lin(pp)
-            member(pp - 2)
-            tally(pp - 3)
-            if pp == 3:
-                mm(col("DA", 64, 104), whole("R"), ch("XSEL"), True, False)
-                mm(col("DA", 64, 104), svm(3), cb("X3"), False, True)
-                mm(col("DA", 0, 40), cb("ONES", rows=R1), cb("VALC", rows=R1), True, False)
-                for k in range(4):
-                    mm(col("DA", 0, 40), svm(k), cb("VALK", 40 * k, 40 * k + 40), False, k == 3)
-            if pp == 4:
-                for k in range(3):
-                    mm(col("PW", k, 384, 3), svm(k + 1), cb("BIGSEL"), False, False)
-        member(6)
-        tally(5)
-        member(7)
-        tt(whole("XB"), col("DA", 64, 104), cf("XCONST"), ADD)
-        same_gate(0)
-        same_gate(1)
-        tally(6)
-        same_gate(2)
-        tally(7)
-        for k in range(3, 8):
-            same_gate(k)
-        act(col("G2", 16 * ga, 2048), IND(XW, col("CO2", ga, L)), AF.Copy)
+            for k in range(4):
+                bank = ("PW", "PQ")[k % 2]
+                mm(whole(bank), cf("WT"), part("IC", k, 512))
+                act(part("YC", k, 512), whole(bank), AF.Copy)
+        for q in range(16):
+            mm(col("L1", 64, 72), cb("W0", 15 - q, 143 - q), col("R", q, L, 16), q == 0, q == 15)
+        cp(whole("OL0"), col("L1", 64, 72))
+        act(whole("X0"), IND(XW, col("OL0", 0, 8)), AF.Copy)
+        mm(part("PS", 1), cb("IDN"), whole("X0"), True, False)
+        mm(part("PS", 1), cb("NID"), whole("A"), False, True)
+        act(whole("AA"), part("PS", 1), AF.Abs)
+        for bank in ("BV", "BS"):
+            mm(col(bank, 0, 256), cb("NTH", L * t, L * t + L, rows=R16), cb("THS", rows=R16), True, False)
+        for l in range(L - NV):
+            act(part("H", l, 64), IND(XW, part("COA", NV + l, 4)), AF.Abs, bias=col("A", NV + l), scale=-1.0)
+        for k in range(4):
+            tt(part("D", k, 1024), IND(XW, part("C2", k, NV)), whole("AR"), SUB)
+        if late:
+            abroad(t - 1)
+            for q in range(16):
+                mm(col("PW", 256, 288), cb("WIDE", 15 - q, 143 - q), col("PG", q, 512, 16), q == 0, q == 15)
+            for k in range(4):
+                mm(V("BV", sl(64 * (k % 2), 64 * (k % 2) + 64), sl(L * (k // 2), L * (k // 2) + L)), col("PG", k, 256, 4), cb("K4"), False, False)
+            for c in range(2):
+                mm(part("BS", c), part("PG", 2 + c), cb("K4"), False, False)
+            ts(whole("PL"), col("PW", 256, 288), float(W), ADD)
+            act(whole("DP"), IND(XS, whole("PL")), AF.Copy)
+            mm(whole("L0"), cb("NID"), whole("A4"), True, False)
+            mm(whole("L0"), cb("IDN"), whole("DP"), False, True)
+            act(whole("RP"), whole("L0"), AF.Abs)
+            for k in range(4):
+                mm(part("PW", 0), cb("BO", 96 - 32 * k, 224 - 32 * k), col("RP", k, 512, 4), k == 0, k == 3)
+            ts(whole("LE2"), part("PW", 0), cf("THC", t, t + 1), GT, 2.0, MUL)
 
-        def lin2(b):
-            bank = "L%d" % (b % 2)
+        def total(bank, src, sel, c, p, end=False):
+            mm(col(bank, L * c + p, L * c + L, 16), col(src, 2048 * c + p, 2048 * c + 2048, 16), sel, False, end)
+        for c in range(2):
+            for p in range(16):
+                total("BS", "H", BO, c, p, c == 1 and p == 15)
+                total("BV", "D", cb("NBO"), c, p)
             for j in range(4):
-                mm(col(bank, L * j, L * j + L), cb("IDN"), col("G2", 4 * b + j, 2048, 16), True, False)
-                mm(col(bank, L * j, L * j + L), cb("NID"), whole("XC2"), False, True)
-            act(col("H2", 512 * b, 512 * b + 512), whole(bank), AF.Abs)
-
-        def red2(b):
-            for p in range(4 * b, 4 * b + 4):
-                mm(col("PQ", p, 128, 16), col("H2", L * p, L * p + L), cb("BO"))
-        far2 = [lambda: lin2(0), lambda: lin2(1), lambda: (red2(0), lin2(2)), lambda: (red2(1), lin2(3)), lambda: red2(2), lambda: red2(3)]
-        if last:
-            act(whole("CF2"), IND(IW, col("GL", 0, 8)), AF.Copy)
-            far2 = [lambda: None] + far2
-
-        def far2_next():
-            far2.pop(0)()
-        act(tf(14), col("XB", 1, 40, 5), AF.Identity, bias=-12288.0)
-        if t == 0:
-            consts_d()
+                ts(col("R2", 2048 * c + j, 2048 * c + 2048, 4), col("D", 2048 * c + j, 2048 * c + 2048, 4), 0.0, MAX, 2.0, MUL)
+                for p in range(j, 16, 4):
+                    total("BV", "R2", BO, c, p, c == 1 and p == 15)
+        cp(whole("C16"), IND(IW, OL))
+        cp(whole("CO2"), IND(IW, GL))
+        act(whole("CF2"), IND(IW, GL), AF.Copy)
+        for k in range(3):
+            mm(part("DL", k), cb("DEL"), col("C16", k + 1, 512, 4))
+        act(whole("AB"), col("DL", 0, 384), AF.Abs)
+        for h, bank in enumerate(("BV", "BS")):
+            act(part("LE", h, 256), col(bank, 0, 256), AF.Sign)
+            scan(part("SC", h, 256), cb("NM16"), part("LE", h, 256), 0.0, MUL, ADD)
+        parts = [(k, sl(0, 64), k // 2, (64 * (k % 2), 64 * (k % 2) + 64)) for k in range(4)]
+        parts += [(k, sl(64 + 32 * c, 96 + 32 * c), 2 + c, (k, L, 4)) for c in range(2) for k in range(4)]
+        if late:
+            mm(col("PS", 0, 40), whole("LE2"), cb("K2"), True, False)
+            mm(part("PW", 0), cb("IDN"), whole("LE2"), True, False)
+        else:
+            mm(col("PS", 0, 40), cb("TWO", rows=R1), cb("CW", rows=R1), True, False)
+            mm(part("PW", 0), cb("ONES", rows=R1), cb("TWO", rows=R1), True, False)
+        for k, to, c, pick in parts:
+            mm(col("PS", 4 - k, 40, 5, rows=to), cb("KID", *pick), col("SC", L * c + 15, L * c + L, 16), False, False)
+        mm(col("PS", 0, 40), cb("ONES", rows=R1), cb("CW", rows=R1), False, True)
+        for k, to, c, pick in parts:
+            mm(V("PW", sl(32 * k, 32 * k + 8), to), col("SC", L * c + 15, L * c + L, 16), cb("IDN", *pick), False, False)
+        mm(part("PW", 0), cb("ONES", rows=R1), cb("ONES", rows=R1), False, True)
+        scan(whole("KEY"), col("PS", 0, 40), col("XB", 0, 40), 0.0, MIN, MAX)
+        ts(whole("KA"), col("KEY", 4, 40, 5), W - 1, AND)
+        spread("KM", col("KA", 0, 8))
+        act(whole("SVG"), part("PW", 0), AF.Sign)
+        mm(col("PS", 64, 72), whole("KM"), BO)
+        cp(whole("FL"), col("PS", 64, 72))
+        cp(whole("FC"), IND(IW, col("FL", 0, 8)))
+        mm(col("PW", 0, 384), whole("SVG"), cb("GW"), True, False)
+        for pp, bank in enumerate(("L0", "L1", "DL", "PQ", "BV", "BS", "L0", "L1")):
+            for k in range(3):
+                mm(part(bank, k), cb("SIG"), col("C16", k + 1, 512, 4), k == 0, False)
+            for k in range(3):
+                mm(part(bank, k), cb("FSEL", L * pp, L * pp + L), whole("FC"), False, k == 2)
+            act(col(bank, 0, 384), col(bank, 0, 384), AF.Abs)
+            tt(V("EE", ALL, pp, ALL), whole("AB"), col(bank, 0, 384), EQ)
+            for k in range(3):
+                mm(col("PW", 3 * (7 - pp) + k, 384, 24), V("EE", ALL, pp, sl(L * k, L * k + L)), cb("WM"), False, pp == 7 and k == 2)
+        mm(col("PS", 0, 8), whole("SVG"), cb("G1W"))
+        mm(part("PS", 1), whole("FC"), cb("PERM"), True, False)
+        mm(part("PS", 1), cb("ONES", rows=R1), cb("RANK", rows=R1), False, True)
+        tt(col("XC", 0, 8), col("KEY", 4, 40, 5), col("PS", 0, 8), MAX)
+        tt(col("XC", 8, 16), col("XC", 0, 8), col("XB", 40, 48), MIN)
         scan(whole("S1"), cb("M3"), col("PW", 0, 384), 0.0, MUL, MAX)
-        scan(whole("XC"), col("DA", 0, 40), whole("XB"), 0.0, MIN, MAX)
-        scan(whole("S2"), col("S1", 2, 384, 3), col("PQ", 0, 128), BIG, MIN, MAX)
-        tt(col("KC", 0, 8), col("S2", 15, 128, 16), col("XC", 4, 40, 5), MIN)
+        scan(whole("S2"), col("S1", 2, 384, 3), part("PS", 1), BIG, MIN, MAX)
+        tt(col("KC", 0, 8), col("S2", 15, L, 16), col("XC", 8, 16), MIN)
         ts(ki(0), col("KC", 0, 8), 4095, AND)
+        ts(ki(3, 2), whole("KC"), W - 1, AND)
         ts(ki(1, 2), whole("KC"), 1, AND)
         ts(whole("LB"), ki(0), 2048.0, ALU.is_lt)
-        mm(col("DA", 0, 8), cb("TRIP"), whole("LB"))
-        mm(col("DA", 8, 16), cb("ONES"), whole("LB"))
-        far2_next()
-        far2_next()
-        ts(ki(3, 2), whole("KC"), W - 1, AND)
-        ts(tf(2, 2), ki(1, 2), -2.0, MUL, -2047.0, ADD)
-        tt(tf(11), tf(9), whole("LB"), MUL)
-        tt(tf(0, 2), tf(2, 2), ki(3, 2), ADD)
-        for k in range(8):
-            ts(V("PA", ALL, ALL, k, ALL), cb("S48"), col("DA", k), EQ, col("TF", k), MUL)
-        for u in range(3):
-            mm(col("PS", 136 + u, 137 + u + u // 2), V("PA", ALL, u, ALL, ALL), ch("ONESH", 0, 1 + u // 2))
-        mm(V("PW", R49, sl(0, 384)), ch("ONESH", 0, 49), whole("PA"), True, False)
-        mm(V("PW", R49, sl(0, 384)), cb("IDN", 0, 49, rows=R48), cb("TRI3", rows=R48), False, False)
-        far2_next()
-        tt(tf(7), ki(3), tf(14), SUB)
-        ts(whole("MA%d" % t), col("PS", 136, 140), float(W), ADD)
-        send(t, "MA%d" % t, "LA%d" % t, "ra%d" % t)
-        cp(col("AL", 0, 4), col("PS", 136, 140))
-        tt(tf(10), tf(7), whole("LB"), MUL)
-        tt(col("AMG", 0, 48), IND(col("AL", 0, 4), lu("LR8", 0, 3)), cb("MK", 0, 48), MUL)
-        tt(tf(12, 2), tf(10, 2), tf(14, 2), ADD)
-        mm(V("PW", R49, sl(0, 384)), col("AMG", 0, 49), ch("NBLK3"), False, True)
-        far2_next()
-        for k in range(8):
-            ts(V("PB", ALL, ALL, k, ALL), cb("S48"), col("DA", k), EQ, col("TF", 8 + k), MUL)
-            if k == 7:
-                ts(V("EQ3", R49, ALL), V("PW", R49, sl(0, 384)), 0.0, EQ)
-        for u in range(3):
-            mm(col("PS", 160 + u), V("PA", ALL, u, ALL, ALL), ch("ONESH", 0, 1), True, False)
-            mm(col("PS", 160 + u), V("EQ3", R49, sl(128 * u, 128 * u + 128)), cb("P4096", 0, 1, rows=R49), False, True)
-        for u in range(3):
-            mm(col("PS", 164 + u), V("PB", ALL, u, ALL, ALL), ch("ONESH", 0, 1))
-        far2_next()
-        act(tf(8), whole("LB"), AF.Copy)
-        act(whole("LR"), IND(col("LB", 0, 8), lu("LR8")), AF.Copy)
-        act(whole("MR"), IND(tf(12), lu("LR8")), AF.Copy)
-        tt(whole("NM"), IND(tf(12), lu("LR8")), cb("MK", 0, L), MUL)
-        mm(col("PW", 400, 408), whole("NM"), ch("BOH"))
-        to_list(col("PS", 160, 163), 3, col("MB%d" % t, 0, 3), 0)
-        ts(col("MB%d" % t, 3, 6), col("PS", 164, 167), float(W), ADD)
-        send(t, "MB%d" % t, "LB%d" % t, "rb%d" % t)
-        cp(whole("NL"), col("PW", 400, 408))
-        act(whole("XN"), IND(XW, col("NL", 0, 8)), AF.Copy)
-        while far2:
-            far2_next()
-        mm(col("L1", 0, L), cb("IDN"), whole("XN"), True, False)
-        mm(col("L1", 0, L), cb("NID"), whole("A"), False, True)
-        act(whole("AA"), col("L1", 0, L), AF.Abs)
-        mm(col("L0", 0, L), cb("IDN"), whole("XN"), True, False)
-        mm(col("L0", 0, L), cb("IDN"), whole("A"), False, False)
-        mm(col("L0", 0, L), whole("LR"), cb("KID"), False, True)
-        mm(col("L0", L, 2 * L), cb("IDN"), whole("AA"), True, False)
-        mm(col("L0", L, 2 * L), whole("LR"), cb("HID"), False, True)
-        mm(col("L1", 0, L), whole("MR"), cf("IDF"), True, False)
-        mm(col("L1", 0, L), cf("NIDF"), whole("CF2"), False, True)
-        act(whole("DV2"), col("L1", 0, L), AF.Copy)
-        rec("v", lambda x, o, i: x.tensor_reduce(o, i, AX.X, ADD), col("TF", 32), col("DA", 8, 16))
-        act(tf(6), whole(cT), AF.Identity, bias=col("TF", 32), scale=37.0)
-        tt(whole("VM"), IND(tf(13), lu("LR8")), cb("MK", 0, L), MUL)
-        tt(ki(5), ki(3), ki(4), MUL)
-
-        def first_of_gate(k):
-            ts(V("EQ2", ALL, ALL, k, ALL), col(("DB", "DL")[k // 4], 128 * (k % 4), 128 * (k % 4) + 128), col(cT, k), EQ, col("TF", 64 + k), MUL)
-        first_of_gate(0)
-        scan(whole("PM2"), cb("NM16"), col("PQ", 0, 128), 0.0, MUL, MAX)
-        first_of_gate(1)
-        cp(whole("PX"), col("PM2", 15, L, 16))
-        first_of_gate(2)
-        tt(col("GE2", 16, 144), IND(col("PX", 0, 8), lu("LR8")), whole("PM2"), EQ)
-        far_mask_b(L, "GE2")
-        first_of_gate(3)
-        first_of_gate(4)
-        ts(whole("AH"), col("L0", 0, L), 0.5, MUL, 512.25, SUB)
-        first_of_gate(5)
-        tt(whole("AO" if last else "A"), whole("AH"), col("L0", L, 2 * L), MAX)
-        if not last:
-            act(whole("AR"), IND(col("A", 0, L), lu("LAR")), AF.Copy)
-        else:
-            dma("s", V("ya", ALL), whole("AO"))
-        if t == 0:
-            consts_e()
-            ts(cb("NE3"), cb("NE3"), Pc, EQ, -1.0, MUL)
-        for k in range(6, 8):
-            first_of_gate(k)
-        mm(col("PS", 192, 200), whole("VM"), ch("BOH"), True, False)
-        for u in range(8):
-            mm(col("PS", 192 + u), V("EQ2", ALL, u, ALL, ALL), cb("P4096", 0, 1), False, u == 7)
-        ts(ki(6), ki(5), 4, SHR)
-        tt(whole("WV2"), col("DA", 0, L), whole("DV2"), MUL)
-        tt(ki(7), ki(6), tf(6), ADD)
-        to_list(col("PS", 192, 200), 8, whole("SL2"), 8)
-        write(L, "2", col("SL2", 0, 8), t)
-        arrive(t, "LA%d" % t, "ra%d" % t)
-        la = col("LA%d" % t, 0, 3)
-        cp(whole("CO3"), IND(IS, la))
-        cp(whole("XC3"), IND(XS, la))
-        act(col("G3", 0, 384), IND(XS, col("CO3", 0, 24)), AF.Copy)
-        mm(V("PW", R48, sl(0, L)), whole("XC3"), cb("IDN"))
-        ts(col("KC", 8, 16), ki(7), W - 1, AND)
-        cp(V("XT3", R48, ALL), V("PW", R48, sl(0, L)))
-        act(whole("CF3"), IND(IS, la), AF.Copy)
-        cp(col("G3", 384, 768), IND(XS, col("CO3", 24, 48)))
-        if not last:
-            tt(whole("CMT"), IND(col("KC", 8, 16), lu("LR8")), cb("MK", 0, L), MUL)
-        for b in range(2):
-            mm(col("L%d" % b, 0, 384), V("XT3", R48, ALL), cb("NE3", 384 * b, 384 * b + 384, rows=R48), True, False)
-            mm(col("L%d" % b, 0, 384), cb("IDN"), col("G3", 384 * b, 384 * b + 384), False, True)
-            act(col("H3", 384 * b, 384 * b + 384), col("L%d" % b, 0, 384), AF.Abs)
-        if not last:
-            mm(col("PS", 144, 152), whole("CMT"), ch("BOH"))
-            mm(col("DL", 2 * L, 3 * L), whole("CMT"), ch("IDH"))
-            cp(whole(cN), col("KC", 8, 16))
-            cp(whole("GL"), col("PS", 144, 152))
-            cp(whole("CMG"), col("DL", 2 * L, 3 * L))
-            options_a()
-        else:
-            patch("2", col("SL2", 0, 8))
-            cp(whole("G16"), col("KC", 8, 16))
-            mm(V("PS", R8, sl(256, 384)), whole("G16"), ch("IDH"))
-        if last:
-            cp(whole("YG"), V("PS", R8, sl(256, 384)))
-            dma("s", V("yg", ALL), whole("YG"))
-        arrive(t, "LB%d" % t, "rb%d" % t)
-        cp(col("BF", 0, 3), col("LB%d" % t, 3, 6))
-        tt(whole("BM"), IND(col("BF", 0, 3), lu("LR8", 0, 3)), cb("MK", 0, 48), MUL)
+        for b in range(4):
+            gather(part("G2", b, 512), IND(XW, part("CO2", b, 32)), b == 3)
+        for b, bank in enumerate(("DL", "BV", "BS", "L0")):
+            for j in range(4):
+                mm(part(bank, j), cb("IDN"), col("G2", 4 * b + j, 2048, 16), True, False)
+                mm(part(bank, j), cb("NID"), whole("XC2"), False, True)
+            act(part("H2", b, 512), whole(bank), AF.Abs)
         for p in range(16):
-            mm(V("PQ", R48, sl(p, 128, 16)), col("H3", p, 768, 16), cb("BO"))
-        mm(col("PW", 0, 48), ch("BLKH"), whole("BM"), True, False)
-        mm(col("PW", 0, 48), cf("NIDF"), whole("CF3"), False, True)
-        act(whole("DV3"), col("PW", 0, 48), AF.Copy)
+            mm(col("PQ", p, L, 16), part("H2", p), BO)
+        farthest(L, "2")
+        act(whole("C5"), whole("cT"), AF.Identity, scale=592.0)
+        mm(col("DL", 0, 8), cb("O16"), whole("LB"))
+        mm(col("PS", 0, 8), cb("TRIP"), whole("LB"))
+        rec("sum", "v", lambda x, o, i: x.tensor_reduce(o, i, AX.X, ADD), cf("E16"), col("DL", 0, 8))
+        spread("NM", ki(0))
+        mm(col("PW", 0, 8), whole("NM"), BO)
+        ts(whole("NL"), col("PW", 0, 8), float(W), MIN)
+        act(whole("XN"), IND(XS, col("NL", 0, 8)), AF.Copy)
+        tt(ki(5), ki(3), ki(4), MUL)
+        tt(ki(6), ki(5), whole("C5"), ADD)
+        ts(tf(2, 2), ki(1, 2), -2.0, MUL, -2047.0, ADD)
+        tt(tf(0, 2), tf(2, 2), ki(3, 2), ADD)
+        ts(ki(7), ki(6), cf("E16"), ADD)
+        ts(col("KC", 8, 16), ki(7), 4, SHR, W - 1, AND)
+        mm(col("BS", 0, 8), whole("CMG"), BO, True, False)
+        mm(col("BS", 0, 8), cb("K4"), whole("LB"), False, False)
+        for k in range(8):
+            mm(col("BS", k), part("EQ2", k), col("LB", k), False, k == 7)
+        ts(whole("ZZ"), col("BS", 0, 8), float(W), ADD, Pc, MIN)
+        for k in range(8):
+            times(part("ZM", k, 16), cb("MK", 0, 16), col("ZZ", k))
+        mm(col("BS", 16, 24), whole("ZM"), cf("BOF"))
+        ts(whole("SL2"), col("BS", 16, 24), float(W), ADD)
+        tt(whole("DV2"), IND(NUM, col("NL", 0, 8)), whole("CF2"), SUB)
+        tt(whole("WV2"), part("PQ", 1), whole("DV2"), MUL)
+        tt(IND(IS, col("SL2", 0, 8)), whole("WV2"), whole("CF2"), ADD)
         if not last:
-            options_b()
-        far_mask_a(48, "PM3", "GE3")
-        far_mask_b(48, "GE3")
+            spread("CMT", col("KC", 8, 16))
+            mm(col("PW", 32, 40), whole("CMT"), BO)
+            mm(part("PW", 1), whole("CMT"), cb("IDN"))
+            cp(GL, col("PW", 32, 40))
+            cp(whole("CMG"), part("PW", 1))
+            cp(whole("cT"), col("KC", 8, 16))
+        for k in range(8):
+            ts(V("PA", ALL, ALL, k, ALL), cb("S48"), col("PS", k), EQ, col("TF", k), MUL)
+        for u in range(3):
+            mm(col("L1", u, 1 + u + u // 2), V("PA", ALL, u, ALL, ALL), cb("ONES", 0, 1 + u // 2))
+        ts(whole("MA%d" % t), col("L1", 0, 4), float(W), ADD)
+        send(t, "A")
+        cp(col("AL", 0, 4), col("L1", 0, 4))
         if not last:
-            options_c()
-        write(48, "3", col("LB%d" % t, 0, 3), t)
-    patch("3", col("LB%d" % (RO - 1), 0, 3))
-    dma("s", V("yc", ALL), V("YC", sl(0, 128, 16), sl(0, W)))
-    emit(g, T, ops)
+            options()
+        mm(part("DL", 0), cb("IDN"), whole("XN"), True, False)
+        mm(part("DL", 0), cb("IDN"), whole("A"), False, True)
+        mm(part("DL", 1), cb("ONES", rows=R1), cb("C1024", rows=R1), True, False)
+        mm(part("DL", 1), cb("IDN"), whole("AA"), False, False)
+        mm(part("DL", 1), cb("NID"), whole("XN"), False, True)
+        ts(whole("AH"), part("DL", 0), 0.5, MUL, 0.25, SUB)
+        tt(whole("AO" if last else "A"), whole("AH"), part("DL", 1), MAX)
+        if last:
+            dma("s", V("ya", ALL), whole("AO"), 0)
+        else:
+            widen()
+        for k in range(8):
+            ts(V("PB", ALL, ALL, k, ALL), cb("S48"), col("PS", k), EQ, col("TF", 8 + k), MUL)
+        tt(col("AMG", 0, 48), IND(col("AL", 0, 4), col("LR8", 0, 3)), cb("MK", 0, 48), MUL)
+        mm(V("L0", R49, sl(0, 384)), cb("ONES", 0, 49), whole("PA"), True, False)
+        mm(V("L0", R49, sl(0, 384)), cb("IDN", 0, 49, rows=R48), cb("TRI3", rows=R48), False, False)
+        mm(V("L0", R49, sl(0, 384)), col("AMG", 0, 49), cb("NBLK3"), False, True)
+        ts(V("EQ3", R49, ALL), V("L0", R49, sl(0, 384)), 0.0, EQ)
+        for u in range(3):
+            mm(col("L1", 20 + u, 21 + u + u // 2), V("PB", ALL, u, ALL, ALL), cb("ONES", 0, 1 + u // 2))
+        for u in range(3):
+            o = col("L1", 16 + u, 17 + u + u // 2)
+            mm(o, V("PA", ALL, u, ALL, ALL), cb("ONES", 0, 1 + u // 2), True, False)
+            mm(o, V("EQ3", R49, sl(L * u, L * u + L)), cb("P4096", 0, 1 + u // 2, rows=R49), False, True)
+        tt(col("ZT", 0, 4), col("L1", 16, 20), cf("DUML", 0, 4), MIN)
+        ts(col("MB%d" % t, 4, 8), col("L1", 20, 24), float(W), ADD)
+        ts(col("MB%d" % t, 0, 4), col("ZT", 0, 4), float(W), ADD)
+        send(t, "B")
+    cp(whole("G16"), col("KC", 8, 16))
+    mm(V("BS", R8, sl(256, 384)), whole("G16"), cb("IDN"))
+    cp(whole("YG"), V("BS", R8, sl(256, 384)))
+    dma("s", V("yg", ALL), whole("YG"), 0)
+    patch(L, "2", "DL", col("SL2", 0, 8))
+    abroad(RO - 1)
+    dma("s", V("yc", ALL), V("YC", sl(0, 128, 16), sl(0, W)), 64)
+    emit(g, T, arrange(ops))
     g.wait_ge(T.sem["snt"], sent[0])

@@ -10,8 +10,8 @@ H16 = "float16"
 NV = 64
 ENG = 8
 FILES = ("H", "D")
-CYCLE, TENSOR, GATHER, SCATTER, WAKE, HOP = 0.00083, 0.00042, 1.56, 3.8, 0.19, 2.3
-PASSES, SHAKE = 30, 0.4
+CYCLE, TENSOR, GATHER, SCATTER, WAKE, HOP = 0.00083, 0.00042, 1.56, 3.0, 0.19, 2.5
+PASSES, SHAKE = 100, 0.5
 
 
 def _pack(items):
@@ -23,12 +23,12 @@ def _pack(items):
 
 
 CB, NCB = _pack([("ONES", 128), ("IDN", 128), ("NID", 128), ("MK", 128), ("BO", 224), ("NBO", 8), ("K2", 40), ("CW", 40), ("TWO", 128),
-                 ("WIDE", 144), ("W0", 144), ("KID", 128), ("THS", 256), ("NTH", 512), ("FG", 384), ("NM16", 256), ("GW", 384), ("G1W", 8), ("WM", 16), ("RANK", 128),
-                 ("TRIP", 128), ("TRI2", 128), ("TRI3", 384), ("S48", 48), ("P4096", 16), ("J", 128), ("M3", 384), ("F16", 128), ("JG", 128),
-                 ("F3", 128), ("F8", 128), ("FP", 128), ("BLKB", 128), ("K4", 128), ("O16", 128), ("C1024", 128),
-                 ("SELO", 512), ("SIG", 128), ("DEL", 128), ("FSEL", 1024), ("PERM", 128), ("XSEL", 48), ("SELG", 1024), ("NBLK3", 384)])
-CF, NCF = _pack([("P", 8), ("PD", 32), ("FO", 128), ("GO", 4), ("FW", 16), ("FX", 48), ("FK", 40), ("FV", 144), ("XCONST", 48), ("UB", 8), ("FR", 128),
-                 ("P16", 3), ("DUML", 8), ("WT", 128), ("SEL8", 128), ("THF", 4), ("THC", 4), ("THP", 12), ("BOF", 8), ("J32", 128), ("E16", 1)])
+                 ("WIDE", 144), ("W0", 144), ("KID", 128), ("THS", 256), ("NTH", 512), ("FG", 432), ("NM16", 256), ("GW", 432), ("G1W", 8), ("WM", 16), ("RANK", 144),
+                 ("TRIP", 128), ("TRI2", 128), ("TRI3", 384), ("S48", 48), ("P4096", 16), ("J", 128), ("F16", 128), ("JG", 128),
+                 ("F3", 128), ("F8", 128), ("FP", 144), ("BLKB", 128), ("K4", 128), ("O16", 128), ("C1024", 128),
+                 ("SELO", 512), ("SIG", 128), ("DEL", 128), ("FSEL", 1024), ("PERM", 144), ("XSEL", 48), ("SELG", 1024), ("NBLK3", 384)])
+CF, NCF = _pack([("P", 8), ("PD", 32), ("FO", 128), ("GO", 4), ("FW", 16), ("FX", 48), ("FK", 40), ("FV", 144), ("XCONST", 48), ("UB", 8), ("FR", 144),
+                 ("P16", 3), ("DUML", 8), ("WT", 128), ("SEL8", 128), ("THF", 4), ("THC", 4), ("THP", 12), ("BOF", 8), ("J32", 128), ("E16", 1), ("RST", 144)])
 S, F, B, I32, U = "sbuf", "float32", "bfloat16", "int32", "uint16"
 SCRATCH = {
     "CB": (S, [128, NCB], B), "CF": (S, [128, NCF], F), "LR8": (S, [128, 8], U), "LI": (S, [128, 8], I32),
@@ -42,8 +42,8 @@ SCRATCH = {
     "LE": (S, [128, 512], B), "LE2": (S, [128, L], B), "SC": (S, [128, 512], B),
     "PG": (S, [128, 512], H16), "PL": (S, [128, 32], U), "DP": (S, [128, 512], B), "RP": (S, [128, 512], B),
     "XB": (S, [128, 48], F), "KEY": (S, [128, 40], I32), "KA": (S, [128, 8], I32), "KM": (S, [128, L], H16), "FL": (S, [128, 8], U), "FC": (S, [128, L], H16),
-    "SVG": (S, [128, L], B), "XC": (S, [128, 16], F), "AB": (S, [128, 384], F), "EE": (S, [128, 8, 384], B),
-    "S1": (S, [128, 384], F), "S2": (S, [128, L], F), "KC": (S, [128, 16], I32), "KI": (S, [128, 64], I32), "TF": (S, [128, 32], F), "LB": (S, [128, 8], B),
+    "SVG": (S, [128, L], B), "XC": (S, [128, 8], F), "AB": (S, [128, 384], F), "EE": (S, [128, 8, 384], B),
+    "S1": (S, [128, 432], F), "S2": (S, [128, 144], I32), "M3": (S, [128, 432], F), "KI": (S, [128, 64], I32), "TF": (S, [128, 32], F), "LB": (S, [128, 8], B),
     "PA": (S, [128, 3, 8, 16], H16), "PB": (S, [128, 3, 8, 16], H16), "EQ3": (S, [128, 384], B), "EQ2": (S, [128, 1024], B),
     "AL": (S, [128, 8], F), "AMG": (S, [128, 64], H16), "ZT": (S, [128, 8], F), "ZZ": (S, [128, 8], F), "ZM": (S, [128, L], F), "SL2": (S, [128, 8], U),
     "NM": (S, [128, L], H16), "NL": (S, [128, 8], U), "X0": (S, [128, L], B), "OL0": (S, [128, 8], U), "AA": (S, [128, L], B),
@@ -251,7 +251,8 @@ def arrange(ops):
         laid = lay(deps, users, gap, way, [0.0] * N)
         best = min(best or laid, laid)
         shake = {}
-        ends = [e + shake.setdefault((o["q"], o["a"][0][1]), SHAKE * math.sin(n * 12.9898 + k * 78.233 + n * k)) for n, (e, o) in enumerate(zip(best[2], ops))]
+        ends = [e + (int(e * 5 / best[0]) == k % 5) * shake.setdefault((o["q"], o["a"][0][1]), SHAKE * math.sin(n * 12.9898 + k * 78.233 + n * k))
+                for n, (e, o) in enumerate(zip(best[2], ops))]
         way = lay(users, deps, lambda n, j: gap(j, n), ends, list(lag))[2]
     ORDERS[like] = best[1]
     return [ops[n] for n in best[1]]
@@ -332,7 +333,7 @@ def rank_program(g, core, T, topo):
 
     def dma(q, out, in_, kb):
         loaded[0] += kb
-        rec("dma", q, lambda x, o, i: x.dma_start(o, i), out, in_, e="d%d" % ndma[0], sem="d%d" % ndma[0], val=16, lag=2.0 + loaded[0] / 280)
+        rec("dma", q, lambda x, o, i: x.dma_start(o, i), out, in_, e="d%d" % ndma[0], sem="d%d" % ndma[0], val=16, lag=2.0 + loaded[0] / 320)
         ndma[0] += 1
 
     def cp(out, in_):
@@ -375,7 +376,7 @@ def rank_program(g, core, T, topo):
         src = [r for r in range(len(cores)) if target(r, t, cores) == core][0]
         hops = 1 if first_hop(src, t, cores, topo)[0] == core else 2
         land = "L%s%d" % (part, t)
-        rec("arrive", None, None, V(land, ALL), e="s" + land, sem="s" + land, val=ENG, after="xM" + land[1:], lag=hops * (HOP if t else HOP + 1.5))
+        rec("arrive", None, None, V(land, ALL), e="s" + land, sem="s" + land, val=ENG, after="xM" + land[1:], lag=hops * (HOP + 1.5 if t == 0 else HOP if t < RO - 1 else 1.2))
 
     EQ, MUL, ADD, SUB, MAX, MIN, GT = ALU.is_equal, ALU.mult, ALU.add, ALU.subtract, ALU.max, ALU.min, ALU.is_gt
     SHR, AND = ALU.arith_shift_right, ALU.bitwise_and
@@ -396,8 +397,8 @@ def rank_program(g, core, T, topo):
     ms(whole("AW"), 0)
     dma("s", whole("GI"), V("gate", ALL), 4)
     dma("a", whole("A"), V("acc0", ALL), 32)
-    for k in range(4):
-        dma("sa"[k % 2], part("IT", k, 512), part("icol", k, 512), 256)
+    dma("s", whole("IT"), V("icol", ALL), 1024)
+    loaded[0] -= 500
     dma("s", V("AW", sl(0, 128, 4)), V("alt", ALL), 256)
     dma("s", XW, V("pat", ALL), 512)
     loaded[0] = 0
@@ -417,14 +418,14 @@ def rank_program(g, core, T, topo):
     iota(cf("FX", 40, 48), [[16, 8]], 12)
     iota(cf("FK"), [[1, 8], [-32, 5]], 128)
     iota(cf("J32"), [[0, 4], [1, 32]])
-    iota(cb("FG"), [[1, 8], [0, 16], [32, 3]], 32)
+    iota(cb("FG"), [[1, 8], [0, 18], [32, 3]], 32)
     iota(cf("XCONST", 0, 40), [[0, 8], [-4096, 5]], 20480)
-    iota(cf("UB"), [[-17, 8]], 141)
+    iota(cf("UB"), [[-18, 8]], 151)
     iota(cb("F3"), [[8, 8], [0, 2], [1, 8]])
     iota(cb("F8"), [[8, 16], [0, 8]])
-    iota(cb("FP"), [[16, 8], [-1, 16]], 15)
+    iota(cb("FP"), [[16, 8], [-8, 2], [-1, 9]], 16)
     iota(cf("FW"), [[2, 8], [-1, 2]], 1)
-    iota(cf("FR"), [[-17, 8], [-1, 16]], 140)
+    iota(cf("FR"), [[-1, 144]], 150)
     iota(cf("P16"), [[-16, 3]], 0, 1)
     iota(cf("DUML"), [[16, 8]])
     iota(cb("S48"), [[1, 48]], -256)
@@ -440,8 +441,11 @@ def rank_program(g, core, T, topo):
     fill(col("IC", W, W + DUM), DUM, 0)
     fill(col("YC", W, W + DUM), DUM, 0)
     fill(col("X", W, W + 16), 16, -1024)
-    for k in range(3):
-        fill(cb("M3", k, 384, 3), 128, min(k, 1))
+    for a in (0, 72):
+        for k in range(1, 3):
+            fill(col("M3", 3 * a + k, 3 * a + 216, 3), 72, 4 * BIG)
+        fill(cf("RST", a, a + 72), 72, 0)
+    fill(cf("RST", 0, 144, 18), 8, 4 * BIG)
     for k in range(2):
         fill(cb("NM16", L * k, L * k + L), 128, 1)
     fill(cb("CW"), 40, CNT)
@@ -479,6 +483,9 @@ def rank_program(g, core, T, topo):
     ts(cb("XSEL"), cf("FX"), Pc, EQ)
     ts(cb("K2"), cf("FK"), Pc, EQ, CNT, MUL)
     act(cb("GW"), cb("GW"), AF.Identity, bias=pd_(16))
+    for k in range(3):
+        times(cb("GW", k, 432, 54), cb("ONES", 0, 8), pd_(17))
+        fill(cb("GW", 27 + k, 432, 54), 8, 0)
     act(cb("G1W"), cb("G1W"), AF.Identity, bias=pd_(17))
     for k in range(2):
         ts(cb("THS", L * k, L * k + L), cb("JG"), pd_(6), EQ)
@@ -507,7 +514,7 @@ def rank_program(g, core, T, topo):
     ms(whole("AMG"), 0.0)
     cp(cf("THF", rows=R8), col("TH", 0, 4, rows=R8))
     mm(col("PQ", 0, 4), cf("SEL8", rows=R8), cf("THF", rows=R8))
-    act(cf("THC"), col("PQ", 0, 4), AF.Copy)
+    act(cf("THC"), col("PQ", 0, 4), AF.Identity, bias=-0.5, scale=-1.0)
     ts(col("TH", 4, 8), col("TH", 0, 4), 4, SHR)
     ts(col("TH", 8, 12), col("TH", 0, 4), 15, AND)
     ts(cf("THP", 0, 4, rows=R16), col("TH", 4, 8), pd_(19, R16), MUL)
@@ -589,7 +596,7 @@ def rank_program(g, core, T, topo):
     spread("CMG", col("GI", 0, 8))
     mm(col("PS", 0, 8), whole("CMG"), BO)
     cp(whole("cT"), col("PS", 0, 8))
-    cp(col("KC", 8, 16), col("PS", 0, 8))
+    cp(ki(4), col("PS", 0, 8))
     for k in range(4):
         cp(part("IC", k, 512), part("IT", k, 512))
     options()
@@ -597,23 +604,17 @@ def rank_program(g, core, T, topo):
     for t in range(RO):
         last, late = t == RO - 1, t > 0
         for h in (1, 0):
-            cp(part("COA", h, 256), IND(IW, part("OL", h, 16)))
+            cp(part("COA", h, 256), IND(IW if late else col("IT", 0, W), part("OL", h, 16)))
         for k in range(4):
             cp(part("C2", k, NV), col("COA", k, 256, 4))
         mm(col("DL", 256, 304), whole("R"), cb("XSEL"))
         tt(whole("XB"), col("DL", 256, 304), cf("XCONST"), ADD)
-        for k in range(8):
-            o = part(("PQ", "DL")[k // 4], k % 4)
-            mm(o, cb("SELG", L * k, L * k + L), whole("CMG"), True, False)
-            mm(o, cb("IDN"), cb("TRI2"), False, True)
-        for k in range(8):
-            ts(part("EQ2", k), part(("PQ", "DL")[k // 4], k % 4), col("cT", k), EQ, 4096.0, MUL)
         act(whole("XC2"), IND(XW, GL), AF.Copy)
         if last:
             for k in range(4):
                 bank = ("PW", "PQ")[k % 2]
                 mm(whole(bank), cf("WT"), part("IC", k, 512))
-                act(part("YC", k, 512), whole(bank), AF.Copy)
+                gather(part("YC", k, 512), whole(bank), k % 2)
         for q in range(16):
             mm(col("L1", 64, 72), cb("W0", 15 - q, 143 - q), col("R", q, L, 16), q == 0, q == 15)
         cp(whole("OL0"), col("L1", 64, 72))
@@ -636,13 +637,11 @@ def rank_program(g, core, T, topo):
             for c in range(2):
                 mm(part("BS", c), part("PG", 2 + c), cb("K4"), False, False)
             ts(whole("PL"), col("PW", 256, 288), float(W), ADD)
-            act(whole("DP"), IND(XS, whole("PL")), AF.Copy)
-            mm(whole("L0"), cb("NID"), whole("A4"), True, False)
-            mm(whole("L0"), cb("IDN"), whole("DP"), False, True)
-            act(whole("RP"), whole("L0"), AF.Abs)
+            tt(whole("DP"), IND(XS, whole("PL")), whole("A4"), SUB)
+            act(whole("RP"), whole("DP"), AF.Abs)
             for k in range(4):
                 mm(part("PW", 0), cb("BO", 96 - 32 * k, 224 - 32 * k), col("RP", k, 512, 4), k == 0, k == 3)
-            ts(whole("LE2"), part("PW", 0), cf("THC", t, t + 1), GT, 2.0, MUL)
+            act(whole("LE2"), part("PW", 0), AF.Sign, bias=cf("THC", t, t + 1))
 
         def total(bank, src, sel, c, p, end=False):
             mm(col(bank, L * c + p, L * c + L, 16), col(src, 2048 * c + p, 2048 * c + 2048, 16), sel, False, end)
@@ -663,20 +662,26 @@ def rank_program(g, core, T, topo):
         for h, bank in enumerate(("BV", "BS")):
             act(part("LE", h, 256), col(bank, 0, 256), AF.Sign)
             scan(part("SC", h, 256), cb("NM16"), part("LE", h, 256), 0.0, MUL, ADD)
+        for h in range(2):
+            for k in range(4 * h, 4 * h + 4):
+                mm(part("BS", k % 4), cb("SELG", L * k, L * k + L), whole("CMG"), True, False)
+                mm(part("BS", k % 4), cb("IDN"), cb("TRI2"), False, True)
+            for k in range(4 * h, 4 * h + 4):
+                ts(part("EQ2", k), part("BS", k % 4), col("cT", k), EQ, 4096.0, MUL)
         parts = [(k, sl(0, 64), k // 2, (64 * (k % 2), 64 * (k % 2) + 64)) for k in range(4)]
         parts += [(k, sl(64 + 32 * c, 96 + 32 * c), 2 + c, (k, L, 4)) for c in range(2) for k in range(4)]
         if late:
             mm(col("PS", 0, 40), whole("LE2"), cb("K2"), True, False)
             mm(part("PW", 0), cb("IDN"), whole("LE2"), True, False)
         else:
-            mm(col("PS", 0, 40), cb("TWO", rows=R1), cb("CW", rows=R1), True, False)
-            mm(part("PW", 0), cb("ONES", rows=R1), cb("TWO", rows=R1), True, False)
+            mm(col("PS", 0, 40), cb("ONES", rows=R1), cb("CW", rows=R1), True, False)
+            mm(part("PW", 0), cb("ONES", rows=R1), cb("ONES", rows=R1), True, False)
         for k, to, c, pick in parts:
             mm(col("PS", 4 - k, 40, 5, rows=to), cb("KID", *pick), col("SC", L * c + 15, L * c + L, 16), False, False)
-        mm(col("PS", 0, 40), cb("ONES", rows=R1), cb("CW", rows=R1), False, True)
+        mm(col("PS", 0, 40), cb("TWO", rows=R1), cb("CW", rows=R1), False, True)
         for k, to, c, pick in parts:
             mm(V("PW", sl(32 * k, 32 * k + 8), to), col("SC", L * c + 15, L * c + L, 16), cb("IDN", *pick), False, False)
-        mm(part("PW", 0), cb("ONES", rows=R1), cb("ONES", rows=R1), False, True)
+        mm(part("PW", 0), cb("ONES", rows=R1), cb("TWO", rows=R1), False, True)
         scan(whole("KEY"), col("PS", 0, 40), col("XB", 0, 40), 0.0, MIN, MAX)
         ts(whole("KA"), col("KEY", 4, 40, 5), W - 1, AND)
         spread("KM", col("KA", 0, 8))
@@ -684,31 +689,34 @@ def rank_program(g, core, T, topo):
         mm(col("PS", 64, 72), whole("KM"), BO)
         cp(whole("FL"), col("PS", 64, 72))
         cp(whole("FC"), IND(IW, col("FL", 0, 8)))
-        mm(col("PW", 0, 384), whole("SVG"), cb("GW"), True, False)
-        for pp, bank in enumerate(("L0", "L1", "DL", "PQ", "BV", "BS", "L0", "L1")):
+        mm(col("PW", 0, 432), whole("SVG"), cb("GW"), True, False)
+        for pp, bank in enumerate(("L0", "L1", "DL", "PQ", "BV", "L0", "L1", "DL")):
             for k in range(3):
                 mm(part(bank, k), cb("SIG"), col("C16", k + 1, 512, 4), k == 0, False)
             for k in range(3):
                 mm(part(bank, k), cb("FSEL", L * pp, L * pp + L), whole("FC"), False, k == 2)
             act(col(bank, 0, 384), col(bank, 0, 384), AF.Abs)
-            tt(V("EE", ALL, pp, ALL), whole("AB"), col(bank, 0, 384), EQ)
+            for a, b in ((0, 384),) if pp < 7 else ((0, 256), (256, 384)):
+                tt(V("EE", ALL, pp, sl(a, b)), col("AB", a, b), col(bank, a, b), EQ)
             for k in range(3):
-                mm(col("PW", 3 * (7 - pp) + k, 384, 24), V("EE", ALL, pp, sl(L * k, L * k + L)), cb("WM"), False, pp == 7 and k == 2)
+                mm(col("PW", 3 * (8 - pp) + k, 432, 27), V("EE", ALL, pp, sl(L * k, L * k + L)), cb("WM"), False, pp == 7 and k == 2)
         mm(col("PS", 0, 8), whole("SVG"), cb("G1W"))
-        mm(part("PS", 1), whole("FC"), cb("PERM"), True, False)
-        mm(part("PS", 1), cb("ONES", rows=R1), cb("RANK", rows=R1), False, True)
-        tt(col("XC", 0, 8), col("KEY", 4, 40, 5), col("PS", 0, 8), MAX)
-        tt(col("XC", 8, 16), col("XC", 0, 8), col("XB", 40, 48), MIN)
-        scan(whole("S1"), cb("M3"), col("PW", 0, 384), 0.0, MUL, MAX)
-        scan(whole("S2"), col("S1", 2, 384, 3), part("PS", 1), BIG, MIN, MAX)
-        tt(col("KC", 0, 8), col("S2", 15, L, 16), col("XC", 8, 16), MIN)
-        ts(ki(0), col("KC", 0, 8), 4095, AND)
-        ts(ki(3, 2), whole("KC"), W - 1, AND)
-        ts(ki(1, 2), whole("KC"), 1, AND)
+        mm(col("PS", L, L + 144), whole("FC"), cb("PERM"), True, False)
+        mm(col("PS", L, L + 144), cb("ONES", rows=R1), cb("RANK", rows=R1), False, True)
+        tt(whole("XC"), col("KEY", 4, 40, 5), col("PS", 0, 8), MAX)
+        act(col("M3", 0, 432, 3), col("PS", L, L + 144), AF.Copy)
+        tt(col("M3", 27, 432, 54), whole("XC"), col("XB", 40, 48), MIN)
+        scan(whole("S1"), whole("M3"), col("PW", 0, 432), BIG, MIN, MAX)
+        scan(whole("S2"), cf("RST"), col("S1", 2, 432, 3), 0.0, ADD, MIN)
+        named = col("S2", 17, 144, 18)
+        ts(ki(0), named, 4095, AND)
+        ts(ki(3), named, W - 1, AND)
+        ts(ki(1), named, 1, AND)
+        ts(ki(2), ki(4), 1, AND)
         ts(whole("LB"), ki(0), 2048.0, ALU.is_lt)
         for b in range(4):
             gather(part("G2", b, 512), IND(XW, part("CO2", b, 32)), b == 3)
-        for b, bank in enumerate(("DL", "BV", "BS", "L0")):
+        for b, bank in enumerate(("PQ", "BV", "BS", "L0")):
             for j in range(4):
                 mm(part(bank, j), cb("IDN"), col("G2", 4 * b + j, 2048, 16), True, False)
                 mm(part(bank, j), cb("NID"), whole("XC2"), False, True)
@@ -729,7 +737,7 @@ def rank_program(g, core, T, topo):
         ts(tf(2, 2), ki(1, 2), -2.0, MUL, -2047.0, ADD)
         tt(tf(0, 2), tf(2, 2), ki(3, 2), ADD)
         ts(ki(7), ki(6), cf("E16"), ADD)
-        ts(col("KC", 8, 16), ki(7), 4, SHR, W - 1, AND)
+        ts(ki(4), ki(7), 4, SHR, W - 1, AND)
         mm(col("BS", 0, 8), whole("CMG"), BO, True, False)
         mm(col("BS", 0, 8), cb("K4"), whole("LB"), False, False)
         for k in range(8):
@@ -743,12 +751,12 @@ def rank_program(g, core, T, topo):
         tt(whole("WV2"), part("PQ", 1), whole("DV2"), MUL)
         tt(IND(IS, col("SL2", 0, 8)), whole("WV2"), whole("CF2"), ADD)
         if not last:
-            spread("CMT", col("KC", 8, 16))
+            spread("CMT", ki(4))
             mm(col("PW", 32, 40), whole("CMT"), BO)
             mm(part("PW", 1), whole("CMT"), cb("IDN"))
             cp(GL, col("PW", 32, 40))
             cp(whole("CMG"), part("PW", 1))
-            cp(whole("cT"), col("KC", 8, 16))
+            cp(whole("cT"), ki(4))
         for k in range(8):
             ts(V("PA", ALL, ALL, k, ALL), cb("S48"), col("PS", k), EQ, col("TF", k), MUL)
         for u in range(3):
@@ -786,7 +794,7 @@ def rank_program(g, core, T, topo):
         ts(col("MB%d" % t, 4, 8), col("L1", 20, 24), float(W), ADD)
         ts(col("MB%d" % t, 0, 4), col("ZT", 0, 4), float(W), ADD)
         send(t, "B")
-    cp(whole("G16"), col("KC", 8, 16))
+    cp(whole("G16"), ki(4))
     mm(V("BS", R8, sl(256, 384)), whole("G16"), cb("IDN"))
     cp(whole("YG"), V("BS", R8, sl(256, 384)))
     dma("s", V("yg", ALL), whole("YG"), 0)

@@ -4,14 +4,32 @@ from concourse.mybir import AluOpType as ALU, AxisListType as AX, ActivationFunc
 
 W, L, RO = 2048, 128, 4
 DUM = 128
-BIG = 2097152.0
-CNT = 65536.0
+BIG = 4194304.0
+CNT = 2097152.0
+RK, SH = 8192, 32
+NONE = 5 * SH + 24
+OFF = 592
+ROUND = 1.5 * 2 ** 32
 H16 = "float16"
 NV = 64
 ENG = 8
 FILES = ("H", "D")
-CYCLE, TENSOR, GATHER, SCATTER, WAKE, HOP = 0.00083, 0.00042, 1.56, 3.0, 0.19, 2.5
-PASSES, SHAKE = 100, 0.5
+XFV, G2V = (0, 1), (2, 3)
+ONV = ("XC3", "G3a", "CF3", "AG", "BG", "PX3", "PG", "A4", "NM", "PX")
+LOADS = "XAI"
+DN, G2N = 2, 8
+EEB, EARLY, LATER = ("B0", "B1", "DL", "PQ", "BV", "B0", "B1", "DL"), (), ("PQ", "BV", "BS", "B0")
+PAV, CN = 8, 1
+EQB = ("BS", "BS")
+CUT = False
+MOVED = 500
+COP = ((16, 20), (0, 16), (20, 32))
+CYCLE, TENSOR = 0.00083, 0.00042
+PACES = ((1.0, 1.56, 3.0, 0.19, 1.3), (1.3, 1.2, 3.0, 0.15, 1.0), (1.15, 1.9, 4.0, 0.25, 2.2))
+PASSES, SHAKE = 30, 0.5
+UNIT = 0.5
+SLACK, STARTS, ANEW = 0.0003, 1, 5
+PIECE, MOVES, SWEEPS = 160, 500, 7
 
 
 def _pack(items):
@@ -22,47 +40,49 @@ def _pack(items):
     return at, n
 
 
-CB, NCB = _pack([("ONES", 128), ("IDN", 128), ("NID", 128), ("MK", 128), ("BO", 224), ("NBO", 8), ("K2", 40), ("CW", 40), ("TWO", 128),
-                 ("WIDE", 144), ("W0", 144), ("KID", 128), ("THS", 256), ("NTH", 512), ("FG", 432), ("NM16", 256), ("GW", 432), ("G1W", 8), ("WM", 16), ("RANK", 144),
-                 ("TRIP", 128), ("TRI2", 128), ("TRI3", 384), ("S48", 48), ("P4096", 16), ("J", 128), ("F16", 128), ("JG", 128),
+CB, NCB = _pack([("ONES", 128), ("IDN", 128), ("NID", 128), ("MK", 128), ("NMK", 16), ("NMK1", 128), ("BO", 224), ("AS", 256), ("XSUM", 128), ("CK", 64), ("K2", 40), ("CW", 40), ("TWO", 128), ("THREE", 128),
+                 ("WIDE", 144), ("W0", 144), ("KID", 128), ("THS", 256), ("BOC", 8), ("NTH", 512), ("FG", 432), ("NM16", 128), ("GW", 432), ("G1W", 8), ("WM", 16),
+                 ("RANK", 144), ("FS", 144), ("TRIP", 128), ("TRI2", 128), ("S48", 48), ("J", 128), ("F16", 128), ("JG", 128),
                  ("F3", 128), ("F8", 128), ("FP", 144), ("BLKB", 128), ("K4", 128), ("O16", 128), ("C1024", 128),
-                 ("SELO", 512), ("SIG", 128), ("DEL", 128), ("FSEL", 1024), ("PERM", 144), ("XSEL", 48), ("SELG", 1024), ("NBLK3", 384)])
-CF, NCF = _pack([("P", 8), ("PD", 32), ("FO", 128), ("GO", 4), ("FW", 16), ("FX", 48), ("FK", 40), ("FV", 144), ("XCONST", 48), ("UB", 8), ("FR", 144),
-                 ("P16", 3), ("DUML", 8), ("WT", 128), ("SEL8", 128), ("THF", 4), ("THC", 4), ("THP", 12), ("BOF", 8), ("J32", 128), ("E16", 1), ("RST", 144)])
+                 ("SELO", 512), ("SIG", 128), ("DEL", 128), ("FSEL", 1024), ("PERM", 144), ("XSEL", 40), ("SELG", 1024)])
+CF, NCF = _pack([("P", 8), ("PD", 32), ("FO", 128), ("GO", 4), ("FW", 16), ("FX", 40), ("FK", 40), ("FV", 144), ("XCONST", 40), ("FR", 144),
+                 ("WS", 16), ("NIF", 128), ("RS8", 64), ("D0", 147), ("NE", 147), ("CPOS", 3),
+                 ("DUML", 3), ("SPARE", 8), ("WT", 128), ("SEL8", 128), ("THF", 4), ("THC", 4), ("THG", 4), ("SELB", 128), ("THP", 12), ("BOF", 8), ("J32", 128), ("RST", 145)])
 S, F, B, I32, U = "sbuf", "float32", "bfloat16", "int32", "uint16"
 SCRATCH = {
-    "CB": (S, [128, NCB], B), "CF": (S, [128, NCF], F), "LR8": (S, [128, 8], U), "LI": (S, [128, 8], I32),
+    "CB": (S, [128, NCB], B), "CF": (S, [128, NCF], F), "LR8": (S, [128, 16], U), "LI": (S, [128, 8], I32),
     "PI": (S, [128, 32], I32), "TH": (S, [16, 12], I32), "GI": (S, [128, 8], I32),
-    "IT": (S, [128, W], I32), "IC": (S, [128, W + DUM], F), "AW": (S, [128, W], I32), "X": (S, [128, W + 16], B), "YC": (S, [128, W + DUM], F),
-    "NUM": (S, [128, W + 16], F),
+    "IT": (S, [128, W], I32), "IC": (S, [128, W + DUM], F), "AW": (S, [128, W], I32), "X": (S, [128, OFF + W + 16], B), "XF": (S, [128, W], F),
+    "YC": (S, [128, W + DUM], F), "NUM": (S, [128, OFF + W + 16], F),
     "A": (S, [128, L], B), "A4": (S, [128, 512], B), "GL": (S, [128, 8], U), "OL": (S, [128, 32], U), "R": (S, [128, L], H16),
-    "cT": (S, [128, 8], F), "C5": (S, [128, 8], F), "CMG": (S, [128, L], H16), "CMT": (S, [128, L], H16),
+    "cT": (S, [128, 8], F), "CMG": (S, [128, L], H16), "CMT": (S, [128, L], H16),
     "COA": (S, [128, 512], U), "C16": (S, [128, 512], H16),
-    "H": (S, [128, 4096], B), "D": (S, [128, 4096], B), "R2": (S, [128, 4096], B), "AR": (S, [128, 1024], B), "C2": (S, [128, 256], U),
-    "LE": (S, [128, 512], B), "LE2": (S, [128, L], B), "SC": (S, [128, 512], B),
-    "PG": (S, [128, 512], H16), "PL": (S, [128, 32], U), "DP": (S, [128, 512], B), "RP": (S, [128, 512], B),
-    "XB": (S, [128, 48], F), "KEY": (S, [128, 40], I32), "KA": (S, [128, 8], I32), "KM": (S, [128, L], H16), "FL": (S, [128, 8], U), "FC": (S, [128, L], H16),
+    "H": (S, [128, 4096], B), "D": (S, [128, 4096], F), "RR": (S, [128, 256], F), "AD": (S, [128, 256], B), "DD": (S, [128, 256], B), "SV": (S, [128, 256], B), "AR": (S, [128, 1024], B), "C2": (S, [128, 256], U),
+    "LE": (S, [128, 512], B), "LE2": (S, [128, L], B),
+    "PG": (S, [128, 512], B), "DP": (S, [128, 512], B), "RP": (S, [128, 512], B),
+    "XB": (S, [128, 40], F), "KEY": (S, [128, 40], I32), "KA": (S, [128, 8], I32), "KM": (S, [128, L], H16), "FL": (S, [128, 8], U), "FC": (S, [128, L], H16),
     "SVG": (S, [128, L], B), "XC": (S, [128, 8], F), "AB": (S, [128, 384], F), "EE": (S, [128, 8, 384], B),
-    "S1": (S, [128, 432], F), "S2": (S, [128, 144], I32), "M3": (S, [128, 432], F), "KI": (S, [128, 64], I32), "TF": (S, [128, 32], F), "LB": (S, [128, 8], B),
-    "PA": (S, [128, 3, 8, 16], H16), "PB": (S, [128, 3, 8, 16], H16), "EQ3": (S, [128, 384], B), "EQ2": (S, [128, 1024], B),
-    "AL": (S, [128, 8], F), "AMG": (S, [128, 64], H16), "ZT": (S, [128, 8], F), "ZZ": (S, [128, 8], F), "ZM": (S, [128, L], F), "SL2": (S, [128, 8], U),
-    "NM": (S, [128, L], H16), "NL": (S, [128, 8], U), "X0": (S, [128, L], B), "OL0": (S, [128, 8], U), "AA": (S, [128, L], B),
+    "S1": (S, [128, 435], F), "S2": (S, [128, 145], I32), "M3": (S, [128, 432], F), "KI": (S, [128, 64], I32), "TF": (S, [128, 16], F), "LB": (S, [128, 8], B),
+    "PA": (S, [128, 3, 8, 16], B), "PB": (S, [128, 3, 8, 16], B), "PC": (S, [128, 3, 8, 16], B), "PF": (S, [128, 8], F), "T16": (S, [128, 16], H16), "SK": (S, [128, 64], F), "EQ2": (S, [128, 1024], B), "AB2": (S, [128, 1024], B),
+    "AL": (S, [128, 4], F), "AG": (S, [128, 48], F), "SD": (S, [128, 147], F), "LD": (S, [128, 4], U),
+    "ZT": (S, [128, 8], F), "ZZ": (S, [128, 8], F), "ZM": (S, [128, L], F), "SL2": (S, [128, 8], U),
+    "NM": (S, [128, L], F), "NL": (S, [128, 8], U), "X0": (S, [128, L], B), "OL0": (S, [128, 8], U), "AA": (S, [128, L], B),
     "XN": (S, [128, L], B), "AH": (S, [128, L], I32), "AO": (S, [128, L], F),
     "CO2": (S, [128, L], U), "CF2": (S, [128, L], F), "XC2": (S, [128, L], B),
     "G2": (S, [128, 2048], B), "H2": (S, [128, 2048], B),
     "PM2": (S, [128, L], F), "GE2": (S, [128, 144], B), "DV2": (S, [128, L], F), "WV2": (S, [128, L], F), "YP2": (S, [128, L], F),
     "CO3": (S, [128, 48], U), "CF3": (S, [128, 48], F), "XC3": (S, [128, 48], B), "G3": (S, [128, 768], B), "H3": (S, [128, 768], B),
     "PM3": (S, [128, L], F), "GE3": (S, [128, 144], B), "DV3": (S, [128, 48], F), "WV3": (S, [128, 48], F), "YP3": (S, [128, 48], F),
-    "BG": (S, [128, 48], F), "OH": (S, [128, 48], F), "PX": (S, [128, 8], F), "G16": (S, [128, 8], H16), "YG": (S, [8, L], F),
+    "BG": (S, [128, 48], B), "OH": (S, [128, 48], B), "PX": (S, [128, L], F), "G16": (S, [128, 8], H16), "YG": (S, [8, L], F),
 }
 for _t in range(RO):
-    for _n, _w in (("MA", 4), ("MB", 8), ("LA", 4), ("LB", 8)):
-        SCRATCH["%s%d" % (_n, _t)] = (S, [128, _w], U)
+    for _n in "OI":
+        SCRATCH["%s%d" % (_n, _t)] = (S, [128, 8], U)
 for _t in range(RO - 1):
-    SCRATCH["PT%d" % _t] = (S, [128, W + DUM], F)
-for _n in ("BV", "BS", "PS", "L0", "L1", "DL", "PW", "PQ"):
+    SCRATCH["PT%d" % _t] = SCRATCH["PN%d" % _t] = (S, [128, W + 64], B)
+for _n in ("BV", "BS", "PS", "B0", "B1", "DL", "PW", "PQ"):
     SCRATCH[_n] = ("psum", [128, 512], F)
-SEMAPHORES = ["cv", "ca", "cp", "cg", "snt"] + ["d%d" % k for k in range(16)] + ["s%s%d" % (n, t) for n in ("LA", "LB", "MA", "MB") for t in range(RO)]
+SEMAPHORES = ["cv", "ca", "cp", "cg", "snt"] + ["d%d" % k for k in range(16)] + ["s%s%d" % (n, t) for n in "IO" for t in range(RO)]
 
 
 def target(r, t, cores):
@@ -80,8 +100,8 @@ def relay(src, cores, topo):
 def first_hop(r, t, cores, topo):
     src, dst = cores[r], target(r, t, cores)
     if topo.may_write(src, dst):
-        return dst, "L"
-    return relay(src, cores, topo), "LM"[[c for c in cores if c in topo.cores_of(src)].index(src)]
+        return dst, "I"
+    return relay(src, cores, topo), "IO"[[c for c in cores if c in topo.cores_of(src)].index(src)]
 
 
 def hand(g, T, topo, src, dst, out, in_):
@@ -92,14 +112,13 @@ def hand(g, T, topo, src, dst, out, in_):
 def relay_program(g, core, T, topo):
     cores, sent = list(T.cores), 0
     for t in range(RO):
-        for part in "AB":
-            for r in range(len(cores)):
-                hop, letter = first_hop(r, t, cores, topo)
-                if hop == core:
-                    buf = "%s%s%d" % (letter, part, t)
-                    g.wait_ge(T.sem["s" + buf], ENG)
-                    hand(g, T, topo, core, target(r, t, cores), "L%s%d" % (part, t), buf)
-                    sent += ENG
+        for r in range(len(cores)):
+            hop, letter = first_hop(r, t, cores, topo)
+            if hop == core:
+                buf = "%s%d" % (letter, t)
+                g.wait_ge(T.sem["s" + buf], ENG)
+                hand(g, T, topo, core, target(r, t, cores), "I%d" % t, buf)
+                sent += ENG
     if sent:
         g.wait_ge(T.sem["snt"], sent)
 
@@ -176,34 +195,368 @@ def needs(ops, banks):
     return out
 
 
-def cost(o):
-    kind, a = o["kind"], [x for x in o["a"] if isinstance(x, tuple)]
+def cost(o, kind, pace):
+    a, (slow, gather, scatter) = [x for x in o["a"] if isinstance(x, tuple)], pace[:3]
     size = lambda x: span(x)[4]
     if kind in ("dma", "send", "arrive"):
         return {"dma": 0.06, "send": 0.6, "arrive": 0.0}[kind]
     ind = [x for x in a if x[0] == "ind"]
     if ind:
-        return (0.05 if o["q"] == "v" else 0.065) + 16 * size(ind[0][2]) * CYCLE * (SCATTER if ind[0] is a[0] else GATHER)
+        return slow * ((0.065 if kind == "act" else 0.05) + 16 * size(ind[0][2]) * CYCLE * (scatter if ind[0] is a[0] else gather))
     n, wide = size(a[0]), [SCRATCH[x[1]][2] in (F, I32) for x in a if size(x) > 1 or x is a[0]]
     if kind == "mm":
-        return max(min(64, size(a[1])), n) * TENSOR * (4 if wide[1] else 1)
+        return slow * max(min(64, size(a[1])), n) * TENSOR * (4 if wide[1] else 1) + sum(cost(x, kind, pace) for x in o.get("also", ()))
     if kind == "iota":
-        return 0.13 + 2 * n * CYCLE
+        return slow * (0.13 + 2 * n * CYCLE)
     if kind == "tt":
         n *= 1 if "psum" in (SCRATCH[a[1][1]][0], SCRATCH[a[2][1]][0]) else 2
     elif kind != "act" and not any(wide):
         n /= 2
-    return max(64, n) * CYCLE
+    return slow * max(64, n) * CYCLE
+
+
+def late_(o, pace):
+    return o["lag"] + o["hops"] * pace[4] + (o["hops"] > 1) * (0.6 + pace[3])
+
+
+def refine(ops, deps, free_, order):
+    N, above = len(ops), []
+    for n in range(N):
+        m = 0
+        for j in deps[n]:
+            m |= above[j] | 1 << j
+        above.append(m)
+    loose = {j for j, n in free_}
+    near, far = [], []
+    for n in range(N):
+        inner = 0
+        for j in deps[n]:
+            inner |= above[j]
+        keep = [j for j in deps[n] if j in loose or not inner >> j & 1]
+        near.append([j for j in keep if (j, n) in free_ or ops[j]["kind"] == ops[n]["kind"] == "mm"])
+        far.append([j for j in keep if j not in near[n]])
+    names = ["v", "a", "p", "g", "s"]
+    q = [names.index(o["q"]) if o["q"] else 5 for o in ops]
+    both = [[[cost(o, o["other"][1] if k and o["other"] else o["kind"], p) for o in ops] for k in range(2)] for p in PACES]
+    hold = [list(b[0]) for b in both]
+    lag = [[late_(o, p) for o in ops] for p in PACES]
+    out = [[x + p[3] for x in l] for l, p in zip(lag, PACES)]
+    last = [n for n, o in enumerate(ops) if o["dma"]][-3:]
+    turned = [0] * N
+
+    def run(seq, at, s, end, fin):
+        free, h, w = [0.0] * 6, hold[s], out[s]
+        seen = 0
+        for i in range(at - 1, -1, -1):
+            k = q[seq[i]]
+            if not seen >> k & 1:
+                seen |= 1 << k
+                free[k] = end[seq[i]]
+                if seen == 7 and i < at - 400 or seen & 15 == 15:
+                    break
+        for i in range(at, N):
+            n = seq[i]
+            k = q[n]
+            t = free[k]
+            for j in near[n]:
+                if end[j] > t:
+                    t = end[j]
+            for j in far[n]:
+                if fin[j] > t:
+                    t = fin[j]
+            t += h[n]
+            end[n] = t
+            fin[n] = t + w[n]
+            if k < 5:
+                free[k] = t
+        return max(end[n] + lag[s][n] for n in last)
+    seq = list(order)
+    ends, fins = [[0.0] * N for p in PACES], [[0.0] * N for p in PACES]
+    base = [run(seq, 0, s, ends[s], fins[s]) for s in range(len(PACES))]
+    now = best = float(len(PACES))
+    kept, seed, arcs = (list(seq), list(turned)), [12345], None
+
+    def draw(n):
+        seed[0] = (seed[0] * 1103515245 + 12345) % 2147483648
+        return (seed[0] >> 8) % n
+    for step in range(MOVES):
+        if arcs is None:
+            seq.sort(key=lambda n: ends[0][n] - hold[0][n])
+            pos, before, prev = [0] * N, [-1] * N, [-1] * 6
+            for i, n in enumerate(seq):
+                pos[n], before[n] = i, prev[q[n]]
+                prev[q[n]] = n
+            arcs = []
+            for s in range(len(PACES)):
+                end, fin = ends[s], fins[s]
+                n = max(last, key=lambda n: end[n] + lag[s][n])
+                while n >= 0:
+                    t, up = end[n] - hold[s][n] - 1e-7, -1
+                    for j in far[n]:
+                        if fin[j] >= t:
+                            up = j
+                    for j in near[n]:
+                        if end[j] >= t:
+                            up = j
+                    if up < 0 and q[n] < 5 and before[n] >= 0 and end[before[n]] >= t:
+                        up = before[n]
+                        arcs.append(n)
+                    n = up
+        n = arcs[draw(len(arcs))]
+        b = before[n]
+        for k in range(draw(4) * draw(3)):
+            if before[b] >= 0:
+                b = before[b]
+        kind, flip = draw(5), -1
+        if kind == 4:
+            flip = n if ops[n]["other"] and draw(2) else b
+            if not ops[flip]["other"]:
+                continue
+            new, at = seq, pos[flip]
+            q[flip], turned[flip] = 1 - q[flip], 1 - turned[flip]
+            for s in range(len(PACES)):
+                hold[s][flip] = both[s][turned[flip]][flip]
+        else:
+            if above[n] >> b & 1:
+                continue
+            at, piece = pos[b], seq[pos[b]:pos[n] + 1]
+            if kind < 2:
+                m = above[n] | 1 << n
+                piece = [x for x in piece if m >> x & 1] + [x for x in piece if not m >> x & 1]
+            else:
+                piece = [x for x in piece if x != b and not above[x] >> b & 1] + [x for x in piece if x == b or above[x] >> b & 1]
+            new = seq[:at] + piece + seq[pos[n] + 1:]
+        limit, total, tried = now + SLACK * (1 - step / MOVES) * draw(100) / 100, 0.0, []
+        for s in range(len(PACES)):
+            end, fin = list(ends[s]), list(fins[s])
+            total += run(new, at, s, end, fin) / base[s]
+            tried.append((end, fin))
+            if s == 0 and total > ends[0][last[2]] / base[0] + 0.03:
+                total = 99.0
+                break
+        if total <= limit:
+            seq, now, arcs = list(new), total, None
+            ends, fins = [x[0] for x in tried], [x[1] for x in tried]
+            if now < best:
+                best, kept = now, (list(seq), list(turned))
+        elif flip >= 0:
+            q[flip], turned[flip] = 1 - q[flip], 1 - turned[flip]
+            for s in range(len(PACES)):
+                hold[s][flip] = both[s][turned[flip]][flip]
+    return kept
+
+
+def refine(ops, deps, free_, order):
+    N, above, S_ = len(ops), [], range(len(PACES))
+    for n in range(N):
+        m = 0
+        for j in deps[n]:
+            m |= above[j] | 1 << j
+        above.append(m)
+    loose = {j for j, n in free_}
+    near, far, after = [], [], [[] for o in ops]
+    for n in range(N):
+        inner = 0
+        for j in deps[n]:
+            inner |= above[j]
+        keep = [j for j in deps[n] if j in loose or not inner >> j & 1]
+        near.append([j for j in keep if (j, n) in free_ or ops[j]["kind"] == ops[n]["kind"] == "mm"])
+        far.append([j for j in keep if j not in near[n]])
+        for j in keep:
+            after[j].append((n, j in far[n]))
+    q = ["vapgs".index(o["q"]) if o["q"] else 5 for o in ops]
+    both = [[[cost(o, o["other"][1] if k and o["other"] else o["kind"], p) for o in ops] for k in range(2)] for p in PACES]
+    hold = [list(b[0]) for b in both]
+    lag = [[late_(o, p) for o in ops] for p in PACES]
+    out = [[x + p[3] for x in l] for l, p in zip(lag, PACES)]
+    turned, seed, seq, name = [0] * N, [12345], list(order), [str(o["a"][0][1]) for o in ops]
+
+    def draw(n):
+        seed[0] = (seed[0] * 1103515245 + 12345) % 2147483648
+        return (seed[0] >> 8) % n
+
+    def run(piece, s, free, end, fin, rest, then, final=(-1,) * 5):
+        free, h, w, top, tip, final = list(free), hold[s], out[s], 0.0, -1, list(final)
+        for n in piece:
+            k = q[n]
+            t = free[k]
+            for j in near[n]:
+                if end[j] > t:
+                    t = end[j]
+            for j in far[n]:
+                if fin[j] > t:
+                    t = fin[j]
+            t += h[n]
+            end[n] = t
+            fin[n] = t + w[n]
+            if k < 5:
+                free[k], final[k] = t, n
+            if t + rest[n] > top:
+                top, tip = t + rest[n], n
+        for k in range(5):
+            if final[k] >= 0 and free[k] + then[k] > top:
+                top, tip = free[k] + then[k], final[k]
+        return top, tip
+
+    def turn(n):
+        q[n], turned[n] = 1 - q[n], 1 - turned[n]
+        for s in S_:
+            hold[s][n] = both[s][turned[n]][n]
+    ends, fins = [[0.0] * N for s in S_], [[0.0] * N for s in S_]
+    base = [run(seq, s, [0.0] * 6, ends[s], fins[s], lag[s], [0.0] * 6)[0] for s in S_]
+    for a in [a for sweep in range(SWEEPS) for a in range(-(sweep % 2) * PIECE // 4, N, PIECE // 2)]:
+        a, b = max(a, 0), min(a + PIECE, N)
+        frees, rests, thens = [], [], []
+        for s in S_:
+            run(seq, s, [0.0] * 6, ends[s], fins[s], lag[s], [0.0] * 6)
+        seq.sort(key=lambda n: ends[0][n] - hold[0][n])
+        inside = set(seq[a:b])
+        for s in S_:
+            free, tail, then = [0.0] * 6, {}, [0.0] * 6
+            for n in seq[:a]:
+                free[q[n]] = ends[s][n] * (q[n] < 5)
+            for n in reversed(seq[b:]):
+                tail[n] = then[q[n]] = hold[s][n] + max([lag[s][n], then[q[n]] * (q[n] < 5)] + [tail[u] + w * out[s][n] for u, w in after[n]])
+            frees.append(free)
+            thens.append(then)
+            rests.append({n: max([lag[s][n]] + [tail[u] + w * out[s][n] for u, w in after[n] if u in tail]) for n in inside})
+        piece, arcs, kept = seq[a:b], None, None
+        tops = [run(piece, s, frees[s], ends[s], fins[s], rests[s], thens[s]) for s in S_]
+        for step in range(MOVES):
+            if arcs is None:
+                now = sum(tops[s][0] / base[s] for s in S_)
+                if kept is None or now <= kept[0]:
+                    kept = now, list(piece), [turned[n] for n in piece]
+                piece.sort(key=lambda n: ends[0][n] - hold[0][n])
+                pos, before, prev, arcs, lasts, high = {}, {}, [-1] * 6, [], [], [[(0.0, -1)] for s in S_]
+                for i, n in enumerate(piece):
+                    lasts.append(prev[:5])
+                    pos[n], before[n] = i, prev[q[n]]
+                    prev[q[n]] = n
+                    for s in S_:
+                        high[s].append(max(high[s][-1], (ends[s][n] + rests[s][n], n)))
+                for s in S_:
+                    end, fin, n = ends[s], fins[s], tops[s][1]
+                    while n in inside:
+                        t, up = end[n] - hold[s][n] - 1e-7, -1
+                        for j in far[n]:
+                            if fin[j] >= t:
+                                up = j
+                        for j in near[n]:
+                            if end[j] >= t:
+                                up = j
+                        if up < 0 and q[n] < 5 and before[n] >= 0 and end[before[n]] >= t:
+                            up = before[n]
+                            arcs.append(n)
+                        n = up
+                if not arcs:
+                    break
+            n = arcs[draw(len(arcs))]
+            v = before[n]
+            for k in range(draw(4) * draw(3)):
+                if before[v] >= 0:
+                    v = before[v]
+            kind, new = draw(5 + ANEW), piece
+            if kind > 4:
+                s, at = draw(len(PACES)), max(0, pos[n] - 10 - draw(40))
+                part, behind = piece[at:pos[n] + 10 + draw(30)], piece[pos[n] + 10:]
+                behind = piece[at + len(part):]
+                way, then, shift, width = {}, list(thens[s]), {}, (1 + draw(6)) / 1000
+                for x in reversed(behind):
+                    way[x] = then[q[x]] = hold[s][x] + max([rests[s][x], then[q[x]] * (q[x] < 5)] + [way[u] + w * out[s][x] for u, w in after[x] if u in way])
+                for x in reversed(part):
+                    way[x] = hold[s][x] + max([rests[s][x], then[q[x]] * (q[x] < 5)] + [way[u] + w * out[s][x] for u, w in after[x] if u in way])
+                for x in part:
+                    way[x] += shift.setdefault(name[x], draw(100) * width)
+                own, ready, left, pool = set(part), {}, {}, [[] for k in range(6)]
+                for x in part:
+                    ready[x] = max([0.0] + [ends[s][j] for j in near[x] if j not in own] + [fins[s][j] for j in far[x] if j not in own])
+                    left[x] = sum(j in own for j in near[x] + far[x])
+                    if not left[x]:
+                        pool[q[x]].append(x)
+                free, new = [ends[s][j] if j >= 0 else x for j, x in zip(lasts[at], frees[s])] + [0.0], []
+                while len(new) < len(part):
+                    t, k = min((max(free[k], min(ready[x] for x in c)), k) for k, c in enumerate(pool) if c)
+                    x = max(pool[k], key=lambda x: way[x] - 2 * max(0.0, ready[x] - t))
+                    pool[k].remove(x)
+                    new.append(x)
+                    t = max(t, ready[x]) + hold[s][x]
+                    free[k] = t * (k < 5)
+                    for u, w in after[x]:
+                        if u in own:
+                            ready[u] = max(ready[u], t + w * out[s][x])
+                            left[u] -= 1
+                            if not left[u]:
+                                pool[q[u]].append(u)
+                new += behind
+            elif kind == 4:
+                n = n if ops[n]["other"] and draw(2) else v
+                if not ops[n]["other"]:
+                    continue
+                turn(n)
+                at = pos[n]
+                new = piece[at:]
+            elif above[n] >> v & 1:
+                continue
+            else:
+                at = pos[v]
+                part = piece[at:pos[n] + 1]
+                first = [x == n or above[n] >> x & 1 for x in part] if kind < 2 else [x != v and not above[x] >> v & 1 for x in part]
+                new = [x for x, f in zip(part, first) if f] + [x for x, f in zip(part, first) if not f] + piece[pos[n] + 1:]
+            total, tried, limit = 0.0, [], SLACK * (1 - step / MOVES) * draw(100) / 100 + 1e-9
+            for s in S_:
+                end, fin = ends[s][:], fins[s][:]
+                free = [end[j] if j >= 0 else x for j, x in zip(lasts[at], frees[s])] + [0.0]
+                top = max(run(new, s, free, end, fin, rests[s], thens[s], lasts[at]), high[s][at])
+                total += top[0] / base[s]
+                tried.append((end, fin, top))
+                if total > sum(tops[r][0] / base[r] for r in range(s + 1)) + 0.004:
+                    total = 99.0
+                    break
+            if total <= now + limit:
+                piece, arcs = piece[:at] + new, None
+                ends, fins, tops = ([x[k] for x in tried] for k in range(3))
+            elif kind == 4:
+                turn(n)
+        for n, k in zip(kept[1], kept[2]):
+            if turned[n] != k:
+                turn(n)
+        seq[a:b] = kept[1]
+    return sum(run(seq, s, [0.0] * 6, ends[s], fins[s], lag[s], [0.0] * 6)[0] / PACES[s][0] for s in S_), seq, turned
 
 
 def arrange(ops):
-    like = tuple(o["lag"] for o in ops)
-    if like in ORDERS:
-        return [ops[n] for n in ORDERS[like]]
-    deps, N = needs(ops, True), len(ops)
+    if not ORDERS:
+        ORDERS["all"] = lay_out(ops)
+    order, turned = ORDERS["all"]
+    for o, k in zip(ops, turned):
+        if o["other"]:
+            if k:
+                o["q"], o["kind"], o["f"], o["a"] = o["other"]
+            o["e"] = o["q"]
+    return [ops[n] for n in order]
+
+
+def lay_out(calls):
+    deps, ops, unit = needs(calls, True), [], []
+    for n, o in enumerate(calls):
+        u = ops[-1] if ops else o
+        outer = {j for j in deps[n] if calls[j]["kind"] != "mm"}
+        if o["kind"] == u["kind"] == "mm" and o["a"][0][1] == u["a"][0][1] and outer <= u["outer"] and cost(u, "mm", PACES[0]) + cost(o, "mm", PACES[0]) < UNIT:
+            u["members"].append(n)
+            u["also"].append(o)
+        else:
+            ops.append(dict(o, members=[n], also=[], outer=outer))
+        unit.append(len(ops) - 1)
+    order, turned = lay_units(ops, [{unit[j] for n in o["members"] for j in deps[n]} - {k} for k, o in enumerate(ops)])
+    return [n for k in order for n in ops[k]["members"]], [turned[k] for k in unit]
+
+
+def lay_units(ops, deps):
+    N = len(ops)
     last, free_ = {}, set()
     for n, o in enumerate(ops):
-        file = o["q"] if o["kind"] in ("dma", "send") else o["a"][0][1] if o["a"][0][1] in FILES else None
+        file = "iota" if o["kind"] == "iota" else o["q"] if o["kind"] in ("dma", "send") else o["a"][0][1] if o["a"][0][1] in FILES else None
         if file in last and last[file] not in deps[n]:
             deps[n].add(last[file])
             free_.add((last[file], n))
@@ -211,9 +564,9 @@ def arrange(ops):
             last[file] = n
         if o["kind"] == "arrive":
             deps[n].add([j for j in range(n) if ops[j]["e"] == o["after"]][0])
-    hold = [cost(o) for o in ops]
-    lag = [o["lag"] for o in ops]
-    gap = lambda j, n: 0.0 if (j, n) in free_ or ops[j]["kind"] == ops[n]["kind"] == "mm" else lag[j] + WAKE
+    hold = [cost(o, o["kind"], PACES[0]) for o in ops]
+    lag = [late_(o, PACES[0]) for o in ops]
+    gap = lambda j, n: 0.0 if (j, n) in free_ or ops[j]["kind"] == ops[n]["kind"] == "mm" else lag[j] + PACES[0][3]
     users = [[] for _ in ops]
     for n in range(N):
         for j in deps[n]:
@@ -246,16 +599,19 @@ def arrange(ops):
                 if not left[u]:
                     pool.setdefault(str(ops[u]["q"]), []).append(u)
         return max(e + x for e, x in zip(end, lag)), order, end
-    best = None
-    for k in range(PASSES):
-        laid = lay(deps, users, gap, way, [0.0] * N)
-        best = min(best or laid, laid)
-        shake = {}
-        ends = [e + (int(e * 5 / best[0]) == k % 5) * shake.setdefault((o["q"], o["a"][0][1]), SHAKE * math.sin(n * 12.9898 + k * 78.233 + n * k))
-                for n, (e, o) in enumerate(zip(best[2], ops))]
-        way = lay(users, deps, lambda n, j: gap(j, n), ends, list(lag))[2]
-    ORDERS[like] = best[1]
-    return [ops[n] for n in best[1]]
+    found, first = [], way
+    for start in range(STARTS):
+        best, way = None, first
+        for k in range(start * PASSES, (start + 1) * PASSES):
+            laid = lay(deps, users, gap, way, [0.0] * N)
+            best = min(best or laid, laid)
+            shake = {}
+            ends = [e + (int(e * 5 / best[0]) == k % 5) * shake.setdefault((o["q"], o["a"][0][1]), SHAKE * math.sin(n * 12.9898 + k * 78.233 + n * k))
+                    for n, (e, o) in enumerate(zip(best[2], ops))]
+            way = lay(users, deps, lambda n, j: gap(j, n), ends, list(lag))[2]
+        found.append(refine(ops, deps, free_, best[1]))
+    SPANS["log"] = [round(x[0], 1) for x in found]
+    return min(found)[1:]
 
 
 def emit(g, T, ops):
@@ -314,7 +670,13 @@ def rank_program(g, core, T, topo):
     cores = list(T.cores)
     ops, ndma, sent, loaded = [], [0], [0], [0]
 
-    def rec(kind, q, f, out, *args, e=None, sem=None, val=None, lag=0.0, after=None, group=None):
+    def either(first, second):
+        first()
+        second()
+        o = ops.pop()
+        ops[-1].update(other=(o["q"], o["kind"], o["f"], o["a"]), e="x%d" % len(ops))
+
+    def rec(kind, q, f, out, *args, e=None, sem=None, val=None, lag=0.0, after=None, group=None, hops=0):
         r, w = [], []
         for a in args:
             if isinstance(a, tuple):
@@ -329,7 +691,8 @@ def rank_program(g, core, T, topo):
                 r.append(out[2])
         acc = [(span(a), False) for a in r] + [(span(a), True) for a in w]
         ops.append({"kind": kind, "q": q, "e": e or q, "f": f, "a": ([] if out is None else [out]) + list(args), "full": full, "group": group,
-                    "acc": [x for x in acc if x[0] is not None], "dma": kind == "dma", "sem": sem, "val": val, "lag": lag, "after": after})
+                    "acc": [x for x in acc if x[0] is not None], "dma": kind == "dma", "sem": sem, "val": val, "lag": lag, "after": after,
+                    "hops": hops, "other": None})
 
     def dma(q, out, in_, kb):
         loaded[0] += kb
@@ -366,23 +729,23 @@ def rank_program(g, core, T, topo):
         else:
             rec("iota", "g", lambda x, o: x.iota(o, pat, base, cm, allow_small_or_imprecise_dtypes=True), out)
 
-    def send(t, part):
+    def send(t):
         hop, letter = first_hop(rank, t, cores, topo)
-        src = "M%s%d" % (part, t)
+        src = "O%d" % t
         rec("send", "g", lambda x, i: hand(g, T, topo, core, hop, letter + src[1:], src), None, V(src, ALL), e="x" + src)
         sent[0] += ENG
 
-    def arrive(t, part):
-        src = [r for r in range(len(cores)) if target(r, t, cores) == core][0]
-        hops = 1 if first_hop(src, t, cores, topo)[0] == core else 2
-        land = "L%s%d" % (part, t)
-        rec("arrive", None, None, V(land, ALL), e="s" + land, sem="s" + land, val=ENG, after="xM" + land[1:], lag=hops * (HOP + 1.5 if t == 0 else HOP if t < RO - 1 else 1.2))
+    def arrive(t):
+        hops = max(1 if first_hop(r, t, cores, topo)[0] == target(r, t, cores) else 2 for r in range(len(cores)))
+        land = "I%d" % t
+        rec("arrive", None, None, V(land, ALL), e="s" + land, sem="s" + land, val=ENG, after="xO" + land[1:], hops=hops, lag=1.5 * hops * (t == 0))
 
     EQ, MUL, ADD, SUB, MAX, MIN, GT = ALU.is_equal, ALU.mult, ALU.add, ALU.subtract, ALU.max, ALU.min, ALU.is_gt
     SHR, AND = ALU.arith_shift_right, ALU.bitwise_and
     whole = lambda n: V(n, ALL)
-    IW, IS, XW, XS, NUM = col("IC", 0, W), col("IC", 0, W + DUM), col("X", 0, W), col("X", 0, W + 16), col("NUM", 0, W + 16)
-    R1, R8, R16, R48, R49 = sl(0, 1), sl(0, 8), sl(0, 16), sl(0, 48), sl(0, 49)
+    IW, IS = col("IC", 0, W), col("IC", 0, W + DUM)
+    XW, XS, NUM = col("X", OFF, OFF + W), col("X", OFF, OFF + W + 16), col("NUM", OFF, OFF + W + 16)
+    R1, R8, R16, R48 = sl(0, 1), sl(0, 8), sl(0, 16), sl(0, 48)
     pd_ = lambda k, rows=ALL: cf("PD", k, k + 1, rows=rows)
     gcol, rcol = pd_(0), pd_(1)
     Pc, BO, GL, OL, LR8 = cf("P", 0, 1), cb("BO", 96, 104), col("GL", 0, 8), col("OL", 0, 32), col("LR8", 0, 8)
@@ -397,10 +760,12 @@ def rank_program(g, core, T, topo):
     ms(whole("AW"), 0)
     dma("s", whole("GI"), V("gate", ALL), 4)
     dma("a", whole("A"), V("acc0", ALL), 32)
-    dma("s", whole("IT"), V("icol", ALL), 1024)
-    loaded[0] -= 500
-    dma("s", V("AW", sl(0, 128, 4)), V("alt", ALL), 256)
-    dma("s", XW, V("pat", ALL), 512)
+    loads = {"I": (whole("IT"), V("icol", ALL), 1024), "A": (V("AW", sl(0, 128, 4)), V("alt", ALL), 256), "X": (XW, V("pat", ALL), 512),
+             "i": (V("IT", sl(0, 64)), V("icol", sl(0, 64)), 512), "j": (V("IT", sl(64, L)), V("icol", sl(64, L)), 512)}
+    for k in LOADS:
+        if k == "A":
+            loaded[0] -= MOVED
+        dma("s", *loads[k])
     loaded[0] = 0
     for k in range(2):
         dma("a", col("TH", 0, 4, rows=sl(8 * k, 8 * k + 8)), V("th", ALL), 0)
@@ -414,24 +779,25 @@ def rank_program(g, core, T, topo):
     iota(cf("FO"), [[16, 8], [1000, 4], [4, 4]])
     iota(cf("GO"), [[1000, 4]], 0, 1)
     iota(cf("FV"), [[1, 144]], -15)
-    iota(cf("FX", 0, 40), [[16, 8], [-4, 5]], 16)
-    iota(cf("FX", 40, 48), [[16, 8]], 12)
+    iota(cf("FX"), [[16, 8], [-4, 5]], 16)
     iota(cf("FK"), [[1, 8], [-32, 5]], 128)
     iota(cf("J32"), [[0, 4], [1, 32]])
     iota(cb("FG"), [[1, 8], [0, 18], [32, 3]], 32)
-    iota(cf("XCONST", 0, 40), [[0, 8], [-4096, 5]], 20480)
-    iota(cf("UB"), [[-18, 8]], 151)
+    iota(cf("XCONST"), [[0, 8], [-RK, 5]], (5 * SH + 5) * RK)
+    iota(cb("FS"), [[1, 8], [0, 18]])
     iota(cb("F3"), [[8, 8], [0, 2], [1, 8]])
     iota(cb("F8"), [[8, 16], [0, 8]])
     iota(cb("FP"), [[16, 8], [-8, 2], [-1, 9]], 16)
     iota(cf("FW"), [[2, 8], [-1, 2]], 1)
-    iota(cf("FR"), [[-1, 144]], 150)
-    iota(cf("P16"), [[-16, 3]], 0, 1)
-    iota(cf("DUML"), [[16, 8]])
+    iota(cf("FR"), [[0, 8], [-1, 18]], 4 * SH + 23)
+    iota(cf("DUML"), [[16, 3]], W + 1)
+    iota(cf("SPARE"), [[16, 8]], W)
     iota(cb("S48"), [[1, 48]], -256)
-    iota(NUM, [[1, W + 16]])
+    iota(whole("NUM"), [[1, OFF + W + 16]], -OFF)
     for t in range(RO - 1):
-        iota(whole("PT%d" % t), [[0, W + DUM]])
+        for h in range(2):
+            iota(part("PT%d" % t, h, W // 2 + 32), [[0, W // 2 + 32]])
+            iota(part("PN%d" % t, h, W // 2 + 32), [[0, W // 2 + 32]], -1024)
 
     def fill(out, n, c):
         act(out, cb("ONES", 0, n), AF.Identity, scale=float(c))
@@ -440,28 +806,41 @@ def rank_program(g, core, T, topo):
         act(out, in_, AF.Identity, scale=c)
     fill(col("IC", W, W + DUM), DUM, 0)
     fill(col("YC", W, W + DUM), DUM, 0)
-    fill(col("X", W, W + 16), 16, -1024)
+    fill(col("X", OFF + W, OFF + W + 16), 16, -1024)
+    ms(col("X", 0, OFF), 0.0)
+    fill(col("S1", 432, 435), 3, BIG)
     for a in (0, 72):
         for k in range(1, 3):
             fill(col("M3", 3 * a + k, 3 * a + 216, 3), 72, 4 * BIG)
         fill(cf("RST", a, a + 72), 72, 0)
-    fill(cf("RST", 0, 144, 18), 8, 4 * BIG)
-    for k in range(2):
-        fill(cb("NM16", L * k, L * k + L), 128, 1)
+    fill(cf("RST", 0, 145, 18), 9, OFF)
+    fill(cf("RST", 1, 144, 18), 8, 4 * BIG)
+    fill(cf("RS8"), 64, 0)
+    fill(cf("RS8", 0, 64, 8), 8, -BIG)
+    for a in (0, 49, 98):
+        fill(cf("D0", a, a + 49), 49, 4096)
+    fill(cf("D0", 0, 147, 49), 3, -4 * BIG)
+    fill(cf("NE", 48, 147, 49), 3, -BIG)
+    fill(cb("NM16"), 128, 1)
     fill(cb("CW"), 40, CNT)
     fill(cb("CW", 0, 40, 5), 8, 0)
-    fill(cb("NM16", 0, 256, 16), 16, 0)
-    for name, n, c in (("P4096", 16, 4096), ("O16", L, 16), ("C1024", L, -1024), ("TWO", L, 2)):
+    fill(cb("NM16", 0, L, 16), 8, 0)
+    for name, n, c in (("O16", L, 16), ("C1024", L, -1024), ("TWO", L, 2), ("THREE", L, 3)):
         fill(cb(name), n, c)
     fill(cb("BO", 0, 96), 96, 0)
     fill(cb("BO", 104, 224), 120, 0)
     fill(whole("PM3"), 128, 0)
+    if PAV < 8:
+        for u in range(3):
+            fill(V("PA", ALL, u, ALL, ALL), 128, 0)
+            fill(V("PC", ALL, u, ALL, ALL), 128, 0)
     fill(col("GE2", 0, 16), 16, 1)
     fill(col("GE3", 0, 16), 16, 1)
     for k, (s1, s2) in enumerate([(4, 7), (0, 15), (1, 63), (3, 15), (0, 1), (0, 112), (0, 7), (0, 31), (3, 1)]):
         ts(col("PI", 8 + k), col("PI", 0), s1, SHR, s2, AND)
     cp(cf("PD", 0, 9), col("PI", 8, 17))
     cp(LR8, whole("LI"))
+    ts(col("LR8", 8, 16), whole("LI"), 16.0, MUL, 15.0, ADD)
     ts(BO, cb("J", 0, 8), gcol, EQ)
     ts(cb("IDN"), cb("J"), Pc, EQ)
     ts(cb("MK"), cb("F16"), rcol, EQ)
@@ -474,6 +853,7 @@ def rank_program(g, core, T, topo):
     times(cb("W0"), cb("WIDE"), pd_(18))
     ts(pd_(14), pd_(4), -2.0, MUL, 1.0, ADD)
     ts(pd_(15), rcol, 1.0, ADD)
+    ts(pd_(27), rcol, -1.0, MUL)
     ts(pd_(16), Pc, 8.0, EQ, BIG / 2, MUL)
     ts(pd_(17), Pc, 8.0, EQ, BIG, MUL)
     ts(pd_(19), pd_(8), 16.0, MUL, -16.0, ADD)
@@ -487,21 +867,40 @@ def rank_program(g, core, T, topo):
         times(cb("GW", k, 432, 54), cb("ONES", 0, 8), pd_(17))
         fill(cb("GW", 27 + k, 432, 54), 8, 0)
     act(cb("G1W"), cb("G1W"), AF.Identity, bias=pd_(17))
-    for k in range(2):
-        ts(cb("THS", L * k, L * k + L), cb("JG"), pd_(6), EQ)
-    for out, src, c in ((cb("NBO"), BO, -1.0), (cf("BOF"), BO, 1.0), (cb("KID"), cb("IDN"), CNT), (cb("NID"), cb("IDN"), -1.0), (cb("K4"), cb("IDN"), -4096.0),
-                        (cb("RANK"), cf("FR"), 4096.0), (cf("WT"), cb("BLKB"), pd_(15))):
+    ts(cb("THS", 0, L), cb("JG"), pd_(6), EQ)
+    fill(cb("THS", L, 2 * L), L, 0)
+    ts(cf("SELB"), cb("JG"), Pc, EQ)
+    times(cb("BOC"), BO, CNT)
+    ts(pd_(21), rcol, 15.0, EQ)
+    ts(pd_(22), rcol, 15.0, ALU.is_lt)
+    ts(pd_(23), pd_(21), -2.0 - 1 / 512, MUL, 2.0, ADD)
+    ts(pd_(24), pd_(21), -511.0, MUL, 512.0, ADD)
+    ts(pd_(25), Pc, 8.0, EQ, float(RK), MUL)
+    ts(cb("RANK"), cb("FS"), pd_(7), EQ, float(SH * RK), MUL)
+    times(cf("FR"), cf("FR"), pd_(25))
+    tt(cb("RANK"), cb("RANK"), cf("FR"), ADD)
+    ts(pd_(26), Pc, -float(W), ADD)
+    times(cb("NMK"), cb("MK", 0, 16), -1.0)
+    act(cb("NMK1"), cb("MK"), AF.Identity, bias=1.0, scale=-1.0)
+    act(cf("SPARE"), cf("SPARE"), AF.Identity, bias=pd_(27), scale=-1.0)
+    cp(cb("XSUM"), cb("IDN"))
+    times(cb("XSUM", 15, L, 16), BO, pd_(24))
+    times(cf("WS", 0, 8), BO, pd_(23))
+    times(cf("WS", 8, 16), BO, pd_(21))
+    ts(cb("AS", 0, L), cb("BLKB"), pd_(22), MUL, -1.0, MUL)
+    ts(cb("AS", L, 2 * L), cb("BLKB"), pd_(21), MUL, -1.0, MUL)
+    for k in range(8):
+        act(cb("CK", 8 * k, 8 * k + 8), BO, AF.Identity, bias=-4096.0, scale=6144.0)
+    for out, src, c in ((cf("NIF"), cb("IDN"), -1.0), (cf("BOF"), BO, 1.0), (cb("KID"), cb("IDN"), CNT), (cb("NID"), cb("IDN"), -1.0), (cb("K4"), cb("IDN"), -4096.0),
+                        (cf("WT"), cb("BLKB"), pd_(15))):
         times(out, src, c)
-    for k in range(3):
-        times(cb("NBLK3", L * k, L * k + L), cb("BLKB"), -1.0)
-        ts(cb("TRI3", L * k, L * k + L), cb("F16"), cf("P16", k, k + 1), ALU.is_le, 4096.0, MUL)
-    act(cf("XCONST", 0, 40, 5), cf("XCONST", 0, 40, 5), AF.Identity, bias=2048.0)
-    act(cf("XCONST", 40, 48), cf("UB"), AF.Identity, bias=2048.0, scale=4096.0)
+    fill(cf("XCONST", 0, 40, 5), 8, NONE * RK + 4096)
     act(cf("DUML"), cf("DUML"), AF.Identity, bias=rcol)
+    act(cf("CPOS"), cf("DUML"), AF.Identity, bias=-4096.0 * (W + 48), scale=4096.0)
     for k in range(8):
         times(cb("SELG", L * k, L * k + L), cb("ONES"), cf("BOF", k, k + 1))
         ts(cb("FSEL", L * k, L * k + L), cb("F8"), cf("P", k, k + 1), EQ, 2.0, MUL)
-    cp(cb("XSEL", 0, 40, 5), cb("XSEL", 40, 48))
+    cp(cb("XSEL", 0, 40, 5), cb("XSEL", 1, 40, 5))
     ts(cb("SIG"), cb("F3"), pd_(2), EQ, -1.0, MUL)
     ts(cb("DEL"), cb("F3"), pd_(2), EQ)
     times(cb("DEL"), cb("DEL"), pd_(14))
@@ -511,44 +910,78 @@ def rank_program(g, core, T, topo):
     ts(cb("TRI2"), cb("J"), Pc, ALU.is_le, 4096.0, MUL)
     ts(cb("PERM"), cb("FP"), Pc, EQ)
     ts(cb("WM"), cf("FW"), pd_(3), EQ, -BIG, MUL)
-    ms(whole("AMG"), 0.0)
     cp(cf("THF", rows=R8), col("TH", 0, 4, rows=R8))
     mm(col("PQ", 0, 4), cf("SEL8", rows=R8), cf("THF", rows=R8))
+    mm(col("PQ", 4, 8), cf("SELB", rows=R8), cf("THF", rows=R8))
     act(cf("THC"), col("PQ", 0, 4), AF.Identity, bias=-0.5, scale=-1.0)
+    act(cf("THG"), col("PQ", 4, 8), AF.Identity, bias=-0.5, scale=-1.0)
     ts(col("TH", 4, 8), col("TH", 0, 4), 4, SHR)
     ts(col("TH", 8, 12), col("TH", 0, 4), 15, AND)
     ts(cf("THP", 0, 4, rows=R16), col("TH", 4, 8), pd_(19, R16), MUL)
-    ts(cf("THP", 4, 8, rows=R16), col("TH", 8, 12), 0.5, ADD, pd_(20, R16), MUL)
+    ts(cf("THP", 4, 8, rows=R16), col("TH", 8, 12), 0.25, ADD, pd_(20, R16), MUL)
     tt(cf("THP", 8, 12, rows=R16), cf("THP", 0, 4, rows=R16), cf("THP", 4, 8, rows=R16), ADD)
     for t in range(RO):
         times(cb("NTH", L * t, L * t + L, rows=R16), cb("ONES", rows=R16), cf("THP", 8 + t, 9 + t, rows=R16))
 
     def widen():
         for j in range(4):
-            cp(col("A4", j, 512, 4), whole("A"))
+            if "A4" in ONV:
+                cp(col("A4", j, 512, 4), whole("A"))
+            else:
+                act(col("A4", j, 512, 4), whole("A"), AF.Copy)
         for j in range(4):
-            cp(col("AR", j, 1024, 4), col("A4", 0, 256))
+            ts(col("AR", j, 1024, 4), col("A4", 0, 256), pd_(22), MUL)
 
     def gather(out, in_, on_vector):
-        if on_vector:
-            cp(out, in_)
-        else:
-            act(out, in_, AF.Copy)
+        forms = (lambda: cp(out, in_), lambda: act(out, in_, AF.Copy))
+        either(*(forms if on_vector else forms[::-1]))
 
     def options():
         cp(whole("R"), IND(col("AW", 0, W), GL))
         for a in range(4):
             mm(col("PW", 256, 288), cb("SELO", L * a, L * a + L), col("R", a, L, 4), a == 0, a == 3)
         cp(OL, col("PW", 256, 288))
+        for h in range(2):
+            if EQB[h] != "BS":
+                alike(h)
+
+    def alike(h):
+        bank = EQB[h]
+        for k in range(4 * h, 4 * h + 4):
+            mm(part(bank, k % 4), cb("SELG", L * k, L * k + L), whole("CMG"), True, False)
+            mm(part(bank, k % 4), cb("IDN"), cb("TRI2"), False, True)
+        for k in range(4 * h, 4 * h + 4):
+            if bank == "BS":
+                ts(part("EQ2", k), part(bank, k % 4), col("cT", k), EQ, 4096.0, MUL)
+            else:
+                act(part("AB2", k), part(bank, k % 4), AF.Abs, bias=col("cT", k), scale=-1.0)
+        for k in range(2 * h, 2 * h + 2) if bank != "BS" else ():
+            either(lambda: act(part("EQ2", k, 256), part("AB2", k, 256), AF.Relu, bias=4096.0, scale=-4096.0),
+                   lambda: ts(part("EQ2", k, 256), part("AB2", k, 256), 0.0, EQ, 4096.0, MUL))
+
+    def apart(b, bank):
+        for j in range(4):
+            mm(part(bank, j), cb("IDN"), col("G2", 4 * b + j, 2048, 16), True, False)
+            mm(part(bank, j), cb("NID"), whole("XC2"), False, True)
+        act(part("H2", b, 512), whole(bank), AF.Abs)
 
     def farthest(n, s):
         rows, GE, o = sl(0, n), "GE" + s, col("PQ", L, L + n)
         scan(V("PM" + s, rows, ALL), cb("NM16", 0, L, rows=rows), V("PQ", rows, sl(0, L)), 0.0, MUL, MAX)
-        cp(whole("PX"), col("PM" + s, 15, L, 16))
-        tt(col(GE, 16, 144), IND(col("PX", 0, 8), LR8), whole("PM" + s), EQ)
+        if "PX" in ONV:
+            scan(V("PX", rows, ALL), cb("NM16", 0, L, rows=rows), V("PQ", rows, sl(0, L)), 0.0, MUL, MAX)
+            tt(col(GE, 16, 144), IND(whole("PX"), col("LR8", 8, 16)), whole("PM" + s), EQ)
+        else:
+            gather(col("PX", 0, 8), col("PM" + s, 15, L, 16), True)
+            tt(col(GE, 16, 144), IND(col("PX", 0, 8), LR8), whole("PM" + s), EQ)
         mm(o, cb("MK", rows=R1), cb("ONES", 0, n, rows=R1), True, False)
         mm(o, col(GE, 16, 144, rows=rows), cb("IDN", 0, n, rows=rows), False, False)
         mm(o, col(GE, 15, 143, rows=rows), cb("NID", 0, n, rows=rows), False, True)
+        if s == "2" and "DV2" not in ONV:
+            o = part("PQ", 2)
+            mm(o, cb("NMK1", rows=R1), cb("ONES", rows=R1), True, False)
+            mm(o, col(GE, 16, 144), cb("NID"), False, False)
+            mm(o, col(GE, 15, 143), cb("IDN"), False, True)
 
     def patch(n, s, bank, lst):
         mm(col(bank, 0, n), cf("WT"), whole("CF" + s), True, False)
@@ -558,39 +991,49 @@ def rank_program(g, core, T, topo):
 
     def abroad(t):
         more = t < RO - 1
-        la, ld, lb = col("LA%d" % t, 0, 3), col("LB%d" % t, 0, 3), col("LB%d" % t, 4, 7)
-        place = lambda p: part("L%d" % (p // 8), p % 8, 48)
-        arrive(t, "A")
+        la, ld, lb = col("I%d" % t, 0, 3), col("LD", 0, 3), col("I%d" % t, 4, 7)
+        place = lambda p: part("B%d" % (p // 8), p % 8, 48)
+        arrive(t)
         cp(whole("CO3"), IND(IS, la))
-        act(whole("XC3"), IND(XS, la), AF.Copy)
+        gather(whole("XC3"), IND(XS, la), more and "XC3" in ONV)
         for p in range(16):
             mm(place(p), cb("NID"), whole("XC3"), p % 8 == 0, False)
-        if more:
-            act(whole("G3"), IND(XS, whole("CO3")), AF.Copy)
-        else:
-            act(col("G3", 0, 384), IND(XS, col("CO3", 0, 24)), AF.Copy)
-            cp(col("G3", 384, 768), IND(XS, col("CO3", 24, 48)))
+        for h in range(2):
+            gather(part("G3", h, 384), IND(XS, part("CO3", h, 24)), "G3" + "ab"[h] in ONV if more else h)
         for p in range(16):
             mm(place(p), cb("IDN"), col("G3", p, 768, 16), False, p % 8 == 7)
         for b in range(2):
-            act(part("H3", b, 384), col("L%d" % b, 0, 384), AF.Abs)
+            act(part("H3", b, 384), col("B%d" % b, 0, 384), AF.Abs)
             for p in range(8 * b, 8 * b + 8):
                 mm(V("PQ", R48, sl(p, L, 16)), part("H3", p, 48), BO)
-        act(whole("CF3"), IND(IS, la), AF.Copy)
-        arrive(t, "B")
+        gather(whole("CF3"), IND(IS, la), more and "CF3" in ONV)
+        gather(whole("AG"), IND(NUM, la), more and "AG" in ONV)
+        cp(col("AL", 0, 3), la)
+        tt(cf("D0", 48, 147, 49), col("AL", 0, 3), cf("CPOS"), ADD)
+        for u in range(3):
+            ts(cf("NE", 49 * u, 49 * u + 48), whole("AG"), col("AL", u), ALU.not_equal, -BIG, MUL)
+        scan(whole("SD"), cf("D0"), cf("NE"), 0.0, ADD, MAX)
+        tt(col("ZT", 0, 3), col("SD", 48, 147, 49), cf("DUML"), MIN)
+        cp(ld, col("ZT", 0, 3))
+        if more:
+            gather(whole("BG"), IND(XS, lb), "BG" in ONV)
+            cp(IND(whole("PN%d" % t), ld), whole("BG"))
+            tt(whole("DP"), IND(col("PN%d" % t, 0, W), OL), whole("A4"), SUB)
         tt(whole("DV3"), IND(NUM, lb), whole("CF3"), SUB)
         farthest(48, "3")
         if more:
-            act(whole("BG"), IND(NUM, lb), AF.Identity, bias=-2048.0)
-            act(whole("OH"), col("PQ", L, L + 48), AF.Copy)
+            gather(whole("OH"), col("PQ", L, L + 48), "OH" in ONV)
         tt(whole("WV3"), col("PQ", L, L + 48), whole("DV3"), MUL)
         if more:
-            tt(IND(col("PT%d" % t, 0, W + DUM), ld), whole("OH"), whole("BG"), MUL)
-            cp(whole("PG"), IND(col("PT%d" % t, 0, W), OL))
+            cp(IND(whole("PT%d" % t), ld), whole("OH"))
+            gather(whole("PG"), IND(col("PT%d" % t, 0, W), OL), "PG" in ONV)
             tt(IND(IS, ld), whole("WV3"), whole("CF3"), ADD)
         if t >= RO - 2:
             patch(48, "3", "PS", ld)
 
+    for k, bank in enumerate(("B0", "B1", "DL", "PQ")):
+        mm(whole(bank), cb("XSUM"), col("X", OFF + 512 * k, OFF + 512 * k + 512))
+        gather(part("XF", k, 512), whole(bank), k in XFV)
     widen()
     cp(GL, whole("GI"))
     spread("CMG", col("GI", 0, 8))
@@ -603,12 +1046,12 @@ def rank_program(g, core, T, topo):
 
     for t in range(RO):
         last, late = t == RO - 1, t > 0
-        for h in (1, 0):
-            cp(part("COA", h, 256), IND(IW if late else col("IT", 0, W), part("OL", h, 16)))
+        for a, b in COP:
+            cp(col("COA", 16 * a, 16 * b), IND(IW if late else col("IT", 0, W), col("OL", a, b)))
         for k in range(4):
             cp(part("C2", k, NV), col("COA", k, 256, 4))
-        mm(col("DL", 256, 304), whole("R"), cb("XSEL"))
-        tt(whole("XB"), col("DL", 256, 304), cf("XCONST"), ADD)
+        mm(col("PS", 256, 296), whole("R"), cb("XSEL"))
+        tt(whole("XB"), col("PS", 256, 296), cf("XCONST"), ADD)
         act(whole("XC2"), IND(XW, GL), AF.Copy)
         if last:
             for k in range(4):
@@ -616,81 +1059,89 @@ def rank_program(g, core, T, topo):
                 mm(whole(bank), cf("WT"), part("IC", k, 512))
                 gather(part("YC", k, 512), whole(bank), k % 2)
         for q in range(16):
-            mm(col("L1", 64, 72), cb("W0", 15 - q, 143 - q), col("R", q, L, 16), q == 0, q == 15)
-        cp(whole("OL0"), col("L1", 64, 72))
-        act(whole("X0"), IND(XW, col("OL0", 0, 8)), AF.Copy)
+            mm(col("B1", 64, 72), cb("W0", 15 - q, 143 - q), col("R", q, L, 16), q == 0, q == 15)
+        cp(whole("OL0"), col("B1", 64, 72))
+        gather(whole("X0"), IND(XW, col("OL0", 0, 8)), "X0" in ONV)
         mm(part("PS", 1), cb("IDN"), whole("X0"), True, False)
         mm(part("PS", 1), cb("NID"), whole("A"), False, True)
         act(whole("AA"), part("PS", 1), AF.Abs)
-        for bank in ("BV", "BS"):
-            mm(col(bank, 0, 256), cb("NTH", L * t, L * t + L, rows=R16), cb("THS", rows=R16), True, False)
         for l in range(L - NV):
             act(part("H", l, 64), IND(XW, part("COA", NV + l, 4)), AF.Abs, bias=col("A", NV + l), scale=-1.0)
         for k in range(4):
-            tt(part("D", k, 1024), IND(XW, part("C2", k, NV)), whole("AR"), SUB)
+            for h in range(DN):
+                tt(part("D", DN * k + h, 1024 // DN), IND(whole("XF"), part("C2", DN * k + h, NV // DN)), part("AR", h, 1024 // DN), MAX)
+        for c, bank in enumerate(("BV", "DL")):
+            mm(col(bank, 0, 256), cb("NTH", L * t, L * t + L, rows=R16), cb("THS", rows=R16), True, False)
+            for h in range(2):
+                mm(V(bank, sl(64 * h, 64 * h + 64), sl(0, 256)), col("A", 0, NV), cb("AS"), False, False)
+            for p in range(16):
+                mm(col(bank, p, 256, 16), col("D", 2048 * c + p, 2048 * c + 2048, 16), cf("WS"), False, p == 15)
+            ts(part("RR", c), part(bank, 1), ROUND, ADD, ROUND, SUB)
+            tt(part("DD", c), part(bank, 1), part("RR", c), SUB)
+            act(part("AD", c), part("DD", c), AF.Abs)
+            tt(part("SV", c), part(bank, 0), part("AD", c), ADD)
+        mm(part("BS", 0, 64), cb("WIDE", 15, 143), col("H", 0, 1024, 16), True, False)
         if late:
             abroad(t - 1)
-            for q in range(16):
-                mm(col("PW", 256, 288), cb("WIDE", 15 - q, 143 - q), col("PG", q, 512, 16), q == 0, q == 15)
-            for k in range(4):
-                mm(V("BV", sl(64 * (k % 2), 64 * (k % 2) + 64), sl(L * (k // 2), L * (k // 2) + L)), col("PG", k, 256, 4), cb("K4"), False, False)
-            for c in range(2):
-                mm(part("BS", c), part("PG", 2 + c), cb("K4"), False, False)
-            ts(whole("PL"), col("PW", 256, 288), float(W), ADD)
-            tt(whole("DP"), IND(XS, whole("PL")), whole("A4"), SUB)
+            mm(col("BV", 0, 256), cb("KID"), col("PG", 0, 256), True, False)
+            for k in range(3 if CUT else 4):
+                mm(part("BS", k, 64), cb("KID"), part("PG", 4 + k, 64), False, False)
             act(whole("RP"), whole("DP"), AF.Abs)
             for k in range(4):
                 mm(part("PW", 0), cb("BO", 96 - 32 * k, 224 - 32 * k), col("RP", k, 512, 4), k == 0, k == 3)
             act(whole("LE2"), part("PW", 0), AF.Sign, bias=cf("THC", t, t + 1))
-
-        def total(bank, src, sel, c, p, end=False):
-            mm(col(bank, L * c + p, L * c + L, 16), col(src, 2048 * c + p, 2048 * c + 2048, 16), sel, False, end)
-        for c in range(2):
-            for p in range(16):
-                total("BS", "H", BO, c, p, c == 1 and p == 15)
-                total("BV", "D", cb("NBO"), c, p)
-            for j in range(4):
-                ts(col("R2", 2048 * c + j, 2048 * c + 2048, 4), col("D", 2048 * c + j, 2048 * c + 2048, 4), 0.0, MAX, 2.0, MUL)
-                for p in range(j, 16, 4):
-                    total("BV", "R2", BO, c, p, c == 1 and p == 15)
-        cp(whole("C16"), IND(IW, OL))
-        cp(whole("CO2"), IND(IW, GL))
-        act(whole("CF2"), IND(IW, GL), AF.Copy)
+        for k in range(4):
+            mm(col("BV", k, 256, 4), part("SV", k // 2), cb("IDN", 64 * (k % 2), 64 * (k % 2) + 64), k == 0 and not late, k == 3)
+        for j in range(4):
+            if CUT and j == 3:
+                act(col("LE", 256, 448), col("BS", 0, 192), AF.Sign, bias=cf("THG", t, t + 1))
+                if late:
+                    mm(part("BS", j, 64), cb("KID"), part("PG", 4 + j, 64), True, False)
+            for p in range(j == 0, 16):
+                mm(part("BS", j, 64), cb("WIDE", 15 - p, 143 - p), col("H", 1024 * j + p, 1024 * j + 1024, 16),
+                   CUT and j == 3 and p == 0 and not late, j >= (2 if CUT else 3) and p == 15)
+        act(col("LE", 448 if CUT else 256, 512), col("BS", 192 if CUT else 0, 256), AF.Sign, bias=cf("THG", t, t + 1))
+        if EQB[0] == "BS":
+            alike(0)
+        ts(ki(2), ki(4), 1, AND)
+        ts(tf(1), ki(2), -2.0, MUL, 1.0 - W, ADD)
+        tt(col("T16", 8, 16), tf(1), ki(4), ADD)
+        for h in range(CN):
+            cp(part("C16", h, 512 // CN), IND(IW, part("OL", h, 32 // CN)))
+        gather(whole("CF2"), IND(IW, GL), "CF2" in ONV)
+        if "CO2" in ONV:
+            cp(whole("CO2"), IND(IW, GL))
+        else:
+            cp(whole("CO2"), whole("CF2"))
+        for b in range(G2N):
+            gather(part("G2", b, 2048 // G2N), IND(XW, part("CO2", b, L // G2N)), b * 4 // G2N in G2V)
         for k in range(3):
             mm(part("DL", k), cb("DEL"), col("C16", k + 1, 512, 4))
         act(whole("AB"), col("DL", 0, 384), AF.Abs)
-        for h, bank in enumerate(("BV", "BS")):
-            act(part("LE", h, 256), col(bank, 0, 256), AF.Sign)
-            scan(part("SC", h, 256), cb("NM16"), part("LE", h, 256), 0.0, MUL, ADD)
-        for h in range(2):
-            for k in range(4 * h, 4 * h + 4):
-                mm(part("BS", k % 4), cb("SELG", L * k, L * k + L), whole("CMG"), True, False)
-                mm(part("BS", k % 4), cb("IDN"), cb("TRI2"), False, True)
-            for k in range(4 * h, 4 * h + 4):
-                ts(part("EQ2", k), part("BS", k % 4), col("cT", k), EQ, 4096.0, MUL)
-        parts = [(k, sl(0, 64), k // 2, (64 * (k % 2), 64 * (k % 2) + 64)) for k in range(4)]
-        parts += [(k, sl(64 + 32 * c, 96 + 32 * c), 2 + c, (k, L, 4)) for c in range(2) for k in range(4)]
+        act(part("LE", 0, 256), col("BV", 0, 256), AF.Sign)
+        for b, bank in enumerate(EARLY):
+            apart(b, bank)
+        if EQB[1] == "BS":
+            alike(1)
+        more = cb("TWO" if late else "THREE", rows=R1)
+        mm(col("PS", 0, 40), more, cb("CW", rows=R1), True, False)
+        mm(part("PW", 1), cb("ONES", rows=R1), more, True, False)
         if late:
-            mm(col("PS", 0, 40), whole("LE2"), cb("K2"), True, False)
-            mm(part("PW", 0), cb("IDN"), whole("LE2"), True, False)
-        else:
-            mm(col("PS", 0, 40), cb("ONES", rows=R1), cb("CW", rows=R1), True, False)
-            mm(part("PW", 0), cb("ONES", rows=R1), cb("ONES", rows=R1), True, False)
-        for k, to, c, pick in parts:
-            mm(col("PS", 4 - k, 40, 5, rows=to), cb("KID", *pick), col("SC", L * c + 15, L * c + L, 16), False, False)
-        mm(col("PS", 0, 40), cb("TWO", rows=R1), cb("CW", rows=R1), False, True)
-        for k, to, c, pick in parts:
-            mm(V("PW", sl(32 * k, 32 * k + 8), to), col("SC", L * c + 15, L * c + L, 16), cb("IDN", *pick), False, False)
-        mm(part("PW", 0), cb("ONES", rows=R1), cb("TWO", rows=R1), False, True)
+            mm(col("PS", 0, 40), whole("LE2"), cb("K2"), False, False)
+            mm(part("PW", 1), cb("IDN"), whole("LE2"), False, False)
+        for k in range(4):
+            mm(col("PS", 4 - k, 40, 5), col("LE", k, 512, 4), cb("BOC"), False, k == 3)
+        for k in range(4):
+            mm(part("PW", 1), cb("BO", 96 - 32 * k, 224 - 32 * k), col("LE", k, 512, 4), False, k == 3)
         scan(whole("KEY"), col("PS", 0, 40), col("XB", 0, 40), 0.0, MIN, MAX)
         ts(whole("KA"), col("KEY", 4, 40, 5), W - 1, AND)
         spread("KM", col("KA", 0, 8))
-        act(whole("SVG"), part("PW", 0), AF.Sign)
+        act(whole("SVG"), part("PW", 1), AF.Sign)
         mm(col("PS", 64, 72), whole("KM"), BO)
         cp(whole("FL"), col("PS", 64, 72))
         cp(whole("FC"), IND(IW, col("FL", 0, 8)))
         mm(col("PW", 0, 432), whole("SVG"), cb("GW"), True, False)
-        for pp, bank in enumerate(("L0", "L1", "DL", "PQ", "BV", "L0", "L1", "DL")):
+        for pp, bank in enumerate(EEB):
             for k in range(3):
                 mm(part(bank, k), cb("SIG"), col("C16", k + 1, 512, 4), k == 0, False)
             for k in range(3):
@@ -702,68 +1153,81 @@ def rank_program(g, core, T, topo):
                 mm(col("PW", 3 * (8 - pp) + k, 432, 27), V("EE", ALL, pp, sl(L * k, L * k + L)), cb("WM"), False, pp == 7 and k == 2)
         mm(col("PS", 0, 8), whole("SVG"), cb("G1W"))
         mm(col("PS", L, L + 144), whole("FC"), cb("PERM"), True, False)
-        mm(col("PS", L, L + 144), cb("ONES", rows=R1), cb("RANK", rows=R1), False, True)
+        mm(col("PS", L, L + 144), whole("SVG"), cb("RANK"), False, True)
         tt(whole("XC"), col("KEY", 4, 40, 5), col("PS", 0, 8), MAX)
         act(col("M3", 0, 432, 3), col("PS", L, L + 144), AF.Copy)
-        tt(col("M3", 27, 432, 54), whole("XC"), col("XB", 40, 48), MIN)
-        scan(whole("S1"), whole("M3"), col("PW", 0, 432), BIG, MIN, MAX)
-        scan(whole("S2"), cf("RST"), col("S1", 2, 432, 3), 0.0, ADD, MIN)
-        named = col("S2", 17, 144, 18)
-        ts(ki(0), named, 4095, AND)
-        ts(ki(3), named, W - 1, AND)
+        tt(col("M3", 27, 432, 54), whole("XC"), col("XB", 0, 40, 5), MIN)
+        scan(col("S1", 0, 432), whole("M3"), col("PW", 0, 432), BIG, MIN, MAX)
+        scan(whole("S2"), cf("RST"), col("S1", 2, 435, 3), 0.0, ADD, MIN)
+        named = col("S2", 18, 145, 18)
+        ts(whole("LB"), named, float(NONE * RK), ALU.is_lt)
+        ts(ki(0), named, RK - 1, AND)
+        ts(ki(3), named, 4095, AND)
         ts(ki(1), named, 1, AND)
-        ts(ki(2), ki(4), 1, AND)
-        ts(whole("LB"), ki(0), 2048.0, ALU.is_lt)
-        for b in range(4):
-            gather(part("G2", b, 512), IND(XW, part("CO2", b, 32)), b == 3)
-        for b, bank in enumerate(("PQ", "BV", "BS", "L0")):
-            for j in range(4):
-                mm(part(bank, j), cb("IDN"), col("G2", 4 * b + j, 2048, 16), True, False)
-                mm(part(bank, j), cb("NID"), whole("XC2"), False, True)
-            act(part("H2", b, 512), whole(bank), AF.Abs)
+        for b, bank in enumerate(LATER):
+            apart(len(EARLY) + b, bank)
         for p in range(16):
             mm(col("PQ", p, L, 16), part("H2", p), BO)
         farthest(L, "2")
-        act(whole("C5"), whole("cT"), AF.Identity, scale=592.0)
-        mm(col("DL", 0, 8), cb("O16"), whole("LB"))
+        for k in range(8):
+            mm(col("DL", 0), cb("O16"), col("LB", k), k == 0, k == 7)
         mm(col("PS", 0, 8), cb("TRIP"), whole("LB"))
-        rec("sum", "v", lambda x, o, i: x.tensor_reduce(o, i, AX.X, ADD), cf("E16"), col("DL", 0, 8))
-        spread("NM", ki(0))
-        mm(col("PW", 0, 8), whole("NM"), BO)
-        ts(whole("NL"), col("PW", 0, 8), float(W), MIN)
-        act(whole("XN"), IND(XS, col("NL", 0, 8)), AF.Copy)
+        if "NM" in ONV:
+            spread("NM", ki(0))
+        else:
+            cp(col("ZT", 0, 8), ki(0))
+            for k in range(8):
+                times(part("NM", k, 16), cb("MK", 0, 16), col("ZT", k))
+        mm(col("BV", 0, 8), whole("NM"), cf("BOF"))
+        ts(whole("NL"), col("BV", 0, 8), float(OFF + W), MIN)
+        act(whole("XN"), IND(whole("X"), col("NL", 0, 8)), AF.Copy)
         tt(ki(5), ki(3), ki(4), MUL)
-        tt(ki(6), ki(5), whole("C5"), ADD)
-        ts(tf(2, 2), ki(1, 2), -2.0, MUL, -2047.0, ADD)
-        tt(tf(0, 2), tf(2, 2), ki(3, 2), ADD)
-        ts(ki(7), ki(6), cf("E16"), ADD)
+        ts(tf(0), ki(1), -2.0, MUL, 1.0 - W - OFF, ADD)
+        tt(col("T16", 0, 8), tf(0), ki(3), ADD)
+        ts(ki(7), ki(5), col("DL", 0), ADD)
         ts(ki(4), ki(7), 4, SHR, W - 1, AND)
         mm(col("BS", 0, 8), whole("CMG"), BO, True, False)
         mm(col("BS", 0, 8), cb("K4"), whole("LB"), False, False)
         for k in range(8):
             mm(col("BS", k), part("EQ2", k), col("LB", k), False, k == 7)
-        ts(whole("ZZ"), col("BS", 0, 8), float(W), ADD, Pc, MIN)
+        act(whole("ZZ"), col("BS", 0, 8), AF.Relu, bias=pd_(26), scale=-1.0)
         for k in range(8):
-            times(part("ZM", k, 16), cb("MK", 0, 16), col("ZZ", k))
-        mm(col("BS", 16, 24), whole("ZM"), cf("BOF"))
-        ts(whole("SL2"), col("BS", 16, 24), float(W), ADD)
-        tt(whole("DV2"), IND(NUM, col("NL", 0, 8)), whole("CF2"), SUB)
+            times(part("ZM", k, 16), cb("NMK"), col("ZZ", k))
+        mm(col("BS", 16, 24), cf("NIF"), cf("SPARE"), True, False)
+        mm(col("BS", 16, 24), whole("ZM"), cf("BOF"), False, True)
+        cp(whole("SL2"), col("BS", 16, 24))
+        if "DV2" in ONV:
+            tt(whole("DV2"), IND(whole("NUM"), col("NL", 0, 8)), whole("CF2"), SUB)
+        else:
+            act(whole("DV2"), IND(whole("NUM"), col("NL", 0, 8)), AF.Copy)
+            tt(whole("CF2"), part("PQ", 2), whole("CF2"), MUL)
         tt(whole("WV2"), part("PQ", 1), whole("DV2"), MUL)
         tt(IND(IS, col("SL2", 0, 8)), whole("WV2"), whole("CF2"), ADD)
         if not last:
             spread("CMT", ki(4))
             mm(col("PW", 32, 40), whole("CMT"), BO)
-            mm(part("PW", 1), whole("CMT"), cb("IDN"))
+            mm(part("B0", 0), whole("CMT"), cb("IDN"))
             cp(GL, col("PW", 32, 40))
-            cp(whole("CMG"), part("PW", 1))
+            cp(whole("CMG"), part("B0", 0))
             cp(whole("cT"), ki(4))
-        for k in range(8):
-            ts(V("PA", ALL, ALL, k, ALL), cb("S48"), col("PS", k), EQ, col("TF", k), MUL)
-        for u in range(3):
-            mm(col("L1", u, 1 + u + u // 2), V("PA", ALL, u, ALL, ALL), cb("ONES", 0, 1 + u // 2))
-        ts(whole("MA%d" % t), col("L1", 0, 4), float(W), ADD)
-        send(t, "A")
-        cp(col("AL", 0, 4), col("L1", 0, 4))
+        if PAV < 8:
+            act(whole("PF"), col("PS", 0, 8), AF.Copy)
+        for k in range(PAV):
+            ts(V("PA", ALL, ALL, k, ALL), cb("S48"), col("PS" if PAV == 8 else "PF", k), EQ)
+        for k in range(PAV, 8):
+            act(V("PB", ALL, ALL, k, ALL), cb("S48"), AF.Abs, bias=col("PF", k), scale=-1.0)
+        if PAV < 8:
+            act(V("PC", ALL, ALL, sl(PAV, 8), ALL), V("PB", ALL, ALL, sl(PAV, 8), ALL), AF.Relu, bias=1.0, scale=-1.0)
+        mm(col("B1", 0, 64), cb("IDN"), cb("CK"), True, False)
+        for h in range(2):
+            for u in range(3):
+                o, end = sl(32 * h + 8 * u, 32 * h + 8 * u + 8), h == 1 and u == 2
+                if PAV < 8:
+                    mm(V("B1", ALL, o), V("PC", ALL, u, ALL, ALL), part("T16", h, 8), False, False)
+                mm(V("B1", ALL, o), V("PA", ALL, u, ALL, ALL), part("T16", h, 8), False, end)
+        scan(whole("SK"), cf("RS8"), col("B1", 0, 64), 0.0, ADD, MAX)
+        cp(whole("O%d" % t), col("SK", 7, 64, 8))
+        send(t)
         if not last:
             options()
         mm(part("DL", 0), cb("IDN"), whole("XN"), True, False)
@@ -777,23 +1241,6 @@ def rank_program(g, core, T, topo):
             dma("s", V("ya", ALL), whole("AO"), 0)
         else:
             widen()
-        for k in range(8):
-            ts(V("PB", ALL, ALL, k, ALL), cb("S48"), col("PS", k), EQ, col("TF", 8 + k), MUL)
-        tt(col("AMG", 0, 48), IND(col("AL", 0, 4), col("LR8", 0, 3)), cb("MK", 0, 48), MUL)
-        mm(V("L0", R49, sl(0, 384)), cb("ONES", 0, 49), whole("PA"), True, False)
-        mm(V("L0", R49, sl(0, 384)), cb("IDN", 0, 49, rows=R48), cb("TRI3", rows=R48), False, False)
-        mm(V("L0", R49, sl(0, 384)), col("AMG", 0, 49), cb("NBLK3"), False, True)
-        ts(V("EQ3", R49, ALL), V("L0", R49, sl(0, 384)), 0.0, EQ)
-        for u in range(3):
-            mm(col("L1", 20 + u, 21 + u + u // 2), V("PB", ALL, u, ALL, ALL), cb("ONES", 0, 1 + u // 2))
-        for u in range(3):
-            o = col("L1", 16 + u, 17 + u + u // 2)
-            mm(o, V("PA", ALL, u, ALL, ALL), cb("ONES", 0, 1 + u // 2), True, False)
-            mm(o, V("EQ3", R49, sl(L * u, L * u + L)), cb("P4096", 0, 1 + u // 2, rows=R49), False, True)
-        tt(col("ZT", 0, 4), col("L1", 16, 20), cf("DUML", 0, 4), MIN)
-        ts(col("MB%d" % t, 4, 8), col("L1", 20, 24), float(W), ADD)
-        ts(col("MB%d" % t, 0, 4), col("ZT", 0, 4), float(W), ADD)
-        send(t, "B")
     cp(whole("G16"), ki(4))
     mm(V("BS", R8, sl(256, 384)), whole("G16"), cb("IDN"))
     cp(whole("YG"), V("BS", R8, sl(256, 384)))

@@ -9,27 +9,36 @@ CNT = 2097152.0
 RK, SH = 8192, 32
 NONE = 5 * SH + 24
 OFF = 592
-ROUND = 1.5 * 2 ** 32
+FINE = 16384.0
+ROUND = 1.5 * 2 ** 37
+FAR = 8192.0
+PEN = 4096.0
 H16 = "float16"
 NV = 64
 ENG = 8
 FILES = ("H", "D")
-XFV, G2V = (0, 1), (2, 3)
-ONV = ("XC3", "G3a", "CF3", "AG", "BG", "PX3", "PG", "A4", "NM", "PX")
+XFV, G2V = (0, 1), ()
+ONV = ("NM", "G3a", "DV2", "cT")
 LOADS = "XAI"
-DN, G2N = 2, 8
-EEB, EARLY, LATER = ("B0", "B1", "DL", "PQ", "BV", "B0", "B1", "DL"), (), ("PQ", "BV", "BS", "B0")
+G2N = 32
+EEB, EARLY, LATER = (("B0", "B1", "PQ", "DL"), ("B0", "B1", "PQ", "DL")), (), ("PQ", "BV", "BS", "B0")
 PAV, CN = 8, 1
-EQB = ("BS", "BS")
-CUT = False
+EQB, EQV, EQAT = ("BV", "BS"), (2, 2), (3, 3)
+YCB, YCN = ("BV", "DL", "PW", "BS"), 8
+WIDEN, LASTC, FCB = ((0, 32, "vv"), (32, 128, "gg")), False, ("BV", "BS")
+PARTS = ((0, 64), (64, 128))
+N2V, NB2, H2N, FAT, F2B = 128, 0, 32, 3, "PQ"
+F3B = ("PQ", 0, "PQ", L)
+CWS, STEEP, MAX2 = None, 64.0, False
+PAS = False
 MOVED = 500
 COP = ((16, 20), (0, 16), (20, 32))
 CYCLE, TENSOR = 0.00083, 0.00042
 PACES = ((1.0, 1.56, 3.0, 0.19, 1.3), (1.3, 1.2, 3.0, 0.15, 1.0), (1.15, 1.9, 4.0, 0.25, 2.2))
-PASSES, SHAKE = 30, 0.5
+PASSES, SHAKE = 6, 0.5
 UNIT = 0.5
 SLACK, STARTS, ANEW = 0.0003, 1, 5
-PIECE, MOVES, SWEEPS = 160, 500, 7
+PIECE, MOVES, SWEEPS = 160, 500, 10
 
 
 def _pack(items):
@@ -40,46 +49,44 @@ def _pack(items):
     return at, n
 
 
-CB, NCB = _pack([("ONES", 128), ("IDN", 128), ("NID", 128), ("MK", 128), ("NMK", 16), ("NMK1", 128), ("BO", 224), ("AS", 256), ("XSUM", 128), ("CK", 64), ("K2", 40), ("CW", 40), ("TWO", 128), ("THREE", 128),
-                 ("WIDE", 144), ("W0", 144), ("KID", 128), ("THS", 256), ("BOC", 8), ("NTH", 512), ("FG", 432), ("NM16", 128), ("GW", 432), ("G1W", 8), ("WM", 16),
-                 ("RANK", 144), ("FS", 144), ("TRIP", 128), ("TRI2", 128), ("S48", 48), ("J", 128), ("F16", 128), ("JG", 128),
-                 ("F3", 128), ("F8", 128), ("FP", 144), ("BLKB", 128), ("K4", 128), ("O16", 128), ("C1024", 128),
-                 ("SELO", 512), ("SIG", 128), ("DEL", 128), ("FSEL", 1024), ("PERM", 144), ("XSEL", 40), ("SELG", 1024)])
-CF, NCF = _pack([("P", 8), ("PD", 32), ("FO", 128), ("GO", 4), ("FW", 16), ("FX", 40), ("FK", 40), ("FV", 144), ("XCONST", 40), ("FR", 144),
+CB, NCB = _pack([("ONES", 128), ("IDN", 128), ("NID", 128), ("MK", 128), ("NMK", 16), ("NMK1", 128), ("BO", 224), ("AS", 256), ("XSUM", 128), ("CK", 64), ("K2", 48), ("THREE", 128), ("PEN", 512), ("RS4", 512), ("S32", 128), ("PRM", 128), ("MAG", 16), ("BOS", 8),
+                 ("WIDE", 144), ("W0", 144), ("KID", 128), ("NKID", 128), ("BO4", 224), ("NBO4", 224), ("THS", 256), ("NTH", 512), ("FG", 432), ("NM16", 128), ("GW", 432), ("FS", 144), ("G5", 48), ("WM", 16),
+                 ("RANK", 144), ("TRIP", 128), ("TRI2", 128), ("S96", 96), ("J", 128), ("F16", 128), ("JG", 128),
+                 ("F3", 128), ("F8", 128), ("BLKB", 128), ("K4", 128), ("O16", 128), ("C1024", 128),
+                 ("SELO", 512), ("SIG", 128), ("DEL", 128), ("FSEL", 1024), ("PERM", 144), ("XSEL", 48), ("SELG", 1024), ("ZERO", 128)])
+CF, NCF = _pack([("P", 8), ("PD", 32), ("PK", 20), ("FV", 144), ("XCONST", 48), ("FR", 144),
                  ("WS", 16), ("NIF", 128), ("RS8", 64), ("D0", 147), ("NE", 147), ("CPOS", 3),
-                 ("DUML", 3), ("SPARE", 8), ("WT", 128), ("SEL8", 128), ("THF", 4), ("THC", 4), ("THG", 4), ("SELB", 128), ("THP", 12), ("BOF", 8), ("J32", 128), ("RST", 145)])
+                 ("DUML", 3), ("SPARE", 8), ("WT", 128), ("SEL8", 128), ("THF", 4), ("THC", 4), ("THG", 4), ("SELB", 128), ("THP", 12), ("BOF", 8), ("J32", 128), ("RST", 144)])
 S, F, B, I32, U = "sbuf", "float32", "bfloat16", "int32", "uint16"
 SCRATCH = {
     "CB": (S, [128, NCB], B), "CF": (S, [128, NCF], F), "LR8": (S, [128, 16], U), "LI": (S, [128, 8], I32),
     "PI": (S, [128, 32], I32), "TH": (S, [16, 12], I32), "GI": (S, [128, 8], I32),
-    "IT": (S, [128, W], I32), "IC": (S, [128, W + DUM], F), "AW": (S, [128, W], I32), "X": (S, [128, OFF + W + 16], B), "XF": (S, [128, W], F),
-    "YC": (S, [128, W + DUM], F), "NUM": (S, [128, OFF + W + 16], F),
+    "IT": (S, [128, W + 64], I32), "IC": (S, [128, W + DUM], F), "AW": (S, [128, W], I32), "X": (S, [128, OFF + W + 16], B), "XF": (S, [128, W], F),
+    "XT": (S, [128, W + 16], B), "NT": (S, [128, W + 16], F), "YC": (S, [128, W + DUM], F), "NUM": (S, [128, OFF + W + 16], F),
     "A": (S, [128, L], B), "A4": (S, [128, 512], B), "GL": (S, [128, 8], U), "OL": (S, [128, 32], U), "R": (S, [128, L], H16),
     "cT": (S, [128, 8], F), "CMG": (S, [128, L], H16), "CMT": (S, [128, L], H16),
-    "COA": (S, [128, 512], U), "C16": (S, [128, 512], H16),
-    "H": (S, [128, 4096], B), "D": (S, [128, 4096], F), "RR": (S, [128, 256], F), "AD": (S, [128, 256], B), "DD": (S, [128, 256], B), "SV": (S, [128, 256], B), "AR": (S, [128, 1024], B), "C2": (S, [128, 256], U),
-    "LE": (S, [128, 512], B), "LE2": (S, [128, L], B),
-    "PG": (S, [128, 512], B), "DP": (S, [128, 512], B), "RP": (S, [128, 512], B),
-    "XB": (S, [128, 40], F), "KEY": (S, [128, 40], I32), "KA": (S, [128, 8], I32), "KM": (S, [128, L], H16), "FL": (S, [128, 8], U), "FC": (S, [128, L], H16),
-    "SVG": (S, [128, L], B), "XC": (S, [128, 8], F), "AB": (S, [128, 384], F), "EE": (S, [128, 8, 384], B),
-    "S1": (S, [128, 435], F), "S2": (S, [128, 145], I32), "M3": (S, [128, 432], F), "KI": (S, [128, 64], I32), "TF": (S, [128, 16], F), "LB": (S, [128, 8], B),
-    "PA": (S, [128, 3, 8, 16], B), "PB": (S, [128, 3, 8, 16], B), "PC": (S, [128, 3, 8, 16], B), "PF": (S, [128, 8], F), "T16": (S, [128, 16], H16), "SK": (S, [128, 64], F), "EQ2": (S, [128, 1024], B), "AB2": (S, [128, 1024], B),
+    "COA": (S, [128, 512], U), "C16": (S, [128, 512], H16), "C0": (S, [128, 512], H16),
+    "H": (S, [128, 4096], B), "D": (S, [128, 4096], F), "RR": (S, [128, 256], F), "AD": (S, [128, 256], B), "SV": (S, [128, 256], B), "AR": (S, [128, 1024], B), "C2": (S, [128, 256], U),
+    "LE": (S, [128, 512], B), "LE2": (S, [128, 2 * L], B),
+    "DP": (S, [128, 512], B), "RP": (S, [128, 512], B),
+    "FC": (S, [128, 512], H16),
+    "SVG": (S, [128, L], B), "XC": (S, [128, 8], F), "AB": (S, [128, 384], F), "EE": (S, [128, 8, 3, L], B),
+    "S1": (S, [128, 432], F), "S2": (S, [128, 144], I32), "M3": (S, [128, 432], F), "KI": (S, [128, 64], I32), "TF": (S, [128, 16], F), "LB": (S, [128, 16], B),
+    "PA": (S, [128, 3, 8, 16], B), "PB": (S, [128, 6, 8, 16], B), "PF": (S, [128, 8], F), "T16": (S, [128, 32], H16), "SK": (S, [128, 64], F), "EQ2": (S, [128, 1024], B), "AB2": (S, [128, 1024], B),
     "AL": (S, [128, 4], F), "AG": (S, [128, 48], F), "SD": (S, [128, 147], F), "LD": (S, [128, 4], U),
     "ZT": (S, [128, 8], F), "ZZ": (S, [128, 8], F), "ZM": (S, [128, L], F), "SL2": (S, [128, 8], U),
     "NM": (S, [128, L], F), "NL": (S, [128, 8], U), "X0": (S, [128, L], B), "OL0": (S, [128, 8], U), "AA": (S, [128, L], B),
     "XN": (S, [128, L], B), "AH": (S, [128, L], I32), "AO": (S, [128, L], F),
     "CO2": (S, [128, L], U), "CF2": (S, [128, L], F), "XC2": (S, [128, L], B),
-    "G2": (S, [128, 2048], B), "H2": (S, [128, 2048], B),
-    "PM2": (S, [128, L], F), "GE2": (S, [128, 144], B), "DV2": (S, [128, L], F), "WV2": (S, [128, L], F), "YP2": (S, [128, L], F),
+    "D2": (S, [128, 2048], F), "RR2": (S, [128, L], F), "SV2": (S, [128, L], F), "AD2": (S, [128, L], B), "CW": (S, [128, 512], F), "X4": (S, [128, 512], B), "XR": (S, [128, 2048], B), "G2": (S, [128, 2048], B), "H2": (S, [128, L, 16], B),
+    "PM2": (S, [128, L], F), "GE2": (S, [128, 144], B), "DV2": (S, [128, L], F), "WV2": (S, [128, L], F),
     "CO3": (S, [128, 48], U), "CF3": (S, [128, 48], F), "XC3": (S, [128, 48], B), "G3": (S, [128, 768], B), "H3": (S, [128, 768], B),
     "PM3": (S, [128, L], F), "GE3": (S, [128, 144], B), "DV3": (S, [128, 48], F), "WV3": (S, [128, 48], F), "YP3": (S, [128, 48], F),
-    "BG": (S, [128, 48], B), "OH": (S, [128, 48], B), "PX": (S, [128, L], F), "G16": (S, [128, 8], H16), "YG": (S, [8, L], F),
+    "BG": (S, [128, 48], B), "PX": (S, [128, L], F), "G16": (S, [128, 8], H16), "YG": (S, [8, L], F),
 }
 for _t in range(RO):
     for _n in "OI":
         SCRATCH["%s%d" % (_n, _t)] = (S, [128, 8], U)
-for _t in range(RO - 1):
-    SCRATCH["PT%d" % _t] = SCRATCH["PN%d" % _t] = (S, [128, W + 64], B)
 for _n in ("BV", "BS", "PS", "B0", "B1", "DL", "PW", "PQ"):
     SCRATCH[_n] = ("psum", [128, 512], F)
 SEMAPHORES = ["cv", "ca", "cp", "cg", "snt"] + ["d%d" % k for k in range(16)] + ["s%s%d" % (n, t) for n in "IO" for t in range(RO)]
@@ -177,7 +184,7 @@ def needs(ops, banks):
             psum = SCRATCH[name][0] == "psum"
             for (j, m2, lo2, hi2, w2) in hist.get((name, True), []) + (hist.get((name, False), []) if w or psum else []):
                 same = ops[j]["e"] == e
-                if same and e == "p":
+                if same and e == "p" or o["dma"] and ops[j]["dma"] and o["a"][0][2][0] != ops[j]["a"][0][2][0]:
                     continue
                 if (psum and not same) or ((w or w2) and ((m & m2) if same else (lo <= hi2 and lo2 <= hi))):
                     deps.add(j)
@@ -198,16 +205,16 @@ def needs(ops, banks):
 def cost(o, kind, pace):
     a, (slow, gather, scatter) = [x for x in o["a"] if isinstance(x, tuple)], pace[:3]
     size = lambda x: span(x)[4]
-    if kind in ("dma", "send", "arrive"):
-        return {"dma": 0.06, "send": 0.6, "arrive": 0.0}[kind]
+    if kind in ("dma", "send", "arrive", "table"):
+        return {"dma": 0.06, "send": 0.6, "arrive": 0.0, "table": 1.4 * slow}[kind]
     ind = [x for x in a if x[0] == "ind"]
     if ind:
         return slow * ((0.065 if kind == "act" else 0.05) + 16 * size(ind[0][2]) * CYCLE * (scatter if ind[0] is a[0] else gather))
     n, wide = size(a[0]), [SCRATCH[x[1]][2] in (F, I32) for x in a if size(x) > 1 or x is a[0]]
     if kind == "mm":
         return slow * max(min(64, size(a[1])), n) * TENSOR * (4 if wide[1] else 1) + sum(cost(x, kind, pace) for x in o.get("also", ()))
-    if kind == "iota":
-        return slow * (0.13 + 2 * n * CYCLE)
+    if kind in ("iota", "sel"):
+        return slow * ((0.13 if kind == "iota" else 0.17) + 2 * n * CYCLE)
     if kind == "tt":
         n *= 1 if "psum" in (SCRATCH[a[1][1]][0], SCRATCH[a[2][1]][0]) else 2
     elif kind != "act" and not any(wide):
@@ -556,7 +563,7 @@ def lay_units(ops, deps):
     N = len(ops)
     last, free_ = {}, set()
     for n, o in enumerate(ops):
-        file = "iota" if o["kind"] == "iota" else o["q"] if o["kind"] in ("dma", "send") else o["a"][0][1] if o["a"][0][1] in FILES else None
+        file = o["file"] if o.get("file") else "iota" if o["kind"] == "iota" else o["q"] if o["kind"] in ("dma", "send") else o["a"][0][1] if o["a"][0][1] in FILES else None
         if file in last and last[file] not in deps[n]:
             deps[n].add(last[file])
             free_.add((last[file], n))
@@ -720,14 +727,17 @@ def rank_program(g, core, T, topo):
     def act(out, in_, func, bias=0.0, scale=1.0):
         rec("act", "a", lambda x, o, i, b, s: x.activation(o, i, func, bias=b, scale=s), out, in_, bias, scale)
 
-    def mm(out, l, r, start=True, stop=True):
-        rec("mm", "p", lambda x, o, i, j: x.matmul(o, i, j, start, stop), out, l, r, group=(start, stop))
+    def mm(out, l, r, start=True, stop=True, bar=False):
+        rec("mm", "p", lambda x, o, i, j: x.matmul(o, i, j, start, stop), out, l, r, group=(start, stop or bar))
 
     def iota(out, pat, base=0, cm=0):
         if SCRATCH[out[1]][2] == I32:
             rec("iota", "g", lambda x, o: x.iota(o, pat, base, cm), out)
         else:
             rec("iota", "g", lambda x, o: x.iota(o, pat, base, cm, allow_small_or_imprecise_dtypes=True), out)
+
+    def copy(out, in_, n):
+        rec("sel", "g", lambda x, o, i: x.affine_select(o, i, [[0, n]], ALU.is_ge, 0.0, 0, 0), out, in_)
 
     def send(t):
         hop, letter = first_hop(rank, t, cores, topo)
@@ -758,10 +768,10 @@ def rank_program(g, core, T, topo):
 
     ms(cb("ONES"), 1.0)
     ms(whole("AW"), 0)
+    ops[0]["file"] = ops[1]["file"] = "fills"
     dma("s", whole("GI"), V("gate", ALL), 4)
     dma("a", whole("A"), V("acc0", ALL), 32)
-    loads = {"I": (whole("IT"), V("icol", ALL), 1024), "A": (V("AW", sl(0, 128, 4)), V("alt", ALL), 256), "X": (XW, V("pat", ALL), 512),
-             "i": (V("IT", sl(0, 64)), V("icol", sl(0, 64)), 512), "j": (V("IT", sl(64, L)), V("icol", sl(64, L)), 512)}
+    loads = {"I": (col("IT", 0, W), V("icol", ALL), 1024), "A": (V("AW", sl(0, 128, 4)), V("alt", ALL), 256), "X": (XW, V("pat", ALL), 512)}
     for k in LOADS:
         if k == "A":
             loaded[0] -= MOVED
@@ -776,45 +786,57 @@ def rank_program(g, core, T, topo):
     iota(cb("F16"), [[0, 8], [1, 16]])
     iota(cb("JG"), [[1, 8], [0, 16]])
     iota(whole("LI"), [[1, 8]])
-    iota(cf("FO"), [[16, 8], [1000, 4], [4, 4]])
-    iota(cf("GO"), [[1000, 4]], 0, 1)
-    iota(cf("FV"), [[1, 144]], -15)
-    iota(cf("FX"), [[16, 8], [-4, 5]], 16)
-    iota(cf("FK"), [[1, 8], [-32, 5]], 128)
-    iota(cf("J32"), [[0, 4], [1, 32]])
-    iota(cb("FG"), [[1, 8], [0, 18], [32, 3]], 32)
-    iota(cf("XCONST"), [[0, 8], [-RK, 5]], (5 * SH + 5) * RK)
-    iota(cb("FS"), [[1, 8], [0, 18]])
-    iota(cb("F3"), [[8, 8], [0, 2], [1, 8]])
-    iota(cb("F8"), [[8, 16], [0, 8]])
-    iota(cb("FP"), [[16, 8], [-8, 2], [-1, 9]], 16)
-    iota(cf("FW"), [[2, 8], [-1, 2]], 1)
-    iota(cf("FR"), [[0, 8], [-1, 18]], 4 * SH + 23)
-    iota(cf("DUML"), [[16, 3]], W + 1)
-    iota(cf("SPARE"), [[16, 8]], W)
-    iota(cb("S48"), [[1, 48]], -256)
-    iota(whole("NUM"), [[1, OFF + W + 16]], -OFF)
-    for t in range(RO - 1):
-        for h in range(2):
-            iota(part("PT%d" % t, h, W // 2 + 32), [[0, W // 2 + 32]])
-            iota(part("PN%d" % t, h, W // 2 + 32), [[0, W // 2 + 32]], -1024)
 
     def fill(out, n, c):
         act(out, cb("ONES", 0, n), AF.Identity, scale=float(c))
 
     def times(out, in_, c):
         act(out, in_, AF.Identity, scale=c)
+
+    def where(out, pat, base=0, c=1.0, in_=None, op=ALU.not_equal, cm=-1):
+        in_ = in_ or (col("PM3", 0, span(out)[4]) if SCRATCH[out[1]][2] == F else cb("ZERO", 0, span(out)[4]))
+        rec("sel", "g", lambda x, o, i: x.affine_select(o, i, pat, op, c, base, cm), out, in_)
+        ops[-1]["file"] = "iota"
+    fill(cb("ZERO"), L, 0)
+    fill(whole("PM3"), L, 0)
+    iota(cf("FV"), [[1, 144]], -15)
+    for a in range(4):
+        where(cb("SELO", L * a, L * a + L), [[16, 8], [1000, 4], [4, 4]], -1000 * a)
+    where(cf("SEL8"), [[0, 4], [1, 32]])
+    where(cf("SELB"), [[1, 8], [0, 16]])
+    iota(cb("F3"), [[8, 8], [0, 2], [1, 8]])
+    iota(cb("F8"), [[8, 16], [0, 8]])
+    iota(cf("PK", 0, 4), [[32, 4]])
+    where(cb("PRM"), [[1, 32], [32, 4]])
+    iota(cb("RS4"), [[0, L], [-32768, 4]], 32768)
+    iota(cb("FG"), [[1, 8], [0, 18], [32, 3]], 32)
+    iota(cb("FS"), [[1, 8], [0, 18]])
+    iota(cf("FR"), [[0, 8], [8, 2], [1, 9]], 4 * SH + 6)
+    for h in range(2):
+        where(cb("PERM", 72 * h, 72 * h + 72), [[16, 4], [8, 2], [1, 9]], 64 * h - 1)
+    where(cb("XSEL"), [[16, 8], [-4, 6]], 20)
+    where(cb("K2"), [[1, 8], [-32, 6]], 160, CNT)
+    iota(cf("XCONST"), [[0, 8], [-1, 6]], 5 * SH + 6)
+    iota(cb("G5"), [[1, 8], [0, 6]])
+    where(cb("TRI2"), [[1, L]], 0, 4096.0, op=GT)
+    for k in range(8):
+        ts(cb("FSEL", L * k, L * k + L), cb("F8"), cf("P", k, k + 1), EQ, 2.0, MUL)
+    where(cb("TRIP"), [[1, L]], 0, 0.0, cb("ONES"), GT)
+    where(cb("TRIP"), [[1, L]], 0, -float(L), cb("TRIP"))
+    iota(cf("DUML"), [[16, 3]], W + 1)
+    iota(cf("SPARE"), [[16, 8]], W)
+    iota(cb("S96"), [[-1, 2], [1, 48]], -L)
+    iota(cf("RST"), [[0, 144]])
+    ms(col("X", 0, OFF), 0.0)
+    iota(whole("NUM"), [[1, OFF + W + 16]], -OFF)
+    ms(col("IT", W, W + 64), 0)
+    iota(whole("NT"), [[2, W // 2 + 8], [-1, 2]], 1)
     fill(col("IC", W, W + DUM), DUM, 0)
     fill(col("YC", W, W + DUM), DUM, 0)
     fill(col("X", OFF + W, OFF + W + 16), 16, -1024)
-    ms(col("X", 0, OFF), 0.0)
-    fill(col("S1", 432, 435), 3, BIG)
-    for a in (0, 72):
-        for k in range(1, 3):
-            fill(col("M3", 3 * a + k, 3 * a + 216, 3), 72, 4 * BIG)
-        fill(cf("RST", a, a + 72), 72, 0)
-    fill(cf("RST", 0, 145, 18), 9, OFF)
-    fill(cf("RST", 1, 144, 18), 8, 4 * BIG)
+    fill(cf("RST", 0, 144, 18), 8, 4 * BIG)
+    for h in range(4):
+        fill(col("M3", 216 * (h // 2) + 1 + h % 2, 216 * (h // 2 + 1), 3), 72, 4 * BIG)
     fill(cf("RS8"), 64, 0)
     fill(cf("RS8", 0, 64, 8), 8, -BIG)
     for a in (0, 49, 98):
@@ -822,19 +844,18 @@ def rank_program(g, core, T, topo):
     fill(cf("D0", 0, 147, 49), 3, -4 * BIG)
     fill(cf("NE", 48, 147, 49), 3, -BIG)
     fill(cb("NM16"), 128, 1)
-    fill(cb("CW"), 40, CNT)
-    fill(cb("CW", 0, 40, 5), 8, 0)
     fill(cb("NM16", 0, L, 16), 8, 0)
-    for name, n, c in (("O16", L, 16), ("C1024", L, -1024), ("TWO", L, 2), ("THREE", L, 3)):
+    for name, n, c in (("O16", L, 16), ("C1024", L, -1024), ("THREE", L, 3)):
         fill(cb(name), n, c)
+    fill(cb("MAG", 0, 8), 8, 3 * BIG)
+    fill(cb("MAG", 8, 16), 8, -3 * BIG)
     fill(cb("BO", 0, 96), 96, 0)
     fill(cb("BO", 104, 224), 120, 0)
-    fill(whole("PM3"), 128, 0)
-    if PAV < 8:
-        for u in range(3):
-            fill(V("PA", ALL, u, ALL, ALL), 128, 0)
-            fill(V("PC", ALL, u, ALL, ALL), 128, 0)
-    fill(col("GE2", 0, 16), 16, 1)
+    if EQV[0] == 2:
+        act(col("GE2", 0, 16), cb("ONES", 0, 16), AF.Sigmoid, scale=STEEP)
+        ops[-1].update(kind="table", file="H")
+    else:
+        fill(col("GE2", 0, 16), 16, 1)
     fill(col("GE3", 0, 16), 16, 1)
     for k, (s1, s2) in enumerate([(4, 7), (0, 15), (1, 63), (3, 15), (0, 1), (0, 112), (0, 7), (0, 31), (3, 1)]):
         ts(col("PI", 8 + k), col("PI", 0), s1, SHR, s2, AND)
@@ -845,9 +866,6 @@ def rank_program(g, core, T, topo):
     ts(cb("IDN"), cb("J"), Pc, EQ)
     ts(cb("MK"), cb("F16"), rcol, EQ)
     ts(cb("BLKB"), cb("JG"), gcol, EQ)
-    ts(cf("SEL8"), cf("J32"), Pc, EQ)
-    for a in range(4):
-        ts(cb("SELO", L * a, L * a + L), cf("FO"), cf("GO", a, a + 1), EQ)
     ts(cb("WIDE"), cf("FV"), pd_(5), EQ)
     ts(pd_(18), rcol, 0.0, EQ)
     times(cb("W0"), cb("WIDE"), pd_(18))
@@ -855,30 +873,40 @@ def rank_program(g, core, T, topo):
     ts(pd_(15), rcol, 1.0, ADD)
     ts(pd_(27), rcol, -1.0, MUL)
     ts(pd_(16), Pc, 8.0, EQ, BIG / 2, MUL)
-    ts(pd_(17), Pc, 8.0, EQ, BIG, MUL)
     ts(pd_(19), pd_(8), 16.0, MUL, -16.0, ADD)
     ts(pd_(20), pd_(8), -1.0, MUL)
     ts(cb("GW"), cb("FG"), Pc, EQ, -BIG / 2, MUL)
-    ts(cb("G1W"), cb("J", 0, 8), pd_(7), EQ, -BIG, MUL)
-    ts(cb("XSEL"), cf("FX"), Pc, EQ)
-    ts(cb("K2"), cf("FK"), Pc, EQ, CNT, MUL)
     act(cb("GW"), cb("GW"), AF.Identity, bias=pd_(16))
-    for k in range(3):
-        times(cb("GW", k, 432, 54), cb("ONES", 0, 8), pd_(17))
-        fill(cb("GW", 27 + k, 432, 54), 8, 0)
-    act(cb("G1W"), cb("G1W"), AF.Identity, bias=pd_(17))
     ts(cb("THS", 0, L), cb("JG"), pd_(6), EQ)
     fill(cb("THS", L, 2 * L), L, 0)
-    ts(cf("SELB"), cb("JG"), Pc, EQ)
-    times(cb("BOC"), BO, CNT)
-    ts(pd_(21), rcol, 15.0, EQ)
-    ts(pd_(22), rcol, 15.0, ALU.is_lt)
-    ts(pd_(23), pd_(21), -2.0 - 1 / 512, MUL, 2.0, ADD)
-    ts(pd_(24), pd_(21), -511.0, MUL, 512.0, ADD)
+    times(cb("BO4"), cb("BO"), 4.0)
+    times(cb("NBO4"), cb("BO"), -4.0)
+    ts(pd_(21), rcol, 15.0, EQ, FINE, MUL)
+    ts(pd_(22), rcol, 15.0, EQ, 256.0, MUL)
+    ts(pd_(23), rcol, 15.0, EQ, -FINE - 2, MUL)
+    ts(pd_(23), pd_(23), 2.0, ADD)
+    ts(pd_(24), rcol, 15.0, EQ, 1 - 1 / FINE, MUL)
+    ts(pd_(24), pd_(24), 1 / FINE, ADD)
+    ts(pd_(28), rcol, 15.0, EQ, FINE + 1, MUL)
+    ts(pd_(28), pd_(28), -1.0, ADD)
+    ts(pd_(29), Pc, 8.0, EQ, PEN / 64, MUL)
+    ts(cf("PK", 4, 8), cf("PK", 0, 4), 32.0, ADD, 96.0, MIN)
+    ts(cf("PK", 8, 12), cf("PK", 4, 8), Pc, GT)
+    ts(cf("PK", 12, 16), cf("PK", 0, 4), Pc, GT, -2.0, MUL)
+    tt(cf("PK", 8, 12), cf("PK", 8, 12), cf("PK", 12, 16), ADD)
+    ts(cf("PK", 16, 20), cf("PK", 4, 8), pd_(29), MUL)
+    ts(cb("S32"), cb("JG"), pd_(7), EQ, PEN / 2, MUL)
+    for k in range(4):
+        act(cb("PEN", L * k, L * k + L), cb("S32"), AF.Identity, bias=cf("PK", 16 + k, 17 + k), scale=cf("PK", 8 + k, 9 + k))
     ts(pd_(25), Pc, 8.0, EQ, float(RK), MUL)
+    ts(pd_(30), Pc, 9.0, EQ, float(OFF), MUL)
     ts(cb("RANK"), cb("FS"), pd_(7), EQ, float(SH * RK), MUL)
-    times(cf("FR"), cf("FR"), pd_(25))
+    act(cf("FR"), cf("FR"), AF.Identity, bias=pd_(30), scale=pd_(25))
     tt(cb("RANK"), cb("RANK"), cf("FR"), ADD)
+    for k in range(3):
+        fill(cb("GW", k, 432, 27), 16, 0)
+    ts(pd_(11), pd_(16), 2.0, MUL)
+    times(cb("GW", 0, 432, 54), cb("ONES", 0, 8), pd_(11))
     ts(pd_(26), Pc, -float(W), ADD)
     times(cb("NMK"), cb("MK", 0, 16), -1.0)
     act(cb("NMK1"), cb("MK"), AF.Identity, bias=1.0, scale=-1.0)
@@ -887,29 +915,33 @@ def rank_program(g, core, T, topo):
     times(cb("XSUM", 15, L, 16), BO, pd_(24))
     times(cf("WS", 0, 8), BO, pd_(23))
     times(cf("WS", 8, 16), BO, pd_(21))
-    ts(cb("AS", 0, L), cb("BLKB"), pd_(22), MUL, -1.0, MUL)
+    ts(cb("AS", 0, L), cb("BLKB"), pd_(28), MUL)
     ts(cb("AS", L, 2 * L), cb("BLKB"), pd_(21), MUL, -1.0, MUL)
     for k in range(8):
-        act(cb("CK", 8 * k, 8 * k + 8), BO, AF.Identity, bias=-4096.0, scale=6144.0)
-    for out, src, c in ((cf("NIF"), cb("IDN"), -1.0), (cf("BOF"), BO, 1.0), (cb("KID"), cb("IDN"), CNT), (cb("NID"), cb("IDN"), -1.0), (cb("K4"), cb("IDN"), -4096.0),
+        act(cb("CK", 8 * k, 8 * k + 8), BO, AF.Identity, bias=-8192.0, scale=12288.0)
+    for out, src, c in ((cf("NIF"), cb("IDN"), -1.0), (cf("BOF"), BO, 1.0), (cb("KID"), cb("IDN"), FAR), (cb("NKID"), cb("IDN"), -FAR), (cb("NID"), cb("IDN"), -1.0), (cb("K4"), cb("IDN"), -4096.0 / (BIG if EQV[0] == 2 else 1)), (cb("BOS"), BO, 1 / BIG),
                         (cf("WT"), cb("BLKB"), pd_(15))):
         times(out, src, c)
-    fill(cf("XCONST", 0, 40, 5), 8, NONE * RK + 4096)
+    ts(pd_(31), Pc, 10.0, EQ, 2 * CNT, MUL)
+    tt(pd_(31), pd_(31), pd_(30), ADD)
+    act(cf("XCONST"), cf("XCONST"), AF.Identity, bias=pd_(31), scale=pd_(25))
+    ts(cb("G5"), cb("G5"), pd_(7), EQ, -CNT / 2, MUL)
+    tt(cb("K2"), cb("K2"), cb("G5"), ADD)
+    tt(cb("K2"), cb("K2"), cf("XCONST"), ADD)
+    ts(pd_(17), pd_(31), 4096.0, MIN)
+    ts(pd_(13), pd_(25), float(NONE), MUL, pd_(17), ADD)
+    times(cb("K2", 1, 48, 6), cb("ONES", 0, 8), pd_(13))
+    cp(cb("RANK", 0, 144, 9), cb("K2", 0, 48, 3))
+    fill(cb("PERM", 0, 144, 9), 16, 0)
     act(cf("DUML"), cf("DUML"), AF.Identity, bias=rcol)
     act(cf("CPOS"), cf("DUML"), AF.Identity, bias=-4096.0 * (W + 48), scale=4096.0)
     for k in range(8):
-        times(cb("SELG", L * k, L * k + L), cb("ONES"), cf("BOF", k, k + 1))
-        ts(cb("FSEL", L * k, L * k + L), cb("F8"), cf("P", k, k + 1), EQ, 2.0, MUL)
-    cp(cb("XSEL", 0, 40, 5), cb("XSEL", 1, 40, 5))
+        either(lambda: ts(cb("SELG", L * k, L * k + L), cb("ONES"), cf("BOF", k, k + 1), MUL), lambda: times(cb("SELG", L * k, L * k + L), cb("ONES"), cf("BOF", k, k + 1)))
+    cp(cb("XSEL", 1, 48, 6), cb("XSEL", 2, 48, 6))
     ts(cb("SIG"), cb("F3"), pd_(2), EQ, -1.0, MUL)
     ts(cb("DEL"), cb("F3"), pd_(2), EQ)
     times(cb("DEL"), cb("DEL"), pd_(14))
-    ts(cb("TRI2"), cb("J"), Pc, GT)
-    ts(cb("TRIP"), cb("J"), Pc, EQ, -256.0, MUL)
-    tt(cb("TRIP"), cb("TRIP"), cb("TRI2"), ADD)
-    ts(cb("TRI2"), cb("J"), Pc, ALU.is_le, 4096.0, MUL)
-    ts(cb("PERM"), cb("FP"), Pc, EQ)
-    ts(cb("WM"), cf("FW"), pd_(3), EQ, -BIG, MUL)
+    ts(cb("WM"), cb("J", 0, 16), pd_(3), EQ, -BIG, MUL)
     cp(cf("THF", rows=R8), col("TH", 0, 4, rows=R8))
     mm(col("PQ", 0, 4), cf("SEL8", rows=R8), cf("THF", rows=R8))
     mm(col("PQ", 4, 8), cf("SELB", rows=R8), cf("THF", rows=R8))
@@ -918,22 +950,25 @@ def rank_program(g, core, T, topo):
     ts(col("TH", 4, 8), col("TH", 0, 4), 4, SHR)
     ts(col("TH", 8, 12), col("TH", 0, 4), 15, AND)
     ts(cf("THP", 0, 4, rows=R16), col("TH", 4, 8), pd_(19, R16), MUL)
-    ts(cf("THP", 4, 8, rows=R16), col("TH", 8, 12), 0.25, ADD, pd_(20, R16), MUL)
+    ts(cf("THP", 4, 8, rows=R16), col("TH", 8, 12), pd_(20, R16), MUL)
     tt(cf("THP", 8, 12, rows=R16), cf("THP", 0, 4, rows=R16), cf("THP", 4, 8, rows=R16), ADD)
     for t in range(RO):
         times(cb("NTH", L * t, L * t + L, rows=R16), cb("ONES", rows=R16), cf("THP", 8 + t, 9 + t, rows=R16))
 
-    def widen():
-        for j in range(4):
-            if "A4" in ONV:
-                cp(col("A4", j, 512, 4), whole("A"))
-            else:
-                act(col("A4", j, 512, 4), whole("A"), AF.Copy)
-        for j in range(4):
-            ts(col("AR", j, 1024, 4), col("A4", 0, 256), pd_(22), MUL)
+    def widen(parts=WIDEN):
+        for a, b, how in parts:
+            for j in range(4):
+                o, i = col("A4", 4 * a + j, 4 * b, 4), col("A", a, b)
+                copy(o, i, b - a) if how[0] == "g" else gather(o, i, how[0] == "v")
+            b = min(b, NV)
+            for j in range(4 * (a < b)):
+                o, i = col("AR", 16 * a + j, 16 * b, 4), col("A4", 4 * a, 4 * b)
+                copy(o, i, 4 * (b - a)) if how[1] == "g" else gather(o, i, how[1] == "v")
 
-    def gather(out, in_, on_vector):
+    def gather(out, in_, on_vector, add=None):
         forms = (lambda: cp(out, in_), lambda: act(out, in_, AF.Copy))
+        if add:
+            forms = (lambda: ts(out, in_, add, ADD), lambda: act(out, in_, AF.Identity, bias=add))
         either(*(forms if on_vector else forms[::-1]))
 
     def options():
@@ -941,35 +976,63 @@ def rank_program(g, core, T, topo):
         for a in range(4):
             mm(col("PW", 256, 288), cb("SELO", L * a, L * a + L), col("R", a, L, 4), a == 0, a == 3)
         cp(OL, col("PW", 256, 288))
-        for h in range(2):
-            if EQB[h] != "BS":
-                alike(h)
+        alike(0)
 
-    def alike(h):
-        bank = EQB[h]
-        for k in range(4 * h, 4 * h + 4):
-            mm(part(bank, k % 4), cb("SELG", L * k, L * k + L), whole("CMG"), True, False)
-            mm(part(bank, k % 4), cb("IDN"), cb("TRI2"), False, True)
-        for k in range(4 * h, 4 * h + 4):
-            if bank == "BS":
-                ts(part("EQ2", k), part(bank, k % 4), col("cT", k), EQ, 4096.0, MUL)
-            else:
-                act(part("AB2", k), part(bank, k % 4), AF.Abs, bias=col("cT", k), scale=-1.0)
-        for k in range(2 * h, 2 * h + 2) if bank != "BS" else ():
-            either(lambda: act(part("EQ2", k, 256), part("AB2", k, 256), AF.Relu, bias=4096.0, scale=-4096.0),
-                   lambda: ts(part("EQ2", k, 256), part("AB2", k, 256), 0.0, EQ, 4096.0, MUL))
+    def gates(c):
+        if EQV[0] == 2:
+            ts(whole("cT"), c, -STEEP, MUL, -math.log(511), ADD)
+        else:
+            cp(whole("cT"), c)
+
+    def alike(at):
+        for h in range(2):
+            if EQAT[h] != at:
+                continue
+            bank = EQB[h]
+            for k in range(4 * h, 4 * h + 4):
+                mm(part(bank, k % 4), cb("SELG", L * k, L * k + L), whole("CMG"), True, False)
+                mm(part(bank, k % 4), cb("IDN"), cb("TRI2"), False, True)
+            for k in range(4 * h, 4 * h + 4):
+                if EQV[h] == 2:
+                    act(part("EQ2", k), part(bank, k % 4), AF.Sigmoid, bias=col("cT", k), scale=STEEP)
+                elif EQV[h]:
+                    ts(part("EQ2", k), part(bank, k % 4), col("cT", k), EQ, 4096.0, MUL)
+                else:
+                    act(part("AB2", k), part(bank, k % 4), AF.Abs, bias=col("cT", k), scale=-1.0)
+            for k in range(2 * h, 2 * h + 2) if not EQV[h] else ():
+                either(lambda: act(part("EQ2", k, 256), part("AB2", k, 256), AF.Relu, bias=4096.0, scale=-4096.0),
+                       lambda: ts(part("EQ2", k, 256), part("AB2", k, 256), 0.0, EQ, 4096.0, MUL))
 
     def apart(b, bank):
-        for j in range(4):
-            mm(part(bank, j), cb("IDN"), col("G2", 4 * b + j, 2048, 16), True, False)
-            mm(part(bank, j), cb("NID"), whole("XC2"), False, True)
-        act(part("H2", b, 512), whole(bank), AF.Abs)
+        n = L - N2V
+        r = 16 // NB2
+        for j in range(r):
+            mm(col(bank, j, n * r, r), cb("IDN"), col("G2", 16 * N2V + r * b + j, 2048, 16), j == 0, False)
+        for j in range(r):
+            mm(col(bank, j, n * r, r), cb("NID"), col("XC2", N2V, L), False, j == r - 1)
+        act(V("H2", ALL, sl(N2V, L), sl(r * b, r * b + r)), col(bank, 0, n * r), AF.Abs)
 
-    def farthest(n, s):
-        rows, GE, o = sl(0, n), "GE" + s, col("PQ", L, L + n)
-        scan(V("PM" + s, rows, ALL), cb("NM16", 0, L, rows=rows), V("PQ", rows, sl(0, L)), 0.0, MUL, MAX)
+    def far(at):
+        if FAT == at and MAX2:
+            mm(col(F2B, 0, 256), whole("XC2"), cb("AS"), True, False)
+            for p in range(16):
+                mm(col(F2B, p, 256, 16), col("D2", p, 2048, 16), cf("WS"), False, p == 15)
+            ts(whole("RR2"), part(F2B, 1), ROUND, ADD, ROUND, SUB)
+            act(whole("AD2"), whole("RR2"), AF.Abs, bias=-256.0, scale=1 / FINE)
+            tt(whole("SV2"), part(F2B, 0), whole("RR2"), ADD)
+            mm(part(F2B, 0), cb("NID"), whole("AD2"), True, False)
+            mm(part(F2B, 0), cf("NIF"), whole("SV2"), False, True)
+            farthest(L, "2", part(F2B, 0), F2B, L, MIN)
+        elif FAT == at:
+            for p in range(16):
+                mm(col(F2B, p, L, 16), V("H2", ALL, ALL, p), BO)
+            farthest(L, "2", part(F2B, 0), F2B, L)
+
+    def farthest(n, s, sums, bank, at, top=MAX):
+        rows, GE, o, sums = sl(0, n), "GE" + s, col(bank, at, at + n), V(sums[1], sl(0, n), sums[2][1])
+        scan(V("PM" + s, rows, ALL), cb("NM16", 0, L, rows=rows), sums, 0.0, MUL, top)
         if "PX" in ONV:
-            scan(V("PX", rows, ALL), cb("NM16", 0, L, rows=rows), V("PQ", rows, sl(0, L)), 0.0, MUL, MAX)
+            scan(V("PX", rows, ALL), cb("NM16", 0, L, rows=rows), sums, 0.0, MUL, top)
             tt(col(GE, 16, 144), IND(whole("PX"), col("LR8", 8, 16)), whole("PM" + s), EQ)
         else:
             gather(col("PX", 0, 8), col("PM" + s, 15, L, 16), True)
@@ -978,7 +1041,7 @@ def rank_program(g, core, T, topo):
         mm(o, col(GE, 16, 144, rows=rows), cb("IDN", 0, n, rows=rows), False, False)
         mm(o, col(GE, 15, 143, rows=rows), cb("NID", 0, n, rows=rows), False, True)
         if s == "2" and "DV2" not in ONV:
-            o = part("PQ", 2)
+            o = part(bank, 2)
             mm(o, cb("NMK1", rows=R1), cb("ONES", rows=R1), True, False)
             mm(o, col(GE, 16, 144), cb("NID"), False, False)
             mm(o, col(GE, 15, 143), cb("IDN"), False, True)
@@ -1005,7 +1068,7 @@ def rank_program(g, core, T, topo):
         for b in range(2):
             act(part("H3", b, 384), col("B%d" % b, 0, 384), AF.Abs)
             for p in range(8 * b, 8 * b + 8):
-                mm(V("PQ", R48, sl(p, L, 16)), part("H3", p, 48), BO)
+                mm(V(F3B[0], R48, sl(F3B[1] + p, F3B[1] + L, 16)), part("H3", p, 48), BO)
         gather(whole("CF3"), IND(IS, la), more and "CF3" in ONV)
         gather(whole("AG"), IND(NUM, la), more and "AG" in ONV)
         cp(col("AL", 0, 3), la)
@@ -1016,29 +1079,27 @@ def rank_program(g, core, T, topo):
         tt(col("ZT", 0, 3), col("SD", 48, 147, 49), cf("DUML"), MIN)
         cp(ld, col("ZT", 0, 3))
         if more:
-            gather(whole("BG"), IND(XS, lb), "BG" in ONV)
-            cp(IND(whole("PN%d" % t), ld), whole("BG"))
-            tt(whole("DP"), IND(col("PN%d" % t, 0, W), OL), whole("A4"), SUB)
-        tt(whole("DV3"), IND(NUM, lb), whole("CF3"), SUB)
-        farthest(48, "3")
+            gather(whole("BG"), IND(whole("XT"), lb), "BG" in ONV)
+            cp(IND(whole("IT"), ld), whole("BG"))
+            tt(whole("DP"), IND(col("IT", 0, W), OL), whole("A4"), SUB)
+        tt(whole("DV3"), IND(whole("NT"), lb), whole("CF3"), SUB)
+        farthest(48, "3", col(F3B[0], F3B[1], F3B[1] + L), F3B[2], F3B[3])
+        tt(whole("WV3"), col(F3B[2], F3B[3], F3B[3] + 48), whole("DV3"), MUL)
         if more:
-            gather(whole("OH"), col("PQ", L, L + 48), "OH" in ONV)
-        tt(whole("WV3"), col("PQ", L, L + 48), whole("DV3"), MUL)
-        if more:
-            cp(IND(whole("PT%d" % t), ld), whole("OH"))
-            gather(whole("PG"), IND(col("PT%d" % t, 0, W), OL), "PG" in ONV)
             tt(IND(IS, ld), whole("WV3"), whole("CF3"), ADD)
-        if t >= RO - 2:
+        else:
             patch(48, "3", "PS", ld)
 
     for k, bank in enumerate(("B0", "B1", "DL", "PQ")):
         mm(whole(bank), cb("XSUM"), col("X", OFF + 512 * k, OFF + 512 * k + 512))
-        gather(part("XF", k, 512), whole(bank), k in XFV)
-    widen()
+        gather(part("XF", k, 512), whole(bank), k in XFV, pd_(22))
+    for h in range(2):
+        copy(col("XT", h, W + 16, 2), col("X", OFF + 1 - h, OFF + W + 16, 2), W // 2 + 8)
+    widen(((0, NV, "av"),))
     cp(GL, whole("GI"))
     spread("CMG", col("GI", 0, 8))
     mm(col("PS", 0, 8), whole("CMG"), BO)
-    cp(whole("cT"), col("PS", 0, 8))
+    gates(col("PS", 0, 8))
     cp(ki(4), col("PS", 0, 8))
     for k in range(4):
         cp(part("IC", k, 512), part("IT", k, 512))
@@ -1046,18 +1107,26 @@ def rank_program(g, core, T, topo):
 
     for t in range(RO):
         last, late = t == RO - 1, t > 0
+        wide = late and CWS is not None
         for a, b in COP:
-            cp(col("COA", 16 * a, 16 * b), IND(IW if late else col("IT", 0, W), col("OL", a, b)))
+            if wide:
+                gather(col("CW", 16 * a, 16 * b), IND(IW, col("OL", a, b)), a not in CWS)
+                if a >= NV // 4:
+                    cp(col("COA", 16 * a, 16 * b), col("CW", 16 * a, 16 * b))
+            else:
+                cp(col("COA", 16 * a, 16 * b), IND(IW if late else col("IT", 0, W), col("OL", a, b)))
         for k in range(4):
-            cp(part("C2", k, NV), col("COA", k, 256, 4))
-        mm(col("PS", 256, 296), whole("R"), cb("XSEL"))
-        tt(whole("XB"), col("PS", 256, 296), cf("XCONST"), ADD)
-        act(whole("XC2"), IND(XW, GL), AF.Copy)
-        if last:
-            for k in range(4):
-                bank = ("PW", "PQ")[k % 2]
-                mm(whole(bank), cf("WT"), part("IC", k, 512))
-                gather(part("YC", k, 512), whole(bank), k % 2)
+            cp(part("C2", k, NV), col("CW" if wide else "COA", k, 256, 4))
+        gather(whole("XC2"), IND(XW, GL), False)
+        if N2V:
+            for j in range(4):
+                copy(col("X4", j, 4 * N2V, 4), col("XC2", 0, N2V), N2V)
+            for j in range(4):
+                copy(col("XR", j, 16 * N2V, 4), col("X4", 0, 4 * N2V), 4 * N2V)
+        if wide:
+            copy(whole("C0"), whole("CW"), 512)
+        else:
+            cp(whole("C0" if late else "C16"), whole("COA"))
         for q in range(16):
             mm(col("B1", 64, 72), cb("W0", 15 - q, 143 - q), col("R", q, L, 16), q == 0, q == 15)
         cp(whole("OL0"), col("B1", 64, 72))
@@ -1067,111 +1136,132 @@ def rank_program(g, core, T, topo):
         act(whole("AA"), part("PS", 1), AF.Abs)
         for l in range(L - NV):
             act(part("H", l, 64), IND(XW, part("COA", NV + l, 4)), AF.Abs, bias=col("A", NV + l), scale=-1.0)
-        for k in range(4):
-            for h in range(DN):
-                tt(part("D", DN * k + h, 1024 // DN), IND(whole("XF"), part("C2", DN * k + h, NV // DN)), part("AR", h, 1024 // DN), MAX)
+        for h in range(2):
+            for k in range(4):
+                tt(part("D", 4 * h + k, 512), IND(whole("XF"), part("C2", 2 * k + h, 32)), part("AR", h, 512), MAX)
         for c, bank in enumerate(("BV", "DL")):
             mm(col(bank, 0, 256), cb("NTH", L * t, L * t + L, rows=R16), cb("THS", rows=R16), True, False)
-            for h in range(2):
-                mm(V(bank, sl(64 * h, 64 * h + 64), sl(0, 256)), col("A", 0, NV), cb("AS"), False, False)
+            for k in range(4):
+                mm(V(bank, sl(32 * k, 32 * k + 32), sl(0, 256)), part("A", c, 32), cb("AS"), False, False)
             for p in range(16):
                 mm(col(bank, p, 256, 16), col("D", 2048 * c + p, 2048 * c + 2048, 16), cf("WS"), False, p == 15)
             ts(part("RR", c), part(bank, 1), ROUND, ADD, ROUND, SUB)
-            tt(part("DD", c), part(bank, 1), part("RR", c), SUB)
-            act(part("AD", c), part("DD", c), AF.Abs)
-            tt(part("SV", c), part(bank, 0), part("AD", c), ADD)
-        mm(part("BS", 0, 64), cb("WIDE", 15, 143), col("H", 0, 1024, 16), True, False)
+            act(part("AD", c), part("RR", c), AF.Abs, bias=-256.0, scale=1 / FINE)
+            tt(part("SV", c), part(bank, 0), part("RR", c), ADD)
         if late:
+            mm(col("BS", 0, 256), cb("NKID"), col("C0", 256, 512), True, False)
+            mm(col("BV", 0, 256), cb("NKID"), col("C0", 0, 256), True, False)
+        for k in range(4):
+            mm(part("BV", k // 2), part(("AD", "SV")[k % 2], k // 2), cb("PRM"), k == 0 and not late, k == 3 and not late)
+        for j in range(4):
+            for p in range(16):
+                mm(part("BS", j, 64), cb("WIDE", 15 - p, 143 - p), col("H", 1024 * j + p, 1024 * j + 1024, 16),
+                   j == p == 0 and not late, j == 3 and p == 15 and not (late and LASTC))
+                if late and not LASTC and j == p == 0:
+                    held = len(ops)
+        if late:
+            rest = ops[held:] if not LASTC else []
+            del ops[len(ops) - len(rest):]
             abroad(t - 1)
-            mm(col("BV", 0, 256), cb("KID"), col("PG", 0, 256), True, False)
-            for k in range(3 if CUT else 4):
-                mm(part("BS", k, 64), cb("KID"), part("PG", 4 + k, 64), False, False)
             act(whole("RP"), whole("DP"), AF.Abs)
             for k in range(4):
                 mm(part("PW", 0), cb("BO", 96 - 32 * k, 224 - 32 * k), col("RP", k, 512, 4), k == 0, k == 3)
-            act(whole("LE2"), part("PW", 0), AF.Sign, bias=cf("THC", t, t + 1))
-        for k in range(4):
-            mm(col("BV", k, 256, 4), part("SV", k // 2), cb("IDN", 64 * (k % 2), 64 * (k % 2) + 64), k == 0 and not late, k == 3)
-        for j in range(4):
-            if CUT and j == 3:
-                act(col("LE", 256, 448), col("BS", 0, 192), AF.Sign, bias=cf("THG", t, t + 1))
-                if late:
-                    mm(part("BS", j, 64), cb("KID"), part("PG", 4 + j, 64), True, False)
-            for p in range(j == 0, 16):
-                mm(part("BS", j, 64), cb("WIDE", 15 - p, 143 - p), col("H", 1024 * j + p, 1024 * j + 1024, 16),
-                   CUT and j == 3 and p == 0 and not late, j >= (2 if CUT else 3) and p == 15)
-        act(col("LE", 448 if CUT else 256, 512), col("BS", 192 if CUT else 0, 256), AF.Sign, bias=cf("THG", t, t + 1))
-        if EQB[0] == "BS":
-            alike(0)
-        ts(ki(2), ki(4), 1, AND)
-        ts(tf(1), ki(2), -2.0, MUL, 1.0 - W, ADD)
-        tt(col("T16", 8, 16), tf(1), ki(4), ADD)
-        for h in range(CN):
-            cp(part("C16", h, 512 // CN), IND(IW, part("OL", h, 32 // CN)))
-        gather(whole("CF2"), IND(IW, GL), "CF2" in ONV)
+            act(part("LE2", 0), part("PW", 0), AF.Sign, bias=cf("THC", t, t + 1))
+            mm(part("PW", 0), cb("IDN"), part("LE2", 0), True, False)
+            for k in range(4):
+                mm(part("PW", 0), cb("NBO4", 96 - 32 * k, 224 - 32 * k), col("C0", k, 512, 4), False, False)
+            for h in range(CN):
+                cp(part("C16", h, 512 // CN), IND(IW, part("OL", h, 32 // CN)))
+            mm(col("BV", 0, 256), cb("KID"), col("C16", 0, 256), False, True)
+            mm(col("BS", 0, 256), cb("KID"), col("C16", 256, 512), False, LASTC)
+            ops.extend(rest)
+            for k in range(4):
+                mm(part("PW", 0), cb("BO4", 96 - 32 * k, 224 - 32 * k), col("C16", k, 512, 4), False, k == 3)
+            act(part("LE2", 1), part("PW", 0), AF.Sign, scale=-1.0)
+        act(col("LE", 256, 512), col("BS", 0, 256), AF.Sign, bias=cf("THG", t, t + 1))
+        alike(1)
+        ts(col("T16", 8, 16), ki(4), -float(W), ADD)
+        gather(whole("CF2"), IND(IW if late else col("IT", 0, W), GL), "CF2" in ONV or not late)
+        if not late:
+            ops[-1].update(other=None, e="v")
         if "CO2" in ONV:
-            cp(whole("CO2"), IND(IW, GL))
+            cp(whole("CO2"), IND(IW if late else col("IT", 0, W), GL))
         else:
             cp(whole("CO2"), whole("CF2"))
-        for b in range(G2N):
-            gather(part("G2", b, 2048 // G2N), IND(XW, part("CO2", b, L // G2N)), b * 4 // G2N in G2V)
-        for k in range(3):
-            mm(part("DL", k), cb("DEL"), col("C16", k + 1, 512, 4))
+        for a in range(0, L, G2N):
+            o, i = col("G2", 16 * a, 16 * (a + G2N)), IND(XW, col("CO2", a, a + G2N))
+            if MAX2:
+                tt(col("D2", 16 * a, 16 * (a + G2N)), IND(whole("XF"), col("CO2", a, a + G2N)), col("XR", 16 * a, 16 * (a + G2N)), MAX)
+            elif a < N2V:
+                tt(o, i, col("XR", 16 * a, 16 * (a + G2N)), SUB)
+            else:
+                gather(o, i, a in G2V)
+        for a in range(0, N2V * (not MAX2), H2N):
+            act(V("H2", ALL, sl(a, a + H2N), ALL), col("G2", 16 * a, 16 * (a + H2N)), AF.Abs)
+        at = 0
+        for a, b in PARTS:
+            for k in range(3):
+                mm(col("DL", at + k * (b - a), at + (k + 1) * (b - a)), cb("DEL"), col("C16", 4 * a + k + 1, 4 * b, 4))
+            at += 3 * (b - a)
         act(whole("AB"), col("DL", 0, 384), AF.Abs)
-        act(part("LE", 0, 256), col("BV", 0, 256), AF.Sign)
+        act(part("LE", 0, 256), col("BV", 0, 256), AF.Sign, bias=-0.5)
         for b, bank in enumerate(EARLY):
             apart(b, bank)
-        if EQB[1] == "BS":
-            alike(1)
-        more = cb("TWO" if late else "THREE", rows=R1)
-        mm(col("PS", 0, 40), more, cb("CW", rows=R1), True, False)
-        mm(part("PW", 1), cb("ONES", rows=R1), more, True, False)
-        if late:
-            mm(col("PS", 0, 40), whole("LE2"), cb("K2"), False, False)
-            mm(part("PW", 1), cb("IDN"), whole("LE2"), False, False)
-        for k in range(4):
-            mm(col("PS", 4 - k, 40, 5), col("LE", k, 512, 4), cb("BOC"), False, k == 3)
-        for k in range(4):
-            mm(part("PW", 1), cb("BO", 96 - 32 * k, 224 - 32 * k), col("LE", k, 512, 4), False, k == 3)
-        scan(whole("KEY"), col("PS", 0, 40), col("XB", 0, 40), 0.0, MIN, MAX)
-        ts(whole("KA"), col("KEY", 4, 40, 5), W - 1, AND)
-        spread("KM", col("KA", 0, 8))
-        act(whole("SVG"), part("PW", 1), AF.Sign)
-        mm(col("PS", 64, 72), whole("KM"), BO)
-        cp(whole("FL"), col("PS", 64, 72))
-        cp(whole("FC"), IND(IW, col("FL", 0, 8)))
-        mm(col("PW", 0, 432), whole("SVG"), cb("GW"), True, False)
-        for pp, bank in enumerate(EEB):
-            for k in range(3):
-                mm(part(bank, k), cb("SIG"), col("C16", k + 1, 512, 4), k == 0, False)
-            for k in range(3):
-                mm(part(bank, k), cb("FSEL", L * pp, L * pp + L), whole("FC"), False, k == 2)
-            act(col(bank, 0, 384), col(bank, 0, 384), AF.Abs)
-            for a, b in ((0, 384),) if pp < 7 else ((0, 256), (256, 384)):
-                tt(V("EE", ALL, pp, sl(a, b)), col("AB", a, b), col(bank, a, b), EQ)
-            for k in range(3):
-                mm(col("PW", 3 * (8 - pp) + k, 432, 27), V("EE", ALL, pp, sl(L * k, L * k + L)), cb("WM"), False, pp == 7 and k == 2)
-        mm(col("PS", 0, 8), whole("SVG"), cb("G1W"))
-        mm(col("PS", L, L + 144), whole("FC"), cb("PERM"), True, False)
-        mm(col("PS", L, L + 144), whole("SVG"), cb("RANK"), False, True)
-        tt(whole("XC"), col("KEY", 4, 40, 5), col("PS", 0, 8), MAX)
-        act(col("M3", 0, 432, 3), col("PS", L, L + 144), AF.Copy)
-        tt(col("M3", 27, 432, 54), whole("XC"), col("XB", 0, 40, 5), MIN)
-        scan(col("S1", 0, 432), whole("M3"), col("PW", 0, 432), BIG, MIN, MAX)
-        scan(whole("S2"), cf("RST"), col("S1", 2, 435, 3), 0.0, ADD, MIN)
-        named = col("S2", 18, 145, 18)
-        ts(whole("LB"), named, float(NONE * RK), ALU.is_lt)
+        FC = col("FC", 3, 512, 4)
+        for h, (a, b) in enumerate(PARTS):
+            n, end = b - a, b == L
+            o = col("PW", L + a, L + b)
+            mm(o, cb("ONES", rows=R1), cb("THREE", 0, n, rows=R1), True, False)
+            for k in range(2 * late):
+                mm(o, cb("IDN"), col("LE2", L * k + a, L * k + b), False, False)
+            for k in range(4):
+                mm(o, cb("BO", 96 - 32 * k, 224 - 32 * k), col("LE", 4 * a + k, 4 * b, 4), False, k == 3)
+            act(col("SVG", a, b), o, AF.Sign)
+            bank = FCB[h]
+            mm(col(bank, 0, 4 * n), cb("IDN"), col("C16", 4 * a, 4 * b), True, False)
+            for k in range(4):
+                mm(col(bank, k, 4 * n, 4), cb("PEN", L * k, L * k + L), col("SVG", a, b), False, k == 3)
+            scan(col("FC", 4 * a, 4 * b), cb("RS4", 0, 4 * n), col(bank, 0, 4 * n), 0.0, MAX, MIN)
+            alike(2 if end else 4)
+            if end:
+                far(2)
+                mm(col("PS", 0, 48), whole("R"), cb("XSEL"), True, False)
+                mm(col("PS", L, L + 144), whole("SVG"), cb("RANK"), False, False, True)
+                mm(col("PS", L, L + 144, 9), whole("R"), cb("XSEL", 0, 48, 3), False, False)
+                mm(col("PS", 0, 48), whole("SVG"), cb("K2"), False, False)
+                mm(col("PS", L, L + 144), FC, cb("PERM"), False, True)
+                gather(col("M3", 0, 432, 3), col("PS", L, L + 144), False)
+                for k in (1, 2):
+                    gather(col("M3", k, 432, 27), col("PS", k, 48, 3), False)
+                mm(col("PW", 0, 432), whole("SVG"), cb("GW"), True, False)
+            two = L // n
+            for j in range(8 // two):
+                bank, rows = EEB[h][j], range(two * j, two * j + two)
+                for pp in rows:
+                    for k in range(3):
+                        mm(part(bank, 3 * (pp % two) + k, n), cb("SIG"), col("C16", 4 * a + k + 1, 4 * b, 4), k == pp % two == 0, False)
+                for pp in rows:
+                    for k in range(3):
+                        mm(part(bank, 3 * (pp % two) + k, n), cb("FSEL", L * pp, L * pp + L), col("FC", 4 * a + 3, 4 * b, 4), False, k == 2 and pp == rows[-1])
+                act(col(bank, 0, 384), col(bank, 0, 384), AF.Abs)
+                for pp in rows:
+                    tt(V("EE", ALL, pp, ALL, sl(a, b)), col("AB", 3 * a, 3 * b), part(bank, pp % two, 3 * n), EQ)
+                    for k in range(3 * end):
+                        mm(col("PW", 3 * (pp + 1) + k, 432, 27), V("EE", ALL, pp, k, ALL), cb("WM"), False, pp == 7 and k == 2)
+        alike(3)
+        scan(whole("S1"), whole("M3"), col("PW", 0, 432), BIG, MIN, MAX)
+        scan(whole("S2"), cf("RST"), col("S1", 2, 432, 3), 0.0, ADD, MIN)
+        named = col("S2", 17, 144, 18)
+        ts(col("LB", 0, 8), named, float(NONE * RK), ALU.is_lt)
         ts(ki(0), named, RK - 1, AND)
         ts(ki(3), named, 4095, AND)
         ts(ki(1), named, 1, AND)
-        for b, bank in enumerate(LATER):
+        for b, bank in enumerate(LATER[:NB2 - len(EARLY)]):
             apart(len(EARLY) + b, bank)
-        for p in range(16):
-            mm(col("PQ", p, L, 16), part("H2", p), BO)
-        farthest(L, "2")
+        far(3)
         for k in range(8):
             mm(col("DL", 0), cb("O16"), col("LB", k), k == 0, k == 7)
-        mm(col("PS", 0, 8), cb("TRIP"), whole("LB"))
+        mm(col("PS", 0, 8), cb("TRIP"), col("LB", 0, 8))
         if "NM" in ONV:
             spread("NM", ki(0))
         else:
@@ -1186,11 +1276,23 @@ def rank_program(g, core, T, topo):
         tt(col("T16", 0, 8), tf(0), ki(3), ADD)
         ts(ki(7), ki(5), col("DL", 0), ADD)
         ts(ki(4), ki(7), 4, SHR, W - 1, AND)
-        mm(col("BS", 0, 8), whole("CMG"), BO, True, False)
-        mm(col("BS", 0, 8), cb("K4"), whole("LB"), False, False)
-        for k in range(8):
-            mm(col("BS", k), part("EQ2", k), col("LB", k), False, k == 7)
-        act(whole("ZZ"), col("BS", 0, 8), AF.Relu, bias=pd_(26), scale=-1.0)
+        if EQV[0] == 2:
+            ts(col("LB", 8, 16), named, float(NONE * RK), ALU.is_lt, -1.0, MUL)
+            mm(col("BS", 0, 8), cb("ONES", rows=R1), cb("MAG", 0, 8, rows=R1), True, False)
+            for k in range(8):
+                mm(col("BS", k), part("EQ2", k), col("LB", 8 + k), False, False)
+            mm(col("BS", 0, 8), cb("ONES", rows=R1), cb("MAG", 8, 16, rows=R1), False, False, True)
+            for k in range(8):
+                mm(col("BS", k), part("EQ2", k), col("LB", k), False, False)
+            mm(col("BS", 0, 8), whole("CMG"), cb("BOS"), False, False, True)
+            mm(col("BS", 0, 8), cb("K4"), col("LB", 0, 8), False, True)
+            act(whole("ZZ"), col("BS", 0, 8), AF.Relu, bias=pd_(26), scale=-BIG)
+        else:
+            mm(col("BS", 0, 8), whole("CMG"), BO, True, False)
+            mm(col("BS", 0, 8), cb("K4"), col("LB", 0, 8), False, False)
+            for k in range(8):
+                mm(col("BS", k), part("EQ2", k), col("LB", k), False, k == 7)
+            act(whole("ZZ"), col("BS", 0, 8), AF.Relu, bias=pd_(26), scale=-1.0)
         for k in range(8):
             times(part("ZM", k, 16), cb("NMK"), col("ZZ", k))
         mm(col("BS", 16, 24), cf("NIF"), cf("SPARE"), True, False)
@@ -1200,8 +1302,8 @@ def rank_program(g, core, T, topo):
             tt(whole("DV2"), IND(whole("NUM"), col("NL", 0, 8)), whole("CF2"), SUB)
         else:
             act(whole("DV2"), IND(whole("NUM"), col("NL", 0, 8)), AF.Copy)
-            tt(whole("CF2"), part("PQ", 2), whole("CF2"), MUL)
-        tt(whole("WV2"), part("PQ", 1), whole("DV2"), MUL)
+            tt(whole("CF2"), part(F2B, 2), whole("CF2"), MUL)
+        tt(whole("WV2"), part(F2B, 1), whole("DV2"), MUL)
         tt(IND(IS, col("SL2", 0, 8)), whole("WV2"), whole("CF2"), ADD)
         if not last:
             spread("CMT", ki(4))
@@ -1209,24 +1311,31 @@ def rank_program(g, core, T, topo):
             mm(part("B0", 0), whole("CMT"), cb("IDN"))
             cp(GL, col("PW", 32, 40))
             cp(whole("CMG"), part("B0", 0))
-            cp(whole("cT"), ki(4))
-        if PAV < 8:
-            act(whole("PF"), col("PS", 0, 8), AF.Copy)
-        for k in range(PAV):
-            ts(V("PA", ALL, ALL, k, ALL), cb("S48"), col("PS" if PAV == 8 else "PF", k), EQ)
-        for k in range(PAV, 8):
-            act(V("PB", ALL, ALL, k, ALL), cb("S48"), AF.Abs, bias=col("PF", k), scale=-1.0)
-        if PAV < 8:
-            act(V("PC", ALL, ALL, sl(PAV, 8), ALL), V("PB", ALL, ALL, sl(PAV, 8), ALL), AF.Relu, bias=1.0, scale=-1.0)
+            if "cT" in ONV:
+                gates(ki(4))
+            else:
+                mm(col("PS", 16, 24), whole("CMG"), BO)
+                act(whole("cT"), col("PS", 16, 24), AF.Identity, bias=-math.log(511), scale=-STEEP)
+        steps = PAS and not last
+        if steps:
+            act(whole("PF"), col("PS", 0, 8), AF.Identity, bias=0.5, scale=-1.0)
+            ts(col("T16", 16, 32), col("T16", 0, 16), -1.0, MUL)
+        for k in range(8):
+            if steps:
+                act(V("PB", ALL, ALL, k, ALL), cb("S96"), AF.Sign, bias=col("PF", k))
+            else:
+                ts(V("PA", ALL, ALL, k, ALL), cb("S96", 0, 48), col("PS", k), EQ, 2.0, MUL)
         mm(col("B1", 0, 64), cb("IDN"), cb("CK"), True, False)
         for h in range(2):
             for u in range(3):
                 o, end = sl(32 * h + 8 * u, 32 * h + 8 * u + 8), h == 1 and u == 2
-                if PAV < 8:
-                    mm(V("B1", ALL, o), V("PC", ALL, u, ALL, ALL), part("T16", h, 8), False, False)
-                mm(V("B1", ALL, o), V("PA", ALL, u, ALL, ALL), part("T16", h, 8), False, end)
+                if steps:
+                    mm(V("B1", ALL, o), V("PB", ALL, 3 + u, ALL, ALL), part("T16", 2 + h, 8), False, False)
+                    mm(V("B1", ALL, o), V("PB", ALL, u, ALL, ALL), part("T16", h, 8), False, end)
+                else:
+                    mm(V("B1", ALL, o), V("PA", ALL, u, ALL, ALL), part("T16", h, 8), False, end)
         scan(whole("SK"), cf("RS8"), col("B1", 0, 64), 0.0, ADD, MAX)
-        cp(whole("O%d" % t), col("SK", 7, 64, 8))
+        ts(whole("O%d" % t), col("SK", 7, 64, 8), 0.5, MUL)
         send(t)
         if not last:
             options()
@@ -1245,7 +1354,10 @@ def rank_program(g, core, T, topo):
     mm(V("BS", R8, sl(256, 384)), whole("G16"), cb("IDN"))
     cp(whole("YG"), V("BS", R8, sl(256, 384)))
     dma("s", V("yg", ALL), whole("YG"), 0)
-    patch(L, "2", "DL", col("SL2", 0, 8))
+    for k in range(YCN):
+        n, bank = W // YCN, YCB[k % len(YCB)]
+        mm(col(bank, 0, n), cf("WT"), part("IC", k, n))
+        gather(part("YC", k, n), col(bank, 0, n), k % 2)
     abroad(RO - 1)
     dma("s", V("yc", ALL), V("YC", sl(0, 128, 16), sl(0, W)), 64)
     emit(g, T, arrange(ops))

import math
import numpy as np
from concourse.mybir import AluOpType as ALU, AxisListType as AX, ActivationFunctionType as AF

W, L, RO = 2048, 128, 4
DUM = 128
BIG = 4194304.0
CNT = 2097152.0
RK, SH = 8192, 32
NONE = 5 * SH + 24
OFF = 592
FINE = 16384.0
ROUND = 1.5 * 2 ** 37
FAR = 8192.0
PEN = 4096.0
H16 = "float16"
NV = 64
ENG = 8
FILES = ("H", "D")
XFV, G2V = (0, 1), ()
ONV = ("NM", "G3a", "DV2", "cT")
LOADS = "XAI"
G2N = 32
EEB, EARLY, LATER = (("B0", "B1", "PQ", "DL"), ("B0", "B1", "PQ", "DL")), (), ("PQ", "BV", "BS", "B0")
PAV, CN = 8, 1
EQB, EQV, EQAT = ("BV", "BS"), (2, 2), (3, 3)
YCB, YCN = ("BV", "DL", "PW", "BS"), 8
WIDEN, LASTC, FCB = ((0, 32, "vv"), (32, 128, "gg")), False, ("BV", "BS")
PARTS = ((0, 64), (64, 128))
N2V, NB2, H2N, FAT, F2B = 128, 0, 32, 3, "PQ"
F3B = ("PQ", 0, "PQ", L)
CWS, STEEP, MAX2 = None, 64.0, False
PAS = False
MOVED = 500
COP = ((16, 20), (0, 16), (20, 32))
CYCLE, TENSOR = 0.00083, 0.00042
PACES = ((1.0, 1.56, 3.0, 0.19, 1.3), (1.3, 1.2, 3.0, 0.15, 1.0), (1.15, 1.9, 4.0, 0.25, 2.2))
PASSES, SHAKE = 6, 0.5
UNIT = 0.5
SLACK, STARTS, ANEW = 0.0003, 1, 5
PIECE, MOVES, SWEEPS = 160, 500, 10


def _pack(items):
    at, n = {}, 0
    for name, w in items:
        at[name] = (n, w)
        n += (w + 15) // 16 * 16
    return at, n


CB, NCB = _pack([("ONES", 128), ("IDN", 128), ("NID", 128), ("MK", 128), ("NMK", 16), ("NMK1", 128), ("BO", 224), ("AS", 256), ("XSUM", 128), ("CK", 64), ("K2", 48), ("THREE", 128), ("PEN", 512), ("RS4", 512), ("S32", 128), ("PRM", 128), ("MAG", 16), ("BOS", 8),
                 ("WIDE", 144), ("W0", 144), ("KID", 128), ("NKID", 128), ("BO4", 224), ("NBO4", 224), ("THS", 256), ("NTH", 512), ("FG", 432), ("NM16", 128), ("GW", 432), ("FS", 144), ("G5", 48), ("WM", 16),
                 ("RANK", 144), ("TRIP", 128), ("TRI2", 128), ("S96", 96), ("J", 128), ("F16", 128), ("JG", 128),
                 ("F3", 128), ("F8", 128), ("BLKB", 128), ("K4", 128), ("O16", 128), ("C1024", 128),
                 ("SELO", 512), ("SIG", 128), ("DEL", 128), ("FSEL", 1024), ("PERM", 144), ("XSEL", 48), ("SELG", 1024), ("ZERO", 128)])
CF, NCF = _pack([("P", 8), ("PD", 32), ("PK", 20), ("FV", 144), ("XCONST", 48), ("FR", 144),
                 ("WS", 16), ("NIF", 128), ("RS8", 64), ("D0", 147), ("NE", 147), ("CPOS", 3),
                 ("DUML", 3), ("SPARE", 8), ("WT", 128), ("SEL8", 128), ("THF", 4), ("THC", 4), ("THG", 4), ("SELB", 128), ("THP", 12), ("BOF", 8), ("J32", 128), ("RST", 144)])
S, F, B, I32, U = "sbuf", "float32", "bfloat16", "int32", "uint16"
SCRATCH = {
    "CB": (S, [128, NCB], B), "CF": (S, [128, NCF], F), "LR8": (S, [128, 16], U), "LI": (S, [128, 8], I32),
    "PI": (S, [128, 32], I32), "TH": (S, [16, 12], I32), "GI": (S, [128, 8], I32),
    "IT": (S, [128, W + 64], I32), "IC": (S, [128, W + DUM], F), "AW": (S, [128, W], I32), "X": (S, [128, OFF + W + 16], B), "XF": (S, [128, W], F),
    "XT": (S, [128, W + 16], B), "NT": (S, [128, W + 16], F), "YC": (S, [128, W + DUM], F), "NUM": (S, [128, OFF + W + 16], F),
    "A": (S, [128, L], B), "A4": (S, [128, 512], B), "GL": (S, [128, 8], U), "OL": (S, [128, 32], U), "R": (S, [128, L], H16),
    "cT": (S, [128, 8], F), "CMG": (S, [128, L], H16), "CMT": (S, [128, L], H16),
    "COA": (S, [128, 512], U), "C16": (S, [128, 512], H16), "C0": (S, [128, 512], H16),
    "H": (S, [128, 4096], B), "D": (S, [128, 4096], F), "RR": (S, [128, 256], F), "AD": (S, [128, 256], B), "SV": (S, [128, 256], B), "AR": (S, [128, 1024], B), "C2": (S, [128, 256], U),
    "LE": (S, [128, 512], B), "LE2": (S, [128, 2 * L], B),
    "DP": (S, [128, 512], B), "RP": (S, [128, 512], B),
    "FC": (S, [128, 512], H16),
    "SVG": (S, [128, L], B), "XC": (S, [128, 8], F), "AB": (S, [128, 384], F), "EE": (S, [128, 8, 3, L], B),
    "S1": (S, [128, 432], F), "S2": (S, [128, 144], I32), "M3": (S, [128, 432], F), "KI": (S, [128, 64], I32), "TF": (S, [128, 16], F), "LB": (S, [128, 16], B),
    "PA": (S, [128, 3, 8, 16], B), "PB": (S, [128, 6, 8, 16], B), "PF": (S, [128, 8], F), "T16": (S, [128, 32], H16), "SK": (S, [128, 64], F), "EQ2": (S, [128, 1024], B), "AB2": (S, [128, 1024], B),
    "AL": (S, [128, 4], F), "AG": (S, [128, 48], F), "SD": (S, [128, 147], F), "LD": (S, [128, 4], U),
    "ZT": (S, [128, 8], F), "ZZ": (S, [128, 8], F), "ZM": (S, [128, L], F), "SL2": (S, [128, 8], U),
    "NM": (S, [128, L], F), "NL": (S, [128, 8], U), "X0": (S, [128, L], B), "OL0": (S, [128, 8], U), "AA": (S, [128, L], B),
    "XN": (S, [128, L], B), "AH": (S, [128, L], I32), "AO": (S, [128, L], F),
    "CO2": (S, [128, L], U), "CF2": (S, [128, L], F), "XC2": (S, [128, L], B),
    "D2": (S, [128, 2048], F), "RR2": (S, [128, L], F), "SV2": (S, [128, L], F), "AD2": (S, [128, L], B), "CW": (S, [128, 512], F), "X4": (S, [128, 512], B), "XR": (S, [128, 2048], B), "G2": (S, [128, 2048], B), "H2": (S, [128, L, 16], B),
    "PM2": (S, [128, L], F), "GE2": (S, [128, 144], B), "DV2": (S, [128, L], F), "WV2": (S, [128, L], F),
    "CO3": (S, [128, 48], U), "CF3": (S, [128, 48], F), "XC3": (S, [128, 48], B), "G3": (S, [128, 768], B), "H3": (S, [128, 768], B),
    "PM3": (S, [128, L], F), "GE3": (S, [128, 144], B), "DV3": (S, [128, 48], F), "WV3": (S, [128, 48], F), "YP3": (S, [128, 48], F),
    "BG": (S, [128, 48], B), "PX": (S, [128, L], F), "G16": (S, [128, 8], H16), "YG": (S, [8, L], F),
}
for _t in range(RO):
    for _n in "OI":
        SCRATCH["%s%d" % (_n, _t)] = (S, [128, 8], U)
for _n in ("BV", "BS", "PS", "B0", "B1", "DL", "PW", "PQ"):
    SCRATCH[_n] = ("psum", [128, 512], F)
SEMAPHORES = ["cv", "ca", "cp", "cg", "snt"] + ["d%d" % k for k in range(16)] + ["s%s%d" % (n, t) for n in "IO" for t in range(RO)]


def target(r, t, cores):
    return cores[(r + 1 + t % (len(cores) - 1)) % len(cores)]


def relay(src, cores, topo):
    own = [r for r, c in enumerate(cores) if c in topo.cores_of(src)]
    r, t = [(r, t) for t in range(RO) for r in own if not topo.may_write(cores[r], target(r, t, cores))][0]
    near = [c for c in topo.cores_of(src) if c not in cores and topo.may_write(c, target(r, t, cores))]
    near.sort(key=lambda c: topo.die(c) != topo.die(cores[r]))
    return near[0]


def first_hop(r, t, cores, topo):
    src, dst = cores[r], target(r, t, cores)
    if topo.may_write(src, dst):
        return dst, "I"
    return relay(src, cores, topo), "IO"[[c for c in cores if c in topo.cores_of(src)].index(src)]


def hand(g, T, topo, src, dst, out, in_):
    rid, pid = topo.addr(dst, src)
    g.remote_dma(T[out][:], T[in_][:], T.sem["s" + out], T.sem["snt"], pid, rid, sum(1 << e for e in topo.engines(src, dst)[:ENG]))


def relay_program(g, core, T, topo):
    cores, sent = list(T.cores), 0
    for t in range(RO):
        for r in range(len(cores)):
            hop, letter = first_hop(r, t, cores, topo)
            if hop == core:
                buf = "%s%d" % (letter, t)
                g.wait_ge(T.sem["s" + buf], ENG)
                hand(g, T, topo, core, target(r, t, cores), "I%d" % t, buf)
                sent += ENG
    if sent:
        g.wait_ge(T.sem["snt"], sent)


def V(name, *idx):
    return ("ap", name, idx)


def IND(win, off):
    return ("ind", win, off)


def sl(a=None, b=None, s=None):
    return slice(a, b, s)


ALL = sl()


def _c(buf, tab):
    def f(name, a=0, b=None, s=None, rows=ALL):
        o, w = tab[name]
        return V(buf, rows, sl(o + a, o + (w if b is None else b), s))
    return f


cb, cf = _c("CB", CB), _c("CF", CF)


def col(name, a, b=None, s=None, rows=ALL):
    return V(name, rows, sl(a, a + 1 if b is None else b, s))


SPANS, ORDERS = {}, {}


def span(ap):
    name, idx = ap[1], ap[2]
    if name not in SCRATCH:
        return None
    key = (name, repr(idx[1:]))
    if key not in SPANS:
        sh = SCRATCH[name][1][1:]
        e = np.arange(int(np.prod(sh))).reshape(sh)[tuple(idx[1:])].reshape(-1)
        m = np.zeros(int(np.prod(sh)) + 8, np.uint8)
        m[e] = 1
        SPANS[key] = name, int.from_bytes(np.packbits(m).tobytes(), "big"), int(e.min()), int(e.max()), len(e)
    return SPANS[key]


def needs(ops, banks):
    hist, tail, out = {}, {}, []
    for n, o in enumerate(ops):
        e, deps = o["e"], set()
        for (name, m, lo, hi, _), w in o["acc"]:
            psum = SCRATCH[name][0] == "psum"
            for (j, m2, lo2, hi2, w2) in hist.get((name, True), []) + (hist.get((name, False), []) if w or psum else []):
                same = ops[j]["e"] == e
                if same and e == "p" or o["dma"] and ops[j]["dma"] and o["a"][0][2][0] != ops[j]["a"][0][2][0]:
                    continue
                if (psum and not same) or ((w or w2) and ((m & m2) if same else (lo <= hi2 and lo2 <= hi))):
                    deps.add(j)
            if banks and psum and e == "p":
                start, stop = o["group"]
                group = tail.get(name, [])
                deps.update(group if start or stop else group[:1])
                tail[name] = [n] if start or stop else group + [n]
        for (name, m, lo, hi, _), w in o["acc"]:
            if w and o["full"] and (e != "p" or o["group"][0]):
                for kind in (True, False):
                    hist[name, kind] = [x for x in hist.get((name, kind), []) if x[1] & ~m]
            hist.setdefault((name, w), []).append((n, m, lo, hi, w))
        out.append(deps)
    return out


def cost(o, kind, pace):
    a, (slow, gather, scatter) = [x for x in o["a"] if isinstance(x, tuple)], pace[:3]
    size = lambda x: span(x)[4]
    if kind in ("dma", "send", "arrive", "table"):
        return {"dma": 0.06, "send": 0.6, "arrive": 0.0, "table": 1.4 * slow}[kind]
    ind = [x for x in a if x[0] == "ind"]
    if ind:
        return slow * ((0.065 if kind == "act" else 0.05) + 16 * size(ind[0][2]) * CYCLE * (scatter if ind[0] is a[0] else gather))
    n, wide = size(a[0]), [SCRATCH[x[1]][2] in (F, I32) for x in a if size(x) > 1 or x is a[0]]
    if kind == "mm":
        return slow * max(min(64, size(a[1])), n) * TENSOR * (4 if wide[1] else 1) + sum(cost(x, kind, pace) for x in o.get("also", ()))
    if kind in ("iota", "sel"):
        return slow * ((0.13 if kind == "iota" else 0.17) + 2 * n * CYCLE)
    if kind == "tt":
        n *= 1 if "psum" in (SCRATCH[a[1][1]][0], SCRATCH[a[2][1]][0]) else 2
    elif kind != "act" and not any(wide):
        n /= 2
    return slow * max(64, n) * CYCLE


def late_(o, pace):
    return o["lag"] + o["hops"] * pace[4] + (o["hops"] > 1) * (0.6 + pace[3])


def refine(ops, deps, free_, order):
    N, above = len(ops), []
    for n in range(N):
        m = 0
        for j in deps[n]:
            m |= above[j] | 1 << j
        above.append(m)
    loose = {j for j, n in free_}
    near, far = [], []
    for n in range(N):
        inner = 0
        for j in deps[n]:
            inner |= above[j]
        keep = [j for j in deps[n] if j in loose or not inner >> j & 1]
        near.append([j for j in keep if (j, n) in free_ or ops[j]["kind"] == ops[n]["kind"] == "mm"])
        far.append([j for j in keep if j not in near[n]])
    names = ["v", "a", "p", "g", "s"]
    q = [names.index(o["q"]) if o["q"] else 5 for o in ops]
    both = [[[cost(o, o["other"][1] if k and o["other"] else o["kind"], p) for o in ops] for k in range(2)] for p in PACES]
    hold = [list(b[0]) for b in both]
    lag = [[late_(o, p) for o in ops] for p in PACES]
    out = [[x + p[3] for x in l] for l, p in zip(lag, PACES)]
    last = [n for n, o in enumerate(ops) if o["dma"]][-3:]
    turned = [0] * N

    def run(seq, at, s, end, fin):
        free, h, w = [0.0] * 6, hold[s], out[s]
        seen = 0
        for i in range(at - 1, -1, -1):
            k = q[seq[i]]
            if not seen >> k & 1:
                seen |= 1 << k
                free[k] = end[seq[i]]
                if seen == 7 and i < at - 400 or seen & 15 == 15:
                    break
        for i in range(at, N):
            n = seq[i]
            k = q[n]
            t = free[k]
            for j in near[n]:
                if end[j] > t:
                    t = end[j]
            for j in far[n]:
                if fin[j] > t:
                    t = fin[j]
            t += h[n]
            end[n] = t
            fin[n] = t + w[n]
            if k < 5:
                free[k] = t
        return max(end[n] + lag[s][n] for n in last)
    seq = list(order)
    ends, fins = [[0.0] * N for p in PACES], [[0.0] * N for p in PACES]
    base = [run(seq, 0, s, ends[s], fins[s]) for s in range(len(PACES))]
    now = best = float(len(PACES))
    kept, seed, arcs = (list(seq), list(turned)), [12345], None

    def draw(n):
        seed[0] = (seed[0] * 1103515245 + 12345) % 2147483648
        return (seed[0] >> 8) % n
    for step in range(MOVES):
        if arcs is None:
            seq.sort(key=lambda n: ends[0][n] - hold[0][n])
            pos, before, prev = [0] * N, [-1] * N, [-1] * 6
            for i, n in enumerate(seq):
                pos[n], before[n] = i, prev[q[n]]
                prev[q[n]] = n
            arcs = []
            for s in range(len(PACES)):
                end, fin = ends[s], fins[s]
                n = max(last, key=lambda n: end[n] + lag[s][n])
                while n >= 0:
                    t, up = end[n] - hold[s][n] - 1e-7, -1
                    for j in far[n]:
                        if fin[j] >= t:
                            up = j
                    for j in near[n]:
                        if end[j] >= t:
                            up = j
                    if up < 0 and q[n] < 5 and before[n] >= 0 and end[before[n]] >= t:
                        up = before[n]
                        arcs.append(n)
                    n = up
        n = arcs[draw(len(arcs))]
        b = before[n]
        for k in range(draw(4) * draw(3)):
            if before[b] >= 0:
                b = before[b]
        kind, flip = draw(5), -1
        if kind == 4:
            flip = n if ops[n]["other"] and draw(2) else b
            if not ops[flip]["other"]:
                continue
            new, at = seq, pos[flip]
            q[flip], turned[flip] = 1 - q[flip], 1 - turned[flip]
            for s in range(len(PACES)):
                hold[s][flip] = both[s][turned[flip]][flip]
        else:
            if above[n] >> b & 1:
                continue
            at, piece = pos[b], seq[pos[b]:pos[n] + 1]
            if kind < 2:
                m = above[n] | 1 << n
                piece = [x for x in piece if m >> x & 1] + [x for x in piece if not m >> x & 1]
            else:
                piece = [x for x in piece if x != b and not above[x] >> b & 1] + [x for x in piece if x == b or above[x] >> b & 1]
            new = seq[:at] + piece + seq[pos[n] + 1:]
        limit, total, tried = now + SLACK * (1 - step / MOVES) * draw(100) / 100, 0.0, []
        for s in range(len(PACES)):
            end, fin = list(ends[s]), list(fins[s])
            total += run(new, at, s, end, fin) / base[s]
            tried.append((end, fin))
            if s == 0 and total > ends[0][last[2]] / base[0] + 0.03:
                total = 99.0
                break
        if total <= limit:
            seq, now, arcs = list(new), total, None
            ends, fins = [x[0] for x in tried], [x[1] for x in tried]
            if now < best:
                best, kept = now, (list(seq), list(turned))
        elif flip >= 0:
            q[flip], turned[flip] = 1 - q[flip], 1 - turned[flip]
            for s in range(len(PACES)):
                hold[s][flip] = both[s][turned[flip]][flip]
    return kept


def refine(ops, deps, free_, order):
    N, above, S_ = len(ops), [], range(len(PACES))
    for n in range(N):
        m = 0
        for j in deps[n]:
            m |= above[j] | 1 << j
        above.append(m)
    loose = {j for j, n in free_}
    near, far, after = [], [], [[] for o in ops]
    for n in range(N):
        inner = 0
        for j in deps[n]:
            inner |= above[j]
        keep = [j for j in deps[n] if j in loose or not inner >> j & 1]
        near.append([j for j in keep if (j, n) in free_ or ops[j]["kind"] == ops[n]["kind"] == "mm"])
        far.append([j for j in keep if j not in near[n]])
        for j in keep:
            after[j].append((n, j in far[n]))
    q = ["vapgs".index(o["q"]) if o["q"] else 5 for o in ops]
    both = [[[cost(o, o["other"][1] if k and o["other"] else o["kind"], p) for o in ops] for k in range(2)] for p in PACES]
    hold = [list(b[0]) for b in both]
    lag = [[late_(o, p) for o in ops] for p in PACES]
    out = [[x + p[3] for x in l] for l, p in zip(lag, PACES)]
    turned, seed, seq, name = [0] * N, [12345], list(order), [str(o["a"][0][1]) for o in ops]

    def draw(n):
        seed[0] = (seed[0] * 1103515245 + 12345) % 2147483648
        return (seed[0] >> 8) % n

    def run(piece, s, free, end, fin, rest, then, final=(-1,) * 5):
        free, h, w, top, tip, final = list(free), hold[s], out[s], 0.0, -1, list(final)
        for n in piece:
            k = q[n]
            t = free[k]
            for j in near[n]:
                if end[j] > t:
                    t = end[j]
            for j in far[n]:
                if fin[j] > t:
                    t = fin[j]
            t += h[n]
            end[n] = t
            fin[n] = t + w[n]
            if k < 5:
                free[k], final[k] = t, n
            if t + rest[n] > top:
                top, tip = t + rest[n], n
        for k in range(5):
            if final[k] >= 0 and free[k] + then[k] > top:
                top, tip = free[k] + then[k], final[k]
        return top, tip

    def turn(n):
        q[n], turned[n] = 1 - q[n], 1 - turned[n]
        for s in S_:
            hold[s][n] = both[s][turned[n]][n]
    ends, fins = [[0.0] * N for s in S_], [[0.0] * N for s in S_]
    base = [run(seq, s, [0.0] * 6, ends[s], fins[s], lag[s], [0.0] * 6)[0] for s in S_]
    for a in [a for sweep in range(SWEEPS) for a in range(-(sweep % 2) * PIECE // 4, N, PIECE // 2)]:
        a, b = max(a, 0), min(a + PIECE, N)
        frees, rests, thens = [], [], []
        for s in S_:
            run(seq, s, [0.0] * 6, ends[s], fins[s], lag[s], [0.0] * 6)
        seq.sort(key=lambda n: ends[0][n] - hold[0][n])
        inside = set(seq[a:b])
        for s in S_:
            free, tail, then = [0.0] * 6, {}, [0.0] * 6
            for n in seq[:a]:
                free[q[n]] = ends[s][n] * (q[n] < 5)
            for n in reversed(seq[b:]):
                tail[n] = then[q[n]] = hold[s][n] + max([lag[s][n], then[q[n]] * (q[n] < 5)] + [tail[u] + w * out[s][n] for u, w in after[n]])
            frees.append(free)
            thens.append(then)
            rests.append({n: max([lag[s][n]] + [tail[u] + w * out[s][n] for u, w in after[n] if u in tail]) for n in inside})
        piece, arcs, kept = seq[a:b], None, None
        tops = [run(piece, s, frees[s], ends[s], fins[s], rests[s], thens[s]) for s in S_]
        for step in range(MOVES):
            if arcs is None:
                now = sum(tops[s][0] / base[s] for s in S_)
                if kept is None or now <= kept[0]:
                    kept = now, list(piece), [turned[n] for n in piece]
                piece.sort(key=lambda n: ends[0][n] - hold[0][n])
                pos, before, prev, arcs, lasts, high = {}, {}, [-1] * 6, [], [], [[(0.0, -1)] for s in S_]
                for i, n in enumerate(piece):
                    lasts.append(prev[:5])
                    pos[n], before[n] = i, prev[q[n]]
                    prev[q[n]] = n
                    for s in S_:
                        high[s].append(max(high[s][-1], (ends[s][n] + rests[s][n], n)))
                for s in S_:
                    end, fin, n = ends[s], fins[s], tops[s][1]
                    while n in inside:
                        t, up = end[n] - hold[s][n] - 1e-7, -1
                        for j in far[n]:
                            if fin[j] >= t:
                                up = j
                        for j in near[n]:
                            if end[j] >= t:
                                up = j
                        if up < 0 and q[n] < 5 and before[n] >= 0 and end[before[n]] >= t:
                            up = before[n]
                            arcs.append(n)
                        n = up
                if not arcs:
                    break
            n = arcs[draw(len(arcs))]
            v = before[n]
            for k in range(draw(4) * draw(3)):
                if before[v] >= 0:
                    v = before[v]
            kind, new = draw(5 + ANEW), piece
            if kind > 4:
                s, at = draw(len(PACES)), max(0, pos[n] - 10 - draw(40))
                part, behind = piece[at:pos[n] + 10 + draw(30)], piece[pos[n] + 10:]
                behind = piece[at + len(part):]
                way, then, shift, width = {}, list(thens[s]), {}, (1 + draw(6)) / 1000
                for x in reversed(behind):
                    way[x] = then[q[x]] = hold[s][x] + max([rests[s][x], then[q[x]] * (q[x] < 5)] + [way[u] + w * out[s][x] for u, w in after[x] if u in way])
                for x in reversed(part):
                    way[x] = hold[s][x] + max([rests[s][x], then[q[x]] * (q[x] < 5)] + [way[u] + w * out[s][x] for u, w in after[x] if u in way])
                for x in part:
                    way[x] += shift.setdefault(name[x], draw(100) * width)
                own, ready, left, pool = set(part), {}, {}, [[] for k in range(6)]
                for x in part:
                    ready[x] = max([0.0] + [ends[s][j] for j in near[x] if j not in own] + [fins[s][j] for j in far[x] if j not in own])
                    left[x] = sum(j in own for j in near[x] + far[x])
                    if not left[x]:
                        pool[q[x]].append(x)
                free, new = [ends[s][j] if j >= 0 else x for j, x in zip(lasts[at], frees[s])] + [0.0], []
                while len(new) < len(part):
                    t, k = min((max(free[k], min(ready[x] for x in c)), k) for k, c in enumerate(pool) if c)
                    x = max(pool[k], key=lambda x: way[x] - 2 * max(0.0, ready[x] - t))
                    pool[k].remove(x)
                    new.append(x)
                    t = max(t, ready[x]) + hold[s][x]
                    free[k] = t * (k < 5)
                    for u, w in after[x]:
                        if u in own:
                            ready[u] = max(ready[u], t + w * out[s][x])
                            left[u] -= 1
                            if not left[u]:
                                pool[q[u]].append(u)
                new += behind
            elif kind == 4:
                n = n if ops[n]["other"] and draw(2) else v
                if not ops[n]["other"]:
                    continue
                turn(n)
                at = pos[n]
                new = piece[at:]
            elif above[n] >> v & 1:
                continue
            else:
                at = pos[v]
                part = piece[at:pos[n] + 1]
                first = [x == n or above[n] >> x & 1 for x in part] if kind < 2 else [x != v and not above[x] >> v & 1 for x in part]
                new = [x for x, f in zip(part, first) if f] + [x for x, f in zip(part, first) if not f] + piece[pos[n] + 1:]
            total, tried, limit = 0.0, [], SLACK * (1 - step / MOVES) * draw(100) / 100 + 1e-9
            for s in S_:
                end, fin = ends[s][:], fins[s][:]
                free = [end[j] if j >= 0 else x for j, x in zip(lasts[at], frees[s])] + [0.0]
                top = max(run(new, s, free, end, fin, rests[s], thens[s], lasts[at]), high[s][at])
                total += top[0] / base[s]
                tried.append((end, fin, top))
                if total > sum(tops[r][0] / base[r] for r in range(s + 1)) + 0.004:
                    total = 99.0
                    break
            if total <= now + limit:
                piece, arcs = piece[:at] + new, None
                ends, fins, tops = ([x[k] for x in tried] for k in range(3))
            elif kind == 4:
                turn(n)
        for n, k in zip(kept[1], kept[2]):
            if turned[n] != k:
                turn(n)
        seq[a:b] = kept[1]
    return sum(run(seq, s, [0.0] * 6, ends[s], fins[s], lag[s], [0.0] * 6)[0] / PACES[s][0] for s in S_), seq, turned


def arrange(ops):
    if not ORDERS:
        ORDERS["all"] = lay_out(ops)
    order, turned = ORDERS["all"]
    for o, k in zip(ops, turned):
        if o["other"]:
            if k:
                o["q"], o["kind"], o["f"], o["a"] = o["other"]
            o["e"] = o["q"]
    return [ops[n] for n in order]


def lay_out(calls):
    deps, ops, unit = needs(calls, True), [], []
    for n, o in enumerate(calls):
        u = ops[-1] if ops else o
        outer = {j for j in deps[n] if calls[j]["kind"] != "mm"}
        if o["kind"] == u["kind"] == "mm" and o["a"][0][1] == u["a"][0][1] and outer <= u["outer"] and cost(u, "mm", PACES[0]) + cost(o, "mm", PACES[0]) < UNIT:
            u["members"].append(n)
            u["also"].append(o)
        else:
            ops.append(dict(o, members=[n], also=[], outer=outer))
        unit.append(len(ops) - 1)
    order, turned = lay_units(ops, [{unit[j] for n in o["members"] for j in deps[n]} - {k} for k, o in enumerate(ops)])
    return [n for k in order for n in ops[k]["members"]], [turned[k] for k in unit]


def lay_units(ops, deps):
    N = len(ops)
    last, free_ = {}, set()
    for n, o in enumerate(ops):
        file = o["file"] if o.get("file") else "iota" if o["kind"] == "iota" else o["q"] if o["kind"] in ("dma", "send") else o["a"][0][1] if o["a"][0][1] in FILES else None
        if file in last and last[file] not in deps[n]:
            deps[n].add(last[file])
            free_.add((last[file], n))
        if file:
            last[file] = n
        if o["kind"] == "arrive":
            deps[n].add([j for j in range(n) if ops[j]["e"] == o["after"]][0])
    hold = [cost(o, o["kind"], PACES[0]) for o in ops]
    lag = [late_(o, PACES[0]) for o in ops]
    gap = lambda j, n: 0.0 if (j, n) in free_ or ops[j]["kind"] == ops[n]["kind"] == "mm" else lag[j] + PACES[0][3]
    users = [[] for _ in ops]
    for n in range(N):
        for j in deps[n]:
            users[j].append(n)
    way, alike = [0.0] * N, {}
    for n in reversed(range(N)):
        key = (ops[n]["q"], ops[n]["a"][0][1])
        way[n] = hold[n] + max([gap(n, u) + way[u] for u in users[n]] + [lag[n]] + [way[u] for u in alike.get(key, ()) if u - n < 5])
        alike[key] = (n,)

    def lay(before, after, wait, rank_, ready):
        left, free, end, pool, order = [len(d) for d in before], {}, [0.0] * N, {}, []
        for n in range(N):
            if not left[n]:
                pool.setdefault(str(ops[n]["q"]), []).append(n)
        while len(order) < N:
            t, q = min((max(free.get(q, 0.0), min(ready[n] for n in c)), q) for q, c in pool.items() if c)
            n = max((n for n in pool[q] if ready[n] <= t), key=lambda n: (rank_[n], -n))
            soon = [u for u in pool[q] if t < ready[u] < t + hold[n] and rank_[u] > rank_[n]]
            if soon:
                u = max(soon, key=lambda u: rank_[u] - ready[u])
                if max(rank_[u], hold[u] + rank_[n]) + 2 * (ready[u] - t) < max(rank_[n], hold[n] + rank_[u]):
                    n, t = u, ready[u]
            pool[q].remove(n)
            free[q] = end[n] = t + hold[n]
            order.append(n)
            for u in after[n]:
                ready[u] = max(ready[u], end[n] + wait(n, u))
                left[u] -= 1
                if not left[u]:
                    pool.setdefault(str(ops[u]["q"]), []).append(u)
        return max(e + x for e, x in zip(end, lag)), order, end
    found, first = [], way
    for start in range(STARTS):
        best, way = None, first
        for k in range(start * PASSES, (start + 1) * PASSES):
            laid = lay(deps, users, gap, way, [0.0] * N)
            best = min(best or laid, laid)
            shake = {}
            ends = [e + (int(e * 5 / best[0]) == k % 5) * shake.setdefault((o["q"], o["a"][0][1]), SHAKE * math.sin(n * 12.9898 + k * 78.233 + n * k))
                    for n, (e, o) in enumerate(zip(best[2], ops))]
            way = lay(users, deps, lambda n, j: gap(j, n), ends, list(lag))[2]
        found.append(refine(ops, deps, free_, best[1]))
    SPANS["log"] = [round(x[0], 1) for x in found]
    return min(found)[1:]


def emit(g, T, ops):
    queue = {"v": g.vector, "a": g.scalar, "p": g.tensor, "g": g, "s": g.sync}
    known, count, need = {q: {} for q in queue}, {}, set()
    for o, deps in zip(ops, needs(ops, False)):
        e = o["e"]
        count[e] = count.get(e, 0) + 1
        o["pos"] = count[e]
        o["waits"] = []
        if o["q"] is None:
            o["clock"] = {e: 1}
            continue
        k = known[o["q"]]
        for j in sorted(deps, reverse=True):
            d = ops[j]
            if k.get(d["e"], 0) < d["pos"]:
                o["waits"].append(j)
                need.add(j)
                for x, y in d["clock"].items():
                    k[x] = max(k.get(x, 0), y)
        o["clock"] = dict(k)
        o["clock"][e] = o["pos"]
    raised = {}

    def real(a):
        if isinstance(a, tuple) and a[0] == "ap":
            return T[a[1]][a[2]]
        if isinstance(a, tuple) and a[0] == "ind":
            return real(a[1]).indirect(real(a[2]))
        return a
    for n, o in enumerate(ops):
        if o["q"] is None:
            continue
        q = queue[o["q"]]
        for j in o["waits"]:
            q.wait_ge(T.sem[ops[j]["sem"]], ops[j]["val"])
        ins = o["f"](q, *[real(a) for a in o["a"]])
        if o["e"] in queue:
            if n in need:
                raised[o["e"]] = raised.get(o["e"], 0) + 1
                o["sem"], o["val"] = "c" + o["e"], raised[o["e"]]
                ins.then_inc(T.sem[o["sem"]], 1)
        elif o["dma"]:
            ins.then_inc(T.sem[o["sem"]], 16)
    for n, o in enumerate(ops):
        if o["dma"] and n not in need:
            queue[o["q"]].wait_ge(T.sem[o["sem"]], 16)


def rank_program(g, core, T, topo):
    rank = T.rank_of(core)
    if rank is None:
        relay_program(g, core, T, topo)
        return
    cores = list(T.cores)
    ops, ndma, sent, loaded = [], [0], [0], [0]

    def either(first, second):
        first()
        second()
        o = ops.pop()
        ops[-1].update(other=(o["q"], o["kind"], o["f"], o["a"]), e="x%d" % len(ops))

    def rec(kind, q, f, out, *args, e=None, sem=None, val=None, lag=0.0, after=None, group=None, hops=0):
        r, w = [], []
        for a in args:
            if isinstance(a, tuple):
                r += [a] if a[0] == "ap" else [a[1], a[2]]
        full = False
        if out is not None:
            if out[0] == "ap":
                w.append(out)
                full = out[2][0] == ALL
            else:
                w.append(out[1])
                r.append(out[2])
        acc = [(span(a), False) for a in r] + [(span(a), True) for a in w]
        ops.append({"kind": kind, "q": q, "e": e or q, "f": f, "a": ([] if out is None else [out]) + list(args), "full": full, "group": group,
                    "acc": [x for x in acc if x[0] is not None], "dma": kind == "dma", "sem": sem, "val": val, "lag": lag, "after": after,
                    "hops": hops, "other": None})

    def dma(q, out, in_, kb):
        loaded[0] += kb
        rec("dma", q, lambda x, o, i: x.dma_start(o, i), out, in_, e="d%d" % ndma[0], sem="d%d" % ndma[0], val=16, lag=2.0 + loaded[0] / 320)
        ndma[0] += 1

    def cp(out, in_):
        rec("cp", "v", lambda x, o, i: x.tensor_copy(o, i), out, in_)

    def ms(out, c):
        rec("ms", "v", lambda x, o: x.memset(o, c), out)

    def tt(out, a, b, op):
        rec("tt", "v", lambda x, o, i, j: x.tensor_tensor(o, i, j, op), out, a, b)

    def ts(out, a, s1, op0, s2=None, op1=None):
        if op1 is None:
            rec("ts", "v", lambda x, o, i, s: x.tensor_scalar(o, i, s, None, op0), out, a, s1)
        else:
            rec("ts", "v", lambda x, o, i, s, u: x.tensor_scalar(o, i, s, u, op0, op1), out, a, s1, s2)

    def scan(out, d0, d1, init, op0, op1):
        rec("scan", "v", lambda x, o, i, j: x.tensor_tensor_scan(o, i, j, init, op0, op1), out, d0, d1)

    def act(out, in_, func, bias=0.0, scale=1.0):
        rec("act", "a", lambda x, o, i, b, s: x.activation(o, i, func, bias=b, scale=s), out, in_, bias, scale)

    def mm(out, l, r, start=True, stop=True, bar=False):
        rec("mm", "p", lambda x, o, i, j: x.matmul(o, i, j, start, stop), out, l, r, group=(start, stop or bar))

    def iota(out, pat, base=0, cm=0):
        if SCRATCH[out[1]][2] == I32:
            rec("iota", "g", lambda x, o: x.iota(o, pat, base, cm), out)
        else:
            rec("iota", "g", lambda x, o: x.iota(o, pat, base, cm, allow_small_or_imprecise_dtypes=True), out)

    def copy(out, in_, n):
        rec("sel", "g", lambda x, o, i: x.affine_select(o, i, [[0, n]], ALU.is_ge, 0.0, 0, 0), out, in_)

    def send(t):
        hop, letter = first_hop(rank, t, cores, topo)
        src = "O%d" % t
        rec("send", "g", lambda x, i: hand(g, T, topo, core, hop, letter + src[1:], src), None, V(src, ALL), e="x" + src)
        sent[0] += ENG

    def arrive(t):
        hops = max(1 if first_hop(r, t, cores, topo)[0] == target(r, t, cores) else 2 for r in range(len(cores)))
        land = "I%d" % t
        rec("arrive", None, None, V(land, ALL), e="s" + land, sem="s" + land, val=ENG, after="xO" + land[1:], hops=hops, lag=1.5 * hops * (t == 0))

    EQ, MUL, ADD, SUB, MAX, MIN, GT = ALU.is_equal, ALU.mult, ALU.add, ALU.subtract, ALU.max, ALU.min, ALU.is_gt
    SHR, AND = ALU.arith_shift_right, ALU.bitwise_and
    whole = lambda n: V(n, ALL)
    IW, IS = col("IC", 0, W), col("IC", 0, W + DUM)
    XW, XS, NUM = col("X", OFF, OFF + W), col("X", OFF, OFF + W + 16), col("NUM", OFF, OFF + W + 16)
    R1, R8, R16, R48 = sl(0, 1), sl(0, 8), sl(0, 16), sl(0, 48)
    pd_ = lambda k, rows=ALL: cf("PD", k, k + 1, rows=rows)
    gcol, rcol = pd_(0), pd_(1)
    Pc, BO, GL, OL, LR8 = cf("P", 0, 1), cb("BO", 96, 104), col("GL", 0, 8), col("OL", 0, 32), col("LR8", 0, 8)
    ki = lambda k, n=1: col("KI", 8 * k, 8 * (k + n))
    tf = lambda k, n=1: col("TF", 8 * k, 8 * (k + n))
    part = lambda name, k, n=L: col(name, n * k, n * k + n)

    def spread(out, src):
        tt(whole(out), IND(src, LR8), cb("MK"), MUL)

    ms(cb("ONES"), 1.0)
    ms(whole("AW"), 0)
    ops[0]["file"] = ops[1]["file"] = "fills"
    dma("s", whole("GI"), V("gate", ALL), 4)
    dma("a", whole("A"), V("acc0", ALL), 32)
    loads = {"I": (col("IT", 0, W), V("icol", ALL), 1024), "A": (V("AW", sl(0, 128, 4)), V("alt", ALL), 256), "X": (XW, V("pat", ALL), 512)}
    for k in LOADS:
        if k == "A":
            loaded[0] -= MOVED
        dma("s", *loads[k])
    loaded[0] = 0
    for k in range(2):
        dma("a", col("TH", 0, 4, rows=sl(8 * k, 8 * k + 8)), V("th", ALL), 0)

    iota(col("PI", 0), [[0, 1]], 0, 1)
    iota(cf("P"), [[-1, 8]], 0, 1)
    iota(cb("J"), [[1, 128]])
    iota(cb("F16"), [[0, 8], [1, 16]])
    iota(cb("JG"), [[1, 8], [0, 16]])
    iota(whole("LI"), [[1, 8]])

    def fill(out, n, c):
        act(out, cb("ONES", 0, n), AF.Identity, scale=float(c))

    def times(out, in_, c):
        act(out, in_, AF.Identity, scale=c)

    def where(out, pat, base=0, c=1.0, in_=None, op=ALU.not_equal, cm=-1):
        in_ = in_ or (col("PM3", 0, span(out)[4]) if SCRATCH[out[1]][2] == F else cb("ZERO", 0, span(out)[4]))
        rec("sel", "g", lambda x, o, i: x.affine_select(o, i, pat, op, c, base, cm), out, in_)
        ops[-1]["file"] = "iota"
    fill(cb("ZERO"), L, 0)
    fill(whole("PM3"), L, 0)
    iota(cf("FV"), [[1, 144]], -15)
    for a in range(4):
        where(cb("SELO", L * a, L * a + L), [[16, 8], [1000, 4], [4, 4]], -1000 * a)
    where(cf("SEL8"), [[0, 4], [1, 32]])
    where(cf("SELB"), [[1, 8], [0, 16]])
    iota(cb("F3"), [[8, 8], [0, 2], [1, 8]])
    iota(cb("F8"), [[8, 16], [0, 8]])
    iota(cf("PK", 0, 4), [[32, 4]])
    where(cb("PRM"), [[1, 32], [32, 4]])
    iota(cb("RS4"), [[0, L], [-32768, 4]], 32768)
    iota(cb("FG"), [[1, 8], [0, 18], [32, 3]], 32)
    iota(cb("FS"), [[1, 8], [0, 18]])
    iota(cf("FR"), [[0, 8], [8, 2], [1, 9]], 4 * SH + 6)
    for h in range(2):
        where(cb("PERM", 72 * h, 72 * h + 72), [[16, 4], [8, 2], [1, 9]], 64 * h - 1)
    where(cb("XSEL"), [[16, 8], [-4, 6]], 20)
    where(cb("K2"), [[1, 8], [-32, 6]], 160, CNT)
    iota(cf("XCONST"), [[0, 8], [-1, 6]], 5 * SH + 6)
    iota(cb("G5"), [[1, 8], [0, 6]])
    where(cb("TRI2"), [[1, L]], 0, 4096.0, op=GT)
    for k in range(8):
        ts(cb("FSEL", L * k, L * k + L), cb("F8"), cf("P", k, k + 1), EQ, 2.0, MUL)
    where(cb("TRIP"), [[1, L]], 0, 0.0, cb("ONES"), GT)
    where(cb("TRIP"), [[1, L]], 0, -float(L), cb("TRIP"))
    iota(cf("DUML"), [[16, 3]], W + 1)
    iota(cf("SPARE"), [[16, 8]], W)
    iota(cb("S96"), [[-1, 2], [1, 48]], -L)
    iota(cf("RST"), [[0, 144]])
    ms(col("X", 0, OFF), 0.0)
    iota(whole("NUM"), [[1, OFF + W + 16]], -OFF)
    ms(col("IT", W, W + 64), 0)
    iota(whole("NT"), [[2, W // 2 + 8], [-1, 2]], 1)
    fill(col("IC", W, W + DUM), DUM, 0)
    fill(col("YC", W, W + DUM), DUM, 0)
    fill(col("X", OFF + W, OFF + W + 16), 16, -1024)
    fill(cf("RST", 0, 144, 18), 8, 4 * BIG)
    for h in range(4):
        fill(col("M3", 216 * (h // 2) + 1 + h % 2, 216 * (h // 2 + 1), 3), 72, 4 * BIG)
    fill(cf("RS8"), 64, 0)
    fill(cf("RS8", 0, 64, 8), 8, -BIG)
    for a in (0, 49, 98):
        fill(cf("D0", a, a + 49), 49, 4096)
    fill(cf("D0", 0, 147, 49), 3, -4 * BIG)
    fill(cf("NE", 48, 147, 49), 3, -BIG)
    fill(cb("NM16"), 128, 1)
    fill(cb("NM16", 0, L, 16), 8, 0)
    for name, n, c in (("O16", L, 16), ("C1024", L, -1024), ("THREE", L, 3)):
        fill(cb(name), n, c)
    fill(cb("MAG", 0, 8), 8, 3 * BIG)
    fill(cb("MAG", 8, 16), 8, -3 * BIG)
    fill(cb("BO", 0, 96), 96, 0)
    fill(cb("BO", 104, 224), 120, 0)
    if EQV[0] == 2:
        act(col("GE2", 0, 16), cb("ONES", 0, 16), AF.Sigmoid, scale=STEEP)
        ops[-1].update(kind="table", file="H")
    else:
        fill(col("GE2", 0, 16), 16, 1)
    fill(col("GE3", 0, 16), 16, 1)
    for k, (s1, s2) in enumerate([(4, 7), (0, 15), (1, 63), (3, 15), (0, 1), (0, 112), (0, 7), (0, 31), (3, 1)]):
        ts(col("PI", 8 + k), col("PI", 0), s1, SHR, s2, AND)
    cp(cf("PD", 0, 9), col("PI", 8, 17))
    cp(LR8, whole("LI"))
    ts(col("LR8", 8, 16), whole("LI"), 16.0, MUL, 15.0, ADD)
    ts(BO, cb("J", 0, 8), gcol, EQ)
    ts(cb("IDN"), cb("J"), Pc, EQ)
    ts(cb("MK"), cb("F16"), rcol, EQ)
    ts(cb("BLKB"), cb("JG"), gcol, EQ)
    ts(cb("WIDE"), cf("FV"), pd_(5), EQ)
    ts(pd_(18), rcol, 0.0, EQ)
    times(cb("W0"), cb("WIDE"), pd_(18))
    ts(pd_(14), pd_(4), -2.0, MUL, 1.0, ADD)
    ts(pd_(15), rcol, 1.0, ADD)
    ts(pd_(27), rcol, -1.0, MUL)
    ts(pd_(16), Pc, 8.0, EQ, BIG / 2, MUL)
    ts(pd_(19), pd_(8), 16.0, MUL, -16.0, ADD)
    ts(pd_(20), pd_(8), -1.0, MUL)
    ts(cb("GW"), cb("FG"), Pc, EQ, -BIG / 2, MUL)
    act(cb("GW"), cb("GW"), AF.Identity, bias=pd_(16))
    ts(cb("THS", 0, L), cb("JG"), pd_(6), EQ)
    fill(cb("THS", L, 2 * L), L, 0)
    times(cb("BO4"), cb("BO"), 4.0)
    times(cb("NBO4"), cb("BO"), -4.0)
    ts(pd_(21), rcol, 15.0, EQ, FINE, MUL)
    ts(pd_(22), rcol, 15.0, EQ, 256.0, MUL)
    ts(pd_(23), rcol, 15.0, EQ, -FINE - 2, MUL)
    ts(pd_(23), pd_(23), 2.0, ADD)
    ts(pd_(24), rcol, 15.0, EQ, 1 - 1 / FINE, MUL)
    ts(pd_(24), pd_(24), 1 / FINE, ADD)
    ts(pd_(28), rcol, 15.0, EQ, FINE + 1, MUL)
    ts(pd_(28), pd_(28), -1.0, ADD)
    ts(pd_(29), Pc, 8.0, EQ, PEN / 64, MUL)
    ts(cf("PK", 4, 8), cf("PK", 0, 4), 32.0, ADD, 96.0, MIN)
    ts(cf("PK", 8, 12), cf("PK", 4, 8), Pc, GT)
    ts(cf("PK", 12, 16), cf("PK", 0, 4), Pc, GT, -2.0, MUL)
    tt(cf("PK", 8, 12), cf("PK", 8, 12), cf("PK", 12, 16), ADD)
    ts(cf("PK", 16, 20), cf("PK", 4, 8), pd_(29), MUL)
    ts(cb("S32"), cb("JG"), pd_(7), EQ, PEN / 2, MUL)
    for k in range(4):
        act(cb("PEN", L * k, L * k + L), cb("S32"), AF.Identity, bias=cf("PK", 16 + k, 17 + k), scale=cf("PK", 8 + k, 9 + k))
    ts(pd_(25), Pc, 8.0, EQ, float(RK), MUL)
    ts(pd_(30), Pc, 9.0, EQ, float(OFF), MUL)
    ts(cb("RANK"), cb("FS"), pd_(7), EQ, float(SH * RK), MUL)
    act(cf("FR"), cf("FR"), AF.Identity, bias=pd_(30), scale=pd_(25))
    tt(cb("RANK"), cb("RANK"), cf("FR"), ADD)
    for k in range(3):
        fill(cb("GW", k, 432, 27), 16, 0)
    ts(pd_(11), pd_(16), 2.0, MUL)
    times(cb("GW", 0, 432, 54), cb("ONES", 0, 8), pd_(11))
    ts(pd_(26), Pc, -float(W), ADD)
    times(cb("NMK"), cb("MK", 0, 16), -1.0)
    act(cb("NMK1"), cb("MK"), AF.Identity, bias=1.0, scale=-1.0)
    act(cf("SPARE"), cf("SPARE"), AF.Identity, bias=pd_(27), scale=-1.0)
    cp(cb("XSUM"), cb("IDN"))
    times(cb("XSUM", 15, L, 16), BO, pd_(24))
    times(cf("WS", 0, 8), BO, pd_(23))
    times(cf("WS", 8, 16), BO, pd_(21))
    ts(cb("AS", 0, L), cb("BLKB"), pd_(28), MUL)
    ts(cb("AS", L, 2 * L), cb("BLKB"), pd_(21), MUL, -1.0, MUL)
    for k in range(8):
        act(cb("CK", 8 * k, 8 * k + 8), BO, AF.Identity, bias=-8192.0, scale=12288.0)
    for out, src, c in ((cf("NIF"), cb("IDN"), -1.0), (cf("BOF"), BO, 1.0), (cb("KID"), cb("IDN"), FAR), (cb("NKID"), cb("IDN"), -FAR), (cb("NID"), cb("IDN"), -1.0), (cb("K4"), cb("IDN"), -4096.0 / (BIG if EQV[0] == 2 else 1)), (cb("BOS"), BO, 1 / BIG),
                        (cf("WT"), cb("BLKB"), pd_(15))):
        times(out, src, c)
    ts(pd_(31), Pc, 10.0, EQ, 2 * CNT, MUL)
    tt(pd_(31), pd_(31), pd_(30), ADD)
    act(cf("XCONST"), cf("XCONST"), AF.Identity, bias=pd_(31), scale=pd_(25))
    ts(cb("G5"), cb("G5"), pd_(7), EQ, -CNT / 2, MUL)
    tt(cb("K2"), cb("K2"), cb("G5"), ADD)
    tt(cb("K2"), cb("K2"), cf("XCONST"), ADD)
    ts(pd_(17), pd_(31), 4096.0, MIN)
    ts(pd_(13), pd_(25), float(NONE), MUL, pd_(17), ADD)
    times(cb("K2", 1, 48, 6), cb("ONES", 0, 8), pd_(13))
    cp(cb("RANK", 0, 144, 9), cb("K2", 0, 48, 3))
    fill(cb("PERM", 0, 144, 9), 16, 0)
    act(cf("DUML"), cf("DUML"), AF.Identity, bias=rcol)
    act(cf("CPOS"), cf("DUML"), AF.Identity, bias=-4096.0 * (W + 48), scale=4096.0)
    for k in range(8):
        either(lambda: ts(cb("SELG", L * k, L * k + L), cb("ONES"), cf("BOF", k, k + 1), MUL), lambda: times(cb("SELG", L * k, L * k + L), cb("ONES"), cf("BOF", k, k + 1)))
    cp(cb("XSEL", 1, 48, 6), cb("XSEL", 2, 48, 6))
    ts(cb("SIG"), cb("F3"), pd_(2), EQ, -1.0, MUL)
    ts(cb("DEL"), cb("F3"), pd_(2), EQ)
    times(cb("DEL"), cb("DEL"), pd_(14))
    ts(cb("WM"), cb("J", 0, 16), pd_(3), EQ, -BIG, MUL)
    cp(cf("THF", rows=R8), col("TH", 0, 4, rows=R8))
    mm(col("PQ", 0, 4), cf("SEL8", rows=R8), cf("THF", rows=R8))
    mm(col("PQ", 4, 8), cf("SELB", rows=R8), cf("THF", rows=R8))
    act(cf("THC"), col("PQ", 0, 4), AF.Identity, bias=-0.5, scale=-1.0)
    act(cf("THG"), col("PQ", 4, 8), AF.Identity, bias=-0.5, scale=-1.0)
    ts(col("TH", 4, 8), col("TH", 0, 4), 4, SHR)
    ts(col("TH", 8, 12), col("TH", 0, 4), 15, AND)
    ts(cf("THP", 0, 4, rows=R16), col("TH", 4, 8), pd_(19, R16), MUL)
    ts(cf("THP", 4, 8, rows=R16), col("TH", 8, 12), pd_(20, R16), MUL)
    tt(cf("THP", 8, 12, rows=R16), cf("THP", 0, 4, rows=R16), cf("THP", 4, 8, rows=R16), ADD)
    for t in range(RO):
        times(cb("NTH", L * t, L * t + L, rows=R16), cb("ONES", rows=R16), cf("THP", 8 + t, 9 + t, rows=R16))

    def widen(parts=WIDEN):
        for a, b, how in parts:
            for j in range(4):
                o, i = col("A4", 4 * a + j, 4 * b, 4), col("A", a, b)
                copy(o, i, b - a) if how[0] == "g" else gather(o, i, how[0] == "v")
            b = min(b, NV)
            for j in range(4 * (a < b)):
                o, i = col("AR", 16 * a + j, 16 * b, 4), col("A4", 4 * a, 4 * b)
                copy(o, i, 4 * (b - a)) if how[1] == "g" else gather(o, i, how[1] == "v")

    def gather(out, in_, on_vector, add=None):
        forms = (lambda: cp(out, in_), lambda: act(out, in_, AF.Copy))
        if add:
            forms = (lambda: ts(out, in_, add, ADD), lambda: act(out, in_, AF.Identity, bias=add))
        either(*(forms if on_vector else forms[::-1]))

    def options():
        cp(whole("R"), IND(col("AW", 0, W), GL))
        for a in range(4):
            mm(col("PW", 256, 288), cb("SELO", L * a, L * a + L), col("R", a, L, 4), a == 0, a == 3)
        cp(OL, col("PW", 256, 288))
        alike(0)

    def gates(c):
        if EQV[0] == 2:
            ts(whole("cT"), c, -STEEP, MUL, -math.log(511), ADD)
        else:
            cp(whole("cT"), c)

    def alike(at):
        for h in range(2):
            if EQAT[h] != at:
                continue
            bank = EQB[h]
            for k in range(4 * h, 4 * h + 4):
                mm(part(bank, k % 4), cb("SELG", L * k, L * k + L), whole("CMG"), True, False)
                mm(part(bank, k % 4), cb("IDN"), cb("TRI2"), False, True)
            for k in range(4 * h, 4 * h + 4):
                if EQV[h] == 2:
                    act(part("EQ2", k), part(bank, k % 4), AF.Sigmoid, bias=col("cT", k), scale=STEEP)
                elif EQV[h]:
                    ts(part("EQ2", k), part(bank, k % 4), col("cT", k), EQ, 4096.0, MUL)
                else:
                    act(part("AB2", k), part(bank, k % 4), AF.Abs, bias=col("cT", k), scale=-1.0)
            for k in range(2 * h, 2 * h + 2) if not EQV[h] else ():
                either(lambda: act(part("EQ2", k, 256), part("AB2", k, 256), AF.Relu, bias=4096.0, scale=-4096.0),
                       lambda: ts(part("EQ2", k, 256), part("AB2", k, 256), 0.0, EQ, 4096.0, MUL))

    def apart(b, bank):
        n = L - N2V
        r = 16 // NB2
        for j in range(r):
            mm(col(bank, j, n * r, r), cb("IDN"), col("G2", 16 * N2V + r * b + j, 2048, 16), j == 0, False)
        for j in range(r):
            mm(col(bank, j, n * r, r), cb("NID"), col("XC2", N2V, L), False, j == r - 1)
        act(V("H2", ALL, sl(N2V, L), sl(r * b, r * b + r)), col(bank, 0, n * r), AF.Abs)

    def far(at):
        if FAT == at and MAX2:
            mm(col(F2B, 0, 256), whole("XC2"), cb("AS"), True, False)
            for p in range(16):
                mm(col(F2B, p, 256, 16), col("D2", p, 2048, 16), cf("WS"), False, p == 15)
            ts(whole("RR2"), part(F2B, 1), ROUND, ADD, ROUND, SUB)
            act(whole("AD2"), whole("RR2"), AF.Abs, bias=-256.0, scale=1 / FINE)
            tt(whole("SV2"), part(F2B, 0), whole("RR2"), ADD)
            mm(part(F2B, 0), cb("NID"), whole("AD2"), True, False)
            mm(part(F2B, 0), cf("NIF"), whole("SV2"), False, True)
            farthest(L, "2", part(F2B, 0), F2B, L, MIN)
        elif FAT == at:
            for p in range(16):
                mm(col(F2B, p, L, 16), V("H2", ALL, ALL, p), BO)
            farthest(L, "2", part(F2B, 0), F2B, L)

    def farthest(n, s, sums, bank, at, top=MAX):
        rows, GE, o, sums = sl(0, n), "GE" + s, col(bank, at, at + n), V(sums[1], sl(0, n), sums[2][1])
        scan(V("PM" + s, rows, ALL), cb("NM16", 0, L, rows=rows), sums, 0.0, MUL, top)
        if "PX" in ONV:
            scan(V("PX", rows, ALL), cb("NM16", 0, L, rows=rows), sums, 0.0, MUL, top)
            tt(col(GE, 16, 144), IND(whole("PX"), col("LR8", 8, 16)), whole("PM" + s), EQ)
        else:
            gather(col("PX", 0, 8), col("PM" + s, 15, L, 16), True)
            tt(col(GE, 16, 144), IND(col("PX", 0, 8), LR8), whole("PM" + s), EQ)
        mm(o, cb("MK", rows=R1), cb("ONES", 0, n, rows=R1), True, False)
        mm(o, col(GE, 16, 144, rows=rows), cb("IDN", 0, n, rows=rows), False, False)
        mm(o, col(GE, 15, 143, rows=rows), cb("NID", 0, n, rows=rows), False, True)
        if s == "2" and "DV2" not in ONV:
            o = part(bank, 2)
            mm(o, cb("NMK1", rows=R1), cb("ONES", rows=R1), True, False)
            mm(o, col(GE, 16, 144), cb("NID"), False, False)
            mm(o, col(GE, 15, 143), cb("IDN"), False, True)

    def patch(n, s, bank, lst):
        mm(col(bank, 0, n), cf("WT"), whole("CF" + s), True, False)
        mm(col(bank, 0, n), cf("WT"), whole("WV" + s), False, True)
        act(whole("YP" + s), col(bank, 0, n), AF.Copy)
        cp(IND(col("YC", 0, W + DUM), lst), whole("YP" + s))

    def abroad(t):
        more = t < RO - 1
        la, ld, lb = col("I%d" % t, 0, 3), col("LD", 0, 3), col("I%d" % t, 4, 7)
        place = lambda p: part("B%d" % (p // 8), p % 8, 48)
        arrive(t)
        cp(whole("CO3"), IND(IS, la))
        gather(whole("XC3"), IND(XS, la), more and "XC3" in ONV)
        for p in range(16):
            mm(place(p), cb("NID"), whole("XC3"), p % 8 == 0, False)
        for h in range(2):
            gather(part("G3", h, 384), IND(XS, part("CO3", h, 24)), "G3" + "ab"[h] in ONV if more else h)
        for p in range(16):
            mm(place(p), cb("IDN"), col("G3", p, 768, 16), False, p % 8 == 7)
        for b in range(2):
            act(part("H3", b, 384), col("B%d" % b, 0, 384), AF.Abs)
            for p in range(8 * b, 8 * b + 8):
                mm(V(F3B[0], R48, sl(F3B[1] + p, F3B[1] + L, 16)), part("H3", p, 48), BO)
        gather(whole("CF3"), IND(IS, la), more and "CF3" in ONV)
        gather(whole("AG"), IND(NUM, la), more and "AG" in ONV)
        cp(col("AL", 0, 3), la)
        tt(cf("D0", 48, 147, 49), col("AL", 0, 3), cf("CPOS"), ADD)
        for u in range(3):
            ts(cf("NE", 49 * u, 49 * u + 48), whole("AG"), col("AL", u), ALU.not_equal, -BIG, MUL)
        scan(whole("SD"), cf("D0"), cf("NE"), 0.0, ADD, MAX)
        tt(col("ZT", 0, 3), col("SD", 48, 147, 49), cf("DUML"), MIN)
        cp(ld, col("ZT", 0, 3))
        if more:
            gather(whole("BG"), IND(whole("XT"), lb), "BG" in ONV)
            cp(IND(whole("IT"), ld), whole("BG"))
            tt(whole("DP"), IND(col("IT", 0, W), OL), whole("A4"), SUB)
        tt(whole("DV3"), IND(whole("NT"), lb), whole("CF3"), SUB)
        farthest(48, "3", col(F3B[0], F3B[1], F3B[1] + L), F3B[2], F3B[3])
        tt(whole("WV3"), col(F3B[2], F3B[3], F3B[3] + 48), whole("DV3"), MUL)
        if more:
            tt(IND(IS, ld), whole("WV3"), whole("CF3"), ADD)
        else:
            patch(48, "3", "PS", ld)

    for k, bank in enumerate(("B0", "B1", "DL", "PQ")):
        mm(whole(bank), cb("XSUM"), col("X", OFF + 512 * k, OFF + 512 * k + 512))
        gather(part("XF", k, 512), whole(bank), k in XFV, pd_(22))
    for h in range(2):
        copy(col("XT", h, W + 16, 2), col("X", OFF + 1 - h, OFF + W + 16, 2), W // 2 + 8)
    widen(((0, NV, "av"),))
    cp(GL, whole("GI"))
    spread("CMG", col("GI", 0, 8))
    mm(col("PS", 0, 8), whole("CMG"), BO)
    gates(col("PS", 0, 8))
    cp(ki(4), col("PS", 0, 8))
    for k in range(4):
        cp(part("IC", k, 512), part("IT", k, 512))
    options()

    for t in range(RO):
        last, late = t == RO - 1, t > 0
        wide = late and CWS is not None
        for a, b in COP:
            if wide:
                gather(col("CW", 16 * a, 16 * b), IND(IW, col("OL", a, b)), a not in CWS)
                if a >= NV // 4:
                    cp(col("COA", 16 * a, 16 * b), col("CW", 16 * a, 16 * b))
            else:
                cp(col("COA", 16 * a, 16 * b), IND(IW if late else col("IT", 0, W), col("OL", a, b)))
        for k in range(4):
            cp(part("C2", k, NV), col("CW" if wide else "COA", k, 256, 4))
        gather(whole("XC2"), IND(XW, GL), False)
        if N2V:
            for j in range(4):
                copy(col("X4", j, 4 * N2V, 4), col("XC2", 0, N2V), N2V)
            for j in range(4):
                copy(col("XR", j, 16 * N2V, 4), col("X4", 0, 4 * N2V), 4 * N2V)
        if wide:
            copy(whole("C0"), whole("CW"), 512)
        else:
            cp(whole("C0" if late else "C16"), whole("COA"))
        for q in range(16):
            mm(col("B1", 64, 72), cb("W0", 15 - q, 143 - q), col("R", q, L, 16), q == 0, q == 15)
        cp(whole("OL0"), col("B1", 64, 72))
        gather(whole("X0"), IND(XW, col("OL0", 0, 8)), "X0" in ONV)
        mm(part("PS", 1), cb("IDN"), whole("X0"), True, False)
        mm(part("PS", 1), cb("NID"), whole("A"), False, True)
        act(whole("AA"), part("PS", 1), AF.Abs)
        for l in range(L - NV):
            act(part("H", l, 64), IND(XW, part("COA", NV + l, 4)), AF.Abs, bias=col("A", NV + l), scale=-1.0)
        for h in range(2):
            for k in range(4):
                tt(part("D", 4 * h + k, 512), IND(whole("XF"), part("C2", 2 * k + h, 32)), part("AR", h, 512), MAX)
        for c, bank in enumerate(("BV", "DL")):
            mm(col(bank, 0, 256), cb("NTH", L * t, L * t + L, rows=R16), cb("THS", rows=R16), True, False)
            for k in range(4):
                mm(V(bank, sl(32 * k, 32 * k + 32), sl(0, 256)), part("A", c, 32), cb("AS"), False, False)
            for p in range(16):
                mm(col(bank, p, 256, 16), col("D", 2048 * c + p, 2048 * c + 2048, 16), cf("WS"), False, p == 15)
            ts(part("RR", c), part(bank, 1), ROUND, ADD, ROUND, SUB)
            act(part("AD", c), part("RR", c), AF.Abs, bias=-256.0, scale=1 / FINE)
            tt(part("SV", c), part(bank, 0), part("RR", c), ADD)
        if late:
            mm(col("BS", 0, 256), cb("NKID"), col("C0", 256, 512), True, False)
            mm(col("BV", 0, 256), cb("NKID"), col("C0", 0, 256), True, False)
        for k in range(4):
            mm(part("BV", k // 2), part(("AD", "SV")[k % 2], k // 2), cb("PRM"), k == 0 and not late, k == 3 and not late)
        for j in range(4):
            for p in range(16):
                mm(part("BS", j, 64), cb("WIDE", 15 - p, 143 - p), col("H", 1024 * j + p, 1024 * j + 1024, 16),
                   j == p == 0 and not late, j == 3 and p == 15 and not (late and LASTC))
                if late and not LASTC and j == p == 0:
                    held = len(ops)
        if late:
            rest = ops[held:] if not LASTC else []
            del ops[len(ops) - len(rest):]
            abroad(t - 1)
            act(whole("RP"), whole("DP"), AF.Abs)
            for k in range(4):
                mm(part("PW", 0), cb("BO", 96 - 32 * k, 224 - 32 * k), col("RP", k, 512, 4), k == 0, k == 3)
            act(part("LE2", 0), part("PW", 0), AF.Sign, bias=cf("THC", t, t + 1))
            mm(part("PW", 0), cb("IDN"), part("LE2", 0), True, False)
            for k in range(4):
                mm(part("PW", 0), cb("NBO4", 96 - 32 * k, 224 - 32 * k), col("C0", k, 512, 4), False, False)
            for h in range(CN):
                cp(part("C16", h, 512 // CN), IND(IW, part("OL", h, 32 // CN)))
            mm(col("BV", 0, 256), cb("KID"), col("C16", 0, 256), False, True)
            mm(col("BS", 0, 256), cb("KID"), col("C16", 256, 512), False, LASTC)
            ops.extend(rest)
            for k in range(4):
                mm(part("PW", 0), cb("BO4", 96 - 32 * k, 224 - 32 * k), col("C16", k, 512, 4), False, k == 3)
            act(part("LE2", 1), part("PW", 0), AF.Sign, scale=-1.0)
        act(col("LE", 256, 512), col("BS", 0, 256), AF.Sign, bias=cf("THG", t, t + 1))
        alike(1)
        ts(col("T16", 8, 16), ki(4), -float(W), ADD)
        gather(whole("CF2"), IND(IW if late else col("IT", 0, W), GL), "CF2" in ONV or not late)
        if not late:
            ops[-1].update(other=None, e="v")
        if "CO2" in ONV:
            cp(whole("CO2"), IND(IW if late else col("IT", 0, W), GL))
        else:
            cp(whole("CO2"), whole("CF2"))
        for a in range(0, L, G2N):
            o, i = col("G2", 16 * a, 16 * (a + G2N)), IND(XW, col("CO2", a, a + G2N))
            if MAX2:
                tt(col("D2", 16 * a, 16 * (a + G2N)), IND(whole("XF"), col("CO2", a, a + G2N)), col("XR", 16 * a, 16 * (a + G2N)), MAX)
            elif a < N2V:
                tt(o, i, col("XR", 16 * a, 16 * (a + G2N)), SUB)
            else:
                gather(o, i, a in G2V)
        for a in range(0, N2V * (not MAX2), H2N):
            act(V("H2", ALL, sl(a, a + H2N), ALL), col("G2", 16 * a, 16 * (a + H2N)), AF.Abs)
        at = 0
        for a, b in PARTS:
            for k in range(3):
                mm(col("DL", at + k * (b - a), at + (k + 1) * (b - a)), cb("DEL"), col("C16", 4 * a + k + 1, 4 * b, 4))
            at += 3 * (b - a)
        act(whole("AB"), col("DL", 0, 384), AF.Abs)
        act(part("LE", 0, 256), col("BV", 0, 256), AF.Sign, bias=-0.5)
        for b, bank in enumerate(EARLY):
            apart(b, bank)
        FC = col("FC", 3, 512, 4)
        for h, (a, b) in enumerate(PARTS):
            n, end = b - a, b == L
            o = col("PW", L + a, L + b)
            mm(o, cb("ONES", rows=R1), cb("THREE", 0, n, rows=R1), True, False)
            for k in range(2 * late):
                mm(o, cb("IDN"), col("LE2", L * k + a, L * k + b), False, False)
            for k in range(4):
                mm(o, cb("BO", 96 - 32 * k, 224 - 32 * k), col("LE", 4 * a + k, 4 * b, 4), False, k == 3)
            act(col("SVG", a, b), o, AF.Sign)
            bank = FCB[h]
            mm(col(bank, 0, 4 * n), cb("IDN"), col("C16", 4 * a, 4 * b), True, False)
            for k in range(4):
                mm(col(bank, k, 4 * n, 4), cb("PEN", L * k, L * k + L), col("SVG", a, b), False, k == 3)
            scan(col("FC", 4 * a, 4 * b), cb("RS4", 0, 4 * n), col(bank, 0, 4 * n), 0.0, MAX, MIN)
            alike(2 if end else 4)
            if end:
                far(2)
                mm(col("PS", 0, 48), whole("R"), cb("XSEL"), True, False)
                mm(col("PS", L, L + 144), whole("SVG"), cb("RANK"), False, False, True)
                mm(col("PS", L, L + 144, 9), whole("R"), cb("XSEL", 0, 48, 3), False, False)
                mm(col("PS", 0, 48), whole("SVG"), cb("K2"), False, False)
                mm(col("PS", L, L + 144), FC, cb("PERM"), False, True)
                gather(col("M3", 0, 432, 3), col("PS", L, L + 144), False)
                for k in (1, 2):
                    gather(col("M3", k, 432, 27), col("PS", k, 48, 3), False)
                mm(col("PW", 0, 432), whole("SVG"), cb("GW"), True, False)
            two = L // n
            for j in range(8 // two):
                bank, rows = EEB[h][j], range(two * j, two * j + two)
                for pp in rows:
                    for k in range(3):
                        mm(part(bank, 3 * (pp % two) + k, n), cb("SIG"), col("C16", 4 * a + k + 1, 4 * b, 4), k == pp % two == 0, False)
                for pp in rows:
                    for k in range(3):
                        mm(part(bank, 3 * (pp % two) + k, n), cb("FSEL", L * pp, L * pp + L), col("FC", 4 * a + 3, 4 * b, 4), False, k == 2 and pp == rows[-1])
                act(col(bank, 0, 384), col(bank, 0, 384), AF.Abs)
                for pp in rows:
                    tt(V("EE", ALL, pp, ALL, sl(a, b)), col("AB", 3 * a, 3 * b), part(bank, pp % two, 3 * n), EQ)
                    for k in range(3 * end):
                        mm(col("PW", 3 * (pp + 1) + k, 432, 27), V("EE", ALL, pp, k, ALL), cb("WM"), False, pp == 7 and k == 2)
        alike(3)
        scan(whole("S1"), whole("M3"), col("PW", 0, 432), BIG, MIN, MAX)
        scan(whole("S2"), cf("RST"), col("S1", 2, 432, 3), 0.0, ADD, MIN)
        named = col("S2", 17, 144, 18)
        ts(col("LB", 0, 8), named, float(NONE * RK), ALU.is_lt)
        ts(ki(0), named, RK - 1, AND)
        ts(ki(3), named, 4095, AND)
        ts(ki(1), named, 1, AND)
        for b, bank in enumerate(LATER[:NB2 - len(EARLY)]):
            apart(len(EARLY) + b, bank)
        far(3)
        for k in range(8):
            mm(col("DL", 0), cb("O16"), col("LB", k), k == 0, k == 7)
        mm(col("PS", 0, 8), cb("TRIP"), col("LB", 0, 8))
        if "NM" in ONV:
            spread("NM", ki(0))
        else:
            cp(col("ZT", 0, 8), ki(0))
            for k in range(8):
                times(part("NM", k, 16), cb("MK", 0, 16), col("ZT", k))
        mm(col("BV", 0, 8), whole("NM"), cf("BOF"))
        ts(whole("NL"), col("BV", 0, 8), float(OFF + W), MIN)
        act(whole("XN"), IND(whole("X"), col("NL", 0, 8)), AF.Copy)
        tt(ki(5), ki(3), ki(4), MUL)
        ts(tf(0), ki(1), -2.0, MUL, 1.0 - W - OFF, ADD)
        tt(col("T16", 0, 8), tf(0), ki(3), ADD)
        ts(ki(7), ki(5), col("DL", 0), ADD)
        ts(ki(4), ki(7), 4, SHR, W - 1, AND)
        if EQV[0] == 2:
            ts(col("LB", 8, 16), named, float(NONE * RK), ALU.is_lt, -1.0, MUL)
            mm(col("BS", 0, 8), cb("ONES", rows=R1), cb("MAG", 0, 8, rows=R1), True, False)
            for k in range(8):
                mm(col("BS", k), part("EQ2", k), col("LB", 8 + k), False, False)
            mm(col("BS", 0, 8), cb("ONES", rows=R1), cb("MAG", 8, 16, rows=R1), False, False, True)
            for k in range(8):
                mm(col("BS", k), part("EQ2", k), col("LB", k), False, False)
            mm(col("BS", 0, 8), whole("CMG"), cb("BOS"), False, False, True)
            mm(col("BS", 0, 8), cb("K4"), col("LB", 0, 8), False, True)
            act(whole("ZZ"), col("BS", 0, 8), AF.Relu, bias=pd_(26), scale=-BIG)
        else:
            mm(col("BS", 0, 8), whole("CMG"), BO, True, False)
            mm(col("BS", 0, 8), cb("K4"), col("LB", 0, 8), False, False)
            for k in range(8):
                mm(col("BS", k), part("EQ2", k), col("LB", k), False, k == 7)
            act(whole("ZZ"), col("BS", 0, 8), AF.Relu, bias=pd_(26), scale=-1.0)
        for k in range(8):
            times(part("ZM", k, 16), cb("NMK"), col("ZZ", k))
        mm(col("BS", 16, 24), cf("NIF"), cf("SPARE"), True, False)
        mm(col("BS", 16, 24), whole("ZM"), cf("BOF"), False, True)
        cp(whole("SL2"), col("BS", 16, 24))
        if "DV2" in ONV:
            tt(whole("DV2"), IND(whole("NUM"), col("NL", 0, 8)), whole("CF2"), SUB)
        else:
            act(whole("DV2"), IND(whole("NUM"), col("NL", 0, 8)), AF.Copy)
            tt(whole("CF2"), part(F2B, 2), whole("CF2"), MUL)
        tt(whole("WV2"), part(F2B, 1), whole("DV2"), MUL)
        tt(IND(IS, col("SL2", 0, 8)), whole("WV2"), whole("CF2"), ADD)
        if not last:
            spread("CMT", ki(4))
            mm(col("PW", 32, 40), whole("CMT"), BO)
            mm(part("B0", 0), whole("CMT"), cb("IDN"))
            cp(GL, col("PW", 32, 40))
            cp(whole("CMG"), part("B0", 0))
            if "cT" in ONV:
                gates(ki(4))
            else:
                mm(col("PS", 16, 24), whole("CMG"), BO)
                act(whole("cT"), col("PS", 16, 24), AF.Identity, bias=-math.log(511), scale=-STEEP)
        steps = PAS and not last
        if steps:
            act(whole("PF"), col("PS", 0, 8), AF.Identity, bias=0.5, scale=-1.0)
            ts(col("T16", 16, 32), col("T16", 0, 16), -1.0, MUL)
        for k in range(8):
            if steps:
                act(V("PB", ALL, ALL, k, ALL), cb("S96"), AF.Sign, bias=col("PF", k))
            else:
                ts(V("PA", ALL, ALL, k, ALL), cb("S96", 0, 48), col("PS", k), EQ, 2.0, MUL)
        mm(col("B1", 0, 64), cb("IDN"), cb("CK"), True, False)
        for h in range(2):
            for u in range(3):
                o, end = sl(32 * h + 8 * u, 32 * h + 8 * u + 8), h == 1 and u == 2
                if steps:
                    mm(V("B1", ALL, o), V("PB", ALL, 3 + u, ALL, ALL), part("T16", 2 + h, 8), False, False)
                    mm(V("B1", ALL, o), V("PB", ALL, u, ALL, ALL), part("T16", h, 8), False, end)
                else:
                    mm(V("B1", ALL, o), V("PA", ALL, u, ALL, ALL), part("T16", h, 8), False, end)
        scan(whole("SK"), cf("RS8"), col("B1", 0, 64), 0.0, ADD, MAX)
        ts(whole("O%d" % t), col("SK", 7, 64, 8), 0.5, MUL)
        send(t)
        if not last:
            options()
        mm(part("DL", 0), cb("IDN"), whole("XN"), True, False)
        mm(part("DL", 0), cb("IDN"), whole("A"), False, True)
        mm(part("DL", 1), cb("ONES", rows=R1), cb("C1024", rows=R1), True, False)
        mm(part("DL", 1), cb("IDN"), whole("AA"), False, False)
        mm(part("DL", 1), cb("NID"), whole("XN"), False, True)
        ts(whole("AH"), part("DL", 0), 0.5, MUL, 0.25, SUB)
        tt(whole("AO" if last else "A"), whole("AH"), part("DL", 1), MAX)
        if last:
            dma("s", V("ya", ALL), whole("AO"), 0)
        else:
            widen()
    cp(whole("G16"), ki(4))
    mm(V("BS", R8, sl(256, 384)), whole("G16"), cb("IDN"))
    cp(whole("YG"), V("BS", R8, sl(256, 384)))
    dma("s", V("yg", ALL), whole("YG"), 0)
    for k in range(YCN):
        n, bank = W // YCN, YCB[k % len(YCB)]
        mm(col(bank, 0, n), cf("WT"), part("IC", k, n))
        gather(part("YC", k, n), col(bank, 0, n), k % 2)
    abroad(RO - 1)
    dma("s", V("yc", ALL), V("YC", sl(0, 128, 16), sl(0, W)), 64)
    emit(g, T, arrange(ops))
    g.wait_ge(T.sem["snt"], sent[0])
